import numpy as np, ml_dtypes
CORES = [5,29,101,125,133,157,229,253]
N = 8
BF = ml_dtypes.bfloat16
W, C, H, CAP, RO = 2048, 512, 512, 32, 5
L = C >> 2
S16 = np.arange(16)
def owner(m):
    mb = np.zeros((8, W + 1), np.int32); mb[np.arange(8)[:, None, None], m] = np.arange(C)[None, :, None]
    return mb[:, :W]
def tight(m):
    return np.take_along_axis(m, np.argsort(m >= W, axis=-1, kind="stable"), -1)
def pick(a, j):
    return np.take_along_axis(a, j[:, :, None], 2)[:, :, 0]
def fill(n, order, s):
    s = np.minimum(s, 16 - n[order]); c = np.add.accumulate(s); left = W - np.add.reduce(n); n = n.copy()
    n[order] = n[order] + np.clip(left - (c - s), 0, s)
    return n
def sizes(rng):
    a = (W // C) * rng.choice(np.array([0.5, 1.0, 1.5]))
    n = fill(np.zeros(C, np.int64), rng.permutation(C), 1 + rng.poisson(a, C))
    return fill(n, rng.permutation(C), np.full(C, 16))
def seat(rng, n):
    m = np.full((C, 16), W, np.int64); m[S16 < n[:, None]] = rng.permutation(W)
    return m
def seats(rng):
    return np.stack([np.stack([seat(rng, sizes(rng)) for g in range(8)]) for q in range(N)])
def people(rng, m):
    typ = rng.integers(0, 16, (8, 24, 16)); own = np.take_along_axis(rng.integers(0, 24, (8, C)), owner(m), 1)
    ty = np.where(rng.random((8, W)) < rng.choice(np.array([0.3, 0.7, 0.95]), (8, 1)), own, rng.integers(0, 24, (8, W)))
    v = typ[np.arange(8)[:, None], ty]
    return np.clip(v + rng.integers(-3, 4, (8, W, 16)), 0, 15)
def wrap(x, a, m, li, w):
    def turn(v): return np.ascontiguousarray(v.transpose(0, 1, 3, 2)).reshape(N, 128, -1)
    return {"x0": turn(x).astype(np.float32).astype(BF), "ac": turn(a).astype(np.int32), "ml": turn(m).astype(np.int32),
            "lims": np.repeat(li, 16, axis=1).astype(np.int32), "wt": w.reshape(N, 128, 1).astype(np.int32)}
def setup_inputs(rng):
    m = seats(rng); x = np.stack([people(rng, b) for b in m])
    li = np.stack([rng.integers(30, 130, (N, 8)), rng.integers(20, 110, (N, 8))], axis=2)
    return wrap(x, rng.integers(0, W, (N, 8, H, 16)), m, li, rng.integers(0, 256, (N, 8, 16)))
def setup_inputs_ends(rng):
    ms, xs, as_, ls = [], [], [], []
    for q in range(N):
        m = []
        for g in range(8):
            n = np.zeros(C, np.int64); n[:4] = 16; n[C - 4:] = 16; o = 4 + rng.permutation(C - 8)
            n = fill(n, o, rng.choice(np.array([1, 1, 1, 16, 16, 8]), C - 8)); n = fill(n, o, np.full(C - 8, 16)); b = seat(rng, n)
            c = C - 4 + (g + q) % 4
            for v, k in ((0, 0), (W - 1, 15)):
                at = np.argwhere(b == v)[0]; b[at[0], at[1]] = b[c, k]; b[c, k] = v
            m.append(b)
        m = np.stack(m); ty = rng.integers(0, 5, (8, C, 1, 1)); ty[:, :4] = 4; ty[:, C - 4:] = 4
        edge = ((S16 != 2) & (S16 != 15))[None, None, :, None]
        val = np.where(ty == 0, True, np.where(ty == 1, False, np.where(ty == 2, rng.random((8, C, 16, 1)) < 0.5, np.where(ty == 3, rng.random((8, C, 16, 16)) < 0.5, edge))))
        x = np.zeros((8, W + 1, 16), np.int64); x[np.arange(8)[:, None, None], m] = 15 * val
        far = rng.random((8, H, 16)) < np.where(rng.random((8, H, 1)) < 0.4, 1.1, 0.55)
        ms.append(m); xs.append(x[:, :W]); as_.append(np.where(far, (W - 1) * rng.integers(0, 2, (8, H, 16)), rng.integers(0, W, (8, H, 16))))
        ls.append(np.array([[0, 0], [0, 240], [240, 0], [240, 240]])[(np.arange(8) // 2 + q) % 4])
    w = 255 * rng.integers(0, 2, (N, 8, 16)); w[:, 3::4] = 255; w[:, 1] = 0
    return wrap(np.stack(xs), np.stack(as_), np.stack(ms), np.stack(ls), w)
def setup_inputs_corners(rng):
    ms, xs, as_, ls = [], [], [], []
    for q in range(N):
        m = []; l = []; x = rng.integers(0, 16, (8, W, 16))
        for g in range(8):
            k = (g + q) & 7; n = np.zeros(C, np.int64); o = rng.permutation(C); z = 4 * rng.permutation(L); u = o[(o & 3) != 0]
            if k < 2:
                n[z[:CAP + k]] = 16; n = fill(n, u, rng.choice(np.array([1, 4, 8, 16]), len(u))); n = fill(n, u, np.full(len(u), 16))
            elif k == 2: n[:] = W // C
            elif k == 3:
                n[:] = W // C; n[o[:3]] = 0; n[o[3:6]] = 2 * (W // C)
            elif k == 4:
                n[z[:L // 2]] = 8; n = fill(n, u, rng.choice(np.array([8, 9]), len(u)))
            elif k == 5: n = fill(n, o, np.full(C, 16))
            elif k == 6:
                n[z] = 1; n = fill(n, u, rng.choice(np.array([15, 16]), len(u)))
            else:
                n = sizes(rng); x[g] = rng.integers(0, 2, (W, 16))
            m.append(seat(rng, n)); l.append(((0, 240), (0, 240), (240, 0), (0, 0), (240, 240), (240, 0), (240, 0), (int(rng.integers(2, 14)), int(rng.integers(2, 9))))[k])
        m = np.stack(m); mb = owner(m); mode = rng.integers(0, 6, (8, H, 1)); a = rng.integers(0, W, (8, H, 16)); zero = []
        for g in range(8):
            c0 = np.nonzero((mb[g] & 3) == 0)[0]
            if len(c0) == 0: c0 = np.arange(W)
            zero.append(c0[rng.integers(0, len(c0), (H, 16))])
        a = np.where(mode == 1, a[:, :, :1], np.where(mode == 2, (W - 1) * rng.integers(0, 2, (8, H, 16)), np.where(mode == 3, np.arange(H)[None, :, None] + H * rng.integers(0, W // H, (8, H, 16)),
            np.where(mode == 4, np.stack(zero), np.where(mode == 5, a[:, :, S16 & 1], a)))))
        ms.append(m); xs.append(x); as_.append(a); ls.append(np.array(l))
    w = np.where(rng.random((N, 8, 16)) < 0.5, rng.integers(0, 256, (N, 8, 16)), rng.choice(np.array([0, 1, 255]), (N, 8, 16)))
    return wrap(np.stack(xs), np.stack(as_), np.stack(ms), np.stack(ls), w)
def setup_inputs_brim(rng):
    ms, xs, as_, ls = [], [], [], []
    for q in range(N):
        m = []; l = []; x = rng.integers(0, 16, (8, W, 16)); a = rng.integers(0, W, (8, H, 16))
        for g in range(8):
            k = (g + q) & 3; n = np.zeros(C, np.int64); o = rng.permutation(C); z = 4 * rng.permutation(L); u = o[(o & 3) != 0][:L]
            if k == 1:
                n[z] = 1; n[u] = 2; n = fill(n, o, rng.choice(np.array([0, 2, 4, 6]), C)); n = fill(n, o, 8 - n[o])
            else:
                n[z] = 4; n = fill(n, rng.permutation(np.concatenate([z, u])), rng.choice(np.array([0, 1, 4, 8, 12]), 2 * L)); n = fill(n, rng.permutation(z), np.full(L, 12))
            b = seat(rng, n)
            if k == 1:
                old = b[z, rng.integers(0, n[z])]; h = rng.permutation(H)[:L]; new = h + H * rng.integers(0, W // H, L); p = np.full(W + 1, W)
                p[old] = new; p[np.setdiff1d(np.arange(W), old)] = rng.permutation(np.setdiff1d(np.arange(W), new)); b = p[b]
                x[g] = rng.integers(1, 16, (W, 16)); x[g, new] = 0
                x[g, b[u, 0]] = np.where(S16 == rng.integers(0, 16, (L, 1)), 0, 12); x[g, b[u, 1]] = np.where(S16 == rng.integers(0, 16, (L, 1)), 1, 12)
                a[g, h] = np.where((rng.random((L, 16)) < 0.25) & (S16 > 1), new[rng.integers(0, L, (L, 16))], np.where((S16 & 1) == 1, b[u, 0][:, None], b[np.roll(u, -1), 1][:, None]))
            elif k == 2:
                p = np.argsort(rng.random((L, 16)), axis=1); j = np.argsort(rng.random((L, 4)), axis=1); x[g] = rng.integers(1, 10, (W, 16))
                x[g, b[z, j[:, 0]]] = 0; x[g, b[z, j[:, 1]]] = np.where(p < 10, 15, np.where(p == 10, 1, 0)); x[g, b[z, j[:, 2]]] = np.where(p >= 6, 15, np.where(p < 2, 1, 0))
            elif k == 3:
                ty = rng.integers(0, 3, (W, 1)); x[g] = np.where(ty == 0, 15, np.where((ty == 1) & (S16 == rng.integers(0, 16, (W, 1))), 1, 0))
            m.append(b); l.append(((0, 0), (240, 0), (0, 0), (0, 239 + (g >> 2)))[k])
        ms.append(np.stack(m)); xs.append(x); as_.append(a); ls.append(np.array(l))
    return wrap(np.stack(xs), np.stack(as_), np.stack(ms), np.stack(ls), rng.integers(0, 256, (N, 8, 16)))
def setup_inputs_ties(rng):
    m = seats(rng); two = np.array([[0, 1], [7, 8], [0, 15], [3, 6]])[(np.arange(8)[None, :] + np.arange(N)[:, None]) & 3]
    pool = rng.integers(0, 2, (N, 8, 12, 16)); pool = np.where(pool == 1, two[:, :, None, 1:], two[:, :, None, :1])
    kind = rng.integers(0, 12, (N, 8, W)); x = pool[np.arange(N)[:, None, None], np.arange(8)[None, :, None], kind]
    step = two[:, :, 1] - two[:, :, 0]; li = np.stack([step * rng.integers(5, 14, (N, 8)), step * rng.integers(3, 11, (N, 8))], axis=2)
    known = rng.integers(0, W, (N, 8, 40)); k = rng.integers(0, 40, (N, 8, H * 16))
    a = np.where(rng.random((N, 8, H, 1)) < 0.5, np.take_along_axis(known, k, 2).reshape(N, 8, H, 16), rng.integers(0, W, (N, 8, H, 16)))
    return wrap(x, a, m, np.minimum(li, 240), rng.integers(0, 256, (N, 8, 16)))
def setup_inputs_spread(rng):
    x = rng.integers(0, 2 ** rng.integers(0, 5, (N, 8, W, 1)), (N, 8, W, 16)); m = []
    for q in range(N):
        for g in range(8):
            n = fill(np.zeros(C, np.int64), rng.permutation(C), rng.choice(np.array([0, 1, 1, 2, 3, 5, 16]), C)); m.append(seat(rng, fill(n, rng.permutation(C), np.full(C, 16))))
    a = np.minimum((W * rng.random((N, 8, H, 16)) ** 3).astype(np.int64), W - 1); w = np.minimum((np.exp2(8 * rng.random((N, 8, 16))) - 1).astype(np.int64), 255)
    return wrap(x, a, np.stack(m).reshape(N, 8, C, 16), rng.integers(0, 241, (N, 8, 2)), w)
def check_inputs(d):
    bad = []
    for k, lo, hi in (("x0", 0, 15), ("ac", 0, W - 1), ("ml", 0, W), ("lims", 0, 240), ("wt", 0, 255)):
        a = np.asarray(d[k]).astype(np.float64)
        if not (np.min(a) >= lo and np.max(a) <= hi): bad.append("range of " + k)
    a = np.asarray(d["x0"]).astype(np.float64)
    if np.any(a != np.floor(a)): bad.append("whole numbers in x0")
    m = np.asarray(d["ml"]).astype(np.int64).reshape(N, 8, 16, C)
    if np.any(np.sort(m.reshape(N, 8, 16 * C), axis=-1) != np.minimum(np.arange(16 * C), W)): bad.append("every agent once in ml")
    if np.any((m[:, :, 1:] < W) & (m[:, :, :-1] >= W)): bad.append("members before empty slots in ml")
    l = np.asarray(d["lims"]).reshape(N, 8, 16, 2)
    if np.any(l != l[:, :, :1]): bad.append("lims alike in a group")
    return bad
def reference(x0, ac, ml, lims, wt):
    X = np.zeros((N, 8, W + 1, 16), np.int32)
    X[:, :, :W] = x0.astype(np.float32).astype(np.int32).reshape(N, 8, 16, W).transpose(0, 1, 3, 2)
    A = ac.reshape(N, 8, 16, H).transpose(0, 1, 3, 2); M = np.array(ml.reshape(N, 8, 16, C).transpose(0, 1, 3, 2))
    lim = lims.reshape(N, 8, 16, 2)[:, :, 0].astype(np.int64); wv = wt.reshape(N, 8, 16).astype(np.int64)
    G = np.arange(8)[:, None]; G3 = G[:, :, None]; low = np.tri(L, L, -1, dtype=bool); z = np.zeros(N, np.int64)
    for t in range(RO):
        cl = t & 3; lane = 4 * np.arange(L) + cl; M2 = M.copy(); X2 = X.copy(); z2 = np.zeros(N, np.int64); go = []
        for r in range(N):
            x, m, mb = X[r], M[r], owner(M[r])
            own = m[:, lane]; here = own < W; live = here[:, :, 0]; tx = x[G3, own]; U = np.max(tx, axis=2)
            gr = np.where(here, np.sum(U[:, :, None] - tx, axis=3), -1); s = pick(own, np.argmax(gr, axis=2)); xs = x[G, s]
            ds = np.where(here, np.sum((tx - xs[:, :, None]) ** 2, axis=3), -1)
            an = A[r][G, s & (H - 1)]; ad = mb[G3, an]; fit = live[:, :, None] & ((ad & 3) != cl); has = np.any(fit, axis=2)
            d = pick(ad, np.argmin(np.where(fit, np.sum((x[G3, an] - xs[:, :, None]) ** 2, axis=3), 2 ** 20), axis=2))
            first = ~np.any((d[:, :, None] == d[:, None, :]) & has[:, None, :] & low, axis=2)
            dm = m[G, d]; dh = dm < W; td = x[G3, dm]; V = np.maximum(U, np.max(td, axis=2))[:, :, None]
            worst = np.maximum(np.max(np.where(here, np.sum(V - tx, axis=3), 0), axis=2), np.max(np.where(dh, np.sum(V - td, axis=3), 0), axis=2))
            mer = has & first & (np.sum(here, axis=2) + np.sum(dh, axis=2) <= 16) & (worst <= lim[r, :, :1] + (z[r] & 15))
            want = live & ~mer & (np.max(gr, axis=2) > lim[r, :, 1:])
            xg = x[G, pick(own, np.argmax(ds, axis=2))]; away = here & (np.sum((tx - xg[:, :, None]) ** 2, axis=3) < ds)
            vacant = m[:, :, 0] >= W; free = np.argsort(~vacant, axis=1, kind="stable")
            k = np.add.accumulate(want.astype(np.int64), axis=1) - want.astype(np.int64)
            spl = want & (k < np.sum(vacant, axis=1)[:, None]); e = np.take_along_axis(free, k, 1)
            both = tight(np.concatenate([own, dm], axis=2))[:, :, :16]
            M2[r][:, lane] = np.where(mer[:, :, None], both, np.where(spl[:, :, None], tight(np.where(away, W, own)), own))
            a, b = np.nonzero(mer); M2[r][a, d[a, b]] = W
            a, b = np.nonzero(spl); M2[r][a, e[a, b]] = tight(np.where(away, own, W))[a, b]
            idle = live & ~mer & ~spl; a, b = np.nonzero(idle & (np.add.accumulate(idle.astype(np.int64), axis=1) <= CAP))
            go.append((a, s[a, b], xs[a, b])); z2[r] = np.sum(mer)
        for r in range(N):
            q = (r + 1 + t % (N - 1)) % N; a, sa, xa = go[r]
            v = np.sum(wv[q][a] * xa, axis=1) & (W - 1); mm = M2[q][a, owner(M2[q])[a, v]]; y = X[q][a[:, None], mm]
            j = np.argmin(np.where(mm < W, np.sum((y - xa[:, None]) ** 2, axis=2), 2 ** 20), axis=1)
            X2[r][a, sa] = (xa + y[np.arange(len(a)), j]) >> 1
        X, M, z = X2, M2, z2
    return {"ym": np.ascontiguousarray(M.transpose(0, 1, 3, 2)).reshape(N, 128, C).astype(np.float32),
            "yx": np.ascontiguousarray(X[:, :, :W].transpose(0, 1, 3, 2)).reshape(N, 128, W).astype(np.float32).astype(BF)}

@@ -1,0 +1,813 @@
+from concourse.mybir import dt, AluOpType as A, AxisListType as AX_, ActivationFunctionType as F
+
+RO = 5
+BIG = 1.0e9
+S, B, H, I, U = "float32", "bfloat16", "float16", "int32", "uint16"
+
+SCRATCH = {}
+
+
+def _sb(names, cols, dtype):
+    for n in names.split():
+        SCRATCH[n] = ("sbuf", [128, cols], dtype)
+
+
+_sb("X", 2304, B)
+_sb("AC4", 2064, I)
+_sb("MI", 512, I)
+_sb("LI", 2, I)
+_sb("WI", 1, I)
+_sb("W", 664, S)
+_sb("OT", 4112, S)
+_sb("VE VG", 2048, S)
+_sb("VF", 128, S)
+_sb("ZE MS", 2048, B)
+_sb("V0 Jf J2f t512a t512b t512c", 512, S)
+_sb("J3", 512, I)
+_sb("Jh", 144, H)
+_sb("J4h J15h", 128, H)
+_sb("MIN", 128, B)
+_sb("FM", 1024, B)
+_sb("T US Z REP SQ AX OG DT", 2048, B)
+_sb("DS", 2176, S)
+_sb("OWN AN DM CREP MVO", 128, U)
+_sb("INO", 512, U)
+_sb("OWNH DMH DSE R16 ID16 ID16x NID16 TRI D1R PD KB KV SEL5 SR PS MR MP WR SPR SPP IR VR VP NVP KP RP EVH Q1 Q2 "
+    "A1 A2 A3 MD NR NP BR BP XP", 128, H)
+_sb("ZS ZD ZN ZBB ZM ZW ZSP ZI ZV ZQ QR8 QP", 128, H)
+_sb("EO ED IDB NIDB BD NBD BT IDE NIDE ID1K CK CKP KA DEAD HWB WTB ONEB Vv WV XB SQS SQB NV", 128, B)
+_sb("ONE16", 128, H)
+_sb("Y", 144, B)
+_sb("S1 S2 S3 SB W16L WL PW2 lv mb L1 cl SM q1a q2a STM EV ELS DUM f128a f128b VFP QPF QSC", 128, S)
+_sb("Pa Pb Mi Aa", 264, I)
+_sb("STI", 256, I)
+_sb("DG", 1024, H)
+_sb("AB ABS", 1024, B)
+_sb("SH", 2048, B)
+_sb("PIi", 4, I)
+_sb("PC", 32, S)
+_sb("J", 512, I)
+_sb("J4 J15", 128, I)
+_sb("blk16 blk128 blkN blkE blkI blk32 blkm blk2k CI C528", 8, H)
+_sb("blkf", 8, S)
+_sb("C640 w32k w8k w2k w512 w1 w2 og0 og1 og2 og3 SEL0", 8, B)
+_sb("k8 sv8 sx8 b8 bb8 a8 d8 q8 qq8", 8, I)
+_sb("lim8 lim28 thr8 live8 gr8 wp8 has8 dp8 nD d18 mn8 tm8 f8 sz8 P0 c8 sp8 ms8 v8 nf8 nfs8", 8, S)
+_sb("S16 B16 D16 N16 K16 TG16 RT16 XT16", 8, U)
+_sb("NFH", 8, H)
+_sb("VC", 512, B)
+_sb("VTb", 32, B)
+_sb("CSs CVp rk", 32, S)
+_sb("CVn", 32, H)
+_sb("F16", 32, U)
+_sb("FREE", 1168, S)
+_sb("mc", 4, S)
+_sb("mci", 4, I)
+_sb("RESW", 160, I)
+_sb("HO EH", 32, B)
+_sb("HL", 32, U)
+_sb("VI VI2", 2, I)
+_sb("VV16 H16 J16", 2, U)
+_sb("QZ QRp QD QS", 512, B)
+_sb("hs", 32, S)
+_sb("YM", 512, S)
+for _t in range(RO):
+    _sb("XV%d" % _t, 160, B)
+    _sb("QI%d" % _t, 32, B)
+    _sb("SN%d RS%d" % (_t, _t), 32, I)
+_ARENA = {}
+
+
+def _pack():
+    keep, pos = {}, {}
+    big = ("X", "T", "W", "XV", "QI", "SN", "RS")
+    for n, (w, sh, d) in SCRATCH.items():
+        if n in ("X", "T", "W", "AC4", "OT", "VF", "FREE", "RESW", "DS", "QD", "WV") or n[:2] in ("XV", "QI", "SN", "RS"):
+            keep[n] = (w, sh, d)
+            _ARENA[n] = (n, 0, sh[1], d)
+        else:
+            c = -(-sh[1] // 16) * 16
+            o = pos.get(d, 0)
+            _ARENA[n] = ("ar_" + d, o, sh[1], d)
+            pos[d] = o + c
+    for d in pos:
+        keep["ar_" + d] = ("sbuf", [128, pos[d]], d)
+    return keep
+
+
+SCRATCH = _pack()
+for _k in range(8):
+    SCRATCH["p%d" % _k] = ("psum", [128, 512], S)
+    _ARENA["p%d" % _k] = ("p%d" % _k, 0, 512, S)
+SEMAPHORES = ["v", "p", "s", "k"] + ["ld%d" % i for i in range(8)] + ["st0", "st1"]
+for _t in range(RO):
+    SEMAPHORES += ["rq%d" % _t, "rs%d" % _t, "lq%d" % _t, "ls%d" % _t, "fq%d" % _t, "fs%d" % _t, "mq%d" % _t, "ms%d" % _t]
+
+
+def _mask(topo, a, b):
+    es = topo.engines(a, b)[:8]
+    return sum(1 << e for e in es), len(es)
+
+
+def _relay(topo, a, b, which):
+    if topo.may_write(a, b):
+        return None
+    c = [h for h in topo.cores_of(a) if h != a and topo.may_write(h, b)]
+    c.sort(key=lambda h: (topo.die(h) != topo.die(a), h))
+    return c[which % len(c)]
+
+
+def _relay_program(g, core, T, topo):
+    used = []
+    for t in range(RO):
+        for r in range(8):
+            a, b = T.cores[r], T.cores[(r + 1 + t % 7) % 8]
+            for (x, y, buf, arr, fwd, loc, which) in ((a, b, "QI", "rq", "fq", "mq", 0), (b, a, "RS", "rs", "fs", "ms", 1)):
+                if _relay(topo, x, y, which) == core:
+                    _, n = _mask(topo, x, core)
+                    m, n2 = _mask(topo, core, y)
+                    rid, pid = topo.addr(y, core)
+                    g.wait_ge(T.sem["%s%d" % (fwd, t)], n)
+                    g.remote_dma(T["%s%d" % (buf, t)][:], T["%s%d" % (buf, t)][:], T.sem["%s%d" % (arr, t)],
+                                 T.sem["%s%d" % (loc, t)], pid, rid, m)
+                    used.append((T.sem["%s%d" % (loc, t)], n2))
+    for s, n in used:
+        g.wait_ge(s, n)
+
+
+def rank_program(g, core, T, topo):
+    rank = T.rank_of(core)
+    if rank is None:
+        _relay_program(g, core, T, topo)
+        return
+    E = {"v": g.vector, "p": g.tensor, "s": g.scalar, "k": g, "y": g.sync}
+    cnt = {"v": 0, "p": 0, "s": 0, "k": 0}
+    known = {e: {} for e in E}
+    snap = {}
+    log = {}
+    total = {}
+
+    def u(name, lo=0, hi=None, st=1, p=None):
+        buf, o, n, _d = _ARENA[name]
+        hi = n if hi is None else hi
+        a, b = o + lo, o + hi
+        rows = slice(None) if p is None else slice(p[0], p[1])
+        t = T[buf]
+        ap = t[rows, a:b:st] if st != 1 else t[rows, a:b]
+        return (ap, [(buf, a, b)])
+
+    def ix(win, off):
+        return (win[0].indirect(off[0]), win[1] + off[1])
+
+    def need(e, reads, writes):
+        w = {}
+
+        def add(sem, val):
+            if w.get(sem, 0) < val:
+                w[sem] = val
+        for kind, lst in ((0, reads), (1, writes)):
+            for (b, lo, hi) in lst:
+                psum = len(b) == 2 and b[0] == "p"
+                for (l2, h2, e2, sem, val, wr) in log.get(b, ()):
+                    if psum:
+                        if e2 == e:
+                            if not (wr and e != "p") or (kind == 1 and not wr) or not (lo < h2 and l2 < hi):
+                                continue
+                        add(sem, val)
+                    elif lo < h2 and l2 < hi and (kind or wr):
+                        if e2 == e and e in ("v", "s", "p") and not wr:
+                            continue
+                        add(sem, val)
+        return w
+
+    def wait(e, w):
+        for sem in w:
+            if known[e].get(sem, 0) < w[sem]:
+                E[e].wait_ge(T.sem[sem], w[sem])
+                known[e][sem] = w[sem]
+                for s2, v2 in snap.get((sem, w[sem]), {}).items():
+                    if known[e].get(s2, 0) < v2:
+                        known[e][s2] = v2
+
+    def note(e, reads, writes, sem, val):
+        d = dict(known[e])
+        d[sem] = max(d.get(sem, 0), val)
+        snap[(sem, val)] = d
+        total[sem] = val
+        for (b, lo, hi) in writes:
+            old = log.get(b, [])
+            log[b] = [x for x in old if not (lo <= x[0] and x[1] <= hi)] + [(lo, hi, e, sem, val, True)]
+        for (b, lo, hi) in reads:
+            old = log.get(b, [])
+            log[b] = [x for x in old if not (x[2] == e and not x[5] and lo <= x[0] and x[1] <= hi and x[3] == sem)] + [(lo, hi, e, sem, val, False)]
+
+    def op(e, fn, outs, ins, dma=None):
+        rd = [r for x in ins for r in x[1]]
+        wr = [r for x in outs for r in x[1]]
+        wait(e, need(e, rd, wr))
+        i = fn()
+        if dma:
+            i.then_inc(T.sem[dma], 16)
+            note(e, rd, wr, dma, 16)
+        else:
+            cnt[e] += 1
+            i.then_inc(T.sem[e], 1)
+            note(e, rd, wr, e, cnt[e])
+
+    def _c(x):
+        return x[0] if isinstance(x, tuple) else x
+
+    def _r(*xs):
+        return [x for x in xs if isinstance(x, tuple)]
+
+    v, sc = g.vector, g.scalar
+
+    def cp(o, i, scatter=None):
+        op("v", lambda: v.tensor_copy(o[0], i[0]), [o], [i] + (scatter or []))
+
+    def ts(o, i, s1, o1, s2=None, o2=None):
+        if o2 is None:
+            op("v", lambda: v.tensor_scalar(o[0], i[0], _c(s1), None, o1), [o], [i] + _r(s1))
+        else:
+            op("v", lambda: v.tensor_scalar(o[0], i[0], _c(s1), _c(s2), o1, o2), [o], [i] + _r(s1, s2))
+
+    def tt(o, a, b, o1):
+        op("v", lambda: v.tensor_tensor(o[0], a[0], b[0], o1), [o], [a, b])
+
+    def scan(o, a, b, o1, o2):
+        op("v", lambda: v.tensor_tensor_scan(o[0], a[0], b[0], 0.0, o1, o2), [o], [a, b])
+
+    def fill(o, c):
+        op("v", lambda: v.memset(o[0], c), [o], [])
+
+    def act(o, i, f, scale=None, bias=None):
+        kw = {}
+        if scale is not None:
+            kw["scale"] = _c(scale)
+        if bias is not None:
+            kw["bias"] = _c(bias)
+        op("s", lambda: sc.activation(o[0], i[0], f, **kw), [o], [i] + _r(scale, bias))
+
+    def mm(items):
+        rd = [r for x in items for y in x[1:] for r in y[1]]
+        wr = [r for x in items for r in x[0][1]]
+        wait("p", need("p", rd, wr))
+        n = len(items)
+        for j, (o, a, b) in enumerate(items):
+            i = g.tensor.matmul(o[0], a[0], b[0], j == 0, j == n - 1)
+        cnt["p"] += 1
+        i.then_inc(T.sem.p, 1)
+        note("p", rd, wr, "p", cnt["p"])
+
+    def dma(e, o, i, sem):
+        op(e, lambda: E[e].dma_start(o[0], i[0]), [o], [i], dma=sem)
+
+    def ext(ap, name):
+        return (ap, [(name, 0, 1)])
+
+    def arrived(e, name, sem, n):
+        if known[e].get(sem, 0) < n:
+            E[e].wait_ge(T.sem[sem], n)
+            known[e][sem] = n
+        total[sem] = n
+
+    def send(dst, buf_src, buf_dst, sem, fwd, loc, which):
+        to = _relay(topo, core, dst, which)
+        d = dst if to is None else to
+        m, n = _mask(topo, core, d)
+        rid, pid = topo.addr(d, core)
+        name = _ARENA[buf_src][0]
+        wait("k", need("k", [(name, 0, 32)], []))
+        g.remote_dma(T[buf_dst][:], T[buf_src][:, 0:32], T.sem[sem if to is None else fwd], T.sem[loc], pid, rid, m)
+        total[loc] = n
+
+    def landed_n(src, which):
+        via = _relay(topo, src, core, which)
+        return _mask(topo, src if via is None else via, core)[1]
+
+    def hold(o, z):
+        scan(o, u("MS", 0, 128), z, A.mult, A.add)
+
+    def k16(name, k, n=128, p=None):
+        return u(name, k, n, 16, p)
+
+    def sums(ps, base, src, w, p=None):
+        return [(u(ps, base + k, base + 128, 16, p), u(src, k, None, 16), u(w)) for k in range(16)]
+
+    fill(u("X", 0, 16), 0.0)
+    fill(u("X", 2048, 2304), 0.0)
+    fill(u("AC4", 0, 8), 0)
+    dma("y", u("MI"), ext(T.ml[:], "in_ml"), "ld0")
+    op("k", lambda: g.iota(u("PIi", 0, 1)[0], [[0, 1]], 0, 1), [u("PIi", 0, 1)], [])
+    op("k", lambda: g.iota(u("J")[0], [[1, 512]], 0, 0), [u("J")], [])
+    dma("s", u("X", 1, 2049), ext(T.x0[:], "in_x"), "ld1")
+    dma("y", u("LI"), ext(T.lims[:], "in_l"), "ld2")
+    dma("s", u("WI"), ext(T.wt[:], "in_w"), "ld3")
+    for q in range(4):
+        dma("y", u("AC4", 1 + 512 * q, 513 + 512 * q), ext(T.ac[:], "in_a"), "ld%d" % (4 + q))
+    op("k", lambda: g.iota(u("J2f")[0], [[1, 128], [0, 4]], 0, 0, allow_small_or_imprecise_dtypes=True), [u("J2f")], [])
+    op("k", lambda: g.iota(u("J3")[0], [[0, 128], [1, 4]], 0, 0), [u("J3")], [])
+    op("k", lambda: g.iota(u("Jf")[0], [[1, 512]], 1, 0, allow_small_or_imprecise_dtypes=True), [u("Jf")], [])
+    op("k", lambda: g.iota(u("OT", 0, 2064)[0], [[0, 2064]], 0, 0, allow_small_or_imprecise_dtypes=True), [u("OT", 0, 2064)], [])
+    op("k", lambda: g.iota(u("Z")[0], [[0, 2048]], 0, 0, allow_small_or_imprecise_dtypes=True), [u("Z")], [])
+
+    fill(u("MS"), 1.0)
+    fill(u("MS", 0, None, 16), 0.0)
+    fill(u("ZE"), 0.0)
+    fill(u("MIN"), -BIG)
+    fill(u("MIN", 0, None, 16), BIG)
+    fill(u("W", 0, 8), 0.0)
+    fill(u("W", 512, 664), 0.0)
+    J, J4, J15 = u("Jh", 0, 128), u("J4h"), u("J15h")
+
+    def col(n):
+        return u("PC", n, n + 1)
+    P, P4, P15 = col(0), col(1), col(2)
+    ts(u("PIi", 1, 2), u("PIi", 0, 1), 4, A.logical_shift_right)
+    ts(u("PIi", 2, 3), u("PIi", 0, 1), 15, A.bitwise_and)
+    cp(u("PC", 0, 3), u("PIi", 0, 3))
+    ts(u("J4"), u("J", 0, 128), 4, A.logical_shift_right)
+    ts(u("J15"), u("J", 0, 128), 15, A.bitwise_and)
+    cp(u("Jh"), u("J", 0, 144))
+    cp(J4, u("J4"))
+    cp(J15, u("J15"))
+    ts(col(3), P15, 4, A.is_equal)
+    ts(col(4), P15, 4, A.is_equal, 128.0, A.mult)
+    ts(col(5), P15, 5, A.is_equal)
+    ts(col(27), P15, 5, A.is_equal, 1024.0, A.mult)
+    act(u("p4"), u("J2f"), F.Identity, scale=col(3), bias=col(4))
+    act(u("p5"), u("Jf"), F.Identity, scale=col(5), bias=col(27))
+    ts(u("t512c"), u("J3"), P15, A.is_equal, 64.0, A.mult)
+    tt(u("t512c"), u("t512c"), u("p4"), A.add)
+    tt(u("V0"), u("t512c"), u("p5"), A.add)
+    ts(col(6), P15, 2064, A.add)
+    ts(u("DUM"), J, 16, A.mult, col(6), A.add)
+
+    def owners(c):
+        a, b = 128 * c, 128 * c + 128
+        ve = "VE" if c % 2 == 0 else "VG"
+        cp(u("ZE", 0, None, 16), u("V0", a, b))
+        scan(u(ve), u("MS"), u("ZE"), A.mult, A.add)
+        ts(u("p5", 0, 128), u("MI", a, b), 2048, A.is_equal)
+        tt(u("p5", 128, 256), u("DUM"), u("p5", 0, 128), A.mult)
+        tt(u("f128a"), u("W", 1 + a, 1 + b), u("p5", 128, 256), A.add)
+        cp(u("INO", a, b), u("f128a"))
+        act(ix(u("OT"), u("INO", a, b)), u(ve), F.Silu)
+
+    ts(u("p6"), u("MI"), 2048, A.is_lt)
+    ts(u("t512c"), u("MI"), 1, A.add)
+    tt(u("W", 1, 513), u("t512c"), u("p6"), A.mult)
+    owners(0)
+    ts(u("IDB"), J, P, A.is_equal)
+    ts(u("NIDB"), J, P, A.is_equal, -1.0, A.mult)
+    ts(u("ID16"), J, P, A.is_equal)
+    ts(u("NID16"), J, P, A.is_equal, -1.0, A.mult)
+    ts(u("ID16x"), J, P, A.is_equal, 16.0, A.mult)
+    ts(u("IDE"), J, P, A.is_equal, 2.0 ** 23, A.mult)
+    ts(u("NIDE"), J, P, A.is_equal, -2.0 ** 23, A.mult)
+    ts(u("ID1K"), J, P, A.is_equal, 1024.0, A.mult)
+    ts(u("BD"), J4, P4, A.is_equal)
+    ts(u("NBD"), J4, P4, A.is_equal, -1.0, A.mult)
+    ts(u("R16"), J15, P15, A.is_equal)
+    ts(u("p3", 0, 128), J15, P15, A.is_equal)
+    ts(u("CK"), J15, 2048.0, A.mult)
+    ts(u("CKP"), J15, 1.0, A.add)
+    ts(u("blk16"), u("J", 0, 8), P4, A.is_equal)
+    ts(u("blkf"), u("J", 0, 8), P4, A.is_equal)
+    ts(u("w32k"), u("BD", 0, None, 16), 32768.0, A.mult)
+    ts(u("w8k"), u("BD", 0, None, 16), 8192.0, A.mult)
+    ts(u("w2k"), u("BD", 0, None, 16), 2048.0, A.mult)
+    ts(u("w512"), u("BD", 0, None, 16), 512.0, A.mult)
+    ts(u("w1"), u("BD", 0, None, 16), 1.0, A.mult)
+    ts(u("w2"), u("BD", 0, None, 16), 2.0, A.mult)
+    owners(1)
+    for z in "ZS ZD ZN ZBB ZM ZW ZSP ZI ZV ZQ".split():
+        ts(u(z), J, 0.0, A.mult)
+
+    def late_constants():
+        ts(col(7), P, -16.0, A.mult, 2047.0, A.add)
+        ts(u("KB"), J15, -1.0, A.mult, col(7), A.add)
+        ts(col(8), P, 16.0, A.mult)
+        ts(u("KV"), J15, col(8), A.add)
+        cp(u("CREP"), J)
+        ts(col(9), P, 0.0, A.is_equal, 512.0, A.mult)
+        ts(col(10), P, 1.0, A.is_equal, -2.0 ** 24, A.mult)
+        ts(u("KA"), J15, col(9), A.mult, col(10), A.add)
+        fill(u("ONEB"), 1.0)
+        cp(u("ONE16"), u("ONEB"))
+        ts(col(11), P15, 0.0, A.is_equal, 2.0 ** 25, A.mult)
+        ts(u("DEAD"), u("BD"), col(11), A.mult)
+        ts(col(12), P15, 4.0, A.is_lt, 1.0 / 64, A.mult)
+        tt(col(12), col(12), P15, A.mult)
+        ts(col(13), P15, 4.0, A.is_equal, 4.0, A.mult)
+        tt(col(12), col(12), col(13), A.add)
+        ts(u("HWB"), u("BD"), col(12), A.mult)
+        for c in range(4):
+            ts(col(14), P15, float(c), A.is_equal, 2.0 ** 19, A.mult)
+            tt(col(15), col(14), col(12), A.add)
+            ts(u("og%d" % c), u("BD", 0, None, 16), col(15), A.mult)
+        ts(u("TRI"), J, P, A.is_gt)
+        fill(u("FM"), -4096.0)
+        fill(u("FM", 0, None, 128), 4096.0)
+        ts(u("blk128"), u("J", 0, 8), P4, A.is_equal, 128.0, A.mult)
+        ts(col(16), P, -1.0, A.mult, -528.0, A.add)
+        ts(u("blkN"), u("J", 0, 8), P4, A.is_equal, col(16), A.mult)
+        ts(col(28), P, -1.0, A.mult, -1552.0, A.add)
+        ts(u("blkE"), u("J", 0, 8), P4, A.is_equal, col(28), A.mult)
+        ts(col(17), P, 16.0, A.add)
+        ts(u("blkI"), u("J", 0, 8), P4, A.is_equal, col(17), A.mult)
+        ts(col(18), P, 32.0, A.add)
+        ts(u("blk32"), u("J", 0, 8), P4, A.is_equal, col(18), A.mult)
+        ts(u("blkm"), u("J", 0, 8), P4, A.is_equal, -640.0, A.mult)
+        ts(u("blk2k"), u("J", 0, 8), P4, A.is_equal, 2048.0, A.mult)
+        fill(u("C640"), 640.0)
+        ts(u("CI"), u("J", 0, 8), 16.0, A.mult, P15, A.add)
+        ts(col(19), P15, 528.0, A.add)
+        ts(u("C528"), u("J", 0, 8), 16.0, A.mult, col(19), A.add)
+        ts(u("SEL5"), u("BD"), col(5), A.mult)
+        ts(u("BT"), J, P, A.is_le, -1.0, A.mult)
+        tt(u("BT"), u("BT"), u("BD"), A.mult)
+        ts(col(20), P, 15.0, A.add)
+        ts(col(21), P15, 0.0, A.is_equal)
+        ts(u("Y"), u("J", 0, 144), col(20), A.is_equal, col(21), A.mult)
+        ts(u("SEL0"), u("BD", 0, None, 16), col(21), A.mult)
+        ts(col(22), P15, 656.0, A.add)
+        ts(u("CVp"), u("J", 0, 32), 16.0, A.mult, col(22), A.add)
+        ts(u("CVn"), u("CVp"), -1.0, A.mult)
+        fill(u("FREE"), 0.0)
+        fill(u("STI", 0, 8), 0)
+        fill(u("DS", 2048, 2176), 0.0)
+        fill(u("RESW"), 0)
+        fill(u("QZ"), 0.0)
+        fill(u("Aa"), 0)
+        for t in range(RO):
+            fill(u("XV%d" % t), 0.0)
+        for s in range(16):
+            o, i = u("SH", 128 * s, 128 * s + 128), u("BD")
+            op("k", lambda: g.affine_select(o[0], i[0], [[1, 128]], A.is_equal, 0.0, -s, -1), [o], [i])
+        cp(u("PC", 24, 26), u("LI"))
+        cp(u("PC", 26, 27), u("WI"))
+        ts(u("WTB"), u("BD"), col(26), A.mult)
+        ts(u("NFH"), u("SEL0"), col(24), A.mult)
+        mm([(u("p6", 0, 8), u("ONE16"), u("NFH"))])
+        cp(u("lim8"), u("p6", 0, 8))
+        cp(u("thr8"), u("p6", 0, 8))
+        ts(u("NFH"), u("SEL0"), col(25), A.mult)
+        mm([(u("p6", 0, 8), u("ONE16"), u("NFH"))])
+        cp(u("lim28"), u("p6", 0, 8))
+
+    def tile(src_rep, prod, blk, out, extra=(), ps="p6"):
+        if src_rep is not None:
+            tt(u(prod), src_rep, u("p3", 0, 128), A.mult)
+        mm([(u(ps, 0, 8), u(prod), u(blk))] + [(u(ps, 0, 8), u(a), u(b)) for a, b in extra])
+        cp(u(out), u(ps, 0, 8))
+
+    def part_own(t):
+        cl = t % 4
+        lanes = u("W", 1 + cl, 513, 4)
+        cp(u("OWN"), lanes)
+        win = u("X", 0, 2064)
+        if t == 0:
+            cp(u("T"), ix(win, u("OWN")))
+        else:
+            act(u("T", 1024, 2048), ix(win, u("OWN", 64, 128)), F.Copy)
+            cp(u("T", 0, 1024), ix(win, u("OWN", 0, 64)))
+        ts(u("EO"), lanes, 0.0, A.is_equal)
+        cp(u("OWNH"), lanes)
+        ts(u("VC"), u("W", 1, 513), 0.0, A.is_equal)
+        mm([(u("p4", 0, 128), u("IDB"), u("CK")), (u("p4", 0, 128), u("EO"), u("IDE")), (u("p4", 0, 128), u("OWNH"), u("ID16"))]
+           + sums("p4", 0, "T", "w32k"))
+        scan(u("US"), u("MS", 0, 2048), u("T"), A.mult, A.max)
+        mm([(u("p7", 32, 40), u("EO"), u("BD", 0, None, 16))])
+        mm([(u("p5", 128, 256), u("OWNH"), u("ID16x"))])
+        mm([(u("p5", 256, 384), u("OWNH"), u("ID16x")), (u("p5", 256, 384), u("IDB"), u("CKP"))])
+        mm([(u("p6", 8, 16), u("US", 15, None, 16), u("BD", 0, None, 16))])
+        scan(u("S1"), u("MIN"), u("p4", 0, 128), A.max, A.min)
+        ts(u("k8"), u("S1", 15, None, 16), -1.0, A.add)
+        ts(u("sv8"), u("k8"), 2047, A.bitwise_and)
+        ts(u("sx8"), u("k8"), 15, A.logical_shift_right)
+        ts(u("ZS", 0, None, 16), u("sv8"), 1.0, A.add)
+        ts(u("live8"), u("S1", 15, None, 16), 2.0 ** 23, A.is_lt)
+        hold(u("SR"), u("ZS"))
+        tile(u("SR"), "PS", "blk16", "S16")
+        cp(u("Z", 0, None, 16), ix(win, u("S16")))
+        mm([(u("p7", 0, 32), u("Y", 15 - r, 143 - r), u("VC", r, None, 16)) for r in range(16)] if t else
+           [(u("p7", 0, 32), u("IDB"), u("VC", 0, 32))])
+        ts(u("ZN", 0, None, 16), u("p7", 32, 40), -1.0, A.mult, 16.0, A.add)
+        tt(u("gr8"), u("p6", 8, 16), u("sx8"), A.subtract)
+        scan(u("REP"), u("MS", 0, 2048), u("Z"), A.mult, A.add)
+
+    def dif(c):
+        a, b = 512 * c, 512 * c + 512
+        ps = "p%d" % (c % 3)
+        mm([(u(ps), u("IDB"), u("T", a, b)), (u(ps), u("NIDB"), u("REP", a, b))])
+        act(u("SQ", a, b), u(ps), F.Square)
+
+    def part_own_squares(t):
+        for c in (2, 3):
+            dif(c)
+        act(u("SQS"), u("Z", 0, None, 16), F.Square)
+        act(u("W16L"), u("p5", 128, 256), F.Copy)
+        act(u("WL"), u("p5", 128, 256), F.Copy, scale=0.0625)
+        act(u("PW2"), u("p5", 256, 384), F.Copy)
+
+    def part_own_end(t):
+        tt(u("gr8"), u("gr8"), u("lim28"), A.is_gt)
+        tt(u("wp8"), u("gr8"), u("live8"), A.mult)
+
+    def part_sizes(t):
+        hold(u("NR"), u("ZN"))
+        tt(u("NP"), u("NR"), u("p3", 0, 128), A.mult)
+        mm([(u("p4", 264, 272), u("NP"), u("blk128")), (u("p4", 264, 272), u("ID16"), u("CI"))])
+
+    def part_split(t):
+        cp(u("N16"), u("p4", 264, 272))
+        cp(u("nf8"), u("p4", 256, 264))
+        mm([(u("p5", 0, 128), u("ID16"), u("KB")), (u("p5", 0, 128), u("EO"), u("NIDE"))] + sums("p5", 0, "SQ", "w2k"))
+        scan(u("SB"), u("MS", 0, 128), u("p5", 0, 128), A.mult, A.max)
+        cp(u("b8"), u("SB", 15, None, 16))
+        ts(u("bb8"), u("b8"), 2047, A.bitwise_and)
+        ts(u("ZBB", 0, None, 16), u("bb8"), -1.0, A.mult, 2047.0, A.add)
+        hold(u("BR"), u("ZBB"))
+        tile(u("BR"), "BP", "blk16", "B16", ps="p7")
+        cp(u("XB"), ix(u("T"), u("B16")))
+        act(u("SQB"), u("XB"), F.Square)
+        tt(u("WV"), u("Z", 0, None, 16), u("XB"), A.subtract)
+        tt(u("AX"), ix(u("WV"), u("CREP")), u("T"), A.mult)
+        mm([(u("p5", 384, 512), u("SQB"), u("BD")), (u("p5", 384, 512), u("SQS"), u("NBD"))] + sums("p5", 384, "AX", "w2"))
+
+    def part_compact(t):
+        ts(u("mb"), u("W16L"), 0.0, A.is_gt)
+        ts(u("p5", 0, 128), u("p5", 384, 512), 0.0, A.is_lt)
+        tt(u("L1"), u("mb"), u("p5", 0, 128), A.mult)
+        scan(u("p5", 128, 256), u("MS", 0, 128), u("L1"), A.mult, A.add)
+        tt(u("SM"), u("mb"), u("L1"), A.subtract)
+        tt(u("p5", 0, 128), u("PW2"), u("p5", 128, 256), A.subtract)
+        tt(u("p5", 256, 384), u("W16L"), u("p5", 128, 256), A.add)
+        tt(u("Pa", 128, 256), u("L1"), u("p5", 0, 128), A.mult)
+        tt(u("Pa", 0, 128), u("SM"), u("p5", 256, 384), A.mult)
+
+    def part_shift(t, steps):
+        for s in steps:
+            a, b = ("Pa", "Pb") if s % 2 == 0 else ("Pb", "Pa")
+            ts(u("Mi", 0, 256), u(a, 0, 256), 1 << s, A.bitwise_and)
+            ts(u("p5", 0, 256), u("Mi", 0, 256), 2.0 ** (16 - s), A.mult)
+            tt(u("p5", 256, 512), u(a, 0, 256), u("p5", 0, 256), A.subtract)
+            tt(u("Aa", 0, 256), u(a, 0, 256), u("p5", 0, 256), A.min)
+            tt(u(b, 0, 256), u("p5", 256, 512), u("Aa", 1 << s, 256 + (1 << s)), A.max)
+        if 3 in steps:
+            ts(u("STI"), u("Pa", 0, 256), 4, A.logical_shift_right)
+            tt(u("STM"), u("STI", 0, 128), u("WL"), A.subtract)
+
+    def move_owners():
+        act(ix(u("OT", 0, 4112), u("MVO")), u("VE"), F.Silu)
+
+    def part_vacant_count(t):
+        if t == 0:
+            mm([(u("p7", 0, 32), u("Y", 15 - r, 143 - r), u("VC", r, None, 16)) for r in range(16)])
+        cp(u("VTb"), u("p7", 0, 32))
+        mm([(u("p7", 0, 32), u("BD"), u("VTb"))])
+        mm([(u("p6", 0, 32), u("BT"), u("VTb")), (u("p6", 0, 32), u("ID16"), u("CVn"))])
+        part_sizes(t)
+
+    def part_vacant(t):
+        scan(u("CSs"), u("ONEB", 0, 32), u("p7", 0, 32), A.mult, A.add)
+        tt(u("rk"), u("CSs"), u("p6", 0, 32), A.add)
+        tt(u("rk"), u("rk"), u("VTb"), A.mult)
+        tt(u("rk"), u("rk"), u("CVp"), A.add)
+        cp(u("F16"), u("rk"))
+        ts(u("NFH"), u("SEL0"), u("CSs", 31, 32), A.mult)
+        mm([(u("p4", 256, 264), u("ONE16"), u("NFH"))])
+
+    def part_near(t):
+        cl = t % 4
+        win = u("X", 0, 2064)
+        i = ix(u("AC4"), u("S16"))
+        ts(u("AN"), i, 1, A.add)
+        act(u("OG"), ix(u("OT", 0, 2064), u("AN")), F.Copy)
+
+    def part_distances(t):
+        cl = t % 4
+        win = u("X", 0, 2064)
+        for h in range(2):
+            a, b = 1024 * h, 1024 * h + 1024
+            tt(u("AX", a, b), ix(win, u("AN", 64 * h, 64 * h + 64)), u("REP", a, b), A.subtract)
+            act(u("SQ", a, b), u("AX", a, b), F.Square)
+        mm([(u("p4", 0, 128), u("ONEB"), u("KA")), (u("p4", 0, 128), u("EO"), u("DEAD"))] + sums("p4", 0, "OG", "og%d" % cl)
+           + sums("p4", 0, "SQ", "w8k"))
+
+    def part_partner(t):
+        win = u("X", 0, 2064)
+        scan(u("S2"), u("MIN"), u("p4", 0, 128), A.max, A.min)
+        cp(u("a8"), u("S2", 15, None, 16))
+        ts(u("has8"), u("S2", 15, None, 16), 14.0e6, A.is_lt)
+        ts(u("d8"), u("a8"), 511, A.bitwise_and)
+        ts(u("dp8"), u("d8"), 1.0, A.add)
+        tt(u("ZD", 0, None, 16), u("dp8"), u("has8"), A.mult)
+        hold(u("D1R"), u("ZD"))
+        tile(u("D1R"), "PD", "blk16", "D16")
+        lists = ix(u("W", 0, 520), u("D16"))
+        cp(u("DM"), lists)
+        act(u("DT", 1024, 2048), ix(win, u("DM", 64, 128)), F.Copy)
+        cp(u("DT", 0, 1024), ix(win, u("DM", 0, 64)))
+        cp(u("DMH"), ix(u("W", 0, 520), u("D16")))
+        ts(u("ED"), u("DM"), 0.0, A.is_equal)
+        ts(u("nD"), u("ZD", 0, None, 16), -1.0, A.mult)
+        tt(u("d18"), u("dp8"), u("has8"), A.mult)
+        for q in range(8):
+            ts(u("DG", 128 * q, 128 * q + 128), u("ID16"), u("d18", q, q + 1), A.mult)
+        for q in range(8):
+            ps = "p%d" % (q // 4)
+            lo = 128 * (q % 4)
+            mm([(u(ps, lo, lo + 128), u("TRI"), u("DG", 128 * q, 128 * q + 128))])
+        mm([(u("p7", 0, 8), u("EO"), u("BD", 0, None, 16)), (u("p7", 0, 8), u("ED"), u("BD", 0, None, 16))])
+        mm([(u("p4", 0, 128), u("ED"), u("ID1K"))] + sums("p4", 0, "DT", "w1"))
+        scan(u("AX"), u("MS", 0, 2048), u("DT"), A.mult, A.max)
+        tt(u("Vv"), u("US", 15, None, 16), u("AX", 15, None, 16), A.max)
+        mm([(u("p6", 0, 8), u("Vv"), u("BD", 0, None, 16))])
+        for q in range(8):
+            ps = "p%d" % (q // 4)
+            lo = 128 * (q % 4)
+            act(u("AB", 128 * q, 128 * q + 128), u(ps, lo, lo + 128), F.Abs, bias=u("nD", q, q + 1))
+        for c in range(4):
+            ps = "p%d" % (2 - 2 * (c % 2))
+            for k in range(4):
+                s = 4 * c + k
+                mm([(u(ps, 128 * k, 128 * k + 128), u("SH", 128 * s, 128 * s + 128), u("DMH"))])
+            act(u("DS", 512 * c, 512 * c + 512), u(ps), F.Copy)
+        act(ix(u("FREE"), u("F16")), u("V0"), F.Silu)
+        ts(u("sz8"), u("p7", 0, 8), 16.0, A.is_ge)
+        scan(u("S3"), u("MIN"), u("p4", 0, 128), A.max, A.min)
+        tt(u("mn8"), u("S3", 15, None, 16), u("sx8"), A.min)
+        tt(u("tm8"), u("mn8"), u("thr8"), A.add)
+        scan(u("ABS"), u("FM"), u("AB"), A.max, A.min)
+        ts(u("f8"), u("ABS", 127, None, 128), 0.5, A.is_ge)
+        tt(u("P0"), u("f8"), u("has8"), A.mult)
+        tt(u("P0"), u("P0"), u("sz8"), A.mult)
+
+    def part_finish(t):
+        cl = t % 4
+        zm, zw, zs, zi, zv = [u(z, 0, None, 16) for z in ("ZM", "ZW", "ZSP", "ZI", "ZV")]
+        tt(u("c8"), u("p6", 0, 8), u("tm8"), A.is_le)
+        tt(zm, u("c8"), u("P0"), A.mult)
+        tt(zw, u("wp8"), zm, A.is_gt)
+        hold(u("WR"), u("ZW"))
+        mm([(u("p7", 0, 128), u("TRI"), u("WR"))])
+        hold(u("MR"), u("ZM"))
+        mm([(u("p4", 0, 128), u("MR"), u("ID16"))])
+        tt(u("sp8"), u("p7", 0, 128, 16), u("nf8"), A.is_lt)
+        tt(zs, u("sp8"), zw, A.mult)
+        tt(u("ms8"), zm, zs, A.add)
+        tt(zi, u("live8"), u("ms8"), A.is_gt)
+        hold(u("IR"), u("ZI"))
+        mm([(u("p6", 128, 256), u("TRI"), u("IR"))])
+        hold(u("p3", 128, 256), u("ZSP"))
+        tt(u("SPP"), u("R16"), u("p3", 128, 256), A.mult)
+        tt(u("KP"), u("p7", 0, 128), u("SPP"), A.mult)
+        ts(u("v8"), u("p6", 128, 256, 16), 32.0, A.is_lt)
+        tt(zv, u("v8"), zi, A.mult)
+        hold(u("p3", 256, 384), u("ZV"))
+        tt(u("VP"), u("R16"), u("p3", 256, 384), A.mult)
+        tt(u("RP"), u("p6", 128, 256), u("VP"), A.mult)
+        tt(u("NVP"), u("p3", 0, 128), u("VP"), A.subtract)
+        tile(None, "RP", "blk16", "RT16", [("NVP", "blk32")])
+        xv = "XV%d" % t
+        cp(ix(u(xv), u("RT16")), u("Z", 0, None, 16))
+        send(T.cores[(rank + 1 + t % 7) % 8], xv, "QI%d" % t, "rq%d" % t, "fq%d" % t, "lq%d" % t, 0)
+        tile(None, "KP", "blk16", "K16", [("SPP", "blkm"), ("IDB", "C640")], ps="p7")
+        cp(u("EV"), ix(u("FREE"), u("K16")))
+        cp(u("EVH"), u("EV"))
+        mm([(u("p7", 0, 128), u("EVH"), u("SEL5"))])
+        tt(u("f128a"), u("p4", 0, 128), u("V0", cl, None, 4), A.mult)
+        tt(u("VF"), u("f128a"), u("EV"), A.add)
+        act(u("VE"), ix(u("VF"), u("CREP")), F.Copy)
+        tt(u("A3"), u("STI", 128, 256), u("p3", 128, 256), A.mult)
+        mm([(u("p5", 128, 256), u("A3"), u("ID16"))])
+        tt(u("MD"), u("p4", 0, 128), u("DMH"), A.mult)
+        mm([(u("p2", 0, 128), u("ID16"), u("MD")), (u("p2", 0, 128), u("A3"), u("ID16"))])
+        cp(u("DSE"), ix(u("DS"), u("N16")))
+        tt(u("A1"), u("p4", 0, 128), u("DSE"), A.mult)
+        tt(u("A2"), u("STM"), u("p3", 128, 256), A.mult)
+        mm([(u("p5", 0, 128), u("ID16"), u("OWNH")), (u("p5", 0, 128), u("ID16"), u("A1")), (u("p5", 0, 128), u("A2"), u("ID16"))])
+        ts(u("p3", 384, 512), u("p2", 0, 128), 0.0, A.is_equal)
+        tt(u("f128b"), u("DUM"), u("p3", 384, 512), A.mult)
+        tt(u("f128b"), u("f128b"), u("p2", 0, 128), A.add)
+        cp(u("MVO"), u("f128b"))
+        tt(u("MP"), u("MR"), u("p3", 0, 128), A.mult)
+        tt(u("Q1"), u("PD"), u("MR"), A.mult)
+        tt(u("Q2"), u("p7", 0, 128), u("SPP"), A.mult)
+        cp(u("ELS"), u("p5", 128, 256))
+        tile(None, "Q1", "blk16", "TG16", [("Q2", "blk16"), ("MP", "blkN"), ("SPP", "blkE"), ("ID16", "C528")])
+        cp(u("W", 1 + cl, 513, 4), u("p5", 0, 128))
+        cp(ix(u("W", 0, 656), u("TG16")), u("ELS"))
+
+    def part_late(t):
+        tt(u("XP"), u("PS"), u("p3", 256, 384), A.mult)
+        tile(None, "XP", "blk16", "XT16", [("NVP", "blkI"), ("NVP", "blk2k")])
+        if t + 1 < RO:
+            mm([(u("p7", 0, 8), u("ONE16"), u("MR", 0, None, 16))])
+            op("v", lambda: v.tensor_reduce(u("mc", 0, 1)[0], u("p7", 0, 8)[0], AX_.X, A.add), [u("mc", 0, 1)], [u("p7", 0, 8)])
+            cp(u("mci", 0, 1), u("mc", 0, 1))
+            ts(u("mci", 1, 2), u("mci", 0, 1), 15, A.bitwise_and)
+            cp(u("mc", 1, 2), u("mci", 1, 2))
+            ts(u("thr8"), u("lim8"), u("mc", 1, 2), A.add)
+
+    def part_serve(t):
+        src = T.cores[(rank - 1 - t % 7) % 8]
+        n = landed_n(src, 0)
+        qi, sn = "QI%d" % t, "SN%d" % t
+        rq = "rq%d" % t
+        p32 = (0, 32)
+        for e in ("p", "v"):
+            arrived(e, qi, rq, n)
+        mm([(u("p6", 0, 128, 1, p32), u(qi), u("WTB"))])
+        cp(u("QZ", 0, None, 16), u(qi))
+        tt(u("VFP", p=p32), u("p6", 0, 128, 1, p32), u("R16", p=p32), A.mult)
+        mm([(u("p7", 0, 2), u("VFP", p=p32), u("blkf", 0, 2, 1, p32))])
+        cp(u("VI"), u("p7", 0, 2))
+        ts(u("VI2"), u("VI"), 2047, A.bitwise_and)
+        ts(u("VV16"), u("VI2"), 1, A.add)
+        scan(u("QRp"), u("MS", 0, 512), u("QZ"), A.mult, A.add)
+        cp(u("HO"), ix(u("OT", 0, 2064), u("VV16")))
+        mm([(u("p6", 0, 128, 1, p32), u("HO"), u("HWB"))])
+        tt(u("QP", p=p32), u("p6", 0, 128, 1, p32), u("R16", p=p32), A.mult)
+        mm([(u("p7", 0, 2), u("QP", p=p32), u("blk16", 0, 2, 1, p32))])
+        ts(u("H16"), u("p7", 0, 2), -511.0, A.add)
+        cp(u("HL"), ix(u("W", 0, 520), u("H16")))
+        tt(u("QD"), ix(u("X", 0, 2064), u("HL")), u("QRp"), A.subtract)
+        ts(u("EH"), u("HL"), 0.0, A.is_equal)
+        act(u("QS"), u("QD"), F.Square)
+
+    def part_serve_met(t):
+        src = T.cores[(rank - 1 - t % 7) % 8]
+        qi, sn = "QI%d" % t, "SN%d" % t
+        p32 = (0, 32)
+        mm([(u("p6", 0, 128, 1, p32), u("ID16", 0, 32), u("KV")), (u("p6", 0, 128, 1, p32), u("EH"), u("IDE"))]
+           + sums("p6", 0, "QS", "w512", p32))
+        scan(u("QSC", p=p32), u("MIN", p=p32), u("p6", 0, 128, 1, p32), A.max, A.min)
+        cp(u("q8", p=p32), u("QSC", 15, None, 16, p32))
+        ts(u("qq8", p=p32), u("q8", p=p32), 511, A.bitwise_and)
+        cp(u("ZQ", 0, None, 16, p32), u("qq8", p=p32))
+        scan(u("QR8", p=p32), u("MS", 0, 128, 1, p32), u("ZQ", p=p32), A.mult, A.add)
+        tt(u("QP", p=p32), u("QR8", p=p32), u("R16", p=p32), A.mult)
+        mm([(u("p7", 0, 2), u("QP", p=p32), u("blk16", 0, 2, 1, p32))])
+        cp(u("J16"), u("p7", 0, 2))
+        ts(u("hs"), ix(u("QD"), u("J16")), -0.5, A.add, 0.5, A.mult)
+        tt(u(sn), u("hs"), u(qi), A.add)
+        send(src, sn, "RS%d" % t, "rs%d" % t, "fs%d" % t, "ls%d" % t, 1)
+
+    def part_apply(t):
+        src = T.cores[(rank + 1 + t % 7) % 8]
+        arrived("v", "RS%d" % t, "rs%d" % t, landed_n(src, 1))
+        cp(u("RESW", 0, 32), u("RS%d" % t))
+        cp(u("NV"), ix(u("RESW"), u("RT16")))
+        cp(ix(u("X"), u("XT16")), u("NV"))
+
+    part_own(0)
+    dif(0)
+    dif(1)
+    part_own_squares(0)
+    owners(2)
+    late_constants()
+    part_own_end(0)
+    owners(3)
+    part_vacant_count(0)
+    part_vacant(0)
+    part_split(0)
+    for t in range(RO):
+        part_near(t)
+        part_compact(t)
+        part_shift(t, (0, 1))
+        if t:
+            part_apply(t - 1)
+        part_distances(t)
+        part_shift(t, (2, 3))
+        part_partner(t)
+        part_finish(t)
+        part_late(t)
+        if t + 1 < RO:
+            part_own(t + 1)
+            move_owners()
+            part_vacant_count(t + 1)
+            dif(0)
+            dif(1)
+            part_own_end(t + 1)
+            part_vacant(t + 1)
+            part_serve(t)
+            part_own_squares(t + 1)
+            part_serve_met(t)
+            part_split(t + 1)
+        else:
+            move_owners()
+            ts(u("t512a"), u("W", 1, 513), 0.0, A.is_equal, 2049.0, A.mult)
+            ts(u("t512b"), u("W", 1, 513), -1.0, A.add)
+            tt(u("YM"), u("t512a"), u("t512b"), A.add)
+            dma("y", ext(T.ym[:], "out_m"), u("YM"), "st0")
+            part_serve(t)
+            part_serve_met(t)
+            part_apply(t)
+            dma("y", ext(T.yx[:], "out_x"), u("X", 1, 2049), "st1")
+    for sem in total:
+        n = total[sem]
+        if known["k"].get(sem, 0) < n:
+            g.wait_ge(T.sem[sem], n)

@@ -3,6 +3,7 @@ from concourse.mybir import dt, AluOpType as A, AxisListType as AX_, ActivationF
 RO = 5
 BIG = 1.0e9
 S, B, H, I, U = "float32", "bfloat16", "float16", "int32", "uint16"
+TAG = [""]
 
 SCRATCH = {}
 
@@ -13,76 +14,62 @@ def _sb(names, cols, dtype):
 
 
 _sb("X", 2304, B)
-_sb("AC4", 2064, I)
+_sb("AC4", 2192, I)
 _sb("MI", 512, I)
 _sb("LI", 2, I)
 _sb("WI", 1, I)
-_sb("W", 664, S)
+_sb("W", 640, S)
 _sb("OT", 4112, S)
 _sb("VE VG", 2048, S)
-_sb("VF", 128, S)
-_sb("ZE MS", 2048, B)
-_sb("V0 Jf J2f t512a t512b t512c", 512, S)
-_sb("J3", 512, I)
-_sb("Jh", 144, H)
-_sb("J4h J15h", 128, H)
-_sb("MIN", 128, B)
-_sb("FM", 1024, B)
-_sb("T US Z REP SQ AX OG DT", 2048, B)
-_sb("DS", 2176, S)
+_sb("FREE", 1536, S)
+_sb("DS", 2304, S)
+_sb("CODE", 512, B)
+_sb("EV", 128, S)
+_sb("T", 2048, B)
+_sb("QD", 512, B)
+_sb("MS IOT VB US REP SQ AX AW SH OG DT DU", 2048, B)
+_sb("Z0 Z1", 2048, B)
+_sb("J2f t512a t512b YM QR", 512, S)
+_sb("J J3 Qi", 512, I)
 _sb("OWN AN DM CREP MVO", 128, U)
 _sb("INO", 512, U)
-_sb("OWNH DMH DSE R16 ID16 ID16x NID16 TRI D1R PD KB KV SEL5 SR PS MR MP WR SPR SPP IR VR VP NVP KP RP EVH Q1 Q2 "
-    "A1 A2 A3 MD NR NP BR BP XP", 128, H)
-_sb("ZS ZD ZN ZBB ZM ZW ZSP ZI ZV ZQ QR8 QP", 128, H)
-_sb("EO ED IDB NIDB BD NBD BT IDE NIDE ID1K CK CKP KA DEAD HWB WTB ONEB Vv WV XB SQS SQB NV", 128, B)
-_sb("ONE16", 128, H)
-_sb("Y", 144, B)
-_sb("S1 S2 S3 SB W16L WL PW2 lv mb L1 cl SM q1a q2a STM EV ELS DUM f128a f128b VFP QPF QSC", 128, S)
+_sb("OCC PEN QZ QRp QS CG", 512, B)
+_sb("kq G4", 4, S)
+_sb("EQ", 1024, B)
+_sb("Jh OWNH DMH ID16 NID16 ONE16 J4h J15h KP RP D1R CMR CMK0 CMK1 CMK2 CMK3 R16", 128, H)
+_sb("ZS HS ZB HB ZD HD ZQ HQ", 144, H)
+_sb("ID2 SL CNT CTG", 256, H)
+_sb("MC IDB NIDB BD NBD BTI ONEB PRE PRD LR L1T ZM ZW WR MR SR XB SQS SQB Vv EVb NV CE CO NFH SEL0R TRIm NTRIm HWN BDn "
+    "N24 N25 N20 P20 P25 N13 P12 P11 KAs KAb KAd KAn KAq K12 K13 K14", 128, B)
+_sb("BTX KAp QN", 256, B)
+_sb("Y Y2 WY HY", 144, B)
+_sb("MINs MINn MIN S1a S1b S2 S3 SB QSC DUM NFR ELS m1 m2 e128", 128, S)
 _sb("Pa Pb Mi Aa", 264, I)
-_sb("STI", 256, I)
-_sb("DG", 1024, H)
-_sb("AB ABS", 1024, B)
-_sb("SH", 2048, B)
 _sb("PIi", 4, I)
-_sb("PC", 32, S)
-_sb("J", 512, I)
+_sb("PC", 48, S)
 _sb("J4 J15", 128, I)
-_sb("blk16 blk128 blkN blkE blkI blk32 blkm blk2k CI C528", 8, H)
-_sb("blkf", 8, S)
-_sb("C640 w32k w8k w2k w512 w1 w2 og0 og1 og2 og3 SEL0", 8, B)
-_sb("k8 sv8 sx8 b8 bb8 a8 d8 q8 qq8", 8, I)
-_sb("lim8 lim28 thr8 live8 gr8 wp8 has8 dp8 nD d18 mn8 tm8 f8 sz8 P0 c8 sp8 ms8 v8 nf8 nfs8", 8, S)
-_sb("S16 B16 D16 N16 K16 TG16 RT16 XT16", 8, U)
-_sb("NFH", 8, H)
-_sb("VC", 512, B)
-_sb("VTb", 32, B)
-_sb("CSs CVp rk", 32, S)
-_sb("CVn", 32, H)
-_sb("F16", 32, U)
-_sb("FREE", 1168, S)
-_sb("mc", 4, S)
-_sb("mci", 4, I)
-_sb("RESW", 160, I)
-_sb("HO EH", 32, B)
-_sb("HL", 32, U)
+_sb("blk nblk CB CQ CT", 8, H)
+_sb("nblkb CN w64k w8k w32 og0 og1 og2 og3 SEL0 L2N THN THZ ROW1 SZ wp8 C25", 8, B)
+_sb("nblkf hi8 hb8 hq8 mn8 z8", 8, S)
+_sb("a8 d8", 8, I)
+_sb("S16a S16b B16 D16 NT16 K16 TG16 RT16a RT16b", 8, U)
+_sb("OCb HO PRH QP", 32, B)
+_sb("CIX", 32, H)
+_sb("CS r1 r2 C512 hs", 32, S)
+_sb("F16 HL", 32, U)
+_sb("mc", 8, S)
 _sb("VI VI2", 2, I)
 _sb("VV16 H16 J16", 2, U)
-_sb("QZ QRp QD QS", 512, B)
-_sb("hs", 32, S)
-_sb("YM", 512, S)
 for _t in range(RO):
-    _sb("XV%d" % _t, 160, B)
-    _sb("QI%d" % _t, 32, B)
-    _sb("SN%d RS%d" % (_t, _t), 32, I)
+    _sb("XV%d" % _t, 256, B)
+    _sb("QI%d SN%d RS%d" % (_t, _t, _t), 32, B)
 _ARENA = {}
 
 
 def _pack():
     keep, pos = {}, {}
-    big = ("X", "T", "W", "XV", "QI", "SN", "RS")
     for n, (w, sh, d) in SCRATCH.items():
-        if n in ("X", "T", "W", "AC4", "OT", "VF", "FREE", "RESW", "DS", "QD", "WV") or n[:2] in ("XV", "QI", "SN", "RS"):
+        if n[:2] in ("XV", "QI", "RS", "SN"):
             keep[n] = (w, sh, d)
             _ARENA[n] = (n, 0, sh[1], d)
         else:
@@ -102,6 +89,9 @@ for _k in range(8):
 SEMAPHORES = ["v", "p", "s", "k"] + ["ld%d" % i for i in range(8)] + ["st0", "st1"]
 for _t in range(RO):
     SEMAPHORES += ["rq%d" % _t, "rs%d" % _t, "lq%d" % _t, "ls%d" % _t, "fq%d" % _t, "fs%d" % _t, "mq%d" % _t, "ms%d" % _t]
+_ORDER = {}
+CYC, WAKE, GAT, SCA, WAY = 0.001, 0.07, 1.5, 3.5, 7.0
+OPT = {"T": 64, "DT": 64, "sc": "vsvs", "mv": 2}
 
 
 def _mask(topo, a, b):
@@ -135,49 +125,684 @@ def _relay_program(g, core, T, topo):
         g.wait_ge(s, n)
 
 
+def _psum(b):
+    return len(b) == 2 and b[0] == "p"
+
+
+def _order(ops):
+    n = len(ops)
+    pred = [set() for _ in range(n)]
+    log = {}
+    for i, o in enumerate(ops):
+        for kind, lst in ((0, o["rd"]), (1, o["wr"])):
+            for (b, lo, hi) in lst:
+                for (l2, h2, j, wr) in log.get(b, ()):
+                    if lo < h2 and l2 < hi and (kind or wr):
+                        pred[i].add(j)
+        for (b, lo, hi) in o["wr"]:
+            log[b] = [x for x in log.get(b, []) if not (lo <= x[0] and x[1] <= hi)] + [(lo, hi, i, True)]
+        for (b, lo, hi) in o["rd"]:
+            log.setdefault(b, []).append((lo, hi, i, False))
+        pred[i].discard(i)
+    succ = [[] for _ in range(n)]
+    for i in range(n):
+        for j in pred[i]:
+            succ[j].append(i)
+    way = [0.0] * n
+    for i in range(n - 1, -1, -1):
+        way[i] = ops[i]["cost"] + ops[i]["lat"] + max([way[j] + WAKE for j in succ[i]] + [0.0])
+    left = [len(p) for p in pred]
+    end = [0.0] * n
+    free, bank, ready, out = {}, {}, {}, []
+    banks = [set(b for (b, _l, _h) in o["rd"] + o["wr"] if _psum(b)) for o in ops]
+    base = [0.0] * n
+    for i in range(n):
+        if not left[i]:
+            ready.setdefault(ops[i]["e"], []).append(i)
+
+    def start(i):
+        e = ops[i]["e"]
+        s = max(base[i], free.get(e, 0.0))
+        for b in banks[i]:
+            for e2, t2 in bank.get(b, {}).items():
+                if e2 != e:
+                    s = max(s, t2 + WAKE)
+        return s
+    while len(out) < n:
+        best = None
+        for e, lst in ready.items():
+            if not lst:
+                continue
+            st = {i: start(i) for i in lst}
+            a = min(lst, key=lambda i: (round(st[i], 2), -way[i]))
+            for b in sorted(lst, key=lambda i: -way[i])[:6]:
+                ca, cb = ops[a]["cost"], ops[b]["cost"]
+                if b != a and st[b] < st[a] + ca and max(st[b] + way[b], st[b] + cb + way[a]) < max(st[a] + way[a], st[a] + ca + way[b]):
+                    a = b
+            if best is None or st[a] < best[0]:
+                best = (st[a], a)
+        s, a = best
+        e = ops[a]["e"]
+        ready[e].remove(a)
+        free[e] = s + ops[a]["cost"]
+        end[a] = free[e] + ops[a]["lat"]
+        for b in banks[a]:
+            bank.setdefault(b, {})[e] = end[a]
+        out.append(a)
+        for j in succ[a]:
+            base[j] = max(base[j], end[a] + WAKE)
+            left[j] -= 1
+            if not left[j]:
+                ready.setdefault(ops[j]["e"], []).append(j)
+    return out
+
+
 def rank_program(g, core, T, topo):
     rank = T.rank_of(core)
     if rank is None:
         _relay_program(g, core, T, topo)
         return
     E = {"v": g.vector, "p": g.tensor, "s": g.scalar, "k": g, "y": g.sync}
-    cnt = {"v": 0, "p": 0, "s": 0, "k": 0}
-    known = {e: {} for e in E}
-    snap = {}
-    log = {}
-    total = {}
+    ops = []
+    v, sc = g.vector, g.scalar
 
     def u(name, lo=0, hi=None, st=1, p=None):
-        buf, o, n, _d = _ARENA[name]
+        buf, o, n, d = _ARENA[name]
         hi = n if hi is None else hi
         a, b = o + lo, o + hi
         rows = slice(None) if p is None else slice(p[0], p[1])
         t = T[buf]
         ap = t[rows, a:b:st] if st != 1 else t[rows, a:b]
-        return (ap, [(buf, a, b)])
+        return (ap, [(buf, a, b)], -(-(hi - lo) // st), d, False)
 
     def ix(win, off):
-        return (win[0].indirect(off[0]), win[1] + off[1])
+        return (win[0].indirect(off[0]), win[1] + off[1], 16 * off[2], win[3], off)
+
+    def op(e, fn, outs, ins, cost, dma=None, lat=0.0, items=None, land=None):
+        rd = [r for x in ins for r in x[1]]
+        wr = []
+        for x in outs:
+            if len(x) > 4 and x[4]:
+                wr += x[1][:1]
+                rd += x[1][1:]
+            else:
+                wr += x[1]
+        ops.append({"e": e, "fn": fn, "rd": rd, "wr": wr, "cost": cost, "dma": dma, "lat": lat, "items": items, "land": land, "tag": TAG[0]})
+
+    def _c(x):
+        return x[0] if isinstance(x, tuple) else x
+
+    def _r(*xs):
+        return [x for x in xs if isinstance(x, tuple)]
+
+    def cost(o, ins, per):
+        if o[4]:
+            return 0.05 + o[2] * SCA * CYC
+        if ins and ins[0][4]:
+            return 0.05 + o[2] * GAT * CYC
+        if per == 0.5 and any(x[3] not in (B, H, U) for x in [o] + ins):
+            per = 1.0
+        return max(64, o[2] * per) * CYC
+
+    def cp(o, i):
+        op("v", lambda: v.tensor_copy(o[0], i[0]), [o], [i], cost(o, [i], 0.5))
+
+    def ts(o, i, s1, o1, s2=None, o2=None):
+        if o2 is None:
+            op("v", lambda: v.tensor_scalar(o[0], i[0], _c(s1), None, o1), [o], [i] + _r(s1), cost(o, [i], 0.5))
+        else:
+            op("v", lambda: v.tensor_scalar(o[0], i[0], _c(s1), _c(s2), o1, o2), [o], [i] + _r(s1, s2), cost(o, [i], 0.5))
+
+    def tt(o, a, b, o1):
+        per = 1.0 if _psum(a[1][0][0]) or _psum(b[1][0][0]) else 2.0
+        op("v", lambda: v.tensor_tensor(o[0], a[0], b[0], o1), [o], [a, b], cost(o, [a, b], per))
+
+    def scan(o, a, b, o1, o2):
+        op("v", lambda: v.tensor_tensor_scan(o[0], a[0], b[0], 0.0, o1, o2), [o], [a, b], cost(o, [a, b], 0.5))
+
+    def fill(o, c):
+        op("v", lambda: v.memset(o[0], c), [o], [], cost(o, [], 0.5))
+
+    def act(o, i, f, scale=None, bias=None, acc=None):
+        kw = {}
+        if scale is not None:
+            kw["scale"] = _c(scale)
+        if bias is not None:
+            kw["bias"] = _c(bias)
+        if acc is not None:
+            kw["accum_out"] = acc[0]
+        op("s", lambda: sc.activation(o[0], i[0], f, **kw), [o] + _r(acc), [i] + _r(scale, bias), cost(o, [i], 1.0) + 0.06)
+
+    def iota(o, pat, base, cm=0):
+        if o[3] == I:
+            op("k", lambda: g.iota(o[0], pat, base, cm), [o], [], 0.13 + 2 * o[2] * CYC)
+        else:
+            op("k", lambda: g.iota(o[0], pat, base, cm, allow_small_or_imprecise_dtypes=True), [o], [], 0.13 + 2 * o[2] * CYC)
+
+    def mm(items):
+        c = sum(max(min(64, a[2]), b[2]) * (4 if a[3] == S else 1) for (_o, a, b) in items) * CYC
+        op("p", None, [x[0] for x in items], [y for x in items for y in x[1:]], c, items=items)
+
+    def dma(e, o, i, sem):
+        op(e, lambda: E[e].dma_start(o[0], i[0]), [o], [i], 0.1, dma=sem, lat=3.0)
+
+    def ext(ap, name):
+        return (ap, [(name, 0, 1)])
+
+    def send(dst, src, buf_dst, sem, fwd, loc, which, back):
+        to = _relay(topo, core, dst, which)
+        d = dst if to is None else to
+        m, n = _mask(topo, core, d)
+        rid, pid = topo.addr(d, core)
+        via = _relay(topo, back, core, which)
+        nb = _mask(topo, back if via is None else via, core)[1]
+        op("k", lambda: g.remote_dma(T[buf_dst][:], src[0], T.sem[sem if to is None else fwd], T.sem[loc], pid, rid, m),
+           [u(buf_dst)], [src], 0.3, lat=WAY, land=(sem, nb, loc, n))
+
+    def e16(name, k=0, n=None, p=None):
+        return u(name, k, n, 16, p)
+
+    def hold(o, z):
+        scan(o, u("MS", 0, 128), z, A.mult, A.add)
+
+    def sums(ps, base, src, w, p=None):
+        return [(u(ps, base + k, base + 128, 16, p), u(src, k, None, 16), u(w)) for k in range(16)]
+
+    def tile(z, h, ps, sign, extra, p=None, n=8):
+        scan(u(h, 0, 128, 1, p), u("MC", p=p), u(z, 0, 128, 1, p), A.mult, A.add)
+        a, b = ("blk", "nblk") if sign > 0 else ("nblk", "blk")
+        mm([(ps, u(h, 0, 128, 1, p), u(a, 0, n, 1, p)), (ps, u(h, 1, 129, 1, p), u(b, 0, n, 1, p)), (ps, u(z, 1, 129, 1, p), u(a, 0, n, 1, p))]
+           + [(ps, x, y) for x, y in extra])
+
+    def low(z, key, hi, step):
+        c = 1.5 * 2.0 ** 23 * step
+        ts(hi, key, c, A.add, c, A.subtract)
+        tt(z, key, hi, A.subtract)
+
+    TAG[0] = "init"
+    fill(u("X", 0, 16), 0.0)
+    fill(u("X", 2048, 2304), 0.0)
+    fill(u("AC4", 0, 8), 0)
+    fill(u("AC4", 2048, 2192), 0)
+    dma("y", u("MI"), ext(T.ml[:], "in_ml"), "ld0")
+    dma("s", u("X", 1, 2049), ext(T.x0[:], "in_x"), "ld1")
+    dma("y", u("LI"), ext(T.lims[:], "in_l"), "ld2")
+    dma("y", u("WI"), ext(T.wt[:], "in_w"), "ld3")
+    for q in range(4):
+        dma("y", u("AC4", 1 + 512 * q, 513 + 512 * q), ext(T.ac[:], "in_a"), "ld%d" % (4 + q))
+    iota(u("PIi", 0, 1), [[0, 1]], 0, 1)
+    iota(u("J", 0, 144), [[1, 144]], 0)
+    iota(u("IOT"), [[1, 128], [0, 16]], 128)
+    iota(u("Z0"), [[0, 2048]], 0)
+    iota(u("J2f"), [[1, 128], [0, 4]], 128)
+    iota(u("J3"), [[0, 128], [1, 4]], 0)
+    iota(u("J", 144, 512), [[1, 368]], 144)
+    iota(u("FREE", 0, 1024), [[0, 1024]], 0)
+    iota(u("Z1"), [[0, 2048]], 0)
+    fill(u("MS"), 1.0)
+    fill(e16("MS"), 0.0)
+    fill(u("OT", 0, 8), 0.0)
+    fill(u("OT", 2048, 2064), 0.0)
+    fill(u("W", 512, 640), 0.0)
+    J, J4, J15 = u("Jh"), u("J4h"), u("J15h")
+    J144, J8 = u("J", 0, 144), u("J", 0, 8)
+    pc = [3]
+
+    def col(src, s1, o1, s2=None, o2=None):
+        c = u("PC", pc[0], pc[0] + 1)
+        pc[0] += 1
+        ts(c, src, s1, o1, s2, o2)
+        return c
+    P, P4, P15 = u("PC", 0, 1), u("PC", 1, 2), u("PC", 2, 3)
+    ts(u("PIi", 1, 2), u("PIi", 0, 1), 4, A.logical_shift_right)
+    ts(u("PIi", 2, 3), u("PIi", 0, 1), 15, A.bitwise_and)
+    cp(u("PC", 0, 3), u("PIi", 0, 3))
+    ts(u("J4"), u("J", 0, 128), 4, A.logical_shift_right)
+    ts(u("J15"), u("J", 0, 128), 15, A.bitwise_and)
+    cp(J, u("J", 0, 128))
+    cp(J4, u("J4"))
+    cp(J15, u("J15"))
+    row4 = col(P15, 4.0, A.is_equal)
+    row0 = col(P15, 0.0, A.is_equal)
+    cls = [col(P15, float(c), A.is_equal, 64.0, A.mult) for c in range(4)]
+    ts(u("DUM"), J, 16.0, A.mult, col(P15, 2064.0, A.add), A.add)
+
+    ts(u("p6"), u("MI"), 2048, A.is_lt)
+    ts(u("t512a"), u("MI"), 1, A.add)
+    tt(u("W", 0, 512), u("t512a"), u("p6"), A.mult)
+
+    def owners(c):
+        ino = u("INO", 128 * c, 128 * c + 128)
+        ts(u("p5", 0, 128), u("MI", c, None, 4), 2048, A.is_equal)
+        tt(u("p5", 128, 256), u("DUM"), u("p5", 0, 128), A.mult)
+        tt(u("e128"), u("W", c, 512, 4), u("p5", 128, 256), A.max)
+        cp(ino, u("e128"))
+        for h in range(2):
+            a, b = 1024 * h, 1024 * h + 1024
+            off = u("INO", 128 * c + 64 * h, 128 * c + 64 * h + 64)
+            if OPT["sc"][c] == "v":
+                ts(u("VB", a, b), u("IOT", a, b), row4, A.mult, cls[c], A.add)
+                cp(ix(u("OT"), off), u("VB", a, b))
+            else:
+                ve = "VE" if c % 2 == 0 else "VG"
+                act(u(ve, a, b), u("IOT", a, b), F.Identity, scale=row4, bias=cls[c])
+                act(ix(u("OT"), off), u(ve, a, b), F.Silu)
+
+    for name, val in (("IDB", 1.0), ("NIDB", -1.0), ("ID16", 1.0), ("NID16", -1.0), ("N24", -2.0 ** 24), ("N20", -2.0 ** 20), ("P20", 2.0 ** 20),
+                      ("P25", 2.0 ** 25), ("N13", -2.0 ** 13), ("P12", 2.0 ** 12), ("P11", 2.0 ** 11)):
+        ts(u(name), J, P, A.is_equal, val, A.mult)
+    ts(u("ID2", 0, 128), J, P, A.is_equal, 16.0, A.mult)
+    ts(u("ID2", 128, 256), J, P, A.is_equal, 16.0, A.mult)
+    ts(u("BD"), J4, P4, A.is_equal)
+    ts(u("NBD"), J4, P4, A.is_equal, -1.0, A.mult)
+    ts(u("BDn"), J4, P4, A.is_equal, -128.0, A.mult)
+    ts(u("R16"), J15, P15, A.is_equal)
+    ts(u("MC"), J15, P15, A.is_le)
+    fill(e16("MC"), 0.0)
+    ts(u("blk"), J8, P4, A.is_equal)
+    ts(u("nblk"), J8, P4, A.is_equal, -1.0, A.mult)
+    ts(u("nblkb"), J8, P4, A.is_equal, -1.0, A.mult)
+    ts(u("nblkf"), J8, P4, A.is_equal, -1.0, A.mult)
+    for name, val in (("w64k", 65536.0), ("w8k", 8192.0), ("w32", 32.0)):
+        ts(u(name), e16("BD"), val, A.mult)
+    fill(u("ONEB"), 1.0)
+    cp(u("ONE16"), u("ONEB"))
+    for z in "ZS HS ZB HB ZD HD ZQ HQ".split():
+        ts(u(z), J144, 0.0, A.mult)
+    fill(u("ZM"), 0.0)
+    fill(u("ZW"), 0.0)
+
+    def rows(name, slope, c1, c2, lo=0):
+        a = col(P, 0.0, A.is_equal, slope, A.mult)
+        b = col(P, 1.0, A.is_equal, c1, A.mult)
+        if c2:
+            tt(b, b, col(P, 2.0, A.is_equal, c2, A.mult), A.add)
+        ts(u(name, lo, lo + 128), J15, a, A.mult, b, A.add)
+    rows("KAs", 4096.0, 2.0 ** 24, -1088.0)
+    rows("KAb", -1.0, -2.0 ** 20, 7.0)
+    rows("KAn", 512.0, 2.0 ** 24, 0)
+    rows("KAq", 1.0, 2.0 ** 20, -8.0)
+    fill(u("KAp", 0, 128), 0.0)
+    rows("KAp", 1.0, -65536.0, 0, 128)
+    fill(u("KAd"), 2.0 ** 17)
+    fill(u("K12"), 2.0 ** 5)
+    fill(u("K13"), 2.0 ** 6)
+    fill(u("K14"), 2.0 ** 7)
+    fill(u("MIN"), -BIG)
+    fill(e16("MIN"), BIG)
+    fill(u("MINs"), -BIG)
+    ts(e16("MINs"), J8, 0.0, A.mult, col(P, 255.0 * 65536 + 2049 - 1088, A.add), A.add)
+    fill(u("MINn"), -BIG)
+    cp(u("CREP"), J)
+    ts(u("SEL0R"), u("BD"), row0, A.mult)
+    ts(u("SEL0"), e16("BD"), row0, A.mult)
+    ts(u("N25"), u("SEL0R"), -2.0 ** 25, A.mult)
+    hw = col(P15, 4.0, A.is_lt, 1.0 / 64, A.mult)
+    tt(hw, hw, P15, A.mult)
+    tt(hw, hw, col(row4, 4.0, A.mult), A.add)
+    ts(u("HWN"), u("NBD"), hw, A.mult)
+    for c in range(4):
+        ts(u("og%d" % c), e16("BD"), col(cls[c], 2.0 ** 13, A.mult, hw, A.add), A.mult)
+    last = col(P4, 16.0, A.mult, 15.0, A.add)
+    ts(u("Y"), J144, last, A.is_equal, row0, A.mult)
+    ts(u("Y2"), J144, last, A.is_equal, 2.0, A.mult)
+    ts(u("HY"), J144, last, A.is_equal, hw, A.mult)
+    ts(u("e128"), J, P, A.is_gt)
+    ts(u("m1"), J, P, A.is_equal, -4096.0, A.mult)
+    tt(u("TRIm"), u("e128"), u("m1"), A.add)
+    ts(u("NTRIm"), u("TRIm"), -1.0, A.mult)
+    tt(u("m2"), u("e128"), u("BD"), A.mult)
+    ts(u("m1"), u("m1"), 16.0, A.mult)
+    tt(u("BTX", 0, 128), u("m2"), u("m1"), A.add)
+    ts(u("BTX", 128, 256), u("BTX", 0, 128), -1.0, A.mult)
+    ts(u("m2"), J, P, A.is_lt)
+    tt(u("BTI"), u("m2"), u("BD"), A.mult)
+    tt(u("BTI"), u("BTI"), u("P12"), A.add)
+    ts(u("m1"), J, P, A.is_equal, -4.0, A.mult)
+    ts(u("m2"), u("m2"), -56.0, A.mult, -8.0, A.add)
+    tt(u("PEN", 0, 128), u("m2"), u("m1"), A.add)
+    cp(u("PEN", 128, 256), u("PEN", 0, 128))
+    cp(u("PEN", 256, 512), u("PEN", 0, 256))
+    ts(u("CMR"), u("R16"), col(P, 128.0, A.add), A.mult)
+    c4 = col(P, 4.0, A.mult, 1024.0, A.add)
+    for c in range(4):
+        ts(u("CMK%d" % c), u("R16"), col(c4, float(c), A.add), A.mult)
+    for name, lo, val in (("CNT", 0, -1920.0), ("CNT", 128, -3968.0)):
+        ts(u(name, lo, lo + 128), u("R16"), 8192.0 + val, A.mult, -8192.0, A.add)
+    for lo, val in ((0, -1536.0), (128, -1024.0)):
+        ts(u("CTG", lo, lo + 128), u("R16"), col(P, 8192.0 + val, A.add), A.mult, -8192.0, A.add)
+    ts(u("CB"), J8, 256.0, A.mult, col(P15, 16.0, A.mult, 7.0, A.add), A.add)
+    ts(u("CQ"), u("CB"), 1.0, A.add)
+    ts(u("CT"), J8, 16.0, A.mult, P15, A.add)
+    ts(u("CIX"), u("J", 0, 32), 16.0, A.mult, P15, A.add)
+    ts(u("C512"), u("CIX"), 512.0, A.add)
+    fill(u("C25"), 2.0 ** 25)
+    fill(u("DS", 2176, 2304), 0.0)
+    fill(u("QZ"), 0.0)
+    fill(u("Aa"), 0)
+    for t in range(RO):
+        fill(u("XV%d" % t), 0.0)
+    V0 = u("FREE", 1024, 1536)
+    act(u("p4"), u("J2f"), F.Identity, scale=row4)
+    ts(u("t512b"), u("J3"), P15, A.is_equal, col(P15, 4.0, A.is_lt, 64.0, A.mult), A.mult)
+    tt(V0, u("t512b"), u("p4"), A.add)
+    half = u("PC", 47, 48)
+    scale2 = u("m1", 0, 16)
+    fill(scale2, 0.5)
+    fill(u("m2", 0, 16), 0.0)
+    op("v", lambda: v.tensor_tensor_scan(u("m1", 16, 32)[0], scale2[0], u("m2", 0, 16)[0], 1.0, A.mult, A.add), [u("m1", 16, 32)], [scale2, u("m2", 0, 16)], 0.07)
+    tt(u("m2", 16, 32), u("m1", 16, 32), u("R16", 0, 16), A.mult)
+    op("v", lambda: v.tensor_reduce(half[0], u("m2", 16, 32)[0], AX_.X, A.add), [half], [u("m2", 16, 32)], 0.07)
+    ts(u("Qi"), u("J"), half, A.mult, -0.499, A.add)
+    ts(u("p7"), u("J"), half, A.mult)
+    tt(u("t512b"), u("Qi"), u("p7"), A.subtract)
+    ts(u("CODE"), u("t512b"), -0.5, A.is_le, 2.0, A.mult)
+    ts(u("CODE"), u("CODE"), -1.0, A.add, col(P15, 9.0, A.is_lt), A.mult)
+    ts(u("m2", 32, 36), u("J", 0, 4), col(P15, -9.0, A.add), A.is_equal, 4.0, A.mult)
+    tt(u("CODE", 0, 4), u("CODE", 0, 4), u("m2", 32, 36), A.add)
+    ts(u("PIi", 3, 4), u("PIi", 1, 2), 3, A.bitwise_and)
+    ts(u("G4"), u("J", 0, 4), col(u("PIi", 3, 4), 1.0, A.mult), A.is_equal)
+    lim, lim2, wt = col(u("LI", 0, 1), -65536.0, A.mult), col(u("LI", 1, 2), -65536.0, A.mult), col(u("WI"), 1.0, A.mult)
+    ts(u("WY"), J144, last, A.is_equal, wt, A.mult)
+    ts(u("ROW1"), J8, 0.0, A.mult, col(P, 1.0, A.is_equal), A.add)
+    ts(u("z8"), u("ROW1"), -2048.0, A.mult)
+    ts(u("L2N"), u("SEL0"), lim2, A.mult)
+    tt(u("L2N"), u("L2N"), u("z8"), A.add)
+    ts(u("THN"), u("SEL0"), lim, A.mult)
+    tt(u("THN"), u("THN"), u("z8"), A.add)
+    ts(u("ROW1"), u("ROW1"), -65536.0, A.mult)
+    fill(u("THZ"), 0.0)
+    for s in range(16):
+        o, i = u("SH", 128 * s, 128 * s + 128), u("BD")
+        op("k", lambda o=o, i=i, s=s: g.affine_select(o[0], i[0], [[1, 128]], A.is_equal, 0.0, -s, -1), [o], [i], 0.43)
+
+    win = u("X", 0, 2192)
+
+    def gather(out, off, cut):
+        if cut:
+            cp(u(out, 0, 16 * cut), ix(win, u(off, 0, cut)))
+        if cut < 128:
+            act(u(out, 16 * cut, 2048), ix(win, u(off, cut, 128)), F.Copy)
+
+    def part_own(t):
+        TAG[0] = "own%d" % t
+        cl = t % 4
+        z, s1, s16 = "Z%d" % (t % 2), "S1" + "ab"[t % 2], "S16" + "ab"[t % 2]
+        lanes = u("W", cl, 512, 4)
+        cp(u("OWN"), lanes)
+        gather("T", "OWN", OPT["T"])
+        act(u("PRE"), lanes, F.Sign)
+        cp(u("OWNH"), lanes)
+        k = u("p3", 0, 128)
+        mm([(k, u("ONEB"), u("KAs")), (k, u("PRE"), u("N24")), (k, u("OWNH"), u("ID16"))] + sums("p3", 0, "T", "w64k"))
+        scan(u(s1), u("MINs"), k, A.max, A.min)
+        low(e16("ZS", 0, 128), e16(s1, 15), u("hi8"), 4096)
+        tile("ZS", "HS", u("p4", 0, 8), 1, [])
+        ts(u(s16), u("p4", 0, 8), 1088.0, A.add)
+        cp(e16(z), ix(win, u(s16)))
+        ts(u("AN"), ix(u("AC4"), u(s16)), 1, A.add)
+        scan(u("REP"), u("MS"), u(z), A.mult, A.add)
+        scan(u("US"), u("MS"), u("T"), A.mult, A.max)
+        mm([(u("p4", 8, 16), u("ONEB"), u("L2N")), (u("p4", 8, 16), e16("US", 15), u("w64k"))])
+        tt(u("wp8"), e16(s1, 15), u("p4", 8, 16), A.is_lt)
+        mm([(u("p6", 0, 128), u("PRE"), u("SEL0R"))])
+        act(u("LR"), u("p6", 0, 128), F.Copy)
+
+    def part_vacant(t):
+        TAG[0] = "vac%d" % t
+        act(u("OCC"), u("W", 0, 512), F.Sign)
+        mm([(u("p6", 128, 160), u("Y", 15 - r, 143 - r), e16("OCC", r)) for r in range(16)])
+        act(u("OCb"), u("p6", 128, 160), F.Copy)
+        mm([(u("p4", 32, 64), u("BD"), u("OCb"))])
+        mm([(u("p4", 64, 96), u("BTI"), u("OCb")), (u("p4", 64, 96), u("ID16"), u("CIX"))])
+        scan(u("CS"), u("ONEB", 0, 32), u("p4", 32, 64), A.mult, A.add)
+        tt(u("r1"), u("p4", 64, 96), u("CS"), A.subtract)
+        tt(u("r2"), u("r1"), u("C512"), A.min)
+        cp(u("F16"), u("r2"))
+        act(ix(u("FREE", 0, 1024), u("F16")), V0, F.Silu)
+        act(u("mc", 0, 1), u("CS", 31, 32), F.Identity, scale=-1.0, bias=512.0)
+        act(u("NFH"), u("SEL0R"), F.Identity, scale=u("mc", 0, 1))
+        mm([(u("p6", 160, 288), u("ONEB"), u("NFH"))])
+        act(u("NFR"), u("p6", 160, 288), F.Copy)
+
+    def part_split(t):
+        TAG[0] = "split%d" % t
+        z = "Z%d" % (t % 2)
+        for c in range(4):
+            a, b = 512 * c, 512 * c + 512
+            ps = u("p%d" % (c % 3))
+            mm([(ps, u("IDB"), u("T", a, b)), (ps, u("NIDB"), u("REP", a, b))])
+            act(u("SQ", a, b), ps, F.Square)
+        act(u("SQS"), e16(z), F.Square)
+        k = u("p3", 128, 256)
+        mm([(k, u("ONEB"), u("KAb")), (k, u("PRE"), u("P20"))] + sums("p3", 128, "SQ", "w32"))
+        scan(u("SB"), u("MS", 0, 128), k, A.mult, A.max)
+        low(e16("ZB", 0, 128), e16("SB", 15), u("hb8"), 32)
+        tile("ZB", "HB", u("p4", 16, 24), -1, [(u("ID16"), u("CB"))])
+        cp(u("B16"), u("p4", 16, 24))
+        act(u("XB"), ix(u("T"), u("B16")), F.Copy)
+        act(u("SQB"), u("XB"), F.Square)
+        wv = u("p5", 0, 128)
+        mm([(wv, u("IDB"), e16(z)), (wv, u("NIDB"), u("XB"))])
+        for k in range(16):
+            tt(u("AW", 128 * k, 128 * k + 128), e16("T", k), wv, A.mult)
+        lv = u("p7", 0, 128)
+        mm([(lv, u("ONEB"), u("K13")), (lv, u("N13"), u("PRE")), (lv, u("BD"), u("SQB")), (lv, u("NBD"), u("SQS"))]
+           + [(lv, u("Y2", 15 - k, 143 - k), u("AW", 128 * k, 128 * k + 128)) for k in range(16)])
+        ts(u("L1T"), lv, 0.0, A.is_lt)
+        pp = u("p7", 128, 384)
+        mm([(pp, u("ONEB"), u("KAp")), (pp, u("OWNH"), u("ID2")), (pp, u("L1T"), u("BTX"))])
+        ts(u("Pa", 0, 256), pp, 0.0, A.max)
+        TAG[0] = "shift%d" % t
+        for s in range(4):
+            a, b = ("Pa", "Pb") if s % 2 == 0 else ("Pb", "Pa")
+            ts(u("Mi", 0, 256), u(a, 0, 256), 1 << s, A.bitwise_and)
+            ts(u("p5", 0, 256), u("Mi", 0, 256), 2.0 ** (16 - s), A.mult)
+            tt(u("p5", 256, 512), u(a, 0, 256), u("p5", 0, 256), A.subtract)
+            tt(u("Aa", 0, 256), u(a, 0, 256), u("p5", 0, 256), A.min)
+            tt(u(b, 0, 256), u("p5", 256, 512), u("Aa", 1 << s, 256 + (1 << s)), A.max)
+        ts(u("Mi", 0, 256), u("Pa", 0, 256), 4, A.logical_shift_right)
+        cp(u("SL"), u("Mi", 0, 256))
+        mm([(u("p6", 288, 416), u("SL", 0, 128), u("ID16")), (u("p6", 288, 416), u("NID16"), u("OWNH"))])
+        act(u("DS", 2048, 2176), u("p6", 288, 416), F.Copy)
+
+    def part_near(t):
+        TAG[0] = "near%d" % t
+        cl = t % 4
+        s1 = "S1" + "ab"[t % 2]
+        iota(e16("MINn"), [[0, 8]], 13 * 2 ** 20 + cl)
+        for h in range(2):
+            a, b = 1024 * h, 1024 * h + 1024
+            act(u("OG", a, b), ix(u("OT", 0, 2064), u("AN", 64 * h, 64 * h + 64)), F.Copy)
+            tt(u("AX", a, b), ix(win, u("AN", 64 * h, 64 * h + 64)), u("REP", a, b), A.subtract)
+            act(u("DU", a, b), u("AX", a, b), F.Square)
+        k = u("p3", 256, 384)
+        mm([(k, u("ONEB"), u("KAn")), (k, u("PRE"), u("N25"))] + sums("p3", 256, "OG", "og%d" % cl) + sums("p3", 256, "DU", "w8k"))
+        scan(u("S2"), u("MINn"), k, A.max, A.min)
+        cp(u("a8"), e16("S2", 15))
+        ts(u("d8"), u("a8"), 511, A.bitwise_and)
+        cp(e16("ZD", 0, 128), u("d8"))
+        tile("ZD", "HD", u("p4", 24, 32), 1, [])
+        cp(u("D16"), u("p4", 24, 32))
+        TAG[0] = "partner%d" % t
+        lists = ix(u("W", 0, 512), u("D16"))
+        cp(u("DM"), lists)
+        gather("DT", "DM", OPT["DT"])
+        act(u("PRD"), lists, F.Sign)
+        cp(u("DMH"), lists)
+        hold(u("D1R"), u("ZD", 0, 128))
+        keep = u("mc", 1, 2)
+        ts(keep, P15, 9.0 + cl, A.is_equal)
+        ts(keep, P15, 9.0, A.is_lt, keep, A.add)
+        ts(u("kq"), u("G4"), keep, A.mult)
+        for q in range(4):
+            act(u("CG", 128 * q, 128 * q + 128), ix(u("CODE"), u("D16")), F.Identity, scale=u("kq", q, q + 1))
+        for h in range(2):
+            ps = "p%d" % h
+            items = [(u(ps), u("IDB"), u("PEN"))]
+            for q in range(4):
+                x = u("CG", 128 * q, 128 * q + 128, 1, (64 * h, 64 * h + 64))
+                items.append((u(ps, 128 * q, 128 * q + 128), x, x))
+            mm(items)
+            act(u("EQ", 512 * h, 512 * h + 512), u(ps), F.Relu)
+        mm([(u("p6", 416, 424), u("PRE"), e16("BD")), (u("p6", 416, 424), u("PRD"), e16("BD"))])
+        act(u("SZ"), u("p6", 416, 424), F.Relu, bias=-16.0)
+        k = u("p3", 384, 512)
+        mm([(k, u("ONEB"), u("KAd")), (k, u("PRD"), u("N24"))] + sums("p3", 384, "DT", "w64k"))
+        scan(u("AX"), u("MS"), u("DT"), A.mult, A.max)
+        tt(u("Vv"), e16("US", 15), e16("AX", 15), A.max)
+        th = u("p4", 96, 104)
+        mm([(th, u("ONEB"), u("THN")), (th, u("ONEB"), u("THZ")), (th, u("P25"), u("SZ"))]
+           + [(u("p4", 96 + q, 97 + q), u("EQ", 128 * q, 128 * q + 128), u("C25", 0, 1)) for q in range(8)] + [(th, u("Vv"), u("w64k"))])
+        scan(u("S3"), u("MIN"), k, A.max, A.min)
+        tt(u("mn8"), e16("S3", 15), e16(s1, 15), A.min)
+        for c in range(4):
+            ps = "p%d" % (2 - c % 2)
+            for q in range(4):
+                s = 4 * c + q
+                mm([(u(ps, 128 * q, 128 * q + 128), u("SH", 128 * s, 128 * s + 128), u("DMH"))])
+            act(u("DS", 512 * c, 512 * c + 512), u(ps), F.Copy)
+
+    def part_finish(t):
+        TAG[0] = "fin%d" % t
+        cl = t % 4
+        z, rt = "Z%d" % (t % 2), "RT16" + "ab"[t % 2]
+        tt(e16("ZM"), u("mn8"), u("p4", 96, 104), A.is_ge)
+        tt(e16("ZW"), u("wp8"), e16("ZM"), A.is_gt)
+        hold(u("WR"), u("ZW"))
+        hold(u("MR"), u("ZM"))
+        k1 = u("p7", 384, 512)
+        mm([(k1, u("ONEB"), u("K12")), (k1, u("TRIm"), u("WR"))])
+        tt(u("SR"), k1, u("NFR"), A.is_lt)
+        tt(u("KP"), k1, u("CMK%d" % cl), A.min)
+        k2 = u("p7", 0, 128)
+        mm([(k2, u("ONEB"), u("K12")), (k2, u("TRIm"), u("LR")), (k2, u("NTRIm"), u("MR")), (k2, u("NTRIm"), u("SR"))])
+        tt(u("RP"), k2, u("CMR"), A.min)
+        mm([(u("p4", 104, 112), u("RP"), u("blk"))])
+        cp(u(rt), u("p4", 104, 112))
+        xv = "XV%d" % t
+        cp(ix(u(xv), u(rt)), e16(z))
+        send(T.cores[(rank + 1 + t % 7) % 8], u(xv, 0, 32), "QI%d" % t, "rq%d" % t, "fq%d" % t, "lq%d" % t, 0, T.cores[(rank - 1 - t % 7) % 8])
+        q = u("p6", 0, 256)
+        mm([(q, u("ID16"), u("CNT")), (u("p6", 0, 128), u("PRE"), u("BDn")), (u("p6", 0, 128), u("P12"), u("MR")), (u("p6", 128, 256), u("P12"), u("SR"))])
+        act(u("QN"), q, F.Relu)
+        nt = u("p4", 112, 120)
+        mm([(nt, u("ID16"), u("CT")), (nt, u("QN", 0, 128), u("nblkb")), (nt, u("QN", 128, 256), u("nblkb"))])
+        ts(u("NT16"), nt, 2176.0, A.add)
+        tt(u("W", cl, 512, 4), ix(u("DS"), u("NT16")), u("OWNH"), A.add)
+        mm([(u("p4", 120, 128), u("KP"), u("blk"))])
+        cp(u("K16"), u("p4", 120, 128))
+        act(u("EVb"), ix(u("FREE"), u("K16")), F.Copy)
+        act(u("EV"), ix(u("FREE"), u("K16")), F.Copy)
+        q = u("p0", 0, 256)
+        mm([(q, u("ID16"), u("CTG")), (u("p0", 0, 128), u("NID16"), u("D1R")), (u("p0", 0, 128), u("P11"), u("MR")),
+            (u("p0", 128, 256), u("P11"), u("SR")), (u("p0", 128, 256), u("EVb"), u("HWN"))])
+        act(u("QR", 0, 256), q, F.Relu)
+        tg = u("p4", 128, 136)
+        mm([(tg, u("ID16"), u("CT")), (tg, u("QR", 0, 128), u("nblkf")), (tg, u("QR", 128, 256), u("nblkf"))])
+        ts(u("TG16"), tg, 512.0, A.add)
+        el = u("p1", 0, 128)
+        mm([(el, u("SL", 128, 256), u("ID16")), (el, u("MR"), u("N13"))])
+        act(u("ELS"), el, F.Relu)
+        cp(ix(u("W"), u("TG16")), u("ELS"))
+        a, b = u("p7", 128, 256), u("p7", 256, 384)
+        mm([(a, u("ONEB"), u("K14")), (a, u("ID16"), u("DMH")), (a, u("N13"), u("PRD")), (a, u("MR"), u("N13"))])
+        mm([(b, u("ONEB"), u("K14")), (b, u("ID16"), u("OWNH")), (b, u("N13"), u("L1T")), (b, u("SR"), u("N13"))])
+        tt(u("m1"), a, u("DUM"), A.min)
+        tt(u("m2"), b, u("m1"), A.min)
+        cp(u("MVO"), u("m2"))
+        n = OPT["mv"]
+        for h in range(n):
+            a, b = 2048 // n * h, 2048 // n * (h + 1)
+            act(u("VE", a, b), ix(u("EV"), u("CREP", a // 16, b // 16)), F.Copy)
+            act(ix(u("OT"), u("MVO", a // 16, b // 16)), u("VE", a, b), F.Silu)
+        if t + 1 < RO:
+            mm([(u("p6", 424, 432), u("ONEB"), e16("ZM"))])
+            act(u("z8"), u("p6", 424, 432), F.Identity, bias=-0.9375, acc=u("mc", 4, 5))
+            c = 1.5 * 2.0 ** 27
+            ts(u("mc", 5, 6), u("mc", 4, 5), c, A.add, c, A.subtract)
+            ts(u("mc", 6, 7), u("mc", 4, 5), u("mc", 5, 6), A.subtract, 7.5, A.add)
+            act(u("THZ"), u("ROW1"), F.Identity, scale=u("mc", 6, 7))
+
+    def part_serve(t):
+        TAG[0] = "serve%d" % t
+        src = T.cores[(rank - 1 - t % 7) % 8]
+        qi, sn = "QI%d" % t, "SN%d" % t
+        p32 = (0, 32)
+        a = u("p4", 136, 138)
+        mm([(a, u("WY", 15 - j, 143 - j), e16(qi, j)) for j in range(16)])
+        cp(u("VI"), a)
+        ts(u("VI2"), u("VI"), 2047, A.bitwise_and)
+        ts(u("VV16"), u("VI2"), 1, A.add)
+        cp(e16("QZ"), u(qi))
+        act(u("QP"), u(qi), F.Identity, bias=128.0)
+        scan(u("QRp"), u("MS", 0, 512), u("QZ"), A.mult, A.add)
+        act(u("HO"), ix(u("OT", 0, 2064), u("VV16")), F.Copy)
+        a = u("p4", 138, 140)
+        mm([(a, u("HY", 15 - j, 143 - j), e16("HO", j)) for j in range(16)])
+        ts(u("H16"), a, -512.0, A.add)
+        cp(u("HL"), ix(u("W", 0, 512), u("H16")))
+        act(u("PRH"), ix(u("W", 0, 512), u("H16")), F.Sign)
+        tt(u("QD"), ix(win, u("HL")), u("QRp"), A.subtract)
+        act(u("QS"), u("QD"), F.Square)
+        k = u("p2", 0, 128, 1, p32)
+        mm([(k, u("ONEB", 0, 32), u("KAq")), (k, u("PRH"), u("N20"))] + sums("p2", 0, "QS", "w32", p32))
+        scan(u("QSC", p=p32), u("MIN", p=p32), k, A.max, A.min)
+        low(e16("ZQ", 0, 128, p32), e16("QSC", 15, None, p32), u("hq8", p=p32), 32)
+        tile("ZQ", "HQ", u("p4", 140, 142), 1, [(u("ID16"), u("CQ", 0, 2))], p32, 2)
+        cp(u("J16"), u("p4", 140, 142))
+        ts(u("hs"), ix(u("QD"), u("J16")), 0.5, A.mult, -0.25, A.add)
+        tt(u(sn), u("hs"), u("QP"), A.add)
+        send(src, u(sn), "RS%d" % t, "rs%d" % t, "fs%d" % t, "ls%d" % t, 1, T.cores[(rank + 1 + t % 7) % 8])
+
+    def part_apply(t):
+        TAG[0] = "apply%d" % t
+        xv = "XV%d" % t
+        act(u(xv, 0, 32), u("RS%d" % t), F.Identity, bias=-128.0)
+        act(u("NV"), ix(u(xv), u("RT16" + "ab"[t % 2])), F.Copy)
+        cp(ix(win, u("S16" + "ab"[t % 2])), u("NV"))
+
+    for c in range(4):
+        TAG[0] = "init"
+        owners(c)
+    part_own(0)
+    part_vacant(0)
+    part_split(0)
+    for t in range(RO):
+        part_near(t)
+        part_finish(t)
+        if t + 1 < RO:
+            part_own(t + 1)
+            part_vacant(t + 1)
+            part_split(t + 1)
+        else:
+            ts(u("t512a"), u("W", 0, 512), 0.0, A.is_equal, 2049.0, A.mult)
+            act(u("p1"), u("W", 0, 512), F.Identity, bias=-1.0)
+            tt(u("YM"), u("t512a"), u("p1"), A.add)
+            dma("y", ext(T.ym[:], "out_m"), u("YM"), "st0")
+        part_serve(t)
+        part_apply(t)
+    dma("y", ext(T.yx[:], "out_x"), u("X", 1, 2049), "st1")
+
+    if "o" not in _ORDER:
+        _ORDER["o"] = _order(ops)
+    cnt = {"v": 0, "p": 0, "s": 0, "k": 0}
+    known = {e: {} for e in E}
+    snap, log, total = {}, {}, {}
 
     def need(e, reads, writes):
         w = {}
-
-        def add(sem, val):
-            if w.get(sem, 0) < val:
-                w[sem] = val
         for kind, lst in ((0, reads), (1, writes)):
             for (b, lo, hi) in lst:
-                psum = len(b) == 2 and b[0] == "p"
+                psum = _psum(b)
                 for (l2, h2, e2, sem, val, wr) in log.get(b, ()):
                     if psum:
-                        if e2 == e:
-                            if not (wr and e != "p") or (kind == 1 and not wr) or not (lo < h2 and l2 < hi):
-                                continue
-                        add(sem, val)
-                    elif lo < h2 and l2 < hi and (kind or wr):
-                        if e2 == e and e in ("v", "s", "p") and not wr:
+                        if e2 == e and (e == "p" or not (lo < h2 and l2 < hi and (kind or wr))):
                             continue
-                        add(sem, val)
+                    elif not (lo < h2 and l2 < hi and (kind or wr)):
+                        continue
+                    if w.get(sem, 0) < val:
+                        w[sem] = val
         return w
 
     def wait(e, w):
@@ -196,617 +821,40 @@ def rank_program(g, core, T, topo):
         total[sem] = val
         for (b, lo, hi) in writes:
             old = log.get(b, [])
-            log[b] = [x for x in old if not (lo <= x[0] and x[1] <= hi)] + [(lo, hi, e, sem, val, True)]
+            log[b] = [x for x in old if not (lo <= x[0] and x[1] <= hi and (x[2] == e or not _psum(b)))] + [(lo, hi, e, sem, val, True)]
         for (b, lo, hi) in reads:
             old = log.get(b, [])
             log[b] = [x for x in old if not (x[2] == e and not x[5] and lo <= x[0] and x[1] <= hi and x[3] == sem)] + [(lo, hi, e, sem, val, False)]
 
-    def op(e, fn, outs, ins, dma=None):
-        rd = [r for x in ins for r in x[1]]
-        wr = [r for x in outs for r in x[1]]
-        wait(e, need(e, rd, wr))
-        i = fn()
-        if dma:
-            i.then_inc(T.sem[dma], 16)
-            note(e, rd, wr, dma, 16)
+    for i in _ORDER["o"]:
+        o = ops[i]
+        e, rd, wr = o["e"], o["rd"], o["wr"]
+        TAG[0] = o["tag"]
+        if o["items"]:
+            wait(e, need(e, [], wr))
+            n = len(o["items"])
+            for j, (x, a, b) in enumerate(o["items"]):
+                wait(e, need(e, a[1] + b[1], []))
+                ins = g.tensor.matmul(x[0], a[0], b[0], j == 0, j == n - 1)
+        elif o["land"]:
+            sem, nb, loc, n = o["land"]
+            wait(e, need(e, rd, []))
+            o["fn"]()
+            note(e, rd, [], loc, n)
+            snap[(loc, n)] = {}
+            log[wr[0][0]] = [(wr[0][1], wr[0][2], "far", sem, nb, True)]
+            total[sem] = nb
+            continue
+        else:
+            wait(e, need(e, rd, wr))
+            ins = o["fn"]()
+        if o["dma"]:
+            ins.then_inc(T.sem[o["dma"]], 16)
+            note(e, rd, wr, o["dma"], 16)
         else:
             cnt[e] += 1
-            i.then_inc(T.sem[e], 1)
+            ins.then_inc(T.sem[e], 1)
             note(e, rd, wr, e, cnt[e])
-
-    def _c(x):
-        return x[0] if isinstance(x, tuple) else x
-
-    def _r(*xs):
-        return [x for x in xs if isinstance(x, tuple)]
-
-    v, sc = g.vector, g.scalar
-
-    def cp(o, i, scatter=None):
-        op("v", lambda: v.tensor_copy(o[0], i[0]), [o], [i] + (scatter or []))
-
-    def ts(o, i, s1, o1, s2=None, o2=None):
-        if o2 is None:
-            op("v", lambda: v.tensor_scalar(o[0], i[0], _c(s1), None, o1), [o], [i] + _r(s1))
-        else:
-            op("v", lambda: v.tensor_scalar(o[0], i[0], _c(s1), _c(s2), o1, o2), [o], [i] + _r(s1, s2))
-
-    def tt(o, a, b, o1):
-        op("v", lambda: v.tensor_tensor(o[0], a[0], b[0], o1), [o], [a, b])
-
-    def scan(o, a, b, o1, o2):
-        op("v", lambda: v.tensor_tensor_scan(o[0], a[0], b[0], 0.0, o1, o2), [o], [a, b])
-
-    def fill(o, c):
-        op("v", lambda: v.memset(o[0], c), [o], [])
-
-    def act(o, i, f, scale=None, bias=None):
-        kw = {}
-        if scale is not None:
-            kw["scale"] = _c(scale)
-        if bias is not None:
-            kw["bias"] = _c(bias)
-        op("s", lambda: sc.activation(o[0], i[0], f, **kw), [o], [i] + _r(scale, bias))
-
-    def mm(items):
-        rd = [r for x in items for y in x[1:] for r in y[1]]
-        wr = [r for x in items for r in x[0][1]]
-        wait("p", need("p", rd, wr))
-        n = len(items)
-        for j, (o, a, b) in enumerate(items):
-            i = g.tensor.matmul(o[0], a[0], b[0], j == 0, j == n - 1)
-        cnt["p"] += 1
-        i.then_inc(T.sem.p, 1)
-        note("p", rd, wr, "p", cnt["p"])
-
-    def dma(e, o, i, sem):
-        op(e, lambda: E[e].dma_start(o[0], i[0]), [o], [i], dma=sem)
-
-    def ext(ap, name):
-        return (ap, [(name, 0, 1)])
-
-    def arrived(e, name, sem, n):
-        if known[e].get(sem, 0) < n:
-            E[e].wait_ge(T.sem[sem], n)
-            known[e][sem] = n
-        total[sem] = n
-
-    def send(dst, buf_src, buf_dst, sem, fwd, loc, which):
-        to = _relay(topo, core, dst, which)
-        d = dst if to is None else to
-        m, n = _mask(topo, core, d)
-        rid, pid = topo.addr(d, core)
-        name = _ARENA[buf_src][0]
-        wait("k", need("k", [(name, 0, 32)], []))
-        g.remote_dma(T[buf_dst][:], T[buf_src][:, 0:32], T.sem[sem if to is None else fwd], T.sem[loc], pid, rid, m)
-        total[loc] = n
-
-    def landed_n(src, which):
-        via = _relay(topo, src, core, which)
-        return _mask(topo, src if via is None else via, core)[1]
-
-    def hold(o, z):
-        scan(o, u("MS", 0, 128), z, A.mult, A.add)
-
-    def k16(name, k, n=128, p=None):
-        return u(name, k, n, 16, p)
-
-    def sums(ps, base, src, w, p=None):
-        return [(u(ps, base + k, base + 128, 16, p), u(src, k, None, 16), u(w)) for k in range(16)]
-
-    fill(u("X", 0, 16), 0.0)
-    fill(u("X", 2048, 2304), 0.0)
-    fill(u("AC4", 0, 8), 0)
-    dma("y", u("MI"), ext(T.ml[:], "in_ml"), "ld0")
-    op("k", lambda: g.iota(u("PIi", 0, 1)[0], [[0, 1]], 0, 1), [u("PIi", 0, 1)], [])
-    op("k", lambda: g.iota(u("J")[0], [[1, 512]], 0, 0), [u("J")], [])
-    dma("s", u("X", 1, 2049), ext(T.x0[:], "in_x"), "ld1")
-    dma("y", u("LI"), ext(T.lims[:], "in_l"), "ld2")
-    dma("s", u("WI"), ext(T.wt[:], "in_w"), "ld3")
-    for q in range(4):
-        dma("y", u("AC4", 1 + 512 * q, 513 + 512 * q), ext(T.ac[:], "in_a"), "ld%d" % (4 + q))
-    op("k", lambda: g.iota(u("J2f")[0], [[1, 128], [0, 4]], 0, 0, allow_small_or_imprecise_dtypes=True), [u("J2f")], [])
-    op("k", lambda: g.iota(u("J3")[0], [[0, 128], [1, 4]], 0, 0), [u("J3")], [])
-    op("k", lambda: g.iota(u("Jf")[0], [[1, 512]], 1, 0, allow_small_or_imprecise_dtypes=True), [u("Jf")], [])
-    op("k", lambda: g.iota(u("OT", 0, 2064)[0], [[0, 2064]], 0, 0, allow_small_or_imprecise_dtypes=True), [u("OT", 0, 2064)], [])
-    op("k", lambda: g.iota(u("Z")[0], [[0, 2048]], 0, 0, allow_small_or_imprecise_dtypes=True), [u("Z")], [])
-
-    fill(u("MS"), 1.0)
-    fill(u("MS", 0, None, 16), 0.0)
-    fill(u("ZE"), 0.0)
-    fill(u("MIN"), -BIG)
-    fill(u("MIN", 0, None, 16), BIG)
-    fill(u("W", 0, 8), 0.0)
-    fill(u("W", 512, 664), 0.0)
-    J, J4, J15 = u("Jh", 0, 128), u("J4h"), u("J15h")
-
-    def col(n):
-        return u("PC", n, n + 1)
-    P, P4, P15 = col(0), col(1), col(2)
-    ts(u("PIi", 1, 2), u("PIi", 0, 1), 4, A.logical_shift_right)
-    ts(u("PIi", 2, 3), u("PIi", 0, 1), 15, A.bitwise_and)
-    cp(u("PC", 0, 3), u("PIi", 0, 3))
-    ts(u("J4"), u("J", 0, 128), 4, A.logical_shift_right)
-    ts(u("J15"), u("J", 0, 128), 15, A.bitwise_and)
-    cp(u("Jh"), u("J", 0, 144))
-    cp(J4, u("J4"))
-    cp(J15, u("J15"))
-    ts(col(3), P15, 4, A.is_equal)
-    ts(col(4), P15, 4, A.is_equal, 128.0, A.mult)
-    ts(col(5), P15, 5, A.is_equal)
-    ts(col(27), P15, 5, A.is_equal, 1024.0, A.mult)
-    act(u("p4"), u("J2f"), F.Identity, scale=col(3), bias=col(4))
-    act(u("p5"), u("Jf"), F.Identity, scale=col(5), bias=col(27))
-    ts(u("t512c"), u("J3"), P15, A.is_equal, 64.0, A.mult)
-    tt(u("t512c"), u("t512c"), u("p4"), A.add)
-    tt(u("V0"), u("t512c"), u("p5"), A.add)
-    ts(col(6), P15, 2064, A.add)
-    ts(u("DUM"), J, 16, A.mult, col(6), A.add)
-
-    def owners(c):
-        a, b = 128 * c, 128 * c + 128
-        ve = "VE" if c % 2 == 0 else "VG"
-        cp(u("ZE", 0, None, 16), u("V0", a, b))
-        scan(u(ve), u("MS"), u("ZE"), A.mult, A.add)
-        ts(u("p5", 0, 128), u("MI", a, b), 2048, A.is_equal)
-        tt(u("p5", 128, 256), u("DUM"), u("p5", 0, 128), A.mult)
-        tt(u("f128a"), u("W", 1 + a, 1 + b), u("p5", 128, 256), A.add)
-        cp(u("INO", a, b), u("f128a"))
-        act(ix(u("OT"), u("INO", a, b)), u(ve), F.Silu)
-
-    ts(u("p6"), u("MI"), 2048, A.is_lt)
-    ts(u("t512c"), u("MI"), 1, A.add)
-    tt(u("W", 1, 513), u("t512c"), u("p6"), A.mult)
-    owners(0)
-    ts(u("IDB"), J, P, A.is_equal)
-    ts(u("NIDB"), J, P, A.is_equal, -1.0, A.mult)
-    ts(u("ID16"), J, P, A.is_equal)
-    ts(u("NID16"), J, P, A.is_equal, -1.0, A.mult)
-    ts(u("ID16x"), J, P, A.is_equal, 16.0, A.mult)
-    ts(u("IDE"), J, P, A.is_equal, 2.0 ** 23, A.mult)
-    ts(u("NIDE"), J, P, A.is_equal, -2.0 ** 23, A.mult)
-    ts(u("ID1K"), J, P, A.is_equal, 1024.0, A.mult)
-    ts(u("BD"), J4, P4, A.is_equal)
-    ts(u("NBD"), J4, P4, A.is_equal, -1.0, A.mult)
-    ts(u("R16"), J15, P15, A.is_equal)
-    ts(u("p3", 0, 128), J15, P15, A.is_equal)
-    ts(u("CK"), J15, 2048.0, A.mult)
-    ts(u("CKP"), J15, 1.0, A.add)
-    ts(u("blk16"), u("J", 0, 8), P4, A.is_equal)
-    ts(u("blkf"), u("J", 0, 8), P4, A.is_equal)
-    ts(u("w32k"), u("BD", 0, None, 16), 32768.0, A.mult)
-    ts(u("w8k"), u("BD", 0, None, 16), 8192.0, A.mult)
-    ts(u("w2k"), u("BD", 0, None, 16), 2048.0, A.mult)
-    ts(u("w512"), u("BD", 0, None, 16), 512.0, A.mult)
-    ts(u("w1"), u("BD", 0, None, 16), 1.0, A.mult)
-    ts(u("w2"), u("BD", 0, None, 16), 2.0, A.mult)
-    owners(1)
-    for z in "ZS ZD ZN ZBB ZM ZW ZSP ZI ZV ZQ".split():
-        ts(u(z), J, 0.0, A.mult)
-
-    def late_constants():
-        ts(col(7), P, -16.0, A.mult, 2047.0, A.add)
-        ts(u("KB"), J15, -1.0, A.mult, col(7), A.add)
-        ts(col(8), P, 16.0, A.mult)
-        ts(u("KV"), J15, col(8), A.add)
-        cp(u("CREP"), J)
-        ts(col(9), P, 0.0, A.is_equal, 512.0, A.mult)
-        ts(col(10), P, 1.0, A.is_equal, -2.0 ** 24, A.mult)
-        ts(u("KA"), J15, col(9), A.mult, col(10), A.add)
-        fill(u("ONEB"), 1.0)
-        cp(u("ONE16"), u("ONEB"))
-        ts(col(11), P15, 0.0, A.is_equal, 2.0 ** 25, A.mult)
-        ts(u("DEAD"), u("BD"), col(11), A.mult)
-        ts(col(12), P15, 4.0, A.is_lt, 1.0 / 64, A.mult)
-        tt(col(12), col(12), P15, A.mult)
-        ts(col(13), P15, 4.0, A.is_equal, 4.0, A.mult)
-        tt(col(12), col(12), col(13), A.add)
-        ts(u("HWB"), u("BD"), col(12), A.mult)
-        for c in range(4):
-            ts(col(14), P15, float(c), A.is_equal, 2.0 ** 19, A.mult)
-            tt(col(15), col(14), col(12), A.add)
-            ts(u("og%d" % c), u("BD", 0, None, 16), col(15), A.mult)
-        ts(u("TRI"), J, P, A.is_gt)
-        fill(u("FM"), -4096.0)
-        fill(u("FM", 0, None, 128), 4096.0)
-        ts(u("blk128"), u("J", 0, 8), P4, A.is_equal, 128.0, A.mult)
-        ts(col(16), P, -1.0, A.mult, -528.0, A.add)
-        ts(u("blkN"), u("J", 0, 8), P4, A.is_equal, col(16), A.mult)
-        ts(col(28), P, -1.0, A.mult, -1552.0, A.add)
-        ts(u("blkE"), u("J", 0, 8), P4, A.is_equal, col(28), A.mult)
-        ts(col(17), P, 16.0, A.add)
-        ts(u("blkI"), u("J", 0, 8), P4, A.is_equal, col(17), A.mult)
-        ts(col(18), P, 32.0, A.add)
-        ts(u("blk32"), u("J", 0, 8), P4, A.is_equal, col(18), A.mult)
-        ts(u("blkm"), u("J", 0, 8), P4, A.is_equal, -640.0, A.mult)
-        ts(u("blk2k"), u("J", 0, 8), P4, A.is_equal, 2048.0, A.mult)
-        fill(u("C640"), 640.0)
-        ts(u("CI"), u("J", 0, 8), 16.0, A.mult, P15, A.add)
-        ts(col(19), P15, 528.0, A.add)
-        ts(u("C528"), u("J", 0, 8), 16.0, A.mult, col(19), A.add)
-        ts(u("SEL5"), u("BD"), col(5), A.mult)
-        ts(u("BT"), J, P, A.is_le, -1.0, A.mult)
-        tt(u("BT"), u("BT"), u("BD"), A.mult)
-        ts(col(20), P, 15.0, A.add)
-        ts(col(21), P15, 0.0, A.is_equal)
-        ts(u("Y"), u("J", 0, 144), col(20), A.is_equal, col(21), A.mult)
-        ts(u("SEL0"), u("BD", 0, None, 16), col(21), A.mult)
-        ts(col(22), P15, 656.0, A.add)
-        ts(u("CVp"), u("J", 0, 32), 16.0, A.mult, col(22), A.add)
-        ts(u("CVn"), u("CVp"), -1.0, A.mult)
-        fill(u("FREE"), 0.0)
-        fill(u("STI", 0, 8), 0)
-        fill(u("DS", 2048, 2176), 0.0)
-        fill(u("RESW"), 0)
-        fill(u("QZ"), 0.0)
-        fill(u("Aa"), 0)
-        for t in range(RO):
-            fill(u("XV%d" % t), 0.0)
-        for s in range(16):
-            o, i = u("SH", 128 * s, 128 * s + 128), u("BD")
-            op("k", lambda: g.affine_select(o[0], i[0], [[1, 128]], A.is_equal, 0.0, -s, -1), [o], [i])
-        cp(u("PC", 24, 26), u("LI"))
-        cp(u("PC", 26, 27), u("WI"))
-        ts(u("WTB"), u("BD"), col(26), A.mult)
-        ts(u("NFH"), u("SEL0"), col(24), A.mult)
-        mm([(u("p6", 0, 8), u("ONE16"), u("NFH"))])
-        cp(u("lim8"), u("p6", 0, 8))
-        cp(u("thr8"), u("p6", 0, 8))
-        ts(u("NFH"), u("SEL0"), col(25), A.mult)
-        mm([(u("p6", 0, 8), u("ONE16"), u("NFH"))])
-        cp(u("lim28"), u("p6", 0, 8))
-
-    def tile(src_rep, prod, blk, out, extra=(), ps="p6"):
-        if src_rep is not None:
-            tt(u(prod), src_rep, u("p3", 0, 128), A.mult)
-        mm([(u(ps, 0, 8), u(prod), u(blk))] + [(u(ps, 0, 8), u(a), u(b)) for a, b in extra])
-        cp(u(out), u(ps, 0, 8))
-
-    def part_own(t):
-        cl = t % 4
-        lanes = u("W", 1 + cl, 513, 4)
-        cp(u("OWN"), lanes)
-        win = u("X", 0, 2064)
-        if t == 0:
-            cp(u("T"), ix(win, u("OWN")))
-        else:
-            act(u("T", 1024, 2048), ix(win, u("OWN", 64, 128)), F.Copy)
-            cp(u("T", 0, 1024), ix(win, u("OWN", 0, 64)))
-        ts(u("EO"), lanes, 0.0, A.is_equal)
-        cp(u("OWNH"), lanes)
-        ts(u("VC"), u("W", 1, 513), 0.0, A.is_equal)
-        mm([(u("p4", 0, 128), u("IDB"), u("CK")), (u("p4", 0, 128), u("EO"), u("IDE")), (u("p4", 0, 128), u("OWNH"), u("ID16"))]
-           + sums("p4", 0, "T", "w32k"))
-        scan(u("US"), u("MS", 0, 2048), u("T"), A.mult, A.max)
-        mm([(u("p7", 32, 40), u("EO"), u("BD", 0, None, 16))])
-        mm([(u("p5", 128, 256), u("OWNH"), u("ID16x"))])
-        mm([(u("p5", 256, 384), u("OWNH"), u("ID16x")), (u("p5", 256, 384), u("IDB"), u("CKP"))])
-        mm([(u("p6", 8, 16), u("US", 15, None, 16), u("BD", 0, None, 16))])
-        scan(u("S1"), u("MIN"), u("p4", 0, 128), A.max, A.min)
-        ts(u("k8"), u("S1", 15, None, 16), -1.0, A.add)
-        ts(u("sv8"), u("k8"), 2047, A.bitwise_and)
-        ts(u("sx8"), u("k8"), 15, A.logical_shift_right)
-        ts(u("ZS", 0, None, 16), u("sv8"), 1.0, A.add)
-        ts(u("live8"), u("S1", 15, None, 16), 2.0 ** 23, A.is_lt)
-        hold(u("SR"), u("ZS"))
-        tile(u("SR"), "PS", "blk16", "S16")
-        cp(u("Z", 0, None, 16), ix(win, u("S16")))
-        mm([(u("p7", 0, 32), u("Y", 15 - r, 143 - r), u("VC", r, None, 16)) for r in range(16)] if t else
-           [(u("p7", 0, 32), u("IDB"), u("VC", 0, 32))])
-        ts(u("ZN", 0, None, 16), u("p7", 32, 40), -1.0, A.mult, 16.0, A.add)
-        tt(u("gr8"), u("p6", 8, 16), u("sx8"), A.subtract)
-        scan(u("REP"), u("MS", 0, 2048), u("Z"), A.mult, A.add)
-
-    def dif(c):
-        a, b = 512 * c, 512 * c + 512
-        ps = "p%d" % (c % 3)
-        mm([(u(ps), u("IDB"), u("T", a, b)), (u(ps), u("NIDB"), u("REP", a, b))])
-        act(u("SQ", a, b), u(ps), F.Square)
-
-    def part_own_squares(t):
-        for c in (2, 3):
-            dif(c)
-        act(u("SQS"), u("Z", 0, None, 16), F.Square)
-        act(u("W16L"), u("p5", 128, 256), F.Copy)
-        act(u("WL"), u("p5", 128, 256), F.Copy, scale=0.0625)
-        act(u("PW2"), u("p5", 256, 384), F.Copy)
-
-    def part_own_end(t):
-        tt(u("gr8"), u("gr8"), u("lim28"), A.is_gt)
-        tt(u("wp8"), u("gr8"), u("live8"), A.mult)
-
-    def part_sizes(t):
-        hold(u("NR"), u("ZN"))
-        tt(u("NP"), u("NR"), u("p3", 0, 128), A.mult)
-        mm([(u("p4", 264, 272), u("NP"), u("blk128")), (u("p4", 264, 272), u("ID16"), u("CI"))])
-
-    def part_split(t):
-        cp(u("N16"), u("p4", 264, 272))
-        cp(u("nf8"), u("p4", 256, 264))
-        mm([(u("p5", 0, 128), u("ID16"), u("KB")), (u("p5", 0, 128), u("EO"), u("NIDE"))] + sums("p5", 0, "SQ", "w2k"))
-        scan(u("SB"), u("MS", 0, 128), u("p5", 0, 128), A.mult, A.max)
-        cp(u("b8"), u("SB", 15, None, 16))
-        ts(u("bb8"), u("b8"), 2047, A.bitwise_and)
-        ts(u("ZBB", 0, None, 16), u("bb8"), -1.0, A.mult, 2047.0, A.add)
-        hold(u("BR"), u("ZBB"))
-        tile(u("BR"), "BP", "blk16", "B16", ps="p7")
-        cp(u("XB"), ix(u("T"), u("B16")))
-        act(u("SQB"), u("XB"), F.Square)
-        tt(u("WV"), u("Z", 0, None, 16), u("XB"), A.subtract)
-        tt(u("AX"), ix(u("WV"), u("CREP")), u("T"), A.mult)
-        mm([(u("p5", 384, 512), u("SQB"), u("BD")), (u("p5", 384, 512), u("SQS"), u("NBD"))] + sums("p5", 384, "AX", "w2"))
-
-    def part_compact(t):
-        ts(u("mb"), u("W16L"), 0.0, A.is_gt)
-        ts(u("p5", 0, 128), u("p5", 384, 512), 0.0, A.is_lt)
-        tt(u("L1"), u("mb"), u("p5", 0, 128), A.mult)
-        scan(u("p5", 128, 256), u("MS", 0, 128), u("L1"), A.mult, A.add)
-        tt(u("SM"), u("mb"), u("L1"), A.subtract)
-        tt(u("p5", 0, 128), u("PW2"), u("p5", 128, 256), A.subtract)
-        tt(u("p5", 256, 384), u("W16L"), u("p5", 128, 256), A.add)
-        tt(u("Pa", 128, 256), u("L1"), u("p5", 0, 128), A.mult)
-        tt(u("Pa", 0, 128), u("SM"), u("p5", 256, 384), A.mult)
-
-    def part_shift(t, steps):
-        for s in steps:
-            a, b = ("Pa", "Pb") if s % 2 == 0 else ("Pb", "Pa")
-            ts(u("Mi", 0, 256), u(a, 0, 256), 1 << s, A.bitwise_and)
-            ts(u("p5", 0, 256), u("Mi", 0, 256), 2.0 ** (16 - s), A.mult)
-            tt(u("p5", 256, 512), u(a, 0, 256), u("p5", 0, 256), A.subtract)
-            tt(u("Aa", 0, 256), u(a, 0, 256), u("p5", 0, 256), A.min)
-            tt(u(b, 0, 256), u("p5", 256, 512), u("Aa", 1 << s, 256 + (1 << s)), A.max)
-        if 3 in steps:
-            ts(u("STI"), u("Pa", 0, 256), 4, A.logical_shift_right)
-            tt(u("STM"), u("STI", 0, 128), u("WL"), A.subtract)
-
-    def move_owners():
-        act(ix(u("OT", 0, 4112), u("MVO")), u("VE"), F.Silu)
-
-    def part_vacant_count(t):
-        if t == 0:
-            mm([(u("p7", 0, 32), u("Y", 15 - r, 143 - r), u("VC", r, None, 16)) for r in range(16)])
-        cp(u("VTb"), u("p7", 0, 32))
-        mm([(u("p7", 0, 32), u("BD"), u("VTb"))])
-        mm([(u("p6", 0, 32), u("BT"), u("VTb")), (u("p6", 0, 32), u("ID16"), u("CVn"))])
-        part_sizes(t)
-
-    def part_vacant(t):
-        scan(u("CSs"), u("ONEB", 0, 32), u("p7", 0, 32), A.mult, A.add)
-        tt(u("rk"), u("CSs"), u("p6", 0, 32), A.add)
-        tt(u("rk"), u("rk"), u("VTb"), A.mult)
-        tt(u("rk"), u("rk"), u("CVp"), A.add)
-        cp(u("F16"), u("rk"))
-        ts(u("NFH"), u("SEL0"), u("CSs", 31, 32), A.mult)
-        mm([(u("p4", 256, 264), u("ONE16"), u("NFH"))])
-
-    def part_near(t):
-        cl = t % 4
-        win = u("X", 0, 2064)
-        i = ix(u("AC4"), u("S16"))
-        ts(u("AN"), i, 1, A.add)
-        act(u("OG"), ix(u("OT", 0, 2064), u("AN")), F.Copy)
-
-    def part_distances(t):
-        cl = t % 4
-        win = u("X", 0, 2064)
-        for h in range(2):
-            a, b = 1024 * h, 1024 * h + 1024
-            tt(u("AX", a, b), ix(win, u("AN", 64 * h, 64 * h + 64)), u("REP", a, b), A.subtract)
-            act(u("SQ", a, b), u("AX", a, b), F.Square)
-        mm([(u("p4", 0, 128), u("ONEB"), u("KA")), (u("p4", 0, 128), u("EO"), u("DEAD"))] + sums("p4", 0, "OG", "og%d" % cl)
-           + sums("p4", 0, "SQ", "w8k"))
-
-    def part_partner(t):
-        win = u("X", 0, 2064)
-        scan(u("S2"), u("MIN"), u("p4", 0, 128), A.max, A.min)
-        cp(u("a8"), u("S2", 15, None, 16))
-        ts(u("has8"), u("S2", 15, None, 16), 14.0e6, A.is_lt)
-        ts(u("d8"), u("a8"), 511, A.bitwise_and)
-        ts(u("dp8"), u("d8"), 1.0, A.add)
-        tt(u("ZD", 0, None, 16), u("dp8"), u("has8"), A.mult)
-        hold(u("D1R"), u("ZD"))
-        tile(u("D1R"), "PD", "blk16", "D16")
-        lists = ix(u("W", 0, 520), u("D16"))
-        cp(u("DM"), lists)
-        act(u("DT", 1024, 2048), ix(win, u("DM", 64, 128)), F.Copy)
-        cp(u("DT", 0, 1024), ix(win, u("DM", 0, 64)))
-        cp(u("DMH"), ix(u("W", 0, 520), u("D16")))
-        ts(u("ED"), u("DM"), 0.0, A.is_equal)
-        ts(u("nD"), u("ZD", 0, None, 16), -1.0, A.mult)
-        tt(u("d18"), u("dp8"), u("has8"), A.mult)
-        for q in range(8):
-            ts(u("DG", 128 * q, 128 * q + 128), u("ID16"), u("d18", q, q + 1), A.mult)
-        for q in range(8):
-            ps = "p%d" % (q // 4)
-            lo = 128 * (q % 4)
-            mm([(u(ps, lo, lo + 128), u("TRI"), u("DG", 128 * q, 128 * q + 128))])
-        mm([(u("p7", 0, 8), u("EO"), u("BD", 0, None, 16)), (u("p7", 0, 8), u("ED"), u("BD", 0, None, 16))])
-        mm([(u("p4", 0, 128), u("ED"), u("ID1K"))] + sums("p4", 0, "DT", "w1"))
-        scan(u("AX"), u("MS", 0, 2048), u("DT"), A.mult, A.max)
-        tt(u("Vv"), u("US", 15, None, 16), u("AX", 15, None, 16), A.max)
-        mm([(u("p6", 0, 8), u("Vv"), u("BD", 0, None, 16))])
-        for q in range(8):
-            ps = "p%d" % (q // 4)
-            lo = 128 * (q % 4)
-            act(u("AB", 128 * q, 128 * q + 128), u(ps, lo, lo + 128), F.Abs, bias=u("nD", q, q + 1))
-        for c in range(4):
-            ps = "p%d" % (2 - 2 * (c % 2))
-            for k in range(4):
-                s = 4 * c + k
-                mm([(u(ps, 128 * k, 128 * k + 128), u("SH", 128 * s, 128 * s + 128), u("DMH"))])
-            act(u("DS", 512 * c, 512 * c + 512), u(ps), F.Copy)
-        act(ix(u("FREE"), u("F16")), u("V0"), F.Silu)
-        ts(u("sz8"), u("p7", 0, 8), 16.0, A.is_ge)
-        scan(u("S3"), u("MIN"), u("p4", 0, 128), A.max, A.min)
-        tt(u("mn8"), u("S3", 15, None, 16), u("sx8"), A.min)
-        tt(u("tm8"), u("mn8"), u("thr8"), A.add)
-        scan(u("ABS"), u("FM"), u("AB"), A.max, A.min)
-        ts(u("f8"), u("ABS", 127, None, 128), 0.5, A.is_ge)
-        tt(u("P0"), u("f8"), u("has8"), A.mult)
-        tt(u("P0"), u("P0"), u("sz8"), A.mult)
-
-    def part_finish(t):
-        cl = t % 4
-        zm, zw, zs, zi, zv = [u(z, 0, None, 16) for z in ("ZM", "ZW", "ZSP", "ZI", "ZV")]
-        tt(u("c8"), u("p6", 0, 8), u("tm8"), A.is_le)
-        tt(zm, u("c8"), u("P0"), A.mult)
-        tt(zw, u("wp8"), zm, A.is_gt)
-        hold(u("WR"), u("ZW"))
-        mm([(u("p7", 0, 128), u("TRI"), u("WR"))])
-        hold(u("MR"), u("ZM"))
-        mm([(u("p4", 0, 128), u("MR"), u("ID16"))])
-        tt(u("sp8"), u("p7", 0, 128, 16), u("nf8"), A.is_lt)
-        tt(zs, u("sp8"), zw, A.mult)
-        tt(u("ms8"), zm, zs, A.add)
-        tt(zi, u("live8"), u("ms8"), A.is_gt)
-        hold(u("IR"), u("ZI"))
-        mm([(u("p6", 128, 256), u("TRI"), u("IR"))])
-        hold(u("p3", 128, 256), u("ZSP"))
-        tt(u("SPP"), u("R16"), u("p3", 128, 256), A.mult)
-        tt(u("KP"), u("p7", 0, 128), u("SPP"), A.mult)
-        ts(u("v8"), u("p6", 128, 256, 16), 32.0, A.is_lt)
-        tt(zv, u("v8"), zi, A.mult)
-        hold(u("p3", 256, 384), u("ZV"))
-        tt(u("VP"), u("R16"), u("p3", 256, 384), A.mult)
-        tt(u("RP"), u("p6", 128, 256), u("VP"), A.mult)
-        tt(u("NVP"), u("p3", 0, 128), u("VP"), A.subtract)
-        tile(None, "RP", "blk16", "RT16", [("NVP", "blk32")])
-        xv = "XV%d" % t
-        cp(ix(u(xv), u("RT16")), u("Z", 0, None, 16))
-        send(T.cores[(rank + 1 + t % 7) % 8], xv, "QI%d" % t, "rq%d" % t, "fq%d" % t, "lq%d" % t, 0)
-        tile(None, "KP", "blk16", "K16", [("SPP", "blkm"), ("IDB", "C640")], ps="p7")
-        cp(u("EV"), ix(u("FREE"), u("K16")))
-        cp(u("EVH"), u("EV"))
-        mm([(u("p7", 0, 128), u("EVH"), u("SEL5"))])
-        tt(u("f128a"), u("p4", 0, 128), u("V0", cl, None, 4), A.mult)
-        tt(u("VF"), u("f128a"), u("EV"), A.add)
-        act(u("VE"), ix(u("VF"), u("CREP")), F.Copy)
-        tt(u("A3"), u("STI", 128, 256), u("p3", 128, 256), A.mult)
-        mm([(u("p5", 128, 256), u("A3"), u("ID16"))])
-        tt(u("MD"), u("p4", 0, 128), u("DMH"), A.mult)
-        mm([(u("p2", 0, 128), u("ID16"), u("MD")), (u("p2", 0, 128), u("A3"), u("ID16"))])
-        cp(u("DSE"), ix(u("DS"), u("N16")))
-        tt(u("A1"), u("p4", 0, 128), u("DSE"), A.mult)
-        tt(u("A2"), u("STM"), u("p3", 128, 256), A.mult)
-        mm([(u("p5", 0, 128), u("ID16"), u("OWNH")), (u("p5", 0, 128), u("ID16"), u("A1")), (u("p5", 0, 128), u("A2"), u("ID16"))])
-        ts(u("p3", 384, 512), u("p2", 0, 128), 0.0, A.is_equal)
-        tt(u("f128b"), u("DUM"), u("p3", 384, 512), A.mult)
-        tt(u("f128b"), u("f128b"), u("p2", 0, 128), A.add)
-        cp(u("MVO"), u("f128b"))
-        tt(u("MP"), u("MR"), u("p3", 0, 128), A.mult)
-        tt(u("Q1"), u("PD"), u("MR"), A.mult)
-        tt(u("Q2"), u("p7", 0, 128), u("SPP"), A.mult)
-        cp(u("ELS"), u("p5", 128, 256))
-        tile(None, "Q1", "blk16", "TG16", [("Q2", "blk16"), ("MP", "blkN"), ("SPP", "blkE"), ("ID16", "C528")])
-        cp(u("W", 1 + cl, 513, 4), u("p5", 0, 128))
-        cp(ix(u("W", 0, 656), u("TG16")), u("ELS"))
-
-    def part_late(t):
-        tt(u("XP"), u("PS"), u("p3", 256, 384), A.mult)
-        tile(None, "XP", "blk16", "XT16", [("NVP", "blkI"), ("NVP", "blk2k")])
-        if t + 1 < RO:
-            mm([(u("p7", 0, 8), u("ONE16"), u("MR", 0, None, 16))])
-            op("v", lambda: v.tensor_reduce(u("mc", 0, 1)[0], u("p7", 0, 8)[0], AX_.X, A.add), [u("mc", 0, 1)], [u("p7", 0, 8)])
-            cp(u("mci", 0, 1), u("mc", 0, 1))
-            ts(u("mci", 1, 2), u("mci", 0, 1), 15, A.bitwise_and)
-            cp(u("mc", 1, 2), u("mci", 1, 2))
-            ts(u("thr8"), u("lim8"), u("mc", 1, 2), A.add)
-
-    def part_serve(t):
-        src = T.cores[(rank - 1 - t % 7) % 8]
-        n = landed_n(src, 0)
-        qi, sn = "QI%d" % t, "SN%d" % t
-        rq = "rq%d" % t
-        p32 = (0, 32)
-        for e in ("p", "v"):
-            arrived(e, qi, rq, n)
-        mm([(u("p6", 0, 128, 1, p32), u(qi), u("WTB"))])
-        cp(u("QZ", 0, None, 16), u(qi))
-        tt(u("VFP", p=p32), u("p6", 0, 128, 1, p32), u("R16", p=p32), A.mult)
-        mm([(u("p7", 0, 2), u("VFP", p=p32), u("blkf", 0, 2, 1, p32))])
-        cp(u("VI"), u("p7", 0, 2))
-        ts(u("VI2"), u("VI"), 2047, A.bitwise_and)
-        ts(u("VV16"), u("VI2"), 1, A.add)
-        scan(u("QRp"), u("MS", 0, 512), u("QZ"), A.mult, A.add)
-        cp(u("HO"), ix(u("OT", 0, 2064), u("VV16")))
-        mm([(u("p6", 0, 128, 1, p32), u("HO"), u("HWB"))])
-        tt(u("QP", p=p32), u("p6", 0, 128, 1, p32), u("R16", p=p32), A.mult)
-        mm([(u("p7", 0, 2), u("QP", p=p32), u("blk16", 0, 2, 1, p32))])
-        ts(u("H16"), u("p7", 0, 2), -511.0, A.add)
-        cp(u("HL"), ix(u("W", 0, 520), u("H16")))
-        tt(u("QD"), ix(u("X", 0, 2064), u("HL")), u("QRp"), A.subtract)
-        ts(u("EH"), u("HL"), 0.0, A.is_equal)
-        act(u("QS"), u("QD"), F.Square)
-
-    def part_serve_met(t):
-        src = T.cores[(rank - 1 - t % 7) % 8]
-        qi, sn = "QI%d" % t, "SN%d" % t
-        p32 = (0, 32)
-        mm([(u("p6", 0, 128, 1, p32), u("ID16", 0, 32), u("KV")), (u("p6", 0, 128, 1, p32), u("EH"), u("IDE"))]
-           + sums("p6", 0, "QS", "w512", p32))
-        scan(u("QSC", p=p32), u("MIN", p=p32), u("p6", 0, 128, 1, p32), A.max, A.min)
-        cp(u("q8", p=p32), u("QSC", 15, None, 16, p32))
-        ts(u("qq8", p=p32), u("q8", p=p32), 511, A.bitwise_and)
-        cp(u("ZQ", 0, None, 16, p32), u("qq8", p=p32))
-        scan(u("QR8", p=p32), u("MS", 0, 128, 1, p32), u("ZQ", p=p32), A.mult, A.add)
-        tt(u("QP", p=p32), u("QR8", p=p32), u("R16", p=p32), A.mult)
-        mm([(u("p7", 0, 2), u("QP", p=p32), u("blk16", 0, 2, 1, p32))])
-        cp(u("J16"), u("p7", 0, 2))
-        ts(u("hs"), ix(u("QD"), u("J16")), -0.5, A.add, 0.5, A.mult)
-        tt(u(sn), u("hs"), u(qi), A.add)
-        send(src, sn, "RS%d" % t, "rs%d" % t, "fs%d" % t, "ls%d" % t, 1)
-
-    def part_apply(t):
-        src = T.cores[(rank + 1 + t % 7) % 8]
-        arrived("v", "RS%d" % t, "rs%d" % t, landed_n(src, 1))
-        cp(u("RESW", 0, 32), u("RS%d" % t))
-        cp(u("NV"), ix(u("RESW"), u("RT16")))
-        cp(ix(u("X"), u("XT16")), u("NV"))
-
-    part_own(0)
-    dif(0)
-    dif(1)
-    part_own_squares(0)
-    owners(2)
-    late_constants()
-    part_own_end(0)
-    owners(3)
-    part_vacant_count(0)
-    part_vacant(0)
-    part_split(0)
-    for t in range(RO):
-        part_near(t)
-        part_compact(t)
-        part_shift(t, (0, 1))
-        if t:
-            part_apply(t - 1)
-        part_distances(t)
-        part_shift(t, (2, 3))
-        part_partner(t)
-        part_finish(t)
-        part_late(t)
-        if t + 1 < RO:
-            part_own(t + 1)
-            move_owners()
-            part_vacant_count(t + 1)
-            dif(0)
-            dif(1)
-            part_own_end(t + 1)
-            part_vacant(t + 1)
-            part_serve(t)
-            part_own_squares(t + 1)
-            part_serve_met(t)
-            part_split(t + 1)
-        else:
-            move_owners()
-            ts(u("t512a"), u("W", 1, 513), 0.0, A.is_equal, 2049.0, A.mult)
-            ts(u("t512b"), u("W", 1, 513), -1.0, A.add)
-            tt(u("YM"), u("t512a"), u("t512b"), A.add)
-            dma("y", ext(T.ym[:], "out_m"), u("YM"), "st0")
-            part_serve(t)
-            part_serve_met(t)
-            part_apply(t)
-            dma("y", ext(T.yx[:], "out_x"), u("X", 1, 2049), "st1")
     for sem in total:
         n = total[sem]
         if known["k"].get(sem, 0) < n:

@@ -27,8 +27,8 @@ _sb("CODE", 512, B)
 _sb("EV", 128, S)
 _sb("T", 2048, B)
 _sb("QD", 512, B)
-_sb("MS IOT VB US REP SQ AX AW SH OG DT DU", 2048, B)
-_sb("Z0 Z1", 2048, B)
+_sb("MS VB US REP SQ AX AW SH OG DT DU", 2048, B)
+_sb("Z0 Z1 ZE", 2048, B)
 _sb("J2f t512a t512b YM QR", 512, S)
 _sb("J J3 Qi", 512, I)
 _sb("OWN AN DM CREP MVO", 128, U)
@@ -38,17 +38,28 @@ _sb("kq G4", 4, S)
 _sb("EQ", 1024, B)
 _sb("Jh OWNH DMH ID16 NID16 ONE16 J4h J15h KP RP D1R CMR CMK0 CMK1 CMK2 CMK3 R16", 128, H)
 _sb("ZS HS ZB HB ZD HD ZQ HQ", 144, H)
-_sb("ID2 SL CNT CTG", 256, H)
+_sb("SL CNT CTG", 256, H)
+_sb("ID2", 256, B)
+_sb("Jb", 144, B)
+_sb("J4b J15b b1 b2 K11 K20 K21", 128, B)
+_sb("E16", 16, S)
+_sb("EP", 4, S)
+_sb("DUM", 512, S)
+_sb("blk nblk", 8, B)
 _sb("MC IDB NIDB BD NBD BTI ONEB PRE PRD LR L1T ZM ZW WR MR SR XB SQS SQB Vv EVb NV CE CO NFH SEL0R TRIm NTRIm HWN BDn "
     "N24 N25 N20 P20 P25 N13 P12 P11 KAs KAb KAd KAn KAq K12 K13 K14", 128, B)
-_sb("BTX KAp QN", 256, B)
+_sb("BTX BT1 KAp KAx QN", 256, B)
+_sb("XF", 768, B)
+_sb("RV0 RV1 RV2", 128, B)
+_sb("KQ", 16, S)
 _sb("Y Y2 WY HY", 144, B)
-_sb("MINs MINn MIN S1a S1b S2 S3 SB QSC DUM NFR ELS m1 m2 e128", 128, S)
-_sb("Pa Pb Mi Aa", 264, I)
+_sb("MINs MINn MIN S1a S1b S2 S3 SB QSC NFR ELS m1 m2 e128", 128, S)
+_sb("Pa Pb", 256, S)
+_sb("Aa", 264, S)
 _sb("PIi", 4, I)
-_sb("PC", 48, S)
+_sb("PC", 64, S)
 _sb("J4 J15", 128, I)
-_sb("blk nblk CB CQ CT", 8, H)
+_sb("CB CQ", 8, H)
 _sb("nblkb CN w64k w8k w32 og0 og1 og2 og3 SEL0 L2N THN THZ ROW1 SZ wp8 C25", 8, B)
 _sb("nblkf hi8 hb8 hq8 mn8 z8", 8, S)
 _sb("a8 d8", 8, I)
@@ -83,15 +94,20 @@ def _pack():
 
 
 SCRATCH = _pack()
+for _n, _first, _len in (("ZALL", "ZS", 1152), ("ZMW", "ZM", 256), ("MIN3", "MINs", 384), ("IDB", "ID2", 128)):
+    _ARENA[_n] = (_ARENA[_first][0], _ARENA[_first][1], _len, _ARENA[_first][3])
+for _n, _m in (("ID16", "IDB"), ("NID16", "NIDB"), ("N13", "N20"), ("P12", "P11"), ("P25", "P20"), ("K12", "K11"), ("K13", "K20"), ("K14", "K21"), ("nblkb", "nblk"), ("CT", "CIX")):
+    _ARENA[_n] = _ARENA[_m]
+_ARENA["CT"] = _ARENA["CIX"][:2] + (8, H)
 for _k in range(8):
     SCRATCH["p%d" % _k] = ("psum", [128, 512], S)
     _ARENA["p%d" % _k] = ("p%d" % _k, 0, 512, S)
-SEMAPHORES = ["v", "p", "s", "k"] + ["ld%d" % i for i in range(8)] + ["st0", "st1"]
+SEMAPHORES = ["v", "p", "s", "k"] + ["ld%d" % i for i in range(10)] + ["st0", "st1"]
 for _t in range(RO):
     SEMAPHORES += ["rq%d" % _t, "rs%d" % _t, "lq%d" % _t, "ls%d" % _t, "fq%d" % _t, "fs%d" % _t, "mq%d" % _t, "ms%d" % _t]
 _ORDER = {}
-CYC, WAKE, GAT, SCA, WAY = 0.001, 0.07, 1.5, 3.5, 7.0
-OPT = {"T": 64, "DT": 64, "sc": "vsvs", "mv": 2}
+CYC, PEC, CALL, WAKE, GAT, SCA, WAY = 0.0009, 0.0005, 0.05, 0.06, 1.5, 3.5, 2.5
+OPT = {"T": 48, "DT": 48, "sc": "ssss", "mv": "wwww", "sh": "s", "nr": 3, "cg": "ssss", "turns": 4, "sv": ("NIDB", "N24", "N20", "P20", "P11"), "T0": 128, "lam": 5, "slip": 0.1, "eq": "ss", "ds": "ssss", "q": "ssss"}
 
 
 def _mask(topo, a, b):
@@ -151,50 +167,86 @@ def _order(ops):
     way = [0.0] * n
     for i in range(n - 1, -1, -1):
         way[i] = ops[i]["cost"] + ops[i]["lat"] + max([way[j] + WAKE for j in succ[i]] + [0.0])
-    left = [len(p) for p in pred]
-    end = [0.0] * n
-    free, bank, ready, out = {}, {}, {}, []
-    banks = [set(b for (b, _l, _h) in o["rd"] + o["wr"] if _psum(b)) for o in ops]
-    base = [0.0] * n
-    for i in range(n):
-        if not left[i]:
-            ready.setdefault(ops[i]["e"], []).append(i)
+    holds = [[o["e"]] + sorted(set(b for (b, _l, _h) in o["rd"] + o["wr"] if _psum(b))) for o in ops]
 
-    def start(i):
-        e = ops[i]["e"]
-        s = max(base[i], free.get(e, 0.0))
-        for b in banks[i]:
-            for e2, t2 in bank.get(b, {}).items():
-                if e2 != e:
-                    s = max(s, t2 + WAKE)
-        return s
-    while len(out) < n:
-        best = None
-        for e, lst in ready.items():
-            if not lst:
-                continue
-            st = {i: start(i) for i in lst}
-            a = min(lst, key=lambda i: (round(st[i], 2), -way[i]))
-            for b in sorted(lst, key=lambda i: -way[i])[:6]:
-                ca, cb = ops[a]["cost"], ops[b]["cost"]
-                if b != a and st[b] < st[a] + ca and max(st[b] + way[b], st[b] + cb + way[a]) < max(st[a] + way[a], st[a] + ca + way[b]):
-                    a = b
-            if best is None or st[a] < best[0]:
-                best = (st[a], a)
-        s, a = best
-        e = ops[a]["e"]
-        ready[e].remove(a)
-        free[e] = s + ops[a]["cost"]
-        end[a] = free[e] + ops[a]["lat"]
-        for b in banks[a]:
-            bank.setdefault(b, {})[e] = end[a]
-        out.append(a)
-        for j in succ[a]:
-            base[j] = max(base[j], end[a] + WAKE)
-            left[j] -= 1
-            if not left[j]:
-                ready.setdefault(ops[j]["e"], []).append(j)
-    return out
+    def place(before, after, rank, back):
+        left = [len(p) for p in before]
+        base, start = [0.0] * n, [0.0] * n
+        busy = {}
+        ready = [i for i in range(n) if not left[i]]
+        while ready:
+            a = max(ready, key=lambda i: rank[i])
+            ready.remove(a)
+            e, c, lat = ops[a]["e"], ops[a]["cost"], ops[a]["lat"]
+            s = base[a] + (lat if back else 0.0)
+            moved = True
+            while moved:
+                moved = False
+                for r in holds[a]:
+                    gap = 0.0 if r == e else WAKE
+                    for (lo, hi, e2) in busy.get(r, ()):
+                        if (r == e or e2 != e) and lo - gap < s + c - 1e-9 and s + 1e-9 < hi + gap:
+                            s, moved = hi + gap, True
+            start[a] = s
+            for r in holds[a]:
+                busy.setdefault(r, []).append((s, s + c, e))
+                if len(busy[r]) > 400:
+                    low = min([base[i] for i in ready] + [s])
+                    busy[r] = [x for x in busy[r] if x[1] + WAKE >= low]
+            for j in after[a]:
+                base[j] = max(base[j], s + c + WAKE + (0.0 if back else lat))
+                left[j] -= 1
+                if not left[j]:
+                    ready.append(j)
+        return start, [start[i] + ops[i]["cost"] + (0.0 if back else ops[i]["lat"]) for i in range(n)]
+    def run(before, after, rank, back):
+        left = [len(p) for p in before]
+        base, start = [0.0] * n, [0.0] * n
+        free, bank, ready = {}, {}, {}
+        for i in range(n):
+            if not left[i]:
+                ready.setdefault(ops[i]["e"], []).append(i)
+
+        def can(i):
+            e = ops[i]["e"]
+            s = max(base[i] + (ops[i]["lat"] if back else 0.0), free.get(e, 0.0))
+            for b in holds[i][1:]:
+                for e2, t2 in bank.get(b, {}).items():
+                    if e2 != e:
+                        s = max(s, t2 + WAKE)
+            return s
+        for _i in range(n):
+            pick = None
+            for e, lst in ready.items():
+                if lst:
+                    st = {i: can(i) for i in lst}
+                    a = max(lst, key=lambda i: rank[i] - OPT["lam"] * st[i])
+                    fit = [i for i in lst if st[i] + ops[i]["cost"] <= st[a] + OPT["slip"]]
+                    a = max(fit, key=lambda i: rank[i]) if fit else a
+                    if pick is None or st[a] < pick[0]:
+                        pick = (st[a], a)
+            s, a = pick
+            e, c = ops[a]["e"], ops[a]["cost"]
+            ready[e].remove(a)
+            start[a], free[e] = s, s + c
+            for b in holds[a][1:]:
+                bank.setdefault(b, {})[e] = s + c
+            for j in after[a]:
+                base[j] = max(base[j], s + c + WAKE + (0.0 if back else ops[a]["lat"]))
+                left[j] -= 1
+                if not left[j]:
+                    ready.setdefault(ops[j]["e"], []).append(j)
+        return start, [start[i] + ops[i]["cost"] + (0.0 if back else ops[i]["lat"]) for i in range(n)]
+    if OPT["lam"]:
+        place = run
+    best = None
+    _ORDER["dbg"] = (ops, succ, list(way))
+    for _turn in range(OPT["turns"]):
+        start, end = place(pred, succ, way, False)
+        if best is None or max(end) < best[0]:
+            best = (max(end), start)
+        way = place(succ, pred, end, True)[1]
+    return sorted(range(n), key=lambda i: (best[1][i], i))
 
 
 def rank_program(g, core, T, topo):
@@ -242,7 +294,7 @@ def rank_program(g, core, T, topo):
             return 0.05 + o[2] * GAT * CYC
         if per == 0.5 and any(x[3] not in (B, H, U) for x in [o] + ins):
             per = 1.0
-        return max(64, o[2] * per) * CYC
+        return CALL + max(64, o[2] * per) * CYC
 
     def cp(o, i):
         op("v", lambda: v.tensor_copy(o[0], i[0]), [o], [i], cost(o, [i], 0.5))
@@ -273,6 +325,18 @@ def rank_program(g, core, T, topo):
             kw["accum_out"] = acc[0]
         op("s", lambda: sc.activation(o[0], i[0], f, **kw), [o] + _r(acc), [i] + _r(scale, bias), cost(o, [i], 1.0) + 0.06)
 
+    def relu(e, o, i):
+        if e == "s":
+            act(o, i, F.Relu)
+        else:
+            ts(o, i, 0.0, A.max)
+
+    def copy(e, o, i):
+        if e == "s":
+            act(o, i, F.Copy)
+        else:
+            cp(o, i)
+
     def iota(o, pat, base, cm=0):
         if o[3] == I:
             op("k", lambda: g.iota(o[0], pat, base, cm), [o], [], 0.13 + 2 * o[2] * CYC)
@@ -280,7 +344,7 @@ def rank_program(g, core, T, topo):
             op("k", lambda: g.iota(o[0], pat, base, cm, allow_small_or_imprecise_dtypes=True), [o], [], 0.13 + 2 * o[2] * CYC)
 
     def mm(items):
-        c = sum(max(min(64, a[2]), b[2]) * (4 if a[3] == S else 1) for (_o, a, b) in items) * CYC
+        c = sum(max(min(64, a[2]), b[2]) * (4 if a[3] == S else 1) for (_o, a, b) in items) * PEC
         op("p", None, [x[0] for x in items], [y for x in items for y in x[1:]], c, items=items)
 
     def dma(e, o, i, sem):
@@ -297,7 +361,7 @@ def rank_program(g, core, T, topo):
         via = _relay(topo, back, core, which)
         nb = _mask(topo, back if via is None else via, core)[1]
         op("k", lambda: g.remote_dma(T[buf_dst][:], src[0], T.sem[sem if to is None else fwd], T.sem[loc], pid, rid, m),
-           [u(buf_dst)], [src], 0.3, lat=WAY, land=(sem, nb, loc, n))
+           [u(buf_dst)], [src], 0.3, lat=WAY * (1 if to is None else 2), land=(sem, nb, loc, n))
 
     def e16(name, k=0, n=None, p=None):
         return u(name, k, n, 16, p)
@@ -325,193 +389,188 @@ def rank_program(g, core, T, topo):
     fill(u("AC4", 0, 8), 0)
     fill(u("AC4", 2048, 2192), 0)
     dma("y", u("MI"), ext(T.ml[:], "in_ml"), "ld0")
-    dma("s", u("X", 1, 2049), ext(T.x0[:], "in_x"), "ld1")
+    dma("y", u("X", 1, 2049), ext(T.x0[:], "in_x"), "ld1")
     dma("y", u("LI"), ext(T.lims[:], "in_l"), "ld2")
     dma("y", u("WI"), ext(T.wt[:], "in_w"), "ld3")
     for q in range(4):
         dma("y", u("AC4", 1 + 512 * q, 513 + 512 * q), ext(T.ac[:], "in_a"), "ld%d" % (4 + q))
-    iota(u("PIi", 0, 1), [[0, 1]], 0, 1)
-    iota(u("J", 0, 144), [[1, 144]], 0)
-    iota(u("IOT"), [[1, 128], [0, 16]], 128)
-    iota(u("Z0"), [[0, 2048]], 0)
-    iota(u("J2f"), [[1, 128], [0, 4]], 128)
-    iota(u("J3"), [[0, 128], [1, 4]], 0)
-    iota(u("J", 144, 512), [[1, 368]], 144)
-    iota(u("FREE", 0, 1024), [[0, 1024]], 0)
-    iota(u("Z1"), [[0, 2048]], 0)
-    fill(u("MS"), 1.0)
-    fill(e16("MS"), 0.0)
-    fill(u("OT", 0, 8), 0.0)
-    fill(u("OT", 2048, 2064), 0.0)
-    fill(u("W", 512, 640), 0.0)
-    J, J4, J15 = u("Jh"), u("J4h"), u("J15h")
-    J144, J8 = u("J", 0, 144), u("J", 0, 8)
-    pc = [3]
+    J, J4, J15, J144, J8 = u("Jb", 0, 128), u("J4b"), u("J15b"), u("Jb"), u("Jb", 0, 8)
+    pc = [16]
 
     def col(src, s1, o1, s2=None, o2=None):
         c = u("PC", pc[0], pc[0] + 1)
         pc[0] += 1
         ts(c, src, s1, o1, s2, o2)
         return c
+
+    def scaled(name, src, val):
+        act(u(name) if isinstance(name, str) else name, src, F.Copy, scale=val)
+    iota(u("PIi", 0, 1), [[0, 1]], 0, 1)
     P, P4, P15 = u("PC", 0, 1), u("PC", 1, 2), u("PC", 2, 3)
+    iota(J144, [[1, 144]], 0)
+    iota(J15, [[0, 8], [1, 16]], 0)
+    iota(J4, [[1, 8], [0, 16]], 0)
+    iota(u("J2f"), [[1, 128], [0, 4]], 0)
+    iota(u("J3"), [[0, 128], [1, 4]], 0)
+    iota(u("DUM"), [[0, 4], [16, 128]], 2064)
+    iota(u("PC", 4, 8), [[1, 4]], 1024, 4)
+    iota(u("PC", 8, 10), [[512, 2]], 8192 - 1536, 1)
+    iota(u("PC", 10, 11), [[0, 1]], 128, 1)
+    iota(u("J"), [[1, 512]], 0)
+    iota(u("FREE", 0, 1024), [[0, 1024]], 0)
+    iota(u("Z1"), [[0, 2048]], 0)
+    iota(u("QZ"), [[0, 512]], 0)
+    iota(u("DS", 2176, 2304), [[0, 128]], 0)
+    for t in range(RO):
+        iota(u("XV%d" % t), [[0, 256]], 0)
+    fill(u("MS"), 1.0)
+    fill(e16("MS"), 0.0)
+    fill(u("ZE"), 0.0)
+    fill(u("Z0"), 0.0)
+    fill(u("OT", 0, 8), 0.0)
+    fill(u("OT", 2048, 2064), 0.0)
+    fill(u("W", 512, 640), 0.0)
     ts(u("PIi", 1, 2), u("PIi", 0, 1), 4, A.logical_shift_right)
     ts(u("PIi", 2, 3), u("PIi", 0, 1), 15, A.bitwise_and)
     cp(u("PC", 0, 3), u("PIi", 0, 3))
-    ts(u("J4"), u("J", 0, 128), 4, A.logical_shift_right)
-    ts(u("J15"), u("J", 0, 128), 15, A.bitwise_and)
-    cp(J, u("J", 0, 128))
-    cp(J4, u("J4"))
-    cp(J15, u("J15"))
-    row4 = col(P15, 4.0, A.is_equal)
-    row0 = col(P15, 0.0, A.is_equal)
-    cls = [col(P15, float(c), A.is_equal, 64.0, A.mult) for c in range(4)]
-    ts(u("DUM"), J, 16.0, A.mult, col(P15, 2064.0, A.add), A.add)
-
-    ts(u("p6"), u("MI"), 2048, A.is_lt)
-    ts(u("t512a"), u("MI"), 1, A.add)
-    tt(u("W", 0, 512), u("t512a"), u("p6"), A.mult)
-
-    def owners(c):
-        ino = u("INO", 128 * c, 128 * c + 128)
-        ts(u("p5", 0, 128), u("MI", c, None, 4), 2048, A.is_equal)
-        tt(u("p5", 128, 256), u("DUM"), u("p5", 0, 128), A.mult)
-        tt(u("e128"), u("W", c, 512, 4), u("p5", 128, 256), A.max)
-        cp(ino, u("e128"))
+    ts(u("E16"), u("J15b", 0, 16), P15, A.is_equal)
+    ts(u("EP"), u("Jb", 0, 4), P, A.is_equal)
+    row0, row4 = u("E16", 0, 1), u("E16", 4, 5)
+    ts(u("DUM"), u("DUM"), P15, A.add)
+    V0 = u("FREE", 1024, 1536)
+    slope = col(row4, u("E16", 10, 11), A.add)
+    base = col(slope, 128.0, A.mult)
+    tt(base, base, col(u("E16", 10, 11), 64.0, A.mult), A.add)
+    act(u("p4"), u("J2f"), F.Identity, scale=slope, bias=base)
+    ts(u("t512b"), u("J3"), P15, A.is_equal, 64.0, A.mult)
+    tt(V0, u("t512b"), u("p4"), A.add)
+    for a, b in ((0, 128), (128, 512)):
+        ts(u("p6", a, b), u("MI", a, b), 2048, A.is_equal, 8192.0, A.mult)
+        ts(u("t512a", a, b), u("MI", a, b), 1, A.add)
+        tt(u("p5", a, b), u("t512a", a, b), u("p6", a, b), A.add)
+        tt(u("YM", a, b), u("DUM", a, b), u("p5", a, b), A.min)
+        cp(u("INO", a, b), u("YM", a, b))
+        tt(u("p5", a, b), u("t512a", a, b), u("p6", a, b), A.subtract)
+        ts(u("W", a, b), u("p5", a, b), 0.0, A.max)
+    for c in range(4):
+        ve = "VG" if c % 2 else "VE"
+        mark = (None, [("row4" + ve, 0, 1)])
+        if c < 2:
+            for h in range(2):
+                a, b = 1024 * h, 1024 * h + 1024
+                cp(u("ZE", a, b, 16), u("FREE", 1024 + 128 * c + 64 * h, 1024 + 128 * c + 64 * h + 64))
+                scan(u(ve, a, b), u("MS", a, b), u("ZE", a, b), A.mult, A.add)
+        else:
+            buf, o, n, _d = _ARENA[ve]
+            op("y", lambda buf=buf, o=o, n=n: g.sync.dma_start(T[buf][4:128:16, o:o + n], T[buf][10:128:16, o:o + n]), [u(ve)], [], 0.1, dma="ld%d" % (6 + c), lat=2.5)
         for h in range(2):
             a, b = 1024 * h, 1024 * h + 1024
-            off = u("INO", 128 * c + 64 * h, 128 * c + 64 * h + 64)
-            if OPT["sc"][c] == "v":
-                ts(u("VB", a, b), u("IOT", a, b), row4, A.mult, cls[c], A.add)
-                cp(ix(u("OT"), off), u("VB", a, b))
-            else:
-                ve = "VE" if c % 2 == 0 else "VG"
-                act(u(ve, a, b), u("IOT", a, b), F.Identity, scale=row4, bias=cls[c])
-                act(ix(u("OT"), off), u(ve, a, b), F.Silu)
+            act(ix(u("OT"), u("INO", 128 * c + 64 * h, 128 * c + 64 * h + 64)), u(ve, a, b), F.Silu)
 
-    for name, val in (("IDB", 1.0), ("NIDB", -1.0), ("ID16", 1.0), ("NID16", -1.0), ("N24", -2.0 ** 24), ("N20", -2.0 ** 20), ("P20", 2.0 ** 20),
-                      ("P25", 2.0 ** 25), ("N13", -2.0 ** 13), ("P12", 2.0 ** 12), ("P11", 2.0 ** 11)):
-        ts(u(name), J, P, A.is_equal, val, A.mult)
-    ts(u("ID2", 0, 128), J, P, A.is_equal, 16.0, A.mult)
-    ts(u("ID2", 128, 256), J, P, A.is_equal, 16.0, A.mult)
+    ts(u("IDB"), J, P, A.is_equal)
     ts(u("BD"), J4, P4, A.is_equal)
-    ts(u("NBD"), J4, P4, A.is_equal, -1.0, A.mult)
-    ts(u("BDn"), J4, P4, A.is_equal, -128.0, A.mult)
+    scaled(u("ID2", 128, 256), u("IDB"), 1.0)
+    for name, val in (("NIDB", -1.0), ("N24", -2.0 ** 24), ("N20", -2.0 ** 20), ("P20", 2.0 ** 20), ("P11", 2.0 ** 11),
+                      ("RV0", -49152.0), ("RV1", -24576.0), ("RV2", -12288.0)):
+        if name in OPT["sv"]:
+            scaled(name, u("IDB"), val)
+        else:
+            ts(u(name), u("IDB"), val, A.mult)
+    ts(u("NBD"), u("BD"), -1.0, A.mult)
+    ts(u("BDn"), u("BD"), -128.0, A.mult)
     ts(u("R16"), J15, P15, A.is_equal)
     ts(u("MC"), J15, P15, A.is_le)
     fill(e16("MC"), 0.0)
     ts(u("blk"), J8, P4, A.is_equal)
-    ts(u("nblk"), J8, P4, A.is_equal, -1.0, A.mult)
-    ts(u("nblkb"), J8, P4, A.is_equal, -1.0, A.mult)
-    ts(u("nblkf"), J8, P4, A.is_equal, -1.0, A.mult)
+    scaled("nblk", u("blk"), -1.0)
+    scaled("nblkf", u("blk"), -1.0)
     for name, val in (("w64k", 65536.0), ("w8k", 8192.0), ("w32", 32.0)):
-        ts(u(name), e16("BD"), val, A.mult)
+        scaled(name, u("blk"), val)
     fill(u("ONEB"), 1.0)
-    cp(u("ONE16"), u("ONEB"))
-    for z in "ZS HS ZB HB ZD HD ZQ HQ".split():
-        ts(u(z), J144, 0.0, A.mult)
-    fill(u("ZM"), 0.0)
-    fill(u("ZW"), 0.0)
-
-    def rows(name, slope, c1, c2, lo=0):
-        a = col(P, 0.0, A.is_equal, slope, A.mult)
-        b = col(P, 1.0, A.is_equal, c1, A.mult)
+    ts(u("ZALL"), u("MS", 0, 1152), 0.0, A.mult)
+    fill(u("ZMW"), 0.0)
+    keys = (("KAs", 4096.0, 2.0 ** 24, -1088.0), ("KAb", -1.0, -2.0 ** 20, 7.0), ("KAn", 512.0, 2.0 ** 24, 0.0), ("KAq", 1.0, 2.0 ** 20, -8.0),
+            ("KAp", 32768.0, 21.0 * 4096 * 160, -2.0 ** 17))
+    for name, slope, c1, c2 in keys:
+        lo = 128 if name == "KAp" else 0
+        b = col(u("EP", 1, 2), c1, A.mult)
         if c2:
-            tt(b, b, col(P, 2.0, A.is_equal, c2, A.mult), A.add)
-        ts(u(name, lo, lo + 128), J15, a, A.mult, b, A.add)
-    rows("KAs", 4096.0, 2.0 ** 24, -1088.0)
-    rows("KAb", -1.0, -2.0 ** 20, 7.0)
-    rows("KAn", 512.0, 2.0 ** 24, 0)
-    rows("KAq", 1.0, 2.0 ** 20, -8.0)
-    fill(u("KAp", 0, 128), 0.0)
-    rows("KAp", 1.0, -65536.0, 0, 128)
-    fill(u("KAd"), 2.0 ** 17)
-    fill(u("K12"), 2.0 ** 5)
-    fill(u("K13"), 2.0 ** 6)
-    fill(u("K14"), 2.0 ** 7)
-    fill(u("MIN"), -BIG)
+            ts(b, u("EP", 2, 3), c2, A.mult, b, A.add)
+        ts(u(name, lo, lo + 128), J15, col(u("EP", 0, 1), slope, A.mult), A.mult, b, A.add)
+    fill(u("KAp", 0, 128), 21.0 * 4096 * 160 / 128)
+    fill(u("KAx", 0, 128), 0.0)
+    ts(u("KAx", 128, 256), J15, u("EP", 0, 1), A.mult)
+    for name, val in (("KAd", 2.0 ** 17), ("K11", 2.0 ** 4), ("K20", 2.0 ** 13), ("K21", 2.0 ** 14), ("C25", 2.0 ** 25), ("THZ", 0.0), ("MIN3", -BIG)):
+        fill(u(name), val)
     fill(e16("MIN"), BIG)
-    fill(u("MINs"), -BIG)
-    ts(e16("MINs"), J8, 0.0, A.mult, col(P, 255.0 * 65536 + 2049 - 1088, A.add), A.add)
-    fill(u("MINn"), -BIG)
-    cp(u("CREP"), J)
+    iota(e16("MINs"), [[0, 8]], 255 * 65536 + 2049 - 1088, 1)
+    cp(u("CREP"), u("J", 0, 128))
     ts(u("SEL0R"), u("BD"), row0, A.mult)
-    ts(u("SEL0"), e16("BD"), row0, A.mult)
+    ts(u("SEL0"), u("blk"), row0, A.mult)
     ts(u("N25"), u("SEL0R"), -2.0 ** 25, A.mult)
-    hw = col(P15, 4.0, A.is_lt, 1.0 / 64, A.mult)
-    tt(hw, hw, P15, A.mult)
-    tt(hw, hw, col(row4, 4.0, A.mult), A.add)
+    hw = col(P15, 4.0, A.is_lt, P15, A.mult)
+    ts(hw, hw, 1.0 / 64, A.mult, col(row4, 4.0, A.mult), A.add)
     ts(u("HWN"), u("NBD"), hw, A.mult)
+    ts(u("kq"), u("E16", 0, 4), 2.0 ** 19, A.mult, hw, A.add)
     for c in range(4):
-        ts(u("og%d" % c), e16("BD"), col(cls[c], 2.0 ** 13, A.mult, hw, A.add), A.mult)
+        ts(u("og%d" % c), u("blk"), u("kq", c, c + 1), A.mult)
     last = col(P4, 16.0, A.mult, 15.0, A.add)
-    ts(u("Y"), J144, last, A.is_equal, row0, A.mult)
     ts(u("Y2"), J144, last, A.is_equal, 2.0, A.mult)
+    ts(u("Y"), J144, last, A.is_equal, row0, A.mult)
     ts(u("HY"), J144, last, A.is_equal, hw, A.mult)
-    ts(u("e128"), J, P, A.is_gt)
-    ts(u("m1"), J, P, A.is_equal, -4096.0, A.mult)
-    tt(u("TRIm"), u("e128"), u("m1"), A.add)
+    ts(u("b1"), J, P, A.is_gt)
+    tt(u("TRIm"), u("b1"), u("P11"), A.subtract)
     ts(u("NTRIm"), u("TRIm"), -1.0, A.mult)
-    tt(u("m2"), u("e128"), u("BD"), A.mult)
-    ts(u("m1"), u("m1"), 16.0, A.mult)
-    tt(u("BTX", 0, 128), u("m2"), u("m1"), A.add)
-    ts(u("BTX", 128, 256), u("BTX", 0, 128), -1.0, A.mult)
-    ts(u("m2"), J, P, A.is_lt)
-    tt(u("BTI"), u("m2"), u("BD"), A.mult)
-    tt(u("BTI"), u("BTI"), u("P12"), A.add)
-    ts(u("m1"), J, P, A.is_equal, -4.0, A.mult)
-    ts(u("m2"), u("m2"), -56.0, A.mult, -8.0, A.add)
-    tt(u("PEN", 0, 128), u("m2"), u("m1"), A.add)
+    tt(u("BT1", 0, 128), u("b1"), u("BD"), A.mult)
+    ts(u("BT1", 128, 256), u("BT1", 0, 128), -1.0, A.mult)
+    ts(u("b2"), u("IDB"), -4.0, A.mult)
+    tt(u("b1"), u("BT1", 0, 128), u("b2"), A.add)
+    ts(u("BTX", 0, 128), u("b1"), 32768.0, A.mult)
+    ts(u("BTX", 128, 256), u("b1"), -32768.0, A.mult)
+    ts(u("b1"), J, P, A.is_lt)
+    tt(u("BTI"), u("b1"), u("BD"), A.mult)
+    tt(u("BTI"), u("BTI"), u("P11"), A.add)
+    ts(u("b1"), u("b1"), -56.0, A.mult, -8.0, A.add)
+    tt(u("PEN", 0, 128), u("b1"), u("b2"), A.add)
     cp(u("PEN", 128, 256), u("PEN", 0, 128))
     cp(u("PEN", 256, 512), u("PEN", 0, 256))
-    ts(u("CMR"), u("R16"), col(P, 128.0, A.add), A.mult)
-    c4 = col(P, 4.0, A.mult, 1024.0, A.add)
+    ts(u("CMR"), u("R16"), u("PC", 10, 11), A.mult)
     for c in range(4):
-        ts(u("CMK%d" % c), u("R16"), col(c4, float(c), A.add), A.mult)
-    for name, lo, val in (("CNT", 0, -1920.0), ("CNT", 128, -3968.0)):
-        ts(u(name, lo, lo + 128), u("R16"), 8192.0 + val, A.mult, -8192.0, A.add)
-    for lo, val in ((0, -1536.0), (128, -1024.0)):
-        ts(u("CTG", lo, lo + 128), u("R16"), col(P, 8192.0 + val, A.add), A.mult, -8192.0, A.add)
-    ts(u("CB"), J8, 256.0, A.mult, col(P15, 16.0, A.mult, 7.0, A.add), A.add)
-    ts(u("CQ"), u("CB"), 1.0, A.add)
-    ts(u("CT"), J8, 16.0, A.mult, P15, A.add)
-    ts(u("CIX"), u("J", 0, 32), 16.0, A.mult, P15, A.add)
+        ts(u("CMK%d" % c), u("R16"), u("PC", 4 + c, 5 + c), A.mult)
+    ts(u("CNT", 0, 128), u("R16"), 8192.0 + 128, A.mult, -8192.0, A.add)
+    ts(u("CNT", 128, 256), u("R16"), 8192.0 - 1920, A.mult, -8192.0, A.add)
+    for q in range(2):
+        ts(u("CTG", 128 * q, 128 * q + 128), u("R16"), u("PC", 8 + q, 9 + q), A.mult, -8192.0, A.add)
+    ts(u("CIX"), u("Jb", 0, 32), 16.0, A.mult, P15, A.add)
+    ts(u("CB"), u("CIX", 0, 8), 16.0, A.mult, 7.0, A.add)
+    ts(u("CQ"), u("CIX", 0, 8), 16.0, A.mult, 8.0, A.add)
     ts(u("C512"), u("CIX"), 512.0, A.add)
-    fill(u("C25"), 2.0 ** 25)
-    fill(u("DS", 2176, 2304), 0.0)
-    fill(u("QZ"), 0.0)
-    fill(u("Aa"), 0)
-    for t in range(RO):
-        fill(u("XV%d" % t), 0.0)
-    V0 = u("FREE", 1024, 1536)
-    act(u("p4"), u("J2f"), F.Identity, scale=row4)
-    ts(u("t512b"), u("J3"), P15, A.is_equal, col(P15, 4.0, A.is_lt, 64.0, A.mult), A.mult)
-    tt(V0, u("t512b"), u("p4"), A.add)
-    half = u("PC", 47, 48)
-    scale2 = u("m1", 0, 16)
-    fill(scale2, 0.5)
+    fill(u("Aa", 256, 264), 0.0)
+    half = u("PC", 63, 64)
+    fill(u("m1", 0, 16), 0.5)
     fill(u("m2", 0, 16), 0.0)
-    op("v", lambda: v.tensor_tensor_scan(u("m1", 16, 32)[0], scale2[0], u("m2", 0, 16)[0], 1.0, A.mult, A.add), [u("m1", 16, 32)], [scale2, u("m2", 0, 16)], 0.07)
-    tt(u("m2", 16, 32), u("m1", 16, 32), u("R16", 0, 16), A.mult)
-    op("v", lambda: v.tensor_reduce(half[0], u("m2", 16, 32)[0], AX_.X, A.add), [half], [u("m2", 16, 32)], 0.07)
-    ts(u("Qi"), u("J"), half, A.mult, -0.499, A.add)
+    op("v", lambda: v.tensor_tensor_scan(u("m1", 16, 32)[0], u("m1", 0, 16)[0], u("m2", 0, 16)[0], 1.0, A.mult, A.add), [u("m1", 16, 32)], [u("m1", 0, 16), u("m2", 0, 16)], 0.11)
+    tt(u("m2", 16, 32), u("m1", 16, 32), u("E16"), A.mult)
+    op("v", lambda: v.tensor_reduce(half[0], u("m2", 16, 32)[0], AX_.X, A.add), [half], [u("m2", 16, 32)], 0.11)
+    ts(u("J3"), u("J"), half, A.mult, -0.499, A.add)
     ts(u("p7"), u("J"), half, A.mult)
-    tt(u("t512b"), u("Qi"), u("p7"), A.subtract)
-    ts(u("CODE"), u("t512b"), -0.5, A.is_le, 2.0, A.mult)
-    ts(u("CODE"), u("CODE"), -1.0, A.add, col(P15, 9.0, A.is_lt), A.mult)
-    ts(u("m2", 32, 36), u("J", 0, 4), col(P15, -9.0, A.add), A.is_equal, 4.0, A.mult)
+    tt(u("t512b"), u("J3"), u("p7"), A.subtract)
+    bits = col(P15, 9.0, A.is_lt)
+    ts(u("CODE"), u("t512b"), -0.5, A.is_le, -0.5, A.add)
+    ts(u("CODE"), u("CODE"), 2.0, A.mult, bits, A.mult)
+    ts(u("m2", 32, 36), u("Jb", 0, 4), col(P15, -9.0, A.add), A.is_equal, 4.0, A.mult)
     tt(u("CODE", 0, 4), u("CODE", 0, 4), u("m2", 32, 36), A.add)
     ts(u("PIi", 3, 4), u("PIi", 1, 2), 3, A.bitwise_and)
-    ts(u("G4"), u("J", 0, 4), col(u("PIi", 3, 4), 1.0, A.mult), A.is_equal)
-    lim, lim2, wt = col(u("LI", 0, 1), -65536.0, A.mult), col(u("LI", 1, 2), -65536.0, A.mult), col(u("WI"), 1.0, A.mult)
-    ts(u("WY"), J144, last, A.is_equal, wt, A.mult)
-    ts(u("ROW1"), J8, 0.0, A.mult, col(P, 1.0, A.is_equal), A.add)
-    ts(u("z8"), u("ROW1"), -2048.0, A.mult)
-    ts(u("L2N"), u("SEL0"), lim2, A.mult)
-    tt(u("L2N"), u("L2N"), u("z8"), A.add)
-    ts(u("THN"), u("SEL0"), lim, A.mult)
-    tt(u("THN"), u("THN"), u("z8"), A.add)
-    ts(u("ROW1"), u("ROW1"), -65536.0, A.mult)
-    fill(u("THZ"), 0.0)
+    ts(u("G4"), u("Jb", 0, 4), col(u("PIi", 3, 4), 1.0, A.mult), A.is_equal)
+    ts(u("m2", 40, 44), u("m2", 32, 36), 0.25, A.mult, bits, A.add)
+    for q in range(4):
+        ts(u("KQ", 4 * q, 4 * q + 4), u("m2", 40, 44), u("G4", q, q + 1), A.mult)
+    ts(u("PC", 12, 14), u("LI"), -65536.0, A.mult)
+    ts(u("WY"), J144, last, A.is_equal, col(u("WI"), 1.0, A.mult), A.mult)
+    less = col(u("EP", 1, 2), -2048.0, A.mult)
+    ts(u("L2N"), u("SEL0"), u("PC", 13, 14), A.mult, less, A.add)
+    ts(u("THN"), u("SEL0"), u("PC", 12, 13), A.mult, less, A.add)
+    ts(u("ROW1"), J8, 0.0, A.mult, col(less, 32.0, A.mult), A.add)
     for s in range(16):
         o, i = u("SH", 128 * s, 128 * s + 128), u("BD")
         op("k", lambda o=o, i=i, s=s: g.affine_select(o[0], i[0], [[1, 128]], A.is_equal, 0.0, -s, -1), [o], [i], 0.43)
@@ -530,8 +589,11 @@ def rank_program(g, core, T, topo):
         z, s1, s16 = "Z%d" % (t % 2), "S1" + "ab"[t % 2], "S16" + "ab"[t % 2]
         lanes = u("W", cl, 512, 4)
         cp(u("OWN"), lanes)
-        gather("T", "OWN", OPT["T"])
-        act(u("PRE"), lanes, F.Sign)
+        gather("T", "OWN", OPT["T"] if t else OPT["T0"])
+        if t:
+            act(u("PRE"), lanes, F.Sign)
+        else:
+            ts(u("PRE"), lanes, 0.0, A.is_gt)
         cp(u("OWNH"), lanes)
         k = u("p3", 0, 128)
         mm([(k, u("ONEB"), u("KAs")), (k, u("PRE"), u("N24")), (k, u("OWNH"), u("ID16"))] + sums("p3", 0, "T", "w64k"))
@@ -591,18 +653,24 @@ def rank_program(g, core, T, topo):
            + [(lv, u("Y2", 15 - k, 143 - k), u("AW", 128 * k, 128 * k + 128)) for k in range(16)])
         ts(u("L1T"), lv, 0.0, A.is_lt)
         pp = u("p7", 128, 384)
-        mm([(pp, u("ONEB"), u("KAp")), (pp, u("OWNH"), u("ID2")), (pp, u("L1T"), u("BTX"))])
-        ts(u("Pa", 0, 256), pp, 0.0, A.max)
+        x = u("p2", 0, 256)
+        mm([(x, u("ONEB"), u("KAx")), (x, u("L1T"), u("BT1"))])
+        for q in range(3):
+            act(u("XF", 256 * q, 256 * q + 256), x, F.Identity, scale=0.5 ** (q + 1), bias=159.5 + 0.5 ** (q + 2))
+        mm([(pp, u("ONEB"), u("KAp")), (pp, u("OWNH"), u("ID2")), (pp, u("L1T"), u("BTX"))]
+           + [(pp, u("RV%d" % q), u("XF", 256 * q, 256 * q + 256)) for q in range(3)])
+        ts(u("Pa"), pp, 0.0, A.max)
         TAG[0] = "shift%d" % t
         for s in range(4):
             a, b = ("Pa", "Pb") if s % 2 == 0 else ("Pb", "Pa")
-            ts(u("Mi", 0, 256), u(a, 0, 256), 1 << s, A.bitwise_and)
-            ts(u("p5", 0, 256), u("Mi", 0, 256), 2.0 ** (16 - s), A.mult)
-            tt(u("p5", 256, 512), u(a, 0, 256), u("p5", 0, 256), A.subtract)
-            tt(u("Aa", 0, 256), u(a, 0, 256), u("p5", 0, 256), A.min)
-            tt(u(b, 0, 256), u("p5", 256, 512), u("Aa", 1 << s, 256 + (1 << s)), A.max)
-        ts(u("Mi", 0, 256), u("Pa", 0, 256), 4, A.logical_shift_right)
-        cp(u("SL"), u("Mi", 0, 256))
+            th = 2.0 ** (15 - s)
+            if OPT["sh"] == "s":
+                act(u("Aa", 0, 256), u(a), F.Relu, bias=-th)
+            else:
+                ts(u("Aa", 0, 256), u(a), -th, A.add, 0.0, A.max)
+            ts(u("p5", 0, 256), u(a), th, A.is_ge, 2 * th, A.mult)
+            tt(u("p5", 256, 512), u(a), u("p5", 0, 256), A.subtract)
+            tt(u(b if s < 3 else "SL"), u("p5", 256, 512), u("Aa", 1 << s, 256 + (1 << s)), A.max)
         mm([(u("p6", 288, 416), u("SL", 0, 128), u("ID16")), (u("p6", 288, 416), u("NID16"), u("OWNH"))])
         act(u("DS", 2048, 2176), u("p6", 288, 416), F.Copy)
 
@@ -614,8 +682,10 @@ def rank_program(g, core, T, topo):
         for h in range(2):
             a, b = 1024 * h, 1024 * h + 1024
             act(u("OG", a, b), ix(u("OT", 0, 2064), u("AN", 64 * h, 64 * h + 64)), F.Copy)
-            tt(u("AX", a, b), ix(win, u("AN", 64 * h, 64 * h + 64)), u("REP", a, b), A.subtract)
-            act(u("DU", a, b), u("AX", a, b), F.Square)
+        cuts = {2: (0, 64, 128), 3: (0, 56, 104, 128), 4: (0, 32, 64, 96, 128)}[OPT["nr"]]
+        for a, b in zip(cuts, cuts[1:]):
+            tt(u("AX", 16 * a, 16 * b), ix(win, u("AN", a, b)), u("REP", 16 * a, 16 * b), A.subtract)
+            act(u("DU", 16 * a, 16 * b), u("AX", 16 * a, 16 * b), F.Square)
         k = u("p3", 256, 384)
         mm([(k, u("ONEB"), u("KAn")), (k, u("PRE"), u("N25"))] + sums("p3", 256, "OG", "og%d" % cl) + sums("p3", 256, "DU", "w8k"))
         scan(u("S2"), u("MINn"), k, A.max, A.min)
@@ -631,12 +701,12 @@ def rank_program(g, core, T, topo):
         act(u("PRD"), lists, F.Sign)
         cp(u("DMH"), lists)
         hold(u("D1R"), u("ZD", 0, 128))
-        keep = u("mc", 1, 2)
-        ts(keep, P15, 9.0 + cl, A.is_equal)
-        ts(keep, P15, 9.0, A.is_lt, keep, A.add)
-        ts(u("kq"), u("G4"), keep, A.mult)
         for q in range(4):
-            act(u("CG", 128 * q, 128 * q + 128), ix(u("CODE"), u("D16")), F.Identity, scale=u("kq", q, q + 1))
+            o, i, keep = u("CG", 128 * q, 128 * q + 128), ix(u("CODE"), u("D16")), u("KQ", 4 * q + cl, 4 * q + cl + 1)
+            if OPT["cg"][q] == "s":
+                act(o, i, F.Identity, scale=keep)
+            else:
+                ts(o, i, keep, A.mult)
         for h in range(2):
             ps = "p%d" % h
             items = [(u(ps), u("IDB"), u("PEN"))]
@@ -644,9 +714,9 @@ def rank_program(g, core, T, topo):
                 x = u("CG", 128 * q, 128 * q + 128, 1, (64 * h, 64 * h + 64))
                 items.append((u(ps, 128 * q, 128 * q + 128), x, x))
             mm(items)
-            act(u("EQ", 512 * h, 512 * h + 512), u(ps), F.Relu)
+            relu(OPT["eq"][h], u("EQ", 512 * h, 512 * h + 512), u(ps))
         mm([(u("p6", 416, 424), u("PRE"), e16("BD")), (u("p6", 416, 424), u("PRD"), e16("BD"))])
-        act(u("SZ"), u("p6", 416, 424), F.Relu, bias=-16.0)
+        act(u("SZ"), u("p6", 416, 424), F.Relu, scale=32.0, bias=-512.0)
         k = u("p3", 384, 512)
         mm([(k, u("ONEB"), u("KAd")), (k, u("PRD"), u("N24"))] + sums("p3", 384, "DT", "w64k"))
         scan(u("AX"), u("MS"), u("DT"), A.mult, A.max)
@@ -661,7 +731,7 @@ def rank_program(g, core, T, topo):
             for q in range(4):
                 s = 4 * c + q
                 mm([(u(ps, 128 * q, 128 * q + 128), u("SH", 128 * s, 128 * s + 128), u("DMH"))])
-            act(u("DS", 512 * c, 512 * c + 512), u(ps), F.Copy)
+            copy(OPT["ds"][c], u("DS", 512 * c, 512 * c + 512), u(ps))
 
     def part_finish(t):
         TAG[0] = "fin%d" % t
@@ -685,37 +755,48 @@ def rank_program(g, core, T, topo):
         send(T.cores[(rank + 1 + t % 7) % 8], u(xv, 0, 32), "QI%d" % t, "rq%d" % t, "fq%d" % t, "lq%d" % t, 0, T.cores[(rank - 1 - t % 7) % 8])
         q = u("p6", 0, 256)
         mm([(q, u("ID16"), u("CNT")), (u("p6", 0, 128), u("PRE"), u("BDn")), (u("p6", 0, 128), u("P12"), u("MR")), (u("p6", 128, 256), u("P12"), u("SR"))])
-        act(u("QN"), q, F.Relu)
+        relu(OPT["q"][0], u("QN"), q)
         nt = u("p4", 112, 120)
         mm([(nt, u("ID16"), u("CT")), (nt, u("QN", 0, 128), u("nblkb")), (nt, u("QN", 128, 256), u("nblkb"))])
         ts(u("NT16"), nt, 2176.0, A.add)
         tt(u("W", cl, 512, 4), ix(u("DS"), u("NT16")), u("OWNH"), A.add)
         mm([(u("p4", 120, 128), u("KP"), u("blk"))])
         cp(u("K16"), u("p4", 120, 128))
-        act(u("EVb"), ix(u("FREE"), u("K16")), F.Copy)
-        act(u("EV"), ix(u("FREE"), u("K16")), F.Copy)
+        copy(OPT["q"][3], u("EVb"), ix(u("FREE"), u("K16")))
+        if "s" in OPT["mv"]:
+            act(u("EV"), ix(u("FREE"), u("K16")), F.Copy)
         q = u("p0", 0, 256)
         mm([(q, u("ID16"), u("CTG")), (u("p0", 0, 128), u("NID16"), u("D1R")), (u("p0", 0, 128), u("P11"), u("MR")),
             (u("p0", 128, 256), u("P11"), u("SR")), (u("p0", 128, 256), u("EVb"), u("HWN"))])
-        act(u("QR", 0, 256), q, F.Relu)
+        relu(OPT["q"][1], u("QR", 0, 256), q)
         tg = u("p4", 128, 136)
         mm([(tg, u("ID16"), u("CT")), (tg, u("QR", 0, 128), u("nblkf")), (tg, u("QR", 128, 256), u("nblkf"))])
         ts(u("TG16"), tg, 512.0, A.add)
         el = u("p1", 0, 128)
         mm([(el, u("SL", 128, 256), u("ID16")), (el, u("MR"), u("N13"))])
-        act(u("ELS"), el, F.Relu)
+        relu(OPT["q"][2], u("ELS"), el)
         cp(ix(u("W"), u("TG16")), u("ELS"))
         a, b = u("p7", 128, 256), u("p7", 256, 384)
         mm([(a, u("ONEB"), u("K14")), (a, u("ID16"), u("DMH")), (a, u("N13"), u("PRD")), (a, u("MR"), u("N13"))])
         mm([(b, u("ONEB"), u("K14")), (b, u("ID16"), u("OWNH")), (b, u("N13"), u("L1T")), (b, u("SR"), u("N13"))])
-        tt(u("m1"), a, u("DUM"), A.min)
+        tt(u("m1"), a, u("DUM", 0, 128), A.min)
         tt(u("m2"), b, u("m1"), A.min)
         cp(u("MVO"), u("m2"))
-        n = OPT["mv"]
+        n = len(OPT["mv"])
         for h in range(n):
             a, b = 2048 // n * h, 2048 // n * (h + 1)
-            act(u("VE", a, b), ix(u("EV"), u("CREP", a // 16, b // 16)), F.Copy)
-            act(ix(u("OT"), u("MVO", a // 16, b // 16)), u("VE", a, b), F.Silu)
+            to = ix(u("OT"), u("MVO", a // 16, b // 16))
+            if OPT["mv"][h] == "s":
+                act(u("VE", a, b), ix(u("EV"), u("CREP", a // 16, b // 16)), F.Copy)
+                act(to, u("VE", a, b), F.Silu)
+            elif OPT["mv"][h] == "w":
+                cp(u("ZE", a, b, 16), u("EVb", a // 16, b // 16))
+                scan(u("VE", a, b), u("MS", a, b), u("ZE", a, b), A.mult, A.add)
+                act(to, u("VE", a, b), F.Silu)
+            else:
+                cp(u("ZE", a, b, 16), u("EVb", a // 16, b // 16))
+                scan(u("VB", a, b), u("MS", a, b), u("ZE", a, b), A.mult, A.add)
+                cp(to, u("VB", a, b))
         if t + 1 < RO:
             mm([(u("p6", 424, 432), u("ONEB"), e16("ZM"))])
             act(u("z8"), u("p6", 424, 432), F.Identity, bias=-0.9375, acc=u("mc", 4, 5))
@@ -745,8 +826,8 @@ def rank_program(g, core, T, topo):
         act(u("PRH"), ix(u("W", 0, 512), u("H16")), F.Sign)
         tt(u("QD"), ix(win, u("HL")), u("QRp"), A.subtract)
         act(u("QS"), u("QD"), F.Square)
-        k = u("p2", 0, 128, 1, p32)
-        mm([(k, u("ONEB", 0, 32), u("KAq")), (k, u("PRH"), u("N20"))] + sums("p2", 0, "QS", "w32", p32))
+        k = u("p4", 256, 384, 1, p32)
+        mm([(k, u("ONEB", 0, 32), u("KAq")), (k, u("PRH"), u("N20"))] + sums("p4", 256, "QS", "w32", p32))
         scan(u("QSC", p=p32), u("MIN", p=p32), k, A.max, A.min)
         low(e16("ZQ", 0, 128, p32), e16("QSC", 15, None, p32), u("hq8", p=p32), 32)
         tile("ZQ", "HQ", u("p4", 140, 142), 1, [(u("ID16"), u("CQ", 0, 2))], p32, 2)
@@ -762,9 +843,6 @@ def rank_program(g, core, T, topo):
         act(u("NV"), ix(u(xv), u("RT16" + "ab"[t % 2])), F.Copy)
         cp(ix(win, u("S16" + "ab"[t % 2])), u("NV"))
 
-    for c in range(4):
-        TAG[0] = "init"
-        owners(c)
     part_own(0)
     part_vacant(0)
     part_split(0)

@@ -1,9 +1,11 @@
+import math
 from concourse.mybir import dt, AluOpType as A, AxisListType as AX_, ActivationFunctionType as F
 
 RO = 5
 BIG = 1.0e9
 S, B, H, I, U = "float32", "bfloat16", "float16", "int32", "uint16"
 TAG = [""]
+BON = [0]
 
 SCRATCH = {}
 
@@ -22,7 +24,7 @@ _sb("W", 640, S)
 _sb("OT", 4112, S)
 _sb("VE VG", 2048, S)
 _sb("FREE", 1536, S)
-_sb("DS", 2304, S)
+_sb("DS", 768, S)
 _sb("CODE", 512, B)
 _sb("EV", 128, S)
 _sb("T", 2048, B)
@@ -36,7 +38,8 @@ _sb("INO", 512, U)
 _sb("OCC PEN QZ QRp QS CG", 512, B)
 _sb("kq G4", 4, S)
 _sb("EQ", 1024, B)
-_sb("Jh OWNH DMH ID16 NID16 ONE16 J4h J15h KP RP D1R CMR CMK0 CMK1 CMK2 CMK3 R16", 128, H)
+_sb("Jh OWNH DMH ID16 NID16 ONE16 J4h J15h KP RP D1R CMR CMK0 CMK1 CMK2 CMK3", 128, H)
+_sb("R16", 128, B)
 _sb("ZS HS ZB HB ZD HD ZQ HQ", 144, H)
 _sb("SL CNT CTG", 256, H)
 _sb("ID2", 256, B)
@@ -56,7 +59,24 @@ _sb("Y Y2 WY HY", 144, B)
 _sb("MINs MINn MIN S1a S1b S2 S3 SB QSC NFR ELS m1 m2 e128", 128, S)
 _sb("Pa Pb", 256, S)
 _sb("Aa", 264, S)
-_sb("PIi", 4, I)
+_sb("PIi", 8, I)
+_sb("EXP", 2048, B)
+_sb("IDT", 2064, S)
+_sb("ZT ZP WTn ID2x B512", 128, B)
+_sb("KQ5", 512, B)
+_sb("MIN5", 512, S)
+_sb("ALT", 640, B)
+_sb("O16", 2, U)
+_sb("VR", 32, S)
+_sb("PA EH PD PM", 32, B)
+_sb("WV A4n B4 CN1 QB K9 MR2 WR2", 128, B)
+_sb("IDF ONEF NFF", 128, S)
+_sb("YF", 144, S)
+_sb("D1", 512, S)
+_sb("DM2", 128, H)
+_sb("KR", 256, H)
+_sb("BT16", 8, U)
+_sb("RKa RKb", 16, U)
 _sb("PC", 64, S)
 _sb("J4 J15", 128, I)
 _sb("CB CQ", 8, H)
@@ -98,20 +118,23 @@ for _n, _first, _len in (("ZALL", "ZS", 1152), ("ZMW", "ZM", 256), ("MIN3", "MIN
     _ARENA[_n] = (_ARENA[_first][0], _ARENA[_first][1], _len, _ARENA[_first][3])
 for _n, _m in (("ID16", "IDB"), ("NID16", "NIDB"), ("N13", "N20"), ("P12", "P11"), ("P25", "P20"), ("K12", "K11"), ("K13", "K20"), ("K14", "K21"), ("nblkb", "nblk"), ("CT", "CIX")):
     _ARENA[_n] = _ARENA[_m]
+_ARENA["MWR"] = _ARENA["MR2"][:2] + (256, B)
+_ARENA["MR"], _ARENA["WR"] = _ARENA["MR2"], _ARENA["WR2"]
 _ARENA["CT"] = _ARENA["CIX"][:2] + (8, H)
 for _k in range(8):
     SCRATCH["p%d" % _k] = ("psum", [128, 512], S)
     _ARENA["p%d" % _k] = ("p%d" % _k, 0, 512, S)
-SEMAPHORES = ["v", "p", "s", "k"] + ["ld%d" % i for i in range(10)] + ["st0", "st1"]
+SEMAPHORES = ["v", "p", "s", "k"] + ["ld%d" % i for i in range(11)] + ["cd%d" % i for i in range(9)] + ["st0", "st1"]
 for _t in range(RO):
     SEMAPHORES += ["rq%d" % _t, "rs%d" % _t, "lq%d" % _t, "ls%d" % _t, "fq%d" % _t, "fs%d" % _t, "mq%d" % _t, "ms%d" % _t]
 _ORDER = {}
-CYC, PEC, CALL, WAKE, GAT, SCA, WAY = 0.0009, 0.0005, 0.05, 0.06, 1.5, 3.5, 2.5
-OPT = {"T": 48, "DT": 48, "sc": "ssss", "mv": "wwww", "sh": "s", "nr": 3, "cg": "ssss", "turns": 4, "sv": ("NIDB", "N24", "N20", "P20", "P11"), "T0": 128, "lam": 5, "slip": 0.1, "eq": "ss", "ds": "ssss", "q": "ssss"}
+CYC, PEC, CALL, WAKE, GAT, SCA, WAY = 0.00087, 0.00055, 0.045, 0.06, 1.5, 3.2, 2.5
+FIRST = 2.5
+OPT = {"lams": ((3, 2, 0.1), (5, 2, 0.1), (8, 2, 0.1), (3, 2, 0.05), (5, 2, 0.05), (8, 2, 0.05), (5, 0, 0.1), (5, 1, 0.08), (12, 1, 0.08), (2, 1, 0.08)), "ls": 3000, "tol": 0.0, "sq": 0, "eta": 0.3, "mu": 1.0, "xw": 0.12, "pec": 0.00055, "os": 0.08, "way": 2.5, "ho": "s", "ap": "vv", "occ": "s", "aw": 1, "vg": 0, "bon": 30, "bot": 0, "T": 96, "DT": 80, "sc": "ssss", "mv": "wwww", "sh": "s", "nr": 3, "cg": "ssss", "turns": 4, "sv": ("NIDB", "N24", "N20", "P20", "P11", "RV0", "RV1", "RV2"), "T0": 128, "lam": 5, "slip": 0.1, "eq": "ss", "ds": "ssss", "q": "sssssvs", "alt": (4,), "sg": "svsv", "nx": "t", "nb": (2, 0, 1, 2, 0), "nc": (0, 32, 64, 96, 120, 128), "dh": 1, "en": 16, "k1": 1, "rk": 0, "look": 2, "lam2": 2, "noise": 0, "rl": 0}
 
 
 def _mask(topo, a, b):
-    es = topo.engines(a, b)[:8]
+    es = topo.engines(a, b)[:OPT["en"]]
     return sum(1 << e for e in es), len(es)
 
 
@@ -120,15 +143,16 @@ def _relay(topo, a, b, which):
         return None
     c = [h for h in topo.cores_of(a) if h != a and topo.may_write(h, b)]
     c.sort(key=lambda h: (topo.die(h) != topo.die(a), h))
-    return c[which % len(c)]
+    return c[which * OPT["rl"] % len(c)]
 
 
 def _relay_program(g, core, T, topo):
     used = []
     for t in range(RO):
-        for r in range(8):
-            a, b = T.cores[r], T.cores[(r + 1 + t % 7) % 8]
-            for (x, y, buf, arr, fwd, loc, which) in ((a, b, "QI", "rq", "fq", "mq", 0), (b, a, "RS", "rs", "fs", "ms", 1)):
+        for which, (buf, arr, fwd, loc) in enumerate((("QI", "rq", "fq", "mq"), ("RS", "rs", "fs", "ms"))):
+            for r in range(8):
+                x, y = T.cores[r], T.cores[(r + 1 + t % 7) % 8]
+                x, y = (y, x) if which else (x, y)
                 if _relay(topo, x, y, which) == core:
                     _, n = _mask(topo, x, core)
                     m, n2 = _mask(topo, core, y)
@@ -161,9 +185,17 @@ def _order(ops):
             log.setdefault(b, []).append((lo, hi, i, False))
         pred[i].discard(i)
     succ = [[] for _ in range(n)]
+    early = {}
     for i in range(n):
         for j in pred[i]:
             succ[j].append(i)
+            if ops[i]["items"] and ops[j]["e"] != "p":
+                at = 0.0
+                for (_o, a, b) in ops[i]["items"]:
+                    if any(x[0] == y[0] and x[1] < y[2] and y[1] < x[2] for x in a[1] + b[1] for y in ops[j]["wr"]):
+                        early[(j, i)] = at
+                        break
+                    at += max(min(64, a[2]), b[2]) * (4 if a[3] == S else 1) * PEC
     way = [0.0] * n
     for i in range(n - 1, -1, -1):
         way[i] = ops[i]["cost"] + ops[i]["lat"] + max([way[j] + WAKE for j in succ[i]] + [0.0])
@@ -199,6 +231,8 @@ def _order(ops):
                 if not left[j]:
                     ready.append(j)
         return start, [start[i] + ops[i]["cost"] + (0.0 if back else ops[i]["lat"]) for i in range(n)]
+    why = {}
+
     def run(before, after, rank, back):
         left = [len(p) for p in before]
         base, start = [0.0] * n, [0.0] * n
@@ -213,40 +247,160 @@ def _order(ops):
             for b in holds[i][1:]:
                 for e2, t2 in bank.get(b, {}).items():
                     if e2 != e:
-                        s = max(s, t2 + WAKE)
+                        s = max(s, t2 + OPT["xw"])
             return s
+
+        def done(a, s, j):
+            return s + ops[a]["cost"] + (WAKE if ops[a]["e"] == ops[j]["e"] else OPT["xw"]) + (0.0 if back else ops[a]["lat"]) - early.get((j, a) if back else (a, j), 0.0)
+        order, user = [], {}
+        why.clear()
         for _i in range(n):
-            pick = None
+            st = {i: can(i) for lst in ready.values() for i in lst}
+            soon, front = {}, st
+            for _d in range(OPT["look"]):
+                nxt, seen = {}, {}
+                for a, s in front.items():
+                    for j in after[a]:
+                        seen[j] = seen.get(j, 0) + 1
+                        nxt[j] = max(nxt.get(j, base[j]), done(a, s, j))
+                front = {j: max(s, free.get(ops[j]["e"], 0.0)) for j, s in nxt.items() if seen[j] == left[j]}
+                for j, s in front.items():
+                    soon.setdefault(ops[j]["e"], []).append((j, s))
+            pick = held = None
             for e, lst in ready.items():
                 if lst:
-                    st = {i: can(i) for i in lst}
                     a = max(lst, key=lambda i: rank[i] - OPT["lam"] * st[i])
-                    fit = [i for i in lst if st[i] + ops[i]["cost"] <= st[a] + OPT["slip"]]
-                    a = max(fit, key=lambda i: rank[i]) if fit else a
-                    if pick is None or st[a] < pick[0]:
+                    limit = st[a]
+                    for j, s in soon.get(e, ()):
+                        if rank[j] - OPT["lam2"] * s > rank[a] - OPT["lam2"] * st[a] and s < st[a] + ops[a]["cost"] - OPT["slip"]:
+                            limit, a = min(limit if a is None else 1e9, s), a
+                            held = (st[a], a) if held is None or st[a] < held[0] else held
+                            fit = [i for i in lst if st[i] + ops[i]["cost"] <= s + OPT["slip"]]
+                            a = max(fit, key=lambda i: rank[i]) if fit else None
+                            break
+                    else:
+                        fit = [i for i in lst if st[i] + ops[i]["cost"] <= limit + OPT["slip"]]
+                        a = max(fit, key=lambda i: rank[i]) if fit else a
+                    if a is not None and (pick is None or st[a] < pick[0]):
                         pick = (st[a], a)
-            s, a = pick
+            s, a = pick or held
             e, c = ops[a]["e"], ops[a]["cost"]
             ready[e].remove(a)
+            order.append(a)
+            if s > base[a] + 1e-9 and s > 0:
+                near = [x for x in [user.get(r) for r in holds[a]] if x is not None]
+                why[a] = max(near, key=lambda x: start[x] + ops[x]["cost"]) if near else why.get(a)
+            for r in holds[a]:
+                user[r] = a
             start[a], free[e] = s, s + c
             for b in holds[a][1:]:
                 bank.setdefault(b, {})[e] = s + c
             for j in after[a]:
-                base[j] = max(base[j], s + c + WAKE + (0.0 if back else ops[a]["lat"]))
+                if done(a, s, j) > base[j]:
+                    why[j] = a
+                base[j] = max(base[j], done(a, s, j))
                 left[j] -= 1
                 if not left[j]:
                     ready.setdefault(ops[j]["e"], []).append(j)
-        return start, [start[i] + ops[i]["cost"] + (0.0 if back else ops[i]["lat"]) for i in range(n)]
+        return order, [start[i] + ops[i]["cost"] + (0.0 if back else ops[i]["lat"]) for i in range(n)]
     if OPT["lam"]:
         place = run
     best = None
     _ORDER["dbg"] = (ops, succ, list(way))
-    for _turn in range(OPT["turns"]):
+    way0 = way
+    for _turn in range(OPT["turns"] * len(OPT["lams"])):
+        OPT["lam"], OPT["look"], OPT["slip"] = OPT["lams"][_turn // OPT["turns"]]
+        if _turn % OPT["turns"] == 0:
+            way = way0
+        way = [x + o["bon"] for x, o in zip(way, ops)]
+        for i in range(n - 1, -1, -1):
+            way[i] = max([way[i]] + [way[j] + 0.01 for j in succ[i]])
         start, end = place(pred, succ, way, False)
         if best is None or max(end) < best[0]:
-            best = (max(end), start)
+            best = (max(end), start, end, way)
+        if OPT["noise"]:
+            end = [x + OPT["noise"] * math.sin(1000.0 * (i + 1) * (_turn + 1)) for i, x in enumerate(best[2])]
         way = place(succ, pred, end, True)[1]
-    return sorted(range(n), key=lambda i: (best[1][i], i))
+    way = list(best[3])
+    for _turn in range(OPT["sq"]):
+        start, end = run(pred, succ, way, False)
+        if max(end) < best[0]:
+            best = (max(end), start, end, list(way))
+        a = max(range(n), key=lambda i: end[i])
+        while a is not None:
+            b = why.get(a)
+            if b is not None and b not in pred[a]:
+                way[a] += OPT["eta"]
+            a = b
+        for i in range(n - 1, -1, -1):
+            way[i] = max([way[i]] + [way[j] + ops[i]["cost"] * OPT["mu"] for j in succ[i]])
+    order = list(best[1])
+    eng = [o["e"] for o in ops]
+    cst = [o["cost"] for o in ops]
+    inc = [[(j, cst[j] + ops[j]["lat"] + (WAKE if eng[j] == eng[i] else OPT["xw"]) - early.get((j, i), 0.0)) for j in pred[i]] for i in range(n)]
+    xw = OPT["xw"]
+
+    def clock(order):
+        start, cause, last, user = [0.0] * n, [None] * n, {}, {}
+        for a in order:
+            s, c = 0.0, None
+            for j, d in inc[a]:
+                x = start[j] + d
+                if x > s:
+                    s, c = x, j
+            e = eng[a]
+            j = last.get(e)
+            if j is not None and start[j] + cst[j] > s:
+                s, c = start[j] + cst[j], j
+            last[e] = a
+            for b in holds[a][1:]:
+                u = user.setdefault(b, {})
+                for e2, j in u.items():
+                    if e2 != e and start[j] + cst[j] + xw > s:
+                        s, c = start[j] + cst[j] + xw, j
+                u[e] = a
+            start[a], cause[a] = s, c
+        z = max(order[-60:], key=lambda i: start[i] + cst[i] + ops[i]["lat"])
+        return start[z] + cst[z] + ops[z]["lat"], z, cause
+    span, z, cause = clock(order)
+    top = (span, order)
+    seed = 12345
+    for _turn in range(OPT["ls"]):
+        pairs, a = [], z
+        while cause[a] is not None:
+            if cause[a] not in pred[a]:
+                pairs.append((cause[a], a))
+            a = cause[a]
+        if not pairs:
+            break
+        seed = (seed * 1103515245 + 12345) % 2147483648
+        b, a = pairs[(seed >> 8) % len(pairs)]
+        i, j = order.index(b), order.index(a)
+        mid = order[i:j + 1]
+        if (seed >> 4) & 1:
+            take = {a}
+            for x in reversed(mid):
+                if any(y in take for y in succ[x]):
+                    take.add(x)
+            if b in take:
+                continue
+            new = [x for x in mid if x in take] + [x for x in mid if x not in take]
+        else:
+            take = {b}
+            for x in mid:
+                if any(y in take for y in pred[x]):
+                    take.add(x)
+            if a in take:
+                continue
+            new = [x for x in mid if x not in take] + [x for x in mid if x in take]
+        trial = order[:i] + new + order[j + 1:]
+        s2, z2, c2 = clock(trial)
+        if s2 <= span + OPT["tol"] * (1 - _turn / OPT["ls"]):
+            order, span, z, cause = trial, s2, z2, c2
+            if span < top[0]:
+                top = (span, order)
+    _ORDER["span"] = top[0]
+    return top[1]
 
 
 def rank_program(g, core, T, topo):
@@ -279,7 +433,8 @@ def rank_program(g, core, T, topo):
                 rd += x[1][1:]
             else:
                 wr += x[1]
-        ops.append({"e": e, "fn": fn, "rd": rd, "wr": wr, "cost": cost, "dma": dma, "lat": lat, "items": items, "land": land, "tag": TAG[0]})
+        ops.append({"e": e, "fn": fn, "rd": rd, "wr": wr, "cost": cost, "dma": dma, "lat": lat, "items": items, "land": land, "bon": BON[0],
+                    "tag": TAG[0] + ":" + ([k for k, x in _ARENA.items() if x[0] == wr[0][0] and x[1] <= wr[0][1] < x[1] + x[2]] + ["?"])[0]})
 
     def _c(x):
         return x[0] if isinstance(x, tuple) else x
@@ -323,7 +478,7 @@ def rank_program(g, core, T, topo):
             kw["bias"] = _c(bias)
         if acc is not None:
             kw["accum_out"] = acc[0]
-        op("s", lambda: sc.activation(o[0], i[0], f, **kw), [o] + _r(acc), [i] + _r(scale, bias), cost(o, [i], 1.0) + 0.06)
+        op("s", lambda: sc.activation(o[0], i[0], f, **kw), [o] + _r(acc), [i] + _r(scale, bias), cost(o, [i], 1.0) + OPT["os"])
 
     def relu(e, o, i):
         if e == "s":
@@ -337,18 +492,20 @@ def rank_program(g, core, T, topo):
         else:
             cp(o, i)
 
-    def iota(o, pat, base, cm=0):
+    def iota(o, pat, base, cm=0, after=None):
         if o[3] == I:
             op("k", lambda: g.iota(o[0], pat, base, cm), [o], [], 0.13 + 2 * o[2] * CYC)
         else:
-            op("k", lambda: g.iota(o[0], pat, base, cm, allow_small_or_imprecise_dtypes=True), [o], [], 0.13 + 2 * o[2] * CYC)
+            op("k", lambda: g.iota(o[0], pat, base, cm, allow_small_or_imprecise_dtypes=True), [o], _r(after), 0.13 + 2 * o[2] * CYC)
 
     def mm(items):
-        c = sum(max(min(64, a[2]), b[2]) * (4 if a[3] == S else 1) for (_o, a, b) in items) * PEC
+        c = sum(max(min(64, a[2]), b[2]) * (4 if a[3] == S else 1) for (_o, a, b) in items) * OPT["pec"]
         op("p", None, [x[0] for x in items], [y for x in items for y in x[1:]], c, items=items)
 
     def dma(e, o, i, sem):
-        op(e, lambda: E[e].dma_start(o[0], i[0]), [o], [i], 0.1, dma=sem, lat=3.0)
+        BON[0] = 50
+        op(e, lambda: E[e].dma_start(o[0], i[0]), [o], [i], 0.1, dma=sem, lat=4.0)
+        BON[0] = 0
 
     def ext(ap, name):
         return (ap, [(name, 0, 1)])
@@ -361,7 +518,7 @@ def rank_program(g, core, T, topo):
         via = _relay(topo, back, core, which)
         nb = _mask(topo, back if via is None else via, core)[1]
         op("k", lambda: g.remote_dma(T[buf_dst][:], src[0], T.sem[sem if to is None else fwd], T.sem[loc], pid, rid, m),
-           [u(buf_dst)], [src], 0.3, lat=WAY * (1 if to is None else 2), land=(sem, nb, loc, n))
+           [u(buf_dst)], [src], 0.3, lat=(OPT["way"] + (FIRST if buf_dst == "QI0" else 0)) * (1 if to is None else 2), land=(sem, nb, loc, n))
 
     def e16(name, k=0, n=None, p=None):
         return u(name, k, n, 16, p)
@@ -384,7 +541,7 @@ def rank_program(g, core, T, topo):
         tt(z, key, hi, A.subtract)
 
     TAG[0] = "init"
-    fill(u("X", 0, 16), 0.0)
+    fill(u("X", 0, 16), -64.0)
     fill(u("X", 2048, 2304), 0.0)
     fill(u("AC4", 0, 8), 0)
     fill(u("AC4", 2048, 2192), 0)
@@ -404,7 +561,7 @@ def rank_program(g, core, T, topo):
         return c
 
     def scaled(name, src, val):
-        act(u(name) if isinstance(name, str) else name, src, F.Copy, scale=val)
+        act(u(name) if isinstance(name, str) else name, src, F.Identity, scale=val)
     iota(u("PIi", 0, 1), [[0, 1]], 0, 1)
     P, P4, P15 = u("PC", 0, 1), u("PC", 1, 2), u("PC", 2, 3)
     iota(J144, [[1, 144]], 0)
@@ -416,17 +573,19 @@ def rank_program(g, core, T, topo):
     iota(u("PC", 4, 8), [[1, 4]], 1024, 4)
     iota(u("PC", 8, 10), [[512, 2]], 8192 - 1536, 1)
     iota(u("PC", 10, 11), [[0, 1]], 128, 1)
-    iota(u("J"), [[1, 512]], 0)
     iota(u("FREE", 0, 1024), [[0, 1024]], 0)
     iota(u("Z1"), [[0, 2048]], 0)
     iota(u("QZ"), [[0, 512]], 0)
-    iota(u("DS", 2176, 2304), [[0, 128]], 0)
-    for t in range(RO):
-        iota(u("XV%d" % t), [[0, 256]], 0)
+    iota(u("DS", 640, 768), [[0, 128]], 0)
+
+    iota(u("XV0"), [[0, 256]], 128)
+    iota(u("MIN5"), [[0, 512]], 1 - 2 ** 24)
+    iota(e16("MIN5"), [[0, 32]], 2 ** 24 - 1)
     fill(u("MS"), 1.0)
     fill(e16("MS"), 0.0)
     fill(u("ZE"), 0.0)
-    fill(u("Z0"), 0.0)
+    if "t" in OPT["nx"]:
+        fill(u("Z0"), 0.0)
     fill(u("OT", 0, 8), 0.0)
     fill(u("OT", 2048, 2064), 0.0)
     fill(u("W", 512, 640), 0.0)
@@ -455,7 +614,11 @@ def rank_program(g, core, T, topo):
     for c in range(4):
         ve = "VG" if c % 2 else "VE"
         mark = (None, [("row4" + ve, 0, 1)])
-        if c < 2:
+        if c == 1 and OPT["vg"]:
+            dma("y", u("VG"), u("VE"), "ld10")
+            buf, o, n, _d = _ARENA[ve]
+            op("y", lambda buf=buf, o=o, n=n: g.sync.dma_start(T[buf][4:128:16, o:o + n], T[buf][9:128:16, o:o + n]), [u(ve)], [], 0.1, dma="ld7b", lat=2.5)
+        elif c < 2:
             for h in range(2):
                 a, b = 1024 * h, 1024 * h + 1024
                 cp(u("ZE", a, b, 16), u("FREE", 1024 + 128 * c + 64 * h, 1024 + 128 * c + 64 * h + 64))
@@ -465,31 +628,39 @@ def rank_program(g, core, T, topo):
             op("y", lambda buf=buf, o=o, n=n: g.sync.dma_start(T[buf][4:128:16, o:o + n], T[buf][10:128:16, o:o + n]), [u(ve)], [], 0.1, dma="ld%d" % (6 + c), lat=2.5)
         for h in range(2):
             a, b = 1024 * h, 1024 * h + 1024
+            BON[0] = OPT["bot"]
             act(ix(u("OT"), u("INO", 128 * c + 64 * h, 128 * c + 64 * h + 64)), u(ve, a, b), F.Silu)
+            BON[0] = 0
 
+    BON[0] = OPT["bon"]
     ts(u("IDB"), J, P, A.is_equal)
     ts(u("BD"), J4, P4, A.is_equal)
+    ts(u("blk"), J8, P4, A.is_equal)
+    ts(u("R16"), J15, P15, A.is_equal)
+    scaled("nblk", u("blk"), -1.0)
+    scaled("nblkf", u("blk"), -1.0)
+    for name, val in (("w64k", 65536.0), ("w8k", 8192.0), ("w32", 32.0)):
+        scaled(name, u("blk"), val)
+    scaled("NBD", u("BD"), -1.0)
+    scaled("IDF", u("IDB"), 1.0)
+    scaled("SEL0R", u("BD"), row0)
+    scaled("SEL0", u("blk"), row0)
+    scaled("N25", u("SEL0R"), -2.0 ** 25)
+    act(u("CN1"), u("R16"), F.Identity, scale=8192.0, bias=-8192.0)
+    scaled(u("KAx", 128, 256), J15, u("EP", 0, 1))
     scaled(u("ID2", 128, 256), u("IDB"), 1.0)
-    for name, val in (("NIDB", -1.0), ("N24", -2.0 ** 24), ("N20", -2.0 ** 20), ("P20", 2.0 ** 20), ("P11", 2.0 ** 11),
+    for name, val in (("NIDB", -1.0), ("N24", -2.0 ** 27), ("N20", -2.0 ** 20), ("P20", 2.0 ** 23), ("P11", 2.0 ** 11),
                       ("RV0", -49152.0), ("RV1", -24576.0), ("RV2", -12288.0)):
         if name in OPT["sv"]:
             scaled(name, u("IDB"), val)
         else:
             ts(u(name), u("IDB"), val, A.mult)
-    ts(u("NBD"), u("BD"), -1.0, A.mult)
-    ts(u("BDn"), u("BD"), -128.0, A.mult)
-    ts(u("R16"), J15, P15, A.is_equal)
+    BON[0] = 0
     ts(u("MC"), J15, P15, A.is_le)
     fill(e16("MC"), 0.0)
-    ts(u("blk"), J8, P4, A.is_equal)
-    scaled("nblk", u("blk"), -1.0)
-    scaled("nblkf", u("blk"), -1.0)
-    for name, val in (("w64k", 65536.0), ("w8k", 8192.0), ("w32", 32.0)):
-        scaled(name, u("blk"), val)
     fill(u("ONEB"), 1.0)
     ts(u("ZALL"), u("MS", 0, 1152), 0.0, A.mult)
-    fill(u("ZMW"), 0.0)
-    keys = (("KAs", 4096.0, 2.0 ** 24, -1088.0), ("KAb", -1.0, -2.0 ** 20, 7.0), ("KAn", 512.0, 2.0 ** 24, 0.0), ("KAq", 1.0, 2.0 ** 20, -8.0),
+    keys = (("KAs", 4096.0, 2.0 ** 27, -1088.0), ("KAb", -1.0, -2.0 ** 23, 7.0), ("KAn", 512.0, 2.0 ** 24, 0.0), ("KQ5", 32.0, -15.0, 0.0),
             ("KAp", 32768.0, 21.0 * 4096 * 160, -2.0 ** 17))
     for name, slope, c1, c2 in keys:
         lo = 128 if name == "KAp" else 0
@@ -497,17 +668,18 @@ def rank_program(g, core, T, topo):
         if c2:
             ts(b, u("EP", 2, 3), c2, A.mult, b, A.add)
         ts(u(name, lo, lo + 128), J15, col(u("EP", 0, 1), slope, A.mult), A.mult, b, A.add)
-    fill(u("KAp", 0, 128), 21.0 * 4096 * 160 / 128)
-    fill(u("KAx", 0, 128), 0.0)
-    ts(u("KAx", 128, 256), J15, u("EP", 0, 1), A.mult)
-    for name, val in (("KAd", 2.0 ** 17), ("K11", 2.0 ** 4), ("K20", 2.0 ** 13), ("K21", 2.0 ** 14), ("C25", 2.0 ** 25), ("THZ", 0.0), ("MIN3", -BIG)):
-        fill(u(name), val)
+    for name, val in (("KAd", 2 ** 20), ("K11", 2 ** 4), ("K20", 2 ** 13), ("K21", 2 ** 14), ("THZ", 0), ("MIN3", 1 - 2 ** 24), ("ZMW", 0),
+                      ("K9", 12), ("ONEF", 1)):
+        iota(u(name), [[0, u(name)[2]]], val)
+    iota(u("KAp", 0, 128), [[0, 128]], 21 * 32 * 160)
+    iota(u("KAx", 0, 128), [[0, 128]], 0)
+    iota(e16("KAd", 15), [[0, 8]], 0)
+    iota(u("Aa", 256, 264), [[0, 8]], 0)
+    fill(u("C25"), 2.0 ** 25)
     fill(e16("MIN"), BIG)
     iota(e16("MINs"), [[0, 8]], 255 * 65536 + 2049 - 1088, 1)
-    cp(u("CREP"), u("J", 0, 128))
-    ts(u("SEL0R"), u("BD"), row0, A.mult)
-    ts(u("SEL0"), u("blk"), row0, A.mult)
-    ts(u("N25"), u("SEL0R"), -2.0 ** 25, A.mult)
+    if "s" in OPT["mv"]:
+        cp(u("CREP"), u("J", 0, 128))
     hw = col(P15, 4.0, A.is_lt, P15, A.mult)
     ts(hw, hw, 1.0 / 64, A.mult, col(row4, 4.0, A.mult), A.add)
     ts(u("HWN"), u("NBD"), hw, A.mult)
@@ -516,7 +688,7 @@ def rank_program(g, core, T, topo):
         ts(u("og%d" % c), u("blk"), u("kq", c, c + 1), A.mult)
     last = col(P4, 16.0, A.mult, 15.0, A.add)
     ts(u("Y2"), J144, last, A.is_equal, 2.0, A.mult)
-    ts(u("Y"), J144, last, A.is_equal, row0, A.mult)
+    ts(u("YF" if OPT["occ"] == "p" else "Y"), J144, last, A.is_equal, row0, A.mult)
     ts(u("HY"), J144, last, A.is_equal, hw, A.mult)
     ts(u("b1"), J, P, A.is_gt)
     tt(u("TRIm"), u("b1"), u("P11"), A.subtract)
@@ -537,43 +709,49 @@ def rank_program(g, core, T, topo):
     ts(u("CMR"), u("R16"), u("PC", 10, 11), A.mult)
     for c in range(4):
         ts(u("CMK%d" % c), u("R16"), u("PC", 4 + c, 5 + c), A.mult)
-    ts(u("CNT", 0, 128), u("R16"), 8192.0 + 128, A.mult, -8192.0, A.add)
+    ts(u("CNT", 0, 128), u("R16"), 8192.0 - 1408, A.mult, -8192.0, A.add)
     ts(u("CNT", 128, 256), u("R16"), 8192.0 - 1920, A.mult, -8192.0, A.add)
     for q in range(2):
         ts(u("CTG", 128 * q, 128 * q + 128), u("R16"), u("PC", 8 + q, 9 + q), A.mult, -8192.0, A.add)
     ts(u("CIX"), u("Jb", 0, 32), 16.0, A.mult, P15, A.add)
     ts(u("CB"), u("CIX", 0, 8), 16.0, A.mult, 7.0, A.add)
-    ts(u("CQ"), u("CIX", 0, 8), 16.0, A.mult, 8.0, A.add)
     ts(u("C512"), u("CIX"), 512.0, A.add)
-    fill(u("Aa", 256, 264), 0.0)
-    half = u("PC", 63, 64)
-    fill(u("m1", 0, 16), 0.5)
-    fill(u("m2", 0, 16), 0.0)
-    op("v", lambda: v.tensor_tensor_scan(u("m1", 16, 32)[0], u("m1", 0, 16)[0], u("m2", 0, 16)[0], 1.0, A.mult, A.add), [u("m1", 16, 32)], [u("m1", 0, 16), u("m2", 0, 16)], 0.11)
-    tt(u("m2", 16, 32), u("m1", 16, 32), u("E16"), A.mult)
-    op("v", lambda: v.tensor_reduce(half[0], u("m2", 16, 32)[0], AX_.X, A.add), [half], [u("m2", 16, 32)], 0.11)
-    ts(u("J3"), u("J"), half, A.mult, -0.499, A.add)
-    ts(u("p7"), u("J"), half, A.mult)
-    tt(u("t512b"), u("J3"), u("p7"), A.subtract)
     bits = col(P15, 9.0, A.is_lt)
-    ts(u("CODE"), u("t512b"), -0.5, A.is_le, -0.5, A.add)
-    ts(u("CODE"), u("CODE"), 2.0, A.mult, bits, A.mult)
+    iota(u("CODE"), [[0, 512]], 0)
     ts(u("m2", 32, 36), u("Jb", 0, 4), col(P15, -9.0, A.add), A.is_equal, 4.0, A.mult)
-    tt(u("CODE", 0, 4), u("CODE", 0, 4), u("m2", 32, 36), A.add)
+    cp(u("CODE", 0, 4), u("m2", 32, 36))
+    buf, o, n, _d = _ARENA["CODE"]
+    for b in range(9):
+        src = u("VB" if b < 4 else "DT" if b < 8 else "QS", 512 * (b % 4), 512 * (b % 4) + 512)
+        iota(src, [x for x in ([0, 256 >> b], [2, 2], [0, 1 << b]) if x[1] > 1], -1)
+        lo = src[1][0][1]
+        op("y", lambda b=b, lo=lo, t=T[buf], o=o: g.sync.dma_start(t[b:128:16, o:o + 512], t[b:128:16, lo:lo + 512]), [(None, [("bit", b, b + 1)])], [src, u("CODE")],
+           0.1, dma="cd%d" % b, lat=2.5)
     ts(u("PIi", 3, 4), u("PIi", 1, 2), 3, A.bitwise_and)
+    ts(u("PIi", 4, 5), u("PIi", 0, 1), 3, A.bitwise_and)
     ts(u("G4"), u("Jb", 0, 4), col(u("PIi", 3, 4), 1.0, A.mult), A.is_equal)
     ts(u("m2", 40, 44), u("m2", 32, 36), 0.25, A.mult, bits, A.add)
     for q in range(4):
         ts(u("KQ", 4 * q, 4 * q + 4), u("m2", 40, 44), u("G4", q, q + 1), A.mult)
     ts(u("PC", 12, 14), u("LI"), -65536.0, A.mult)
-    ts(u("WY"), J144, last, A.is_equal, col(u("WI"), 1.0, A.mult), A.mult)
+    wt = col(u("WI"), 1.0, A.mult)
+    ts(u("WY"), J144, last, A.is_equal, wt, A.mult)
+    ts(u("WTn"), u("BD"), wt, A.mult, -128.0, A.mult)
+    ts(u("ID2x"), u("IDB"), 2.0, A.mult)
+    ts(u("B512"), u("BD"), 512.0, A.mult)
+    cp(u("KQ5", 128, 256), u("KQ5", 0, 128))
+    cp(u("KQ5", 256, 512), u("KQ5", 0, 256))
     less = col(u("EP", 1, 2), -2048.0, A.mult)
     ts(u("L2N"), u("SEL0"), u("PC", 13, 14), A.mult, less, A.add)
     ts(u("THN"), u("SEL0"), u("PC", 12, 13), A.mult, less, A.add)
     ts(u("ROW1"), J8, 0.0, A.mult, col(less, 32.0, A.mult), A.add)
-    for s in range(16):
+    for s in (1, 2, 3, 4, 8, 12):
         o, i = u("SH", 128 * s, 128 * s + 128), u("BD")
         op("k", lambda o=o, i=i, s=s: g.affine_select(o[0], i[0], [[1, 128]], A.is_equal, 0.0, -s, -1), [o], [i], 0.43)
+    op("k", lambda: g.affine_select(u("EXP")[0], u("Z1")[0], [[-1, 128], [0, 16]], A.not_equal, 1.0, 0, 1), [u("EXP")], [u("Z1")], 3.9)
+    fourth = col(u("PIi", 4, 5), 3.0, A.is_equal, -128.0, A.mult)
+    ts(u("A4n"), u("BD"), fourth, A.mult)
+    ts(u("B4"), u("BD"), col(fourth, 4.0, A.mult, 128.0, A.add), A.mult)
 
     win = u("X", 0, 2192)
 
@@ -603,18 +781,33 @@ def rank_program(g, core, T, topo):
         ts(u(s16), u("p4", 0, 8), 1088.0, A.add)
         cp(e16(z), ix(win, u(s16)))
         ts(u("AN"), ix(u("AC4"), u(s16)), 1, A.add)
-        scan(u("REP"), u("MS"), u(z), A.mult, A.add)
+        if "t" in OPT["nx"]:
+            scan(u("REP"), u("MS"), u(z), A.mult, A.add)
+        else:
+            mm([(u("p6", 288, 416), e16(z), u("NIDB"))])
+            act(u("ZT"), u("p6", 288, 416), F.Copy)
         scan(u("US"), u("MS"), u("T"), A.mult, A.max)
         mm([(u("p4", 8, 16), u("ONEB"), u("L2N")), (u("p4", 8, 16), e16("US", 15), u("w64k"))])
         tt(u("wp8"), e16(s1, 15), u("p4", 8, 16), A.is_lt)
         mm([(u("p6", 0, 128), u("PRE"), u("SEL0R"))])
         act(u("LR"), u("p6", 0, 128), F.Copy)
+        q = u("p6", 160, 288)
+        mm([(q, u("IDB"), u("CN1")), (q, u("PRE"), u("B4"))])
+        act(u("QB"), q, F.Relu)
+        mm([(u("p4", 144, 152), u("IDB"), u("CT")), (u("p4", 144, 152), u("QB"), u("blk"))])
+        cp(u("BT16"), u("p4", 144, 152))
 
     def part_vacant(t):
         TAG[0] = "vac%d" % t
-        act(u("OCC"), u("W", 0, 512), F.Sign)
-        mm([(u("p6", 128, 160), u("Y", 15 - r, 143 - r), e16("OCC", r)) for r in range(16)])
-        act(u("OCb"), u("p6", 128, 160), F.Copy)
+        if OPT["occ"] == "p":
+            mm([(u("p6", 128, 160), u("YF", 15 - r, 143 - r), e16("W", r, 512)) for r in range(16)])
+        else:
+            if OPT["occ"] == "s":
+                act(u("OCC"), u("W", 0, 512), F.Sign)
+            else:
+                ts(u("OCC"), u("W", 0, 512), 0.0, A.is_gt)
+            mm([(u("p6", 128, 160), u("Y", 15 - r, 143 - r), e16("OCC", r)) for r in range(16)])
+        act(u("OCb"), u("p6", 128, 160), F.Sign)
         mm([(u("p4", 32, 64), u("BD"), u("OCb"))])
         mm([(u("p4", 64, 96), u("BTI"), u("OCb")), (u("p4", 64, 96), u("ID16"), u("CIX"))])
         scan(u("CS"), u("ONEB", 0, 32), u("p4", 32, 64), A.mult, A.add)
@@ -622,10 +815,7 @@ def rank_program(g, core, T, topo):
         tt(u("r2"), u("r1"), u("C512"), A.min)
         cp(u("F16"), u("r2"))
         act(ix(u("FREE", 0, 1024), u("F16")), V0, F.Silu)
-        act(u("mc", 0, 1), u("CS", 31, 32), F.Identity, scale=-1.0, bias=512.0)
-        act(u("NFH"), u("SEL0R"), F.Identity, scale=u("mc", 0, 1))
-        mm([(u("p6", 160, 288), u("ONEB"), u("NFH"))])
-        act(u("NFR"), u("p6", 160, 288), F.Copy)
+        act(u("NFF"), u("SEL0R"), F.Identity, scale=u("CS", 31, 32))
 
     def part_split(t):
         TAG[0] = "split%d" % t
@@ -633,9 +823,10 @@ def rank_program(g, core, T, topo):
         for c in range(4):
             a, b = 512 * c, 512 * c + 512
             ps = u("p%d" % (c % 3))
-            mm([(ps, u("IDB"), u("T", a, b)), (ps, u("NIDB"), u("REP", a, b))])
+            mm([(ps, u("IDB"), u("T", a, b)), (ps, u("NIDB"), u("REP", a, b)) if "t" in OPT["nx"] else (ps, u("ZT"), u("EXP", a, b))])
             act(u("SQ", a, b), ps, F.Square)
         act(u("SQS"), e16(z), F.Square)
+        act(u("ZP"), e16(z), F.Identity, bias=128.0)
         k = u("p3", 128, 256)
         mm([(k, u("ONEB"), u("KAb")), (k, u("PRE"), u("P20"))] + sums("p3", 128, "SQ", "w32"))
         scan(u("SB"), u("MS", 0, 128), k, A.mult, A.max)
@@ -644,13 +835,23 @@ def rank_program(g, core, T, topo):
         cp(u("B16"), u("p4", 16, 24))
         act(u("XB"), ix(u("T"), u("B16")), F.Copy)
         act(u("SQB"), u("XB"), F.Square)
-        wv = u("p5", 0, 128)
-        mm([(wv, u("IDB"), e16(z)), (wv, u("NIDB"), u("XB"))])
-        for k in range(16):
-            tt(u("AW", 128 * k, 128 * k + 128), e16("T", k), wv, A.mult)
+        wv = u("p6", 288, 416)
+        if OPT["aw"]:
+            mm([(wv, e16(z), u("IDB")), (wv, u("XB"), u("NIDB"))])
+            copy(OPT["q"][4], u("WV"), wv)
+        else:
+            wv = u("p1", 0, 128)
+            mm([(wv, u("IDB"), e16(z)), (wv, u("NIDB"), u("XB"))])
+            for k in range(16):
+                tt(e16("AW", k), e16("T", k), wv, A.mult)
+        for c in range(4 * OPT["aw"]):
+            a, b = 512 * c, 512 * c + 512
+            ps = u("p%d" % (c % 2))
+            mm([(ps, u("WV"), u("EXP", a, b))])
+            tt(u("AW", a, b), u("T", a, b), ps, A.mult)
         lv = u("p7", 0, 128)
         mm([(lv, u("ONEB"), u("K13")), (lv, u("N13"), u("PRE")), (lv, u("BD"), u("SQB")), (lv, u("NBD"), u("SQS"))]
-           + [(lv, u("Y2", 15 - k, 143 - k), u("AW", 128 * k, 128 * k + 128)) for k in range(16)])
+           + [(lv, u("Y2", 15 - k, 143 - k), e16("AW", k)) for k in range(16)])
         ts(u("L1T"), lv, 0.0, A.is_lt)
         pp = u("p7", 128, 384)
         x = u("p2", 0, 256)
@@ -668,11 +869,14 @@ def rank_program(g, core, T, topo):
                 act(u("Aa", 0, 256), u(a), F.Relu, bias=-th)
             else:
                 ts(u("Aa", 0, 256), u(a), -th, A.add, 0.0, A.max)
-            ts(u("p5", 0, 256), u(a), th, A.is_ge, 2 * th, A.mult)
+            if OPT["sg"][s] == "s":
+                act(u("p5", 0, 256), u(a), F.Relu, scale=2.0 ** 18, bias=(0.5 - th) * 2.0 ** 18)
+            else:
+                ts(u("p5", 0, 256), u(a), th, A.is_ge, 2 * th, A.mult)
             tt(u("p5", 256, 512), u(a), u("p5", 0, 256), A.subtract)
             tt(u(b if s < 3 else "SL"), u("p5", 256, 512), u("Aa", 1 << s, 256 + (1 << s)), A.max)
         mm([(u("p6", 288, 416), u("SL", 0, 128), u("ID16")), (u("p6", 288, 416), u("NID16"), u("OWNH"))])
-        act(u("DS", 2048, 2176), u("p6", 288, 416), F.Copy)
+        act(u("DS", 512, 640), u("p6", 288, 416), F.Copy)
 
     def part_near(t):
         TAG[0] = "near%d" % t
@@ -683,7 +887,14 @@ def rank_program(g, core, T, topo):
             a, b = 1024 * h, 1024 * h + 1024
             act(u("OG", a, b), ix(u("OT", 0, 2064), u("AN", 64 * h, 64 * h + 64)), F.Copy)
         cuts = {2: (0, 64, 128), 3: (0, 56, 104, 128), 4: (0, 32, 64, 96, 128)}[OPT["nr"]]
-        for a, b in zip(cuts, cuts[1:]):
+        for c in range(len(OPT["nc"]) - 1):
+            if "t" not in OPT["nx"]:
+                a, b = 16 * OPT["nc"][c], 16 * OPT["nc"][c + 1]
+                ps = u("p%d" % OPT["nb"][c], 0, b - a)
+                copy(OPT["nx"][c], u("AX", a, b), ix(win, u("AN", a // 16, b // 16)))
+                mm([(ps, u("ZT"), u("EXP", a, b)), (ps, u("IDB"), u("AX", a, b))])
+                act(u("DU", a, b), ps, F.Square)
+        for a, b in zip(cuts, cuts[1:]) if "t" in OPT["nx"] else ():
             tt(u("AX", 16 * a, 16 * b), ix(win, u("AN", a, b)), u("REP", 16 * a, 16 * b), A.subtract)
             act(u("DU", 16 * a, 16 * b), u("AX", 16 * a, 16 * b), F.Square)
         k = u("p3", 256, 384)
@@ -700,9 +911,9 @@ def rank_program(g, core, T, topo):
         gather("DT", "DM", OPT["DT"])
         act(u("PRD"), lists, F.Sign)
         cp(u("DMH"), lists)
-        hold(u("D1R"), u("ZD", 0, 128))
         for q in range(4):
             o, i, keep = u("CG", 128 * q, 128 * q + 128), ix(u("CODE"), u("D16")), u("KQ", 4 * q + cl, 4 * q + cl + 1)
+            i = (i[0], i[1] + [("bit", 0, 9)]) + i[2:]
             if OPT["cg"][q] == "s":
                 act(o, i, F.Identity, scale=keep)
             else:
@@ -718,56 +929,61 @@ def rank_program(g, core, T, topo):
         mm([(u("p6", 416, 424), u("PRE"), e16("BD")), (u("p6", 416, 424), u("PRD"), e16("BD"))])
         act(u("SZ"), u("p6", 416, 424), F.Relu, scale=32.0, bias=-512.0)
         k = u("p3", 384, 512)
-        mm([(k, u("ONEB"), u("KAd")), (k, u("PRD"), u("N24"))] + sums("p3", 384, "DT", "w64k"))
-        scan(u("AX"), u("MS"), u("DT"), A.mult, A.max)
-        tt(u("Vv"), e16("US", 15), e16("AX", 15), A.max)
+        cuts = (0, 16 * OPT["DT"], 2048) if OPT["dh"] else (0, 2048)
+        for a, b in zip(cuts, cuts[1:]):
+            copy(OPT["q"][5], u("DT", a + 15, b, 16), u("US", a + 15, b, 16))
+            scan(u("AX", a, b), u("MS", a, b), u("DT", a, b), A.mult, A.max)
+        mm([(k, u("ONEB"), u("KAd")), (k, u("PRD"), u("N24")), (e16("p3", 399), u("IDF"), e16(s1, 15))] + sums("p3", 384, "DT", "w64k")[:15])
         th = u("p4", 96, 104)
         mm([(th, u("ONEB"), u("THN")), (th, u("ONEB"), u("THZ")), (th, u("P25"), u("SZ"))]
-           + [(u("p4", 96 + q, 97 + q), u("EQ", 128 * q, 128 * q + 128), u("C25", 0, 1)) for q in range(8)] + [(th, u("Vv"), u("w64k"))])
+           + [(u("p4", 96 + q, 97 + q), u("EQ", 128 * q, 128 * q + 128), u("C25", 0, 1)) for q in range(8)] + [(th, e16("AX", 15), u("w64k"))])
         scan(u("S3"), u("MIN"), k, A.max, A.min)
-        tt(u("mn8"), e16("S3", 15), e16(s1, 15), A.min)
-        for c in range(4):
-            ps = "p%d" % (2 - c % 2)
+        for c, (src, step, out) in enumerate((("DMH", 1, "D1"), ("DM2", 4, "DS"))):
             for q in range(4):
-                s = 4 * c + q
-                mm([(u(ps, 128 * q, 128 * q + 128), u("SH", 128 * s, 128 * s + 128), u("DMH"))])
-            copy(OPT["ds"][c], u("DS", 512 * c, 512 * c + 512), u(ps))
+                s = step * q
+                mm([(u("p2", 128 * q, 128 * q + 128), u("SH", 128 * s, 128 * s + 128) if s else u("IDB"), u(src))])
+            copy(OPT["ds"][c], u(out, 0, 512), u("p2"))
+            if c == 0:
+                cp(u("DM2"), ix(u("D1"), u("BT16")))
 
     def part_finish(t):
         TAG[0] = "fin%d" % t
         cl = t % 4
-        z, rt = "Z%d" % (t % 2), "RT16" + "ab"[t % 2]
-        tt(e16("ZM"), u("mn8"), u("p4", 96, 104), A.is_ge)
+        z, rk = "Z%d" % (t % 2), "RK" + "ab"[t % 2]
+        tt(e16("ZM"), e16("S3", 15), u("p4", 96, 104), A.is_ge)
         tt(e16("ZW"), u("wp8"), e16("ZM"), A.is_gt)
-        hold(u("WR"), u("ZW"))
-        hold(u("MR"), u("ZM"))
-        k1 = u("p7", 384, 512)
-        mm([(k1, u("ONEB"), u("K12")), (k1, u("TRIm"), u("WR"))])
-        tt(u("SR"), k1, u("NFR"), A.is_lt)
-        tt(u("KP"), k1, u("CMK%d" % cl), A.min)
+        scan(u("MWR"), u("MS", 0, 256), u("ZMW"), A.mult, A.add)
+        k0, k1 = u("p7", 384, 512), u("p5", 0, 128)
+        mm([(k0, u("ONEB"), u("K9")), (k0, u("ONEF"), u("NFF")), (k0, u("TRIm"), u("WR"))])
+        mm([(k1, u("ONEB"), u("K12")), (k1, u("TRIm"), u("WR"))] if OPT["k1"] else [])
+        ts(u("SR"), k0, 0.0, A.is_lt)
+        tt(u("KR", 128, 256), k1, u("CMK%d" % cl), A.min)
         k2 = u("p7", 0, 128)
         mm([(k2, u("ONEB"), u("K12")), (k2, u("TRIm"), u("LR")), (k2, u("NTRIm"), u("MR")), (k2, u("NTRIm"), u("SR"))])
-        tt(u("RP"), k2, u("CMR"), A.min)
-        mm([(u("p4", 104, 112), u("RP"), u("blk"))])
-        cp(u(rt), u("p4", 104, 112))
+        tt(u("KR", 0, 128), k2, u("CMR"), A.min)
+        if OPT["rk"]:
+            mm([(u("p4", 104, 112), u("KR", 0, 128), u("blk"))])
+            mm([(u("p4", 112, 120), u("KR", 128, 256), u("blk"))])
+            cp(u(rk), u("p4", 104, 120))
+        else:
+            mm([(u("p4", 112, 120), u("KR", 128, 256), u("blk"))])
+            cp(u(rk, 8, 16), u("p4", 112, 120))
+            mm([(u("p4", 104, 112), u("KR", 0, 128), u("blk"))])
+            cp(u(rk, 0, 8), u("p4", 104, 112))
         xv = "XV%d" % t
-        cp(ix(u(xv), u(rt)), e16(z))
+        cp(ix(u(xv), u(rk, 0, 8)), u("ZP"))
         send(T.cores[(rank + 1 + t % 7) % 8], u(xv, 0, 32), "QI%d" % t, "rq%d" % t, "fq%d" % t, "lq%d" % t, 0, T.cores[(rank - 1 - t % 7) % 8])
         q = u("p6", 0, 256)
-        mm([(q, u("ID16"), u("CNT")), (u("p6", 0, 128), u("PRE"), u("BDn")), (u("p6", 0, 128), u("P12"), u("MR")), (u("p6", 128, 256), u("P12"), u("SR"))])
+        mm([(q, u("ID16"), u("CNT")), (u("p6", 0, 128), u("PRE"), u("A4n")), (u("p6", 0, 128), u("P12"), u("MR")), (u("p6", 128, 256), u("P12"), u("SR"))])
         relu(OPT["q"][0], u("QN"), q)
-        nt = u("p4", 112, 120)
+        nt = u("p4", 120, 128)
         mm([(nt, u("ID16"), u("CT")), (nt, u("QN", 0, 128), u("nblkb")), (nt, u("QN", 128, 256), u("nblkb"))])
-        ts(u("NT16"), nt, 2176.0, A.add)
+        ts(u("NT16"), nt, 640.0, A.add)
         tt(u("W", cl, 512, 4), ix(u("DS"), u("NT16")), u("OWNH"), A.add)
-        mm([(u("p4", 120, 128), u("KP"), u("blk"))])
-        cp(u("K16"), u("p4", 120, 128))
-        copy(OPT["q"][3], u("EVb"), ix(u("FREE"), u("K16")))
-        if "s" in OPT["mv"]:
-            act(u("EV"), ix(u("FREE"), u("K16")), F.Copy)
+        copy(OPT["q"][3], e16("ZE"), ix(u("FREE"), u(rk, 8, 16)))
         q = u("p0", 0, 256)
-        mm([(q, u("ID16"), u("CTG")), (u("p0", 0, 128), u("NID16"), u("D1R")), (u("p0", 0, 128), u("P11"), u("MR")),
-            (u("p0", 128, 256), u("P11"), u("SR")), (u("p0", 128, 256), u("EVb"), u("HWN"))])
+        mm([(q, u("ID16"), u("CTG")), (u("p0", 0, 128), u("NID16"), u("HD", 0, 128)), (u("p0", 0, 128), u("P11"), u("MR")),
+            (u("p0", 128, 256), u("P11"), u("SR")), (u("p0", 128, 256), e16("ZE"), u("HWN"))])
         relu(OPT["q"][1], u("QR", 0, 256), q)
         tg = u("p4", 128, 136)
         mm([(tg, u("ID16"), u("CT")), (tg, u("QR", 0, 128), u("nblkf")), (tg, u("QR", 128, 256), u("nblkf"))])
@@ -776,12 +992,35 @@ def rank_program(g, core, T, topo):
         mm([(el, u("SL", 128, 256), u("ID16")), (el, u("MR"), u("N13"))])
         relu(OPT["q"][2], u("ELS"), el)
         cp(ix(u("W"), u("TG16")), u("ELS"))
+        if t in OPT["alt"]:
+            copy(OPT["q"][6], u("ALT", cl, 512, 4), e16("ZE"))
+            cp(ix(u("ALT"), u("TG16")), e16("ZE"))
+        else:
+            part_move(t)
+        if t + 1 < RO:
+            mm([(u("p6", 424, 432), u("ONEB"), e16("ZM"))])
+            act(u("z8"), u("p6", 424, 432), F.Identity, bias=-0.9375, acc=u("mc", 4, 5))
+            c = 1.5 * 2.0 ** 27
+            ts(u("mc", 5, 6), u("mc", 4, 5), c, A.add, c, A.subtract)
+            ts(u("mc", 6, 7), u("mc", 4, 5), u("mc", 5, 6), A.subtract, 7.5, A.add)
+            act(u("THZ"), u("ROW1"), F.Identity, scale=u("mc", 6, 7))
+        if t in OPT["alt"] and t + 1 < RO:
+            part_movers(t)
+
+    def part_movers(t):
         a, b = u("p7", 128, 256), u("p7", 256, 384)
         mm([(a, u("ONEB"), u("K14")), (a, u("ID16"), u("DMH")), (a, u("N13"), u("PRD")), (a, u("MR"), u("N13"))])
         mm([(b, u("ONEB"), u("K14")), (b, u("ID16"), u("OWNH")), (b, u("N13"), u("L1T")), (b, u("SR"), u("N13"))])
         tt(u("m1"), a, u("DUM", 0, 128), A.min)
         tt(u("m2"), b, u("m1"), A.min)
         cp(u("MVO"), u("m2"))
+        if "s" in OPT["mv"]:
+            cp(u("EV"), e16("ZE"))
+
+    def part_move(t):
+        TAG[0] = "move%d" % t
+        if t not in OPT["alt"]:
+            part_movers(t)
         n = len(OPT["mv"])
         for h in range(n):
             a, b = 2048 // n * h, 2048 // n * (h + 1)
@@ -790,57 +1029,70 @@ def rank_program(g, core, T, topo):
                 act(u("VE", a, b), ix(u("EV"), u("CREP", a // 16, b // 16)), F.Copy)
                 act(to, u("VE", a, b), F.Silu)
             elif OPT["mv"][h] == "w":
-                cp(u("ZE", a, b, 16), u("EVb", a // 16, b // 16))
                 scan(u("VE", a, b), u("MS", a, b), u("ZE", a, b), A.mult, A.add)
                 act(to, u("VE", a, b), F.Silu)
             else:
-                cp(u("ZE", a, b, 16), u("EVb", a // 16, b // 16))
                 scan(u("VB", a, b), u("MS", a, b), u("ZE", a, b), A.mult, A.add)
                 cp(to, u("VB", a, b))
-        if t + 1 < RO:
-            mm([(u("p6", 424, 432), u("ONEB"), e16("ZM"))])
-            act(u("z8"), u("p6", 424, 432), F.Identity, bias=-0.9375, acc=u("mc", 4, 5))
-            c = 1.5 * 2.0 ** 27
-            ts(u("mc", 5, 6), u("mc", 4, 5), c, A.add, c, A.subtract)
-            ts(u("mc", 6, 7), u("mc", 4, 5), u("mc", 5, 6), A.subtract, 7.5, A.add)
-            act(u("THZ"), u("ROW1"), F.Identity, scale=u("mc", 6, 7))
 
     def part_serve(t):
         TAG[0] = "serve%d" % t
         src = T.cores[(rank - 1 - t % 7) % 8]
         qi, sn = "QI%d" % t, "SN%d" % t
-        p32 = (0, 32)
+        if t + 1 < RO:
+            iota(u("XV%d" % (t + 1)), [[0, 256]], 128, after=u(qi))
+        if t + 2 == RO:
+            iota(u("ALT"), [[0, 640]], 0, after=u(qi))
+        if t == 1:
+            iota(u("IDT", 0, 1024), [[1, 1024]], 0, after=u(qi))
+        if t == 2:
+            iota(u("IDT", 1024, 2064), [[1, 1040]], 1024, after=u(qi))
         a = u("p4", 136, 138)
-        mm([(a, u("WY", 15 - j, 143 - j), e16(qi, j)) for j in range(16)])
+        mm([(a, u("WTn"), u("ONEB", 0, 2))] + [(a, u("WY", 15 - j, 143 - j), e16(qi, j)) for j in range(16)])
         cp(u("VI"), a)
         ts(u("VI2"), u("VI"), 2047, A.bitwise_and)
         ts(u("VV16"), u("VI2"), 1, A.add)
-        cp(e16("QZ"), u(qi))
-        act(u("QP"), u(qi), F.Identity, bias=128.0)
+        ts(e16("QZ"), u(qi), -128.0, A.add)
         scan(u("QRp"), u("MS", 0, 512), u("QZ"), A.mult, A.add)
-        act(u("HO"), ix(u("OT", 0, 2064), u("VV16")), F.Copy)
+        copy(OPT["ho"], u("HO"), ix(u("OT", 0, 2064), u("VV16")))
         a = u("p4", 138, 140)
         mm([(a, u("HY", 15 - j, 143 - j), e16("HO", j)) for j in range(16)])
+        if t in OPT["alt"]:
+            ts(u("O16"), a, -512.0, A.add)
+            act(u("VR"), ix(u("IDT"), u("VV16")), F.Copy)
+            act(u("PA"), ix(u("ALT"), u("O16")), F.Copy)
+            tt(u("EH"), ix(u("W", 0, 512), u("O16")), u("VR"), A.is_equal)
+            mm([(u("p4", 160, 192), u("BD"), u("EH"))])
+            tt(u("PD"), u("HO"), u("PA"), A.subtract)
+            tt(u("PM"), u("PD"), u("p4", 160, 192), A.mult)
+            a = u("p4", 142, 144)
+            mm([(a, u("HY", 15 - j, 143 - j), e16(x, j)) for x in ("PA", "PM") for j in range(16)])
+            if t + 1 < RO:
+                part_move(t)
+            TAG[0] = "serve%d" % t
         ts(u("H16"), a, -512.0, A.add)
         cp(u("HL"), ix(u("W", 0, 512), u("H16")))
-        act(u("PRH"), ix(u("W", 0, 512), u("H16")), F.Sign)
-        tt(u("QD"), ix(win, u("HL")), u("QRp"), A.subtract)
-        act(u("QS"), u("QD"), F.Square)
-        k = u("p4", 256, 384, 1, p32)
-        mm([(k, u("ONEB", 0, 32), u("KAq")), (k, u("PRH"), u("N20"))] + sums("p4", 256, "QS", "w32", p32))
-        scan(u("QSC", p=p32), u("MIN", p=p32), k, A.max, A.min)
-        low(e16("ZQ", 0, 128, p32), e16("QSC", 15, None, p32), u("hq8", p=p32), 32)
-        tile("ZQ", "HQ", u("p4", 140, 142), 1, [(u("ID16"), u("CQ", 0, 2))], p32, 2)
-        cp(u("J16"), u("p4", 140, 142))
-        ts(u("hs"), ix(u("QD"), u("J16")), 0.5, A.mult, -0.25, A.add)
-        tt(u(sn), u("hs"), u("QP"), A.add)
+        k = u("p5")
+        for a, b in ((0, 256), (256, 512)):
+            tt(u("QD", a, b), ix(win, u("HL", a // 16, b // 16)), u("QRp", a, b), A.subtract)
+            act(u("QS", a, b), u("QD", a, b), F.Square)
+            x = u("p5", a, b)
+            mm([(x, u("ONEB"), u("KQ5", a, b)), (x, u("ID2x"), u("QRp", a, b)), (x, u("IDB"), u("QD", a, b)), (x, u("B512"), u("QS", a, b))])
+        scan(u("QR"), u("MIN5"), k, A.max, A.min)
+        low(u(sn), e16("QR", 15), u("hs"), 32)
         send(src, u(sn), "RS%d" % t, "rs%d" % t, "fs%d" % t, "ls%d" % t, 1, T.cores[(rank + 1 + t % 7) % 8])
 
     def part_apply(t):
         TAG[0] = "apply%d" % t
         xv = "XV%d" % t
-        act(u(xv, 0, 32), u("RS%d" % t), F.Identity, bias=-128.0)
-        act(u("NV"), ix(u(xv), u("RT16" + "ab"[t % 2])), F.Copy)
+        if OPT["ap"][0] == "s":
+            act(u(xv, 0, 32), u("RS%d" % t), F.Identity, scale=0.5, bias=135.25)
+        else:
+            ts(u(xv, 0, 32), u("RS%d" % t), 0.5, A.mult, 135.25, A.add)
+        if OPT["ap"][1] == "s":
+            act(u("NV"), ix(u(xv), u("RK" + "ab"[t % 2], 0, 8)), F.Identity, bias=-128.0)
+        else:
+            ts(u("NV"), ix(u(xv), u("RK" + "ab"[t % 2], 0, 8)), -128.0, A.add)
         cp(ix(win, u("S16" + "ab"[t % 2])), u("NV"))
 
     part_own(0)
@@ -849,16 +1101,16 @@ def rank_program(g, core, T, topo):
     for t in range(RO):
         part_near(t)
         part_finish(t)
-        if t + 1 < RO:
-            part_own(t + 1)
-            part_vacant(t + 1)
-            part_split(t + 1)
-        else:
+        if t + 1 == RO:
             ts(u("t512a"), u("W", 0, 512), 0.0, A.is_equal, 2049.0, A.mult)
             act(u("p1"), u("W", 0, 512), F.Identity, bias=-1.0)
             tt(u("YM"), u("t512a"), u("p1"), A.add)
             dma("y", ext(T.ym[:], "out_m"), u("YM"), "st0")
         part_serve(t)
+        if t + 1 < RO:
+            part_own(t + 1)
+            part_vacant(t + 1)
+            part_split(t + 1)
         part_apply(t)
     dma("y", ext(T.yx[:], "out_x"), u("X", 1, 2049), "st1")
 

@@ -1,166 +1,100 @@
-import math
-from concourse.mybir import dt, AluOpType as A, AxisListType as AX_, ActivationFunctionType as F
+from concourse.mybir import AluOpType as A, ActivationFunctionType as F
 
 RO = 5
-BIG = 1.0e9
 S, B, H, I, U = "float32", "bfloat16", "float16", "int32", "uint16"
-TAG = [""]
-BON = [0]
-
-SCRATCH = {}
+LOW = 1 - 2 ** 24
+_BUF = []
 
 
-def _sb(names, cols, dtype):
-    for n in names.split():
-        SCRATCH[n] = ("sbuf", [128, cols], dtype)
+def _sb(dtype, cols, names):
+    _BUF.extend((n, cols, dtype) for n in names.split())
 
 
-_sb("X", 2304, B)
-_sb("AC4", 2192, I)
-_sb("MI", 512, I)
-_sb("LI", 2, I)
-_sb("WI", 1, I)
-_sb("W", 640, S)
-_sb("OT", 4112, S)
-_sb("VE VG", 2048, S)
-_sb("FREE", 1536, S)
-_sb("DS", 768, S)
-_sb("CODE", 512, B)
-_sb("EV", 128, S)
-_sb("T", 2048, B)
-_sb("QD", 512, B)
-_sb("MS VB US REP SQ AX AW SH OG DT DU", 2048, B)
-_sb("Z0 Z1 ZE", 2048, B)
-_sb("J2f t512a t512b YM QR", 512, S)
-_sb("J J3 Qi", 512, I)
-_sb("OWN AN DM CREP MVO", 128, U)
-_sb("INO", 512, U)
-_sb("OCC PEN QZ QRp QS CG", 512, B)
-_sb("kq G4", 4, S)
-_sb("EQ", 1024, B)
-_sb("Jh OWNH DMH ID16 NID16 ONE16 J4h J15h KP RP D1R CMR CMK0 CMK1 CMK2 CMK3", 128, H)
-_sb("R16", 128, B)
-_sb("ZS HS ZB HB ZD HD ZQ HQ", 144, H)
-_sb("SL CNT CTG", 256, H)
-_sb("ID2", 256, B)
-_sb("Jb", 144, B)
-_sb("J4b J15b b1 b2 K11 K20 K21", 128, B)
-_sb("E16", 16, S)
-_sb("EP", 4, S)
-_sb("DUM", 512, S)
-_sb("blk nblk", 8, B)
-_sb("MC IDB NIDB BD NBD BTI ONEB PRE PRD LR L1T ZM ZW WR MR SR XB SQS SQB Vv EVb NV CE CO NFH SEL0R TRIm NTRIm HWN BDn "
-    "N24 N25 N20 P20 P25 N13 P12 P11 KAs KAb KAd KAn KAq K12 K13 K14", 128, B)
-_sb("BTX BT1 KAp KAx QN", 256, B)
-_sb("XF", 768, B)
-_sb("RV0 RV1 RV2", 128, B)
-_sb("KQ", 16, S)
-_sb("Y Y2 WY HY", 144, B)
-_sb("MINs MINn MIN S1a S1b S2 S3 SB QSC NFR ELS m1 m2 e128", 128, S)
-_sb("Pa Pb", 256, S)
-_sb("Aa", 264, S)
-_sb("PIi", 8, I)
-_sb("EXP", 2048, B)
-_sb("IDT", 2064, S)
-_sb("ZT ZP WTn ID2x B512", 128, B)
-_sb("KQ5", 512, B)
-_sb("MIN5", 512, S)
-_sb("ALT", 640, B)
-_sb("O16", 2, U)
-_sb("VR", 32, S)
-_sb("PA EH PD PM", 32, B)
-_sb("WV A4n B4 CN1 QB K9 MR2 WR2", 128, B)
-_sb("IDF ONEF NFF", 128, S)
-_sb("YF", 144, S)
-_sb("D1", 512, S)
-_sb("DM2", 128, H)
-_sb("KR", 256, H)
-_sb("BT16", 8, U)
-_sb("RKa RKb", 16, U)
-_sb("PC", 64, S)
-_sb("J4 J15", 128, I)
-_sb("CB CQ", 8, H)
-_sb("nblkb CN w64k w8k w32 og0 og1 og2 og3 SEL0 L2N THN THZ ROW1 SZ wp8 C25", 8, B)
-_sb("nblkf hi8 hb8 hq8 mn8 z8", 8, S)
-_sb("a8 d8", 8, I)
-_sb("S16a S16b B16 D16 NT16 K16 TG16 RT16a RT16b", 8, U)
-_sb("OCb HO PRH QP", 32, B)
-_sb("CIX", 32, H)
-_sb("CS r1 r2 C512 hs", 32, S)
-_sb("F16 HL", 32, U)
-_sb("mc", 8, S)
-_sb("VI VI2", 2, I)
-_sb("VV16 H16 J16", 2, U)
+_sb(B, 2304, "X")
+_sb(B, 2048, "T MS VB US REP SQ AX AW SH OG DT DU Z0 Z1 ZE EXP")
+_sb(B, 1024, "EQ")
+_sb(B, 768, "XF")
+_sb(B, 640, "ALT")
+_sb(B, 512, "CODE QD OCC PEN QZ QRp QS CG KQ5")
+_sb(B, 256, "ID2 KAp QN LN XC ZMW MWR")
+_sb(B, 144, "Jb Y")
+_sb(B, 128, "J4b J15b b1 b2 R16 MC NIDB BD NBD BTI ONEB PRE PRD LR SR XB SQS SQB NV SEL0R TRIm NTRIm HWN N27 N25 N20 P23 P15 P11 "
+            "RV0 RV1 RV2 KAs KAb KAd KAn K9 K11 K20 K21 WV A4n B4 CN1 QB ZP WTm WTn ID2x B512")
+_sb(B, 32, "OCb HO PA EH PD PM PENW")
+_sb(B, 8, "blk nblk w64k w8k w32 w2 og0 og1 og2 og3 SEL0 L2N THN THZ ROW1 SZ wp8 C25")
+_sb(H, 256, "SL CNT CTG KR")
+_sb(H, 144, "ZS HS ZB HB ZD HD")
+_sb(H, 128, "OWNH DMH DM2 CMR CMK0 CMK1 CMK2 CMK3")
+_sb(H, 32, "CIX")
+_sb(H, 8, "CB")
+_sb(S, 4112, "OT")
+_sb(S, 2064, "IDT")
+_sb(S, 2048, "VE VG")
+_sb(S, 1536, "FREE")
+_sb(S, 768, "DS")
+_sb(S, 640, "W")
+_sb(S, 512, "J2f J3f t512a t512b YM QR DUM D1 MIN5")
+_sb(S, 264, "Aa")
+_sb(S, 256, "Pa Pb")
+_sb(S, 128, "MINs MINn MIN S10 S11 S2 S3 SB ELS m1 m2 IDF ONEF NFF")
+_sb(S, 64, "PC")
+_sb(S, 32, "CS r1 r2 C512 hs VR WP")
+_sb(S, 16, "E16 KQ")
+_sb(S, 8, "nblkf hi8 hb8 z8 mc kq G4 EP sp4 kp4")
+_sb(I, 2192, "AC4")
+_sb(I, 512, "MI")
+_sb(I, 8, "PIi a8 d8")
+_sb(I, 2, "LI WI VI VI2")
+_sb(U, 512, "INO")
+_sb(U, 128, "OWN AN DM MVO")
+_sb(U, 32, "F16 HL")
+_sb(U, 16, "RK0 RK1")
+_sb(U, 8, "S160 S161 B16 D16 NT16 TG16 BT16")
+_sb(U, 2, "VV16 H16 O16")
+_AT, _end = {}, {}
+for _n, _c, _d in _BUF:
+    _AT[_n] = ("ar_" + _d, _end.get(_d, 0), _c, _d)
+    _end[_d] = _end.get(_d, 0) + -(-_c // 16) * 16
+SCRATCH = {"ar_" + _d: ("sbuf", [128, _c], _d) for _d, _c in _end.items()}
+for _n, _m, _o, _c in (("IDB", "ID2", 0, 128), ("ZM", "ZMW", 0, 128), ("ZW", "ZMW", 128, 128), ("MR", "MWR", 0, 128), ("WR", "MWR", 128, 128),
+                       ("ZALL", "ZS", 0, 864), ("MIN3", "MINs", 0, 384), ("CT", "CIX", 0, 8)):
+    _AT[_n] = (_AT[_m][0], _AT[_m][1] + _o, _c, _AT[_m][3])
 for _t in range(RO):
-    _sb("XV%d" % _t, 256, B)
-    _sb("QI%d SN%d RS%d" % (_t, _t, _t), 32, B)
-_ARENA = {}
-
-
-def _pack():
-    keep, pos = {}, {}
-    for n, (w, sh, d) in SCRATCH.items():
-        if n[:2] in ("XV", "QI", "RS", "SN"):
-            keep[n] = (w, sh, d)
-            _ARENA[n] = (n, 0, sh[1], d)
-        else:
-            c = -(-sh[1] // 16) * 16
-            o = pos.get(d, 0)
-            _ARENA[n] = ("ar_" + d, o, sh[1], d)
-            pos[d] = o + c
-    for d in pos:
-        keep["ar_" + d] = ("sbuf", [128, pos[d]], d)
-    return keep
-
-
-SCRATCH = _pack()
-for _n, _first, _len in (("ZALL", "ZS", 1152), ("ZMW", "ZM", 256), ("MIN3", "MINs", 384), ("IDB", "ID2", 128)):
-    _ARENA[_n] = (_ARENA[_first][0], _ARENA[_first][1], _len, _ARENA[_first][3])
-for _n, _m in (("ID16", "IDB"), ("NID16", "NIDB"), ("N13", "N20"), ("P12", "P11"), ("P25", "P20"), ("K12", "K11"), ("K13", "K20"), ("K14", "K21"), ("nblkb", "nblk"), ("CT", "CIX")):
-    _ARENA[_n] = _ARENA[_m]
-_ARENA["MWR"] = _ARENA["MR2"][:2] + (256, B)
-_ARENA["MR"], _ARENA["WR"] = _ARENA["MR2"], _ARENA["WR2"]
-_ARENA["CT"] = _ARENA["CIX"][:2] + (8, H)
+    for _n, _c in (("XV", 256), ("QI", 32), ("SN", 32), ("RS", 32)):
+        SCRATCH["%s%d" % (_n, _t)] = ("sbuf", [128, _c], B)
+        _AT["%s%d" % (_n, _t)] = ("%s%d" % (_n, _t), 0, _c, B)
 for _k in range(8):
     SCRATCH["p%d" % _k] = ("psum", [128, 512], S)
-    _ARENA["p%d" % _k] = ("p%d" % _k, 0, 512, S)
-SEMAPHORES = ["v", "p", "s", "k"] + ["ld%d" % i for i in range(11)] + ["cd%d" % i for i in range(9)] + ["st0", "st1"]
+    _AT["p%d" % _k] = ("p%d" % _k, 0, 512, S)
+SEMAPHORES = ["v", "p", "s", "k", "st0", "st1"] + ["ld%d" % i for i in range(10)] + ["cd%d" % i for i in range(9)]
 for _t in range(RO):
-    SEMAPHORES += ["rq%d" % _t, "rs%d" % _t, "lq%d" % _t, "ls%d" % _t, "fq%d" % _t, "fs%d" % _t, "mq%d" % _t, "ms%d" % _t]
+    SEMAPHORES += [n + str(_t) for n in ("rq", "rs", "lq", "ls", "fq", "fs", "mq", "ms")]
+
+CYC, PEC, GAT, SCA, WAKE, XWAKE, WAY, FIRST = 0.00085, 0.0005, 1.6, 3.7, 0.24, 0.12, 2.3, 2.5
+VIEWS = ((0.27, 0.09, 1.0, 0.92, 0.8), (0.21, 0.16, 1.0, 0.92, 0.8), (0.27, 0.1, 1.22, 1.4, 1.65))
+RULES = ((3, 2, 0.1), (5, 2, 0.1), (8, 2, 0.1), (3, 2, 0.05), (5, 2, 0.05), (8, 2, 0.05), (5, 0, 0.1), (5, 1, 0.08), (12, 1, 0.08), (2, 1, 0.08))
 _ORDER = {}
-CYC, PEC, CALL, WAKE, GAT, SCA, WAY = 0.00087, 0.00055, 0.045, 0.06, 1.5, 3.2, 2.5
-FIRST = 2.5
-OPT = {"lams": ((3, 2, 0.1), (5, 2, 0.1), (8, 2, 0.1), (3, 2, 0.05), (5, 2, 0.05), (8, 2, 0.05), (5, 0, 0.1), (5, 1, 0.08), (12, 1, 0.08), (2, 1, 0.08)), "ls": 3000, "tol": 0.0, "sq": 0, "eta": 0.3, "mu": 1.0, "xw": 0.12, "pec": 0.00055, "os": 0.08, "way": 2.5, "ho": "s", "ap": "vv", "occ": "s", "aw": 1, "vg": 0, "bon": 30, "bot": 0, "T": 96, "DT": 80, "sc": "ssss", "mv": "wwww", "sh": "s", "nr": 3, "cg": "ssss", "turns": 4, "sv": ("NIDB", "N24", "N20", "P20", "P11", "RV0", "RV1", "RV2"), "T0": 128, "lam": 5, "slip": 0.1, "eq": "ss", "ds": "ssss", "q": "sssssvs", "alt": (4,), "sg": "svsv", "nx": "t", "nb": (2, 0, 1, 2, 0), "nc": (0, 32, 64, 96, 120, 128), "dh": 1, "en": 16, "k1": 1, "rk": 0, "look": 2, "lam2": 2, "noise": 0, "rl": 0}
 
 
-def _mask(topo, a, b):
-    es = topo.engines(a, b)[:OPT["en"]]
-    return sum(1 << e for e in es), len(es)
-
-
-def _relay(topo, a, b, which):
+def _relay(topo, a, b):
     if topo.may_write(a, b):
         return None
-    c = [h for h in topo.cores_of(a) if h != a and topo.may_write(h, b)]
-    c.sort(key=lambda h: (topo.die(h) != topo.die(a), h))
-    return c[which * OPT["rl"] % len(c)]
+    return min((h for h in topo.cores_of(a) if h != a and topo.may_write(h, b)), key=lambda h: (topo.die(h) != topo.die(a), h))
 
 
 def _relay_program(g, core, T, topo):
     used = []
     for t in range(RO):
-        for which, (buf, arr, fwd, loc) in enumerate((("QI", "rq", "fq", "mq"), ("RS", "rs", "fs", "ms"))):
+        for back, (buf, arr, fwd, loc) in enumerate((("QI", "rq", "fq", "mq"), ("RS", "rs", "fs", "ms"))):
             for r in range(8):
                 x, y = T.cores[r], T.cores[(r + 1 + t % 7) % 8]
-                x, y = (y, x) if which else (x, y)
-                if _relay(topo, x, y, which) == core:
-                    _, n = _mask(topo, x, core)
-                    m, n2 = _mask(topo, core, y)
+                x, y = (y, x) if back else (x, y)
+                if _relay(topo, x, y) == core:
                     rid, pid = topo.addr(y, core)
-                    g.wait_ge(T.sem["%s%d" % (fwd, t)], n)
+                    g.wait_ge(T.sem["%s%d" % (fwd, t)], len(topo.engines(x, core)))
                     g.remote_dma(T["%s%d" % (buf, t)][:], T["%s%d" % (buf, t)][:], T.sem["%s%d" % (arr, t)],
-                                 T.sem["%s%d" % (loc, t)], pid, rid, m)
-                    used.append((T.sem["%s%d" % (loc, t)], n2))
+                                 T.sem["%s%d" % (loc, t)], pid, rid, topo.mask(core, y))
+                    used.append((T.sem["%s%d" % (loc, t)], len(topo.engines(core, y))))
     for s, n in used:
         g.wait_ge(s, n)
 
@@ -169,23 +103,23 @@ def _psum(b):
     return len(b) == 2 and b[0] == "p"
 
 
+def _cycles(a, b):
+    return max(min(64, a[2]), b[2]) * (4 if a[3] == S else 1)
+
+
 def _order(ops):
     n = len(ops)
-    pred = [set() for _ in range(n)]
-    log = {}
+    pred, log = [set() for _ in range(n)], {}
     for i, o in enumerate(ops):
         for kind, lst in ((0, o["rd"]), (1, o["wr"])):
             for (b, lo, hi) in lst:
-                for (l2, h2, j, wr) in log.get(b, ()):
-                    if lo < h2 and l2 < hi and (kind or wr):
-                        pred[i].add(j)
+                pred[i].update(j for (l2, h2, j, wr) in log.get(b, ()) if lo < h2 and l2 < hi and (kind or wr))
         for (b, lo, hi) in o["wr"]:
             log[b] = [x for x in log.get(b, []) if not (lo <= x[0] and x[1] <= hi)] + [(lo, hi, i, True)]
         for (b, lo, hi) in o["rd"]:
             log.setdefault(b, []).append((lo, hi, i, False))
         pred[i].discard(i)
-    succ = [[] for _ in range(n)]
-    early = {}
+    succ, early = [[] for _ in range(n)], {}
     for i in range(n):
         for j in pred[i]:
             succ[j].append(i)
@@ -195,212 +129,124 @@ def _order(ops):
                     if any(x[0] == y[0] and x[1] < y[2] and y[1] < x[2] for x in a[1] + b[1] for y in ops[j]["wr"]):
                         early[(j, i)] = at
                         break
-                    at += max(min(64, a[2]), b[2]) * (4 if a[3] == S else 1) * PEC
-    way = [0.0] * n
+                    at += _cycles(a, b) * PEC
+    eng, cost, lat = [o["e"] for o in ops], [o["cost"] for o in ops], [o["lat"] for o in ops]
+    banks = [sorted(set(b for (b, _l, _h) in o["rd"] + o["wr"] if _psum(b))) for o in ops]
+    way0 = [0.0] * n
     for i in range(n - 1, -1, -1):
-        way[i] = ops[i]["cost"] + ops[i]["lat"] + max([way[j] + WAKE for j in succ[i]] + [0.0])
-    holds = [[o["e"]] + sorted(set(b for (b, _l, _h) in o["rd"] + o["wr"] if _psum(b))) for o in ops]
+        way0[i] = cost[i] + lat[i] + max([way0[j] + WAKE for j in succ[i]] + [0.0])
 
-    def place(before, after, rank, back):
-        left = [len(p) for p in before]
-        base, start = [0.0] * n, [0.0] * n
-        busy = {}
-        ready = [i for i in range(n) if not left[i]]
-        while ready:
-            a = max(ready, key=lambda i: rank[i])
-            ready.remove(a)
-            e, c, lat = ops[a]["e"], ops[a]["cost"], ops[a]["lat"]
-            s = base[a] + (lat if back else 0.0)
-            moved = True
-            while moved:
-                moved = False
-                for r in holds[a]:
-                    gap = 0.0 if r == e else WAKE
-                    for (lo, hi, e2) in busy.get(r, ()):
-                        if (r == e or e2 != e) and lo - gap < s + c - 1e-9 and s + 1e-9 < hi + gap:
-                            s, moved = hi + gap, True
-            start[a] = s
-            for r in holds[a]:
-                busy.setdefault(r, []).append((s, s + c, e))
-                if len(busy[r]) > 400:
-                    low = min([base[i] for i in ready] + [s])
-                    busy[r] = [x for x in busy[r] if x[1] + WAKE >= low]
-            for j in after[a]:
-                base[j] = max(base[j], s + c + WAKE + (0.0 if back else lat))
-                left[j] -= 1
-                if not left[j]:
-                    ready.append(j)
-        return start, [start[i] + ops[i]["cost"] + (0.0 if back else ops[i]["lat"]) for i in range(n)]
-    why = {}
-
-    def run(before, after, rank, back):
-        left = [len(p) for p in before]
-        base, start = [0.0] * n, [0.0] * n
-        free, bank, ready = {}, {}, {}
+    def run(before, after, rank, back, rule):
+        haste, look, slip = rule
+        left, base, start = [len(p) for p in before], [0.0] * n, [0.0] * n
+        free, bank, ready, order = {}, {}, {}, []
         for i in range(n):
             if not left[i]:
-                ready.setdefault(ops[i]["e"], []).append(i)
+                ready.setdefault(eng[i], []).append(i)
 
         def can(i):
-            e = ops[i]["e"]
-            s = max(base[i] + (ops[i]["lat"] if back else 0.0), free.get(e, 0.0))
-            for b in holds[i][1:]:
-                for e2, t2 in bank.get(b, {}).items():
-                    if e2 != e:
-                        s = max(s, t2 + OPT["xw"])
-            return s
+            return max([base[i] + (lat[i] if back else 0.0), free.get(eng[i], 0.0)]
+                       + [t + XWAKE for b in banks[i] for e, t in bank.get(b, {}).items() if e != eng[i]])
 
         def done(a, s, j):
-            return s + ops[a]["cost"] + (WAKE if ops[a]["e"] == ops[j]["e"] else OPT["xw"]) + (0.0 if back else ops[a]["lat"]) - early.get((j, a) if back else (a, j), 0.0)
-        order, user = [], {}
-        why.clear()
+            return s + cost[a] + (WAKE if eng[a] == eng[j] else XWAKE) + (0.0 if back else lat[a]) - early.get((j, a) if back else (a, j), 0.0)
         for _i in range(n):
             st = {i: can(i) for lst in ready.values() for i in lst}
             soon, front = {}, st
-            for _d in range(OPT["look"]):
+            for _d in range(look):
                 nxt, seen = {}, {}
                 for a, s in front.items():
                     for j in after[a]:
                         seen[j] = seen.get(j, 0) + 1
                         nxt[j] = max(nxt.get(j, base[j]), done(a, s, j))
-                front = {j: max(s, free.get(ops[j]["e"], 0.0)) for j, s in nxt.items() if seen[j] == left[j]}
+                front = {j: max(s, free.get(eng[j], 0.0)) for j, s in nxt.items() if seen[j] == left[j]}
                 for j, s in front.items():
-                    soon.setdefault(ops[j]["e"], []).append((j, s))
+                    soon.setdefault(eng[j], []).append((j, s))
             pick = held = None
             for e, lst in ready.items():
                 if lst:
-                    a = max(lst, key=lambda i: rank[i] - OPT["lam"] * st[i])
-                    limit = st[a]
-                    for j, s in soon.get(e, ()):
-                        if rank[j] - OPT["lam2"] * s > rank[a] - OPT["lam2"] * st[a] and s < st[a] + ops[a]["cost"] - OPT["slip"]:
-                            limit, a = min(limit if a is None else 1e9, s), a
-                            held = (st[a], a) if held is None or st[a] < held[0] else held
-                            fit = [i for i in lst if st[i] + ops[i]["cost"] <= s + OPT["slip"]]
-                            a = max(fit, key=lambda i: rank[i]) if fit else None
-                            break
-                    else:
-                        fit = [i for i in lst if st[i] + ops[i]["cost"] <= limit + OPT["slip"]]
-                        a = max(fit, key=lambda i: rank[i]) if fit else a
+                    a = max(lst, key=lambda i: rank[i] - haste * st[i])
+                    wait = [s for j, s in soon.get(e, ()) if rank[j] - 2 * s > rank[a] - 2 * st[a] and s < st[a] + cost[a] - slip]
+                    fit = [i for i in lst if st[i] + cost[i] <= (wait[0] if wait else st[a]) + slip]
+                    if wait and (held is None or st[a] < held[0]):
+                        held = (st[a], a)
+                    a = max(fit, key=lambda i: rank[i]) if fit else None if wait else a
                     if a is not None and (pick is None or st[a] < pick[0]):
                         pick = (st[a], a)
             s, a = pick or held
-            e, c = ops[a]["e"], ops[a]["cost"]
-            ready[e].remove(a)
+            ready[eng[a]].remove(a)
             order.append(a)
-            if s > base[a] + 1e-9 and s > 0:
-                near = [x for x in [user.get(r) for r in holds[a]] if x is not None]
-                why[a] = max(near, key=lambda x: start[x] + ops[x]["cost"]) if near else why.get(a)
-            for r in holds[a]:
-                user[r] = a
-            start[a], free[e] = s, s + c
-            for b in holds[a][1:]:
-                bank.setdefault(b, {})[e] = s + c
+            start[a], free[eng[a]] = s, s + cost[a]
+            for b in banks[a]:
+                bank.setdefault(b, {})[eng[a]] = s + cost[a]
             for j in after[a]:
-                if done(a, s, j) > base[j]:
-                    why[j] = a
                 base[j] = max(base[j], done(a, s, j))
                 left[j] -= 1
                 if not left[j]:
-                    ready.setdefault(ops[j]["e"], []).append(j)
-        return order, [start[i] + ops[i]["cost"] + (0.0 if back else ops[i]["lat"]) for i in range(n)]
-    if OPT["lam"]:
-        place = run
+                    ready.setdefault(eng[j], []).append(j)
+        return order, [start[i] + cost[i] + (0.0 if back else lat[i]) for i in range(n)]
     best = None
-    _ORDER["dbg"] = (ops, succ, list(way))
-    way0 = way
-    for _turn in range(OPT["turns"] * len(OPT["lams"])):
-        OPT["lam"], OPT["look"], OPT["slip"] = OPT["lams"][_turn // OPT["turns"]]
-        if _turn % OPT["turns"] == 0:
-            way = way0
-        way = [x + o["bon"] for x, o in zip(way, ops)]
-        for i in range(n - 1, -1, -1):
-            way[i] = max([way[i]] + [way[j] + 0.01 for j in succ[i]])
-        start, end = place(pred, succ, way, False)
-        if best is None or max(end) < best[0]:
-            best = (max(end), start, end, way)
-        if OPT["noise"]:
-            end = [x + OPT["noise"] * math.sin(1000.0 * (i + 1) * (_turn + 1)) for i, x in enumerate(best[2])]
-        way = place(succ, pred, end, True)[1]
-    way = list(best[3])
-    for _turn in range(OPT["sq"]):
-        start, end = run(pred, succ, way, False)
-        if max(end) < best[0]:
-            best = (max(end), start, end, list(way))
-        a = max(range(n), key=lambda i: end[i])
-        while a is not None:
-            b = why.get(a)
-            if b is not None and b not in pred[a]:
-                way[a] += OPT["eta"]
-            a = b
-        for i in range(n - 1, -1, -1):
-            way[i] = max([way[i]] + [way[j] + ops[i]["cost"] * OPT["mu"] for j in succ[i]])
-    order = list(best[1])
-    eng = [o["e"] for o in ops]
-    cst = [o["cost"] for o in ops]
-    inc = [[(j, cst[j] + ops[j]["lat"] + (WAKE if eng[j] == eng[i] else OPT["xw"]) - early.get((j, i), 0.0)) for j in pred[i]] for i in range(n)]
-    xw = OPT["xw"]
+    for rule in RULES:
+        way = way0
+        for _turn in range(4):
+            way = [x + o["first"] for x, o in zip(way, ops)]
+            for i in range(n - 1, -1, -1):
+                way[i] = max([way[i]] + [way[j] + 0.01 for j in succ[i]])
+            order, end = run(pred, succ, way, False, rule)
+            if best is None or max(end) < best[0]:
+                best = (max(end), order)
+            way = run(succ, pred, end, True, rule)[1]
+    views = []
+    for wake, xw, mul, gat, sca in VIEWS:
+        c = [cost[i] * (mul, gat, sca)[ops[i]["how"]] for i in range(n)]
+        views.append((c, xw, [[(j, c[j] + lat[j] + (wake if eng[j] == eng[i] else xw) - mul * early.get((j, i), 0.0)) for j in pred[i]] for i in range(n)]))
 
     def clock(order):
-        start, cause, last, user = [0.0] * n, [None] * n, {}, {}
-        for a in order:
-            s, c = 0.0, None
-            for j, d in inc[a]:
-                x = start[j] + d
-                if x > s:
-                    s, c = x, j
-            e = eng[a]
-            j = last.get(e)
-            if j is not None and start[j] + cst[j] > s:
-                s, c = start[j] + cst[j], j
-            last[e] = a
-            for b in holds[a][1:]:
-                u = user.setdefault(b, {})
-                for e2, j in u.items():
-                    if e2 != e and start[j] + cst[j] + xw > s:
-                        s, c = start[j] + cst[j] + xw, j
-                u[e] = a
-            start[a], cause[a] = s, c
-        z = max(order[-60:], key=lambda i: start[i] + cst[i] + ops[i]["lat"])
-        return start[z] + cst[z] + ops[z]["lat"], z, cause
-    span, z, cause = clock(order)
-    top = (span, order)
+        total, pairs = 0.0, []
+        for c, xw, inc in views:
+            start, by, last, user = [0.0] * n, [None] * n, {}, {}
+            for a in order:
+                s, w = 0.0, None
+                for j, d in inc[a]:
+                    if start[j] + d > s:
+                        s, w = start[j] + d, j
+                j = last.get(eng[a])
+                if j is not None and start[j] + c[j] > s:
+                    s, w = start[j] + c[j], j
+                last[eng[a]] = a
+                for b in banks[a]:
+                    for e, j in user.setdefault(b, {}).items():
+                        if e != eng[a] and start[j] + c[j] + xw > s:
+                            s, w = start[j] + c[j] + xw, j
+                    user[b][eng[a]] = a
+                start[a], by[a] = s, w
+            a = max(order[-60:], key=lambda i: start[i] + c[i] + lat[i])
+            total += start[a] + c[a] + lat[a]
+            while by[a] is not None:
+                if by[a] not in pred[a]:
+                    pairs.append((by[a], a))
+                a = by[a]
+        return total / len(views), pairs
+    order = best[1]
+    span, pairs = clock(order)
     seed = 12345
-    for _turn in range(OPT["ls"]):
-        pairs, a = [], z
-        while cause[a] is not None:
-            if cause[a] not in pred[a]:
-                pairs.append((cause[a], a))
-            a = cause[a]
-        if not pairs:
-            break
+    for _turn in range(2500):
         seed = (seed * 1103515245 + 12345) % 2147483648
         b, a = pairs[(seed >> 8) % len(pairs)]
-        i, j = order.index(b), order.index(a)
-        mid = order[i:j + 1]
-        if (seed >> 4) & 1:
-            take = {a}
-            for x in reversed(mid):
-                if any(y in take for y in succ[x]):
-                    take.add(x)
-            if b in take:
-                continue
-            new = [x for x in mid if x in take] + [x for x in mid if x not in take]
-        else:
-            take = {b}
-            for x in mid:
-                if any(y in take for y in pred[x]):
-                    take.add(x)
-            if a in take:
-                continue
-            new = [x for x in mid if x not in take] + [x for x in mid if x in take]
-        trial = order[:i] + new + order[j + 1:]
-        s2, z2, c2 = clock(trial)
-        if s2 <= span + OPT["tol"] * (1 - _turn / OPT["ls"]):
-            order, span, z, cause = trial, s2, z2, c2
-            if span < top[0]:
-                top = (span, order)
-    _ORDER["span"] = top[0]
-    return top[1]
+        mid = order[order.index(b):order.index(a) + 1]
+        up = (seed >> 4) & 1
+        take = {a if up else b}
+        for x in reversed(mid) if up else mid:
+            if any(y in take for y in (succ[x] if up else pred[x])):
+                take.add(x)
+        if (b if up else a) in take:
+            continue
+        i = order.index(b)
+        trial = order[:i] + [x for x in mid if (x in take) == bool(up)] + [x for x in mid if (x in take) != bool(up)] + order[i + len(mid):]
+        s2, p2 = clock(trial)
+        if s2 <= span:
+            order, span, pairs = trial, s2, p2
+    return order
 
 
 def rank_program(g, core, T, topo):
@@ -409,32 +255,30 @@ def rank_program(g, core, T, topo):
         _relay_program(g, core, T, topo)
         return
     E = {"v": g.vector, "p": g.tensor, "s": g.scalar, "k": g, "y": g.sync}
-    ops = []
     v, sc = g.vector, g.scalar
+    ops, first = [], [0]
 
     def u(name, lo=0, hi=None, st=1, p=None):
-        buf, o, n, d = _ARENA[name]
+        buf, o, n, d = _AT[name]
         hi = n if hi is None else hi
-        a, b = o + lo, o + hi
         rows = slice(None) if p is None else slice(p[0], p[1])
-        t = T[buf]
-        ap = t[rows, a:b:st] if st != 1 else t[rows, a:b]
-        return (ap, [(buf, a, b)], -(-(hi - lo) // st), d, False)
+        ap = T[buf][rows, o + lo:o + hi:st] if st != 1 else T[buf][rows, o + lo:o + hi]
+        return (ap, [(buf, o + lo, o + hi)], -(-(hi - lo) // st), d, None)
+
+    def e16(name, k=0, hi=None):
+        return u(name, k, hi, 16)
 
     def ix(win, off):
         return (win[0].indirect(off[0]), win[1] + off[1], 16 * off[2], win[3], off)
 
+    def mark(name, lo=0, hi=1, ap=None):
+        return (ap, [(name, lo, hi)], 0, None, None)
+
     def op(e, fn, outs, ins, cost, dma=None, lat=0.0, items=None, land=None):
-        rd = [r for x in ins for r in x[1]]
-        wr = []
-        for x in outs:
-            if len(x) > 4 and x[4]:
-                wr += x[1][:1]
-                rd += x[1][1:]
-            else:
-                wr += x[1]
-        ops.append({"e": e, "fn": fn, "rd": rd, "wr": wr, "cost": cost, "dma": dma, "lat": lat, "items": items, "land": land, "bon": BON[0],
-                    "tag": TAG[0] + ":" + ([k for k, x in _ARENA.items() if x[0] == wr[0][0] and x[1] <= wr[0][1] < x[1] + x[2]] + ["?"])[0]})
+        rd = [r for x in ins for r in x[1]] + [r for x in outs if x[4] for r in x[1][1:]]
+        wr = [r for x in outs for r in (x[1][:1] if x[4] else x[1])]
+        ops.append({"e": e, "fn": fn, "rd": rd, "wr": wr, "cost": cost, "dma": dma, "lat": lat, "items": items, "land": land, "first": first[0],
+                    "how": 2 if outs[0][4] else 1 if ins and ins[0][4] else 0})
 
     def _c(x):
         return x[0] if isinstance(x, tuple) else x
@@ -443,13 +287,11 @@ def rank_program(g, core, T, topo):
         return [x for x in xs if isinstance(x, tuple)]
 
     def cost(o, ins, per):
-        if o[4]:
-            return 0.05 + o[2] * SCA * CYC
-        if ins and ins[0][4]:
-            return 0.05 + o[2] * GAT * CYC
+        if o[4] or (ins and ins[0][4]):
+            return 0.05 + o[2] * (SCA if o[4] else GAT) * CYC
         if per == 0.5 and any(x[3] not in (B, H, U) for x in [o] + ins):
             per = 1.0
-        return CALL + max(64, o[2] * per) * CYC
+        return 0.005 + max(64, o[2] * per) * CYC
 
     def cp(o, i):
         op("v", lambda: v.tensor_copy(o[0], i[0]), [o], [i], cost(o, [i], 0.5))
@@ -471,138 +313,101 @@ def rank_program(g, core, T, topo):
         op("v", lambda: v.memset(o[0], c), [o], [], cost(o, [], 0.5))
 
     def act(o, i, f, scale=None, bias=None, acc=None):
-        kw = {}
-        if scale is not None:
-            kw["scale"] = _c(scale)
-        if bias is not None:
-            kw["bias"] = _c(bias)
-        if acc is not None:
-            kw["accum_out"] = acc[0]
-        op("s", lambda: sc.activation(o[0], i[0], f, **kw), [o] + _r(acc), [i] + _r(scale, bias), cost(o, [i], 1.0) + OPT["os"])
-
-    def relu(e, o, i):
-        if e == "s":
-            act(o, i, F.Relu)
-        else:
-            ts(o, i, 0.0, A.max)
-
-    def copy(e, o, i):
-        if e == "s":
-            act(o, i, F.Copy)
-        else:
-            cp(o, i)
+        kw = {k: _c(x) for k, x in (("scale", scale), ("bias", bias), ("accum_out", acc)) if x is not None}
+        op("s", lambda: sc.activation(o[0], i[0], f, **kw), [o] + _r(acc), [i] + _r(scale, bias), cost(o, [i], 1.0) + 0.02)
 
     def iota(o, pat, base, cm=0, after=None):
-        if o[3] == I:
-            op("k", lambda: g.iota(o[0], pat, base, cm), [o], [], 0.13 + 2 * o[2] * CYC)
-        else:
-            op("k", lambda: g.iota(o[0], pat, base, cm, allow_small_or_imprecise_dtypes=True), [o], _r(after), 0.13 + 2 * o[2] * CYC)
+        kw = {} if o[3] == I else {"allow_small_or_imprecise_dtypes": True}
+        op("k", lambda: g.iota(o[0], pat, base, cm, **kw), [o], _r(after), 0.13 + 2 * o[2] * CYC)
 
-    def mm(items):
-        c = sum(max(min(64, a[2]), b[2]) * (4 if a[3] == S else 1) for (_o, a, b) in items) * OPT["pec"]
-        op("p", None, [x[0] for x in items], [y for x in items for y in x[1:]], c, items=items)
+    def select(o, i, pat, test, other, base, cm):
+        op("k", lambda: g.affine_select(o[0], i[0], pat, test, other, base, cm), [o], [i], 0.2 + 2 * o[2] * CYC)
 
-    def dma(e, o, i, sem):
-        BON[0] = 50
-        op(e, lambda: E[e].dma_start(o[0], i[0]), [o], [i], 0.1, dma=sem, lat=4.0)
-        BON[0] = 0
+    def mm(out, *pairs):
+        items = [(x[2] if len(x) > 2 else out, x[0], x[1]) for x in pairs]
+        op("p", None, [x[0] for x in items], [y for x in items for y in x[1:]], sum(_cycles(a, b) for _o, a, b in items) * PEC, items=items)
 
-    def ext(ap, name):
-        return (ap, [(name, 0, 1)])
+    def dma(o, i, sem):
+        first[0] = 50
+        op("y", lambda: g.sync.dma_start(o[0], i[0]), [o], [i], 0.1, dma=sem, lat=4.0)
+        first[0] = 0
 
-    def send(dst, src, buf_dst, sem, fwd, loc, which, back):
-        to = _relay(topo, core, dst, which)
+    def rows(dst, row, src, src_row, outs, ins, sem):
+        (b1, l1, h1), (b2, l2, h2) = dst[1][0], src[1][0]
+        op("y", lambda: g.sync.dma_start(T[b1][row:128:16, l1:h1], T[b2][src_row:128:16, l2:h2]), outs, ins, 0.1, dma=sem, lat=2.5)
+
+    def send(dst, src, buf, sem, fwd, loc, back):
+        to, via = _relay(topo, core, dst), _relay(topo, back, core)
         d = dst if to is None else to
-        m, n = _mask(topo, core, d)
         rid, pid = topo.addr(d, core)
-        via = _relay(topo, back, core, which)
-        nb = _mask(topo, back if via is None else via, core)[1]
-        op("k", lambda: g.remote_dma(T[buf_dst][:], src[0], T.sem[sem if to is None else fwd], T.sem[loc], pid, rid, m),
-           [u(buf_dst)], [src], 0.3, lat=(OPT["way"] + (FIRST if buf_dst == "QI0" else 0)) * (1 if to is None else 2), land=(sem, nb, loc, n))
+        op("k", lambda: g.remote_dma(T[buf][:], src[0], T.sem[sem if to is None else fwd], T.sem[loc], pid, rid, topo.mask(core, d)),
+           [u(buf)], [src], 0.3, lat=(WAY + (FIRST if buf == "QI0" else 0)) * (1 if to is None else 2),
+           land=(sem, len(topo.engines(back if via is None else via, core)), loc, len(topo.engines(core, d))))
 
-    def e16(name, k=0, n=None, p=None):
-        return u(name, k, n, 16, p)
+    def sums(ps, base, src, w):
+        return [(e16(src, k), u(w), u(ps, base + k, base + 128, 16)) for k in range(16)]
 
-    def hold(o, z):
-        scan(o, u("MS", 0, 128), z, A.mult, A.add)
-
-    def sums(ps, base, src, w, p=None):
-        return [(u(ps, base + k, base + 128, 16, p), u(src, k, None, 16), u(w)) for k in range(16)]
-
-    def tile(z, h, ps, sign, extra, p=None, n=8):
-        scan(u(h, 0, 128, 1, p), u("MC", p=p), u(z, 0, 128, 1, p), A.mult, A.add)
+    def tile(z, h, ps, sign, *more):
+        scan(u(h, 0, 128), u("MC"), u(z, 0, 128), A.mult, A.add)
         a, b = ("blk", "nblk") if sign > 0 else ("nblk", "blk")
-        mm([(ps, u(h, 0, 128, 1, p), u(a, 0, n, 1, p)), (ps, u(h, 1, 129, 1, p), u(b, 0, n, 1, p)), (ps, u(z, 1, 129, 1, p), u(a, 0, n, 1, p))]
-           + [(ps, x, y) for x, y in extra])
+        mm(ps, (u(h, 0, 128), u(a)), (u(h, 1, 129), u(b)), (u(z, 1, 129), u(a)), *more)
 
     def low(z, key, hi, step):
         c = 1.5 * 2.0 ** 23 * step
         ts(hi, key, c, A.add, c, A.subtract)
         tt(z, key, hi, A.subtract)
 
-    TAG[0] = "init"
     fill(u("X", 0, 16), -64.0)
     fill(u("X", 2048, 2304), 0.0)
     fill(u("AC4", 0, 8), 0)
     fill(u("AC4", 2048, 2192), 0)
-    dma("y", u("MI"), ext(T.ml[:], "in_ml"), "ld0")
-    dma("y", u("X", 1, 2049), ext(T.x0[:], "in_x"), "ld1")
-    dma("y", u("LI"), ext(T.lims[:], "in_l"), "ld2")
-    dma("y", u("WI"), ext(T.wt[:], "in_w"), "ld3")
+    dma(u("MI"), mark("ml", ap=T.ml[:]), "ld0")
+    dma(u("X", 1, 2049), mark("x0", ap=T.x0[:]), "ld1")
+    dma(u("LI"), mark("lims", ap=T.lims[:]), "ld2")
+    dma(u("WI", 0, 1), mark("wt", ap=T.wt[:]), "ld3")
     for q in range(4):
-        dma("y", u("AC4", 1 + 512 * q, 513 + 512 * q), ext(T.ac[:], "in_a"), "ld%d" % (4 + q))
+        dma(u("AC4", 1 + 512 * q, 513 + 512 * q), mark("ac", ap=T.ac[:]), "ld%d" % (4 + q))
     J, J4, J15, J144, J8 = u("Jb", 0, 128), u("J4b"), u("J15b"), u("Jb"), u("Jb", 0, 8)
-    pc = [16]
+    P, P4, P15 = u("PC", 0, 1), u("PC", 1, 2), u("PC", 2, 3)
+    IDB, NIDB, ONE, BD, NBD = u("IDB"), u("NIDB"), u("ONEB"), u("BD"), u("NBD")
+    used = [16]
 
     def col(src, s1, o1, s2=None, o2=None):
-        c = u("PC", pc[0], pc[0] + 1)
-        pc[0] += 1
+        c = u("PC", used[0], used[0] + 1)
+        used[0] += 1
         ts(c, src, s1, o1, s2, o2)
         return c
-
-    def scaled(name, src, val):
-        act(u(name) if isinstance(name, str) else name, src, F.Identity, scale=val)
     iota(u("PIi", 0, 1), [[0, 1]], 0, 1)
-    P, P4, P15 = u("PC", 0, 1), u("PC", 1, 2), u("PC", 2, 3)
     iota(J144, [[1, 144]], 0)
     iota(J15, [[0, 8], [1, 16]], 0)
     iota(J4, [[1, 8], [0, 16]], 0)
-    iota(u("J2f"), [[1, 128], [0, 4]], 0)
-    iota(u("J3"), [[0, 128], [1, 4]], 0)
-    iota(u("DUM"), [[0, 4], [16, 128]], 2064)
+    for a, b in ((0, 128), (128, 512)):
+        iota(u("J2f", a, b), [[1, (b - a) // 4], [0, 4]], a // 4)
+        iota(u("J3f", a, b), [[0, (b - a) // 4], [1, 4]], 0)
+        iota(u("DUM", a, b), [[0, (b - a) // 128], [16, 128]], 2064)
     iota(u("PC", 4, 8), [[1, 4]], 1024, 4)
     iota(u("PC", 8, 10), [[512, 2]], 8192 - 1536, 1)
     iota(u("PC", 10, 11), [[0, 1]], 128, 1)
-    iota(u("FREE", 0, 1024), [[0, 1024]], 0)
-    iota(u("Z1"), [[0, 2048]], 0)
-    iota(u("QZ"), [[0, 512]], 0)
-    iota(u("DS", 640, 768), [[0, 128]], 0)
-
-    iota(u("XV0"), [[0, 256]], 128)
-    iota(u("MIN5"), [[0, 512]], 1 - 2 ** 24)
-    iota(e16("MIN5"), [[0, 32]], 2 ** 24 - 1)
-    fill(u("MS"), 1.0)
-    fill(e16("MS"), 0.0)
-    fill(u("ZE"), 0.0)
-    if "t" in OPT["nx"]:
-        fill(u("Z0"), 0.0)
-    fill(u("OT", 0, 8), 0.0)
-    fill(u("OT", 2048, 2064), 0.0)
-    fill(u("W", 512, 640), 0.0)
+    for o, val in ((u("FREE", 0, 1024), 0), (u("Z1"), 0), (u("QZ"), 0), (u("DS", 640, 768), 0), (u("XV0"), 128), (u("MIN5"), LOW), (e16("MIN5"), -LOW)):
+        iota(o, [[0, o[2]]], val)
+    for o, val in ((u("MS"), 1.0), (e16("MS"), 0.0), (u("ZE"), 0.0), (u("Z0"), 0.0), (u("OT", 0, 8), 0.0), (u("OT", 2048, 2064), 0.0), (u("W", 512, 640), 0.0)):
+        fill(o, val)
     ts(u("PIi", 1, 2), u("PIi", 0, 1), 4, A.logical_shift_right)
     ts(u("PIi", 2, 3), u("PIi", 0, 1), 15, A.bitwise_and)
     cp(u("PC", 0, 3), u("PIi", 0, 3))
     ts(u("E16"), u("J15b", 0, 16), P15, A.is_equal)
-    ts(u("EP"), u("Jb", 0, 4), P, A.is_equal)
-    row0, row4 = u("E16", 0, 1), u("E16", 4, 5)
-    ts(u("DUM"), u("DUM"), P15, A.add)
+    ts(u("EP", 0, 4), u("Jb", 0, 4), P, A.is_equal)
+    row0, row4, row10 = u("E16", 0, 1), u("E16", 4, 5), u("E16", 10, 11)
     V0 = u("FREE", 1024, 1536)
-    slope = col(row4, u("E16", 10, 11), A.add)
+    slope = col(row4, row10, A.add)
     base = col(slope, 128.0, A.mult)
-    tt(base, base, col(u("E16", 10, 11), 64.0, A.mult), A.add)
-    act(u("p4"), u("J2f"), F.Identity, scale=slope, bias=base)
-    ts(u("t512b"), u("J3"), P15, A.is_equal, 64.0, A.mult)
-    tt(V0, u("t512b"), u("p4"), A.add)
+    tt(base, base, col(row10, 64.0, A.mult), A.add)
+    for a, b in ((0, 128), (128, 512)):
+        ps = u("p4" if a else "p3", a, b)
+        ts(u("DUM", a, b), u("DUM", a, b), P15, A.add)
+        act(ps, u("J2f", a, b), F.Identity, scale=slope, bias=base)
+        ts(u("t512b", a, b), u("J3f", a, b), P15, A.is_equal, 64.0, A.mult)
+        tt(u("FREE", 1024 + a, 1024 + b), u("t512b", a, b), ps, A.add)
     for a, b in ((0, 128), (128, 512)):
         ts(u("p6", a, b), u("MI", a, b), 2048, A.is_equal, 8192.0, A.mult)
         ts(u("t512a", a, b), u("MI", a, b), 1, A.add)
@@ -613,203 +418,143 @@ def rank_program(g, core, T, topo):
         ts(u("W", a, b), u("p5", a, b), 0.0, A.max)
     for c in range(4):
         ve = "VG" if c % 2 else "VE"
-        mark = (None, [("row4" + ve, 0, 1)])
-        if c == 1 and OPT["vg"]:
-            dma("y", u("VG"), u("VE"), "ld10")
-            buf, o, n, _d = _ARENA[ve]
-            op("y", lambda buf=buf, o=o, n=n: g.sync.dma_start(T[buf][4:128:16, o:o + n], T[buf][9:128:16, o:o + n]), [u(ve)], [], 0.1, dma="ld7b", lat=2.5)
-        elif c < 2:
-            for h in range(2):
-                a, b = 1024 * h, 1024 * h + 1024
-                cp(u("ZE", a, b, 16), u("FREE", 1024 + 128 * c + 64 * h, 1024 + 128 * c + 64 * h + 64))
-                scan(u(ve, a, b), u("MS", a, b), u("ZE", a, b), A.mult, A.add)
-        else:
-            buf, o, n, _d = _ARENA[ve]
-            op("y", lambda buf=buf, o=o, n=n: g.sync.dma_start(T[buf][4:128:16, o:o + n], T[buf][10:128:16, o:o + n]), [u(ve)], [], 0.1, dma="ld%d" % (6 + c), lat=2.5)
-        for h in range(2):
-            a, b = 1024 * h, 1024 * h + 1024
-            BON[0] = OPT["bot"]
-            act(ix(u("OT"), u("INO", 128 * c + 64 * h, 128 * c + 64 * h + 64)), u(ve, a, b), F.Silu)
-            BON[0] = 0
-
-    BON[0] = OPT["bon"]
-    ts(u("IDB"), J, P, A.is_equal)
-    ts(u("BD"), J4, P4, A.is_equal)
+        if c >= 2:
+            rows(u(ve), 4, u(ve), 10, [u(ve)], [], "ld%d" % (6 + c))
+        for a in (0, 1024) if c < 2 else ():
+            cp(u("ZE", a, a + 1024, 16), u("FREE", 1024 + 128 * c + a // 16, 1088 + 128 * c + a // 16))
+            scan(u(ve, a, a + 1024), u("MS", a, a + 1024), u("ZE", a, a + 1024), A.mult, A.add)
+        first[0] = 14
+        for a in (0, 1024):
+            act(ix(u("OT"), u("INO", 128 * c + a // 16, 128 * c + a // 16 + 64)), u(ve, a, a + 1024), F.Silu)
+        first[0] = 0
+    first[0] = 30
+    ts(IDB, J, P, A.is_equal)
+    ts(BD, J4, P4, A.is_equal)
     ts(u("blk"), J8, P4, A.is_equal)
     ts(u("R16"), J15, P15, A.is_equal)
-    scaled("nblk", u("blk"), -1.0)
-    scaled("nblkf", u("blk"), -1.0)
-    for name, val in (("w64k", 65536.0), ("w8k", 8192.0), ("w32", 32.0)):
-        scaled(name, u("blk"), val)
-    scaled("NBD", u("BD"), -1.0)
-    scaled("IDF", u("IDB"), 1.0)
-    scaled("SEL0R", u("BD"), row0)
-    scaled("SEL0", u("blk"), row0)
-    scaled("N25", u("SEL0R"), -2.0 ** 25)
+    for name, src, val in (("nblk", "blk", -1.0), ("nblkf", "blk", -1.0), ("w64k", "blk", 65536.0), ("w8k", "blk", 8192.0), ("w32", "blk", 32.0),
+                           ("NBD", "BD", -1.0), ("IDF", "IDB", 1.0), ("SEL0R", "BD", row0), ("SEL0", "blk", row0), ("N25", "SEL0R", -2.0 ** 25),
+                           ("NIDB", "IDB", -1.0), ("N27", "IDB", -2.0 ** 27), ("N20", "IDB", -2.0 ** 20), ("P23", "IDB", 2.0 ** 23),
+                           ("P11", "IDB", 2.0 ** 11), ("RV0", "IDB", -49152.0), ("RV1", "IDB", -24576.0), ("RV2", "IDB", -12288.0)):
+        act(u(name), u(src), F.Identity, scale=val)
     act(u("CN1"), u("R16"), F.Identity, scale=8192.0, bias=-8192.0)
-    scaled(u("KAx", 128, 256), J15, u("EP", 0, 1))
-    scaled(u("ID2", 128, 256), u("IDB"), 1.0)
-    for name, val in (("NIDB", -1.0), ("N24", -2.0 ** 27), ("N20", -2.0 ** 20), ("P20", 2.0 ** 23), ("P11", 2.0 ** 11),
-                      ("RV0", -49152.0), ("RV1", -24576.0), ("RV2", -12288.0)):
-        if name in OPT["sv"]:
-            scaled(name, u("IDB"), val)
-        else:
-            ts(u(name), u("IDB"), val, A.mult)
-    BON[0] = 0
+    act(u("ID2", 128, 256), IDB, F.Identity)
+    first[0] = 0
     ts(u("MC"), J15, P15, A.is_le)
     fill(e16("MC"), 0.0)
-    fill(u("ONEB"), 1.0)
-    ts(u("ZALL"), u("MS", 0, 1152), 0.0, A.mult)
-    keys = (("KAs", 4096.0, 2.0 ** 27, -1088.0), ("KAb", -1.0, -2.0 ** 23, 7.0), ("KAn", 512.0, 2.0 ** 24, 0.0), ("KQ5", 32.0, -15.0, 0.0),
-            ("KAp", 32768.0, 21.0 * 4096 * 160, -2.0 ** 17))
-    for name, slope, c1, c2 in keys:
-        lo = 128 if name == "KAp" else 0
+    fill(ONE, 1.0)
+    ts(u("ZALL"), u("MS", 0, 864), 0.0, A.mult)
+    for name, slope, c1, c2 in (("KAs", 4096.0, 2.0 ** 27, -1088.0), ("KAb", -1.0, -2.0 ** 23, 7.0), ("KAn", 512.0, 2.0 ** 24, 0.0), ("KQ5", 32.0, -15.0, 0.0)):
         b = col(u("EP", 1, 2), c1, A.mult)
         if c2:
             ts(b, u("EP", 2, 3), c2, A.mult, b, A.add)
-        ts(u(name, lo, lo + 128), J15, col(u("EP", 0, 1), slope, A.mult), A.mult, b, A.add)
-    for name, val in (("KAd", 2 ** 20), ("K11", 2 ** 4), ("K20", 2 ** 13), ("K21", 2 ** 14), ("THZ", 0), ("MIN3", 1 - 2 ** 24), ("ZMW", 0),
-                      ("K9", 12), ("ONEF", 1)):
-        iota(u(name), [[0, u(name)[2]]], val)
-    iota(u("KAp", 0, 128), [[0, 128]], 21 * 32 * 160)
-    iota(u("KAx", 0, 128), [[0, 128]], 0)
-    iota(e16("KAd", 15), [[0, 8]], 0)
-    iota(u("Aa", 256, 264), [[0, 8]], 0)
+        ts(u(name, 0, 128), J15, col(u("EP", 0, 1), slope, A.mult), A.mult, b, A.add)
+    cp(u("KQ5", 128, 256), u("KQ5", 0, 128))
+    cp(u("KQ5", 256, 512), u("KQ5", 0, 256))
+    for o, val in ((u("KAd"), 2 ** 20), (u("K11"), 2 ** 4), (u("K20"), 2 ** 13), (u("K21"), 2 ** 14), (u("THZ"), 0), (u("MIN3"), LOW), (u("ZMW"), 0),
+                   (u("K9"), 12), (u("ONEF"), 1), (u("KAp"), 21 * 32 * 160), (e16("KAd", 15), 0), (u("Aa", 256, 264), 0), (e16("MIN"), -LOW), (u("CODE"), 0)):
+        iota(o, [[0, o[2]]], val)
     fill(u("C25"), 2.0 ** 25)
-    fill(e16("MIN"), BIG)
     iota(e16("MINs"), [[0, 8]], 255 * 65536 + 2049 - 1088, 1)
-    if "s" in OPT["mv"]:
-        cp(u("CREP"), u("J", 0, 128))
     hw = col(P15, 4.0, A.is_lt, P15, A.mult)
     ts(hw, hw, 1.0 / 64, A.mult, col(row4, 4.0, A.mult), A.add)
-    ts(u("HWN"), u("NBD"), hw, A.mult)
-    ts(u("kq"), u("E16", 0, 4), 2.0 ** 19, A.mult, hw, A.add)
+    ts(u("HWN"), NBD, hw, A.mult)
+    ts(u("kq", 0, 4), u("E16", 0, 4), 2.0 ** 19, A.mult, hw, A.add)
     for c in range(4):
         ts(u("og%d" % c), u("blk"), u("kq", c, c + 1), A.mult)
-    last = col(P4, 16.0, A.mult, 15.0, A.add)
-    ts(u("Y2"), J144, last, A.is_equal, 2.0, A.mult)
-    ts(u("YF" if OPT["occ"] == "p" else "Y"), J144, last, A.is_equal, row0, A.mult)
-    ts(u("HY"), J144, last, A.is_equal, hw, A.mult)
+    ts(u("Y"), J144, col(P4, 16.0, A.mult, 15.0, A.add), A.is_equal, row0, A.mult)
     ts(u("b1"), J, P, A.is_gt)
     tt(u("TRIm"), u("b1"), u("P11"), A.subtract)
     ts(u("NTRIm"), u("TRIm"), -1.0, A.mult)
-    tt(u("BT1", 0, 128), u("b1"), u("BD"), A.mult)
-    ts(u("BT1", 128, 256), u("BT1", 0, 128), -1.0, A.mult)
-    ts(u("b2"), u("IDB"), -4.0, A.mult)
-    tt(u("b1"), u("BT1", 0, 128), u("b2"), A.add)
-    ts(u("BTX", 0, 128), u("b1"), 32768.0, A.mult)
-    ts(u("BTX", 128, 256), u("b1"), -32768.0, A.mult)
+    ts(u("b2"), IDB, -4.0, A.mult)
     ts(u("b1"), J, P, A.is_lt)
-    tt(u("BTI"), u("b1"), u("BD"), A.mult)
+    tt(u("BTI"), u("b1"), BD, A.mult)
     tt(u("BTI"), u("BTI"), u("P11"), A.add)
     ts(u("b1"), u("b1"), -56.0, A.mult, -8.0, A.add)
     tt(u("PEN", 0, 128), u("b1"), u("b2"), A.add)
     cp(u("PEN", 128, 256), u("PEN", 0, 128))
     cp(u("PEN", 256, 512), u("PEN", 0, 256))
+    for name, src, val in (("P15", IDB, 32768.0), ("w2", u("blk"), 2.0), ("ID2x", IDB, 2.0), ("B512", BD, 512.0)):
+        ts(u(name), src, val, A.mult)
     ts(u("CMR"), u("R16"), u("PC", 10, 11), A.mult)
     for c in range(4):
         ts(u("CMK%d" % c), u("R16"), u("PC", 4 + c, 5 + c), A.mult)
-    ts(u("CNT", 0, 128), u("R16"), 8192.0 - 1408, A.mult, -8192.0, A.add)
-    ts(u("CNT", 128, 256), u("R16"), 8192.0 - 1920, A.mult, -8192.0, A.add)
-    for q in range(2):
+    for q, val in enumerate((640 - 2048, 128 - 2048)):
+        ts(u("CNT", 128 * q, 128 * q + 128), u("R16"), 8192.0 + val, A.mult, -8192.0, A.add)
         ts(u("CTG", 128 * q, 128 * q + 128), u("R16"), u("PC", 8 + q, 9 + q), A.mult, -8192.0, A.add)
+    ts(u("PENW"), u("R16", 0, 32), -2.0 ** 17, A.mult, 2.0 ** 17, A.add)
     ts(u("CIX"), u("Jb", 0, 32), 16.0, A.mult, P15, A.add)
-    ts(u("CB"), u("CIX", 0, 8), 16.0, A.mult, 7.0, A.add)
+    ts(u("CB"), u("CT"), 16.0, A.mult, 7.0, A.add)
     ts(u("C512"), u("CIX"), 512.0, A.add)
-    bits = col(P15, 9.0, A.is_lt)
-    iota(u("CODE"), [[0, 512]], 0)
-    ts(u("m2", 32, 36), u("Jb", 0, 4), col(P15, -9.0, A.add), A.is_equal, 4.0, A.mult)
-    cp(u("CODE", 0, 4), u("m2", 32, 36))
-    buf, o, n, _d = _ARENA["CODE"]
+    ts(u("sp4", 0, 4), u("Jb", 0, 4), col(P15, -9.0, A.add), A.is_equal, 4.0, A.mult)
+    cp(u("CODE", 0, 4), u("sp4", 0, 4))
     for b in range(9):
         src = u("VB" if b < 4 else "DT" if b < 8 else "QS", 512 * (b % 4), 512 * (b % 4) + 512)
         iota(src, [x for x in ([0, 256 >> b], [2, 2], [0, 1 << b]) if x[1] > 1], -1)
-        lo = src[1][0][1]
-        op("y", lambda b=b, lo=lo, t=T[buf], o=o: g.sync.dma_start(t[b:128:16, o:o + 512], t[b:128:16, lo:lo + 512]), [(None, [("bit", b, b + 1)])], [src, u("CODE")],
-           0.1, dma="cd%d" % b, lat=2.5)
+        rows(u("CODE"), b, src, b, [mark("bit", b, b + 1)], [src, u("CODE")], "cd%d" % b)
     ts(u("PIi", 3, 4), u("PIi", 1, 2), 3, A.bitwise_and)
     ts(u("PIi", 4, 5), u("PIi", 0, 1), 3, A.bitwise_and)
-    ts(u("G4"), u("Jb", 0, 4), col(u("PIi", 3, 4), 1.0, A.mult), A.is_equal)
-    ts(u("m2", 40, 44), u("m2", 32, 36), 0.25, A.mult, bits, A.add)
+    ts(u("G4", 0, 4), u("Jb", 0, 4), col(u("PIi", 3, 4), 1.0, A.mult), A.is_equal)
+    ts(u("kp4", 0, 4), u("sp4", 0, 4), 0.25, A.mult, col(P15, 9.0, A.is_lt), A.add)
     for q in range(4):
-        ts(u("KQ", 4 * q, 4 * q + 4), u("m2", 40, 44), u("G4", q, q + 1), A.mult)
+        ts(u("KQ", 4 * q, 4 * q + 4), u("kp4", 0, 4), u("G4", q, q + 1), A.mult)
     ts(u("PC", 12, 14), u("LI"), -65536.0, A.mult)
-    wt = col(u("WI"), 1.0, A.mult)
-    ts(u("WY"), J144, last, A.is_equal, wt, A.mult)
-    ts(u("WTn"), u("BD"), wt, A.mult, -128.0, A.mult)
-    ts(u("ID2x"), u("IDB"), 2.0, A.mult)
-    ts(u("B512"), u("BD"), 512.0, A.mult)
-    cp(u("KQ5", 128, 256), u("KQ5", 0, 128))
-    cp(u("KQ5", 256, 512), u("KQ5", 0, 256))
+    wt = col(u("WI", 0, 1), 1.0, A.mult)
+    ts(u("WTm"), NBD, wt, A.mult)
+    ts(u("WTn"), BD, wt, A.mult, 128.0, A.mult)
     less = col(u("EP", 1, 2), -2048.0, A.mult)
     ts(u("L2N"), u("SEL0"), u("PC", 13, 14), A.mult, less, A.add)
     ts(u("THN"), u("SEL0"), u("PC", 12, 13), A.mult, less, A.add)
     ts(u("ROW1"), J8, 0.0, A.mult, col(less, 32.0, A.mult), A.add)
     for s in (1, 2, 3, 4, 8, 12):
-        o, i = u("SH", 128 * s, 128 * s + 128), u("BD")
-        op("k", lambda o=o, i=i, s=s: g.affine_select(o[0], i[0], [[1, 128]], A.is_equal, 0.0, -s, -1), [o], [i], 0.43)
-    op("k", lambda: g.affine_select(u("EXP")[0], u("Z1")[0], [[-1, 128], [0, 16]], A.not_equal, 1.0, 0, 1), [u("EXP")], [u("Z1")], 3.9)
+        select(u("SH", 128 * s, 128 * s + 128), BD, [[1, 128]], A.is_equal, 0.0, -s, -1)
+    select(u("EXP"), u("Z1"), [[-1, 128], [0, 16]], A.not_equal, 1.0, 0, 1)
     fourth = col(u("PIi", 4, 5), 3.0, A.is_equal, -128.0, A.mult)
-    ts(u("A4n"), u("BD"), fourth, A.mult)
-    ts(u("B4"), u("BD"), col(fourth, 4.0, A.mult, 128.0, A.add), A.mult)
+    ts(u("A4n"), BD, fourth, A.mult)
+    ts(u("B4"), BD, col(fourth, 4.0, A.mult, 128.0, A.add), A.mult)
 
-    win = u("X", 0, 2192)
+    X, LISTS, OWNERS = u("X", 0, 2192), u("W", 0, 512), u("OT", 0, 2064)
 
     def gather(out, off, cut):
-        if cut:
-            cp(u(out, 0, 16 * cut), ix(win, u(off, 0, cut)))
+        cp(u(out, 0, 16 * cut), ix(X, u(off, 0, cut)))
         if cut < 128:
-            act(u(out, 16 * cut, 2048), ix(win, u(off, cut, 128)), F.Copy)
+            act(u(out, 16 * cut, 2048), ix(X, u(off, cut, 128)), F.Copy)
 
     def part_own(t):
-        TAG[0] = "own%d" % t
-        cl = t % 4
-        z, s1, s16 = "Z%d" % (t % 2), "S1" + "ab"[t % 2], "S16" + "ab"[t % 2]
-        lanes = u("W", cl, 512, 4)
+        z, s1, s16 = "Z%d" % (t % 2), "S1%d" % (t % 2), "S16%d" % (t % 2)
+        lanes = u("W", t % 4, 512, 4)
         cp(u("OWN"), lanes)
-        gather("T", "OWN", OPT["T"] if t else OPT["T0"])
+        gather("T", "OWN", 112 if t else 128)
         if t:
             act(u("PRE"), lanes, F.Sign)
         else:
             ts(u("PRE"), lanes, 0.0, A.is_gt)
         cp(u("OWNH"), lanes)
         k = u("p3", 0, 128)
-        mm([(k, u("ONEB"), u("KAs")), (k, u("PRE"), u("N24")), (k, u("OWNH"), u("ID16"))] + sums("p3", 0, "T", "w64k"))
+        mm(k, (ONE, u("KAs")), (u("PRE"), u("N27")), (u("OWNH"), IDB), *sums("p3", 0, "T", "w64k"))
         scan(u(s1), u("MINs"), k, A.max, A.min)
         low(e16("ZS", 0, 128), e16(s1, 15), u("hi8"), 4096)
-        tile("ZS", "HS", u("p4", 0, 8), 1, [])
+        tile("ZS", "HS", u("p4", 0, 8), 1)
         ts(u(s16), u("p4", 0, 8), 1088.0, A.add)
-        cp(e16(z), ix(win, u(s16)))
+        cp(e16(z), ix(X, u(s16)))
         ts(u("AN"), ix(u("AC4"), u(s16)), 1, A.add)
-        if "t" in OPT["nx"]:
-            scan(u("REP"), u("MS"), u(z), A.mult, A.add)
-        else:
-            mm([(u("p6", 288, 416), e16(z), u("NIDB"))])
-            act(u("ZT"), u("p6", 288, 416), F.Copy)
+        scan(u("REP"), u("MS"), u(z), A.mult, A.add)
         scan(u("US"), u("MS"), u("T"), A.mult, A.max)
-        mm([(u("p4", 8, 16), u("ONEB"), u("L2N")), (u("p4", 8, 16), e16("US", 15), u("w64k"))])
+        mm(u("p4", 8, 16), (ONE, u("L2N")), (e16("US", 15), u("w64k")))
         tt(u("wp8"), e16(s1, 15), u("p4", 8, 16), A.is_lt)
-        mm([(u("p6", 0, 128), u("PRE"), u("SEL0R"))])
+        mm(u("p6", 0, 128), (u("PRE"), u("SEL0R")))
         act(u("LR"), u("p6", 0, 128), F.Copy)
-        q = u("p6", 160, 288)
-        mm([(q, u("IDB"), u("CN1")), (q, u("PRE"), u("B4"))])
-        act(u("QB"), q, F.Relu)
-        mm([(u("p4", 144, 152), u("IDB"), u("CT")), (u("p4", 144, 152), u("QB"), u("blk"))])
+        mm(u("p6", 160, 288), (IDB, u("CN1")), (u("PRE"), u("B4")))
+        act(u("QB"), u("p6", 160, 288), F.Relu)
+        mm(u("p4", 144, 152), (IDB, u("CT")), (u("QB"), u("blk")))
         cp(u("BT16"), u("p4", 144, 152))
 
-    def part_vacant(t):
-        TAG[0] = "vac%d" % t
-        if OPT["occ"] == "p":
-            mm([(u("p6", 128, 160), u("YF", 15 - r, 143 - r), e16("W", r, 512)) for r in range(16)])
-        else:
-            if OPT["occ"] == "s":
-                act(u("OCC"), u("W", 0, 512), F.Sign)
-            else:
-                ts(u("OCC"), u("W", 0, 512), 0.0, A.is_gt)
-            mm([(u("p6", 128, 160), u("Y", 15 - r, 143 - r), e16("OCC", r)) for r in range(16)])
-        act(u("OCb"), u("p6", 128, 160), F.Sign)
-        mm([(u("p4", 32, 64), u("BD"), u("OCb"))])
-        mm([(u("p4", 64, 96), u("BTI"), u("OCb")), (u("p4", 64, 96), u("ID16"), u("CIX"))])
+    def part_vacant():
+        act(u("OCC"), LISTS, F.Sign)
+        mm(u("p6", 128, 160), *[(u("Y", 15 - r, 143 - r), e16("OCC", r)) for r in range(16)])
+        act(u("OCb"), u("p6", 128, 160), F.Copy)
+        mm(u("p4", 32, 64), (BD, u("OCb")))
+        mm(u("p4", 64, 96), (u("BTI"), u("OCb")), (IDB, u("CIX")))
         scan(u("CS"), u("ONEB", 0, 32), u("p4", 32, 64), A.mult, A.add)
         tt(u("r1"), u("p4", 64, 96), u("CS"), A.subtract)
         tt(u("r2"), u("r1"), u("C512"), A.min)
@@ -818,301 +563,209 @@ def rank_program(g, core, T, topo):
         act(u("NFF"), u("SEL0R"), F.Identity, scale=u("CS", 31, 32))
 
     def part_split(t):
-        TAG[0] = "split%d" % t
-        z = "Z%d" % (t % 2)
+        s = e16("Z%d" % (t % 2))
         for c in range(4):
-            a, b = 512 * c, 512 * c + 512
-            ps = u("p%d" % (c % 3))
-            mm([(ps, u("IDB"), u("T", a, b)), (ps, u("NIDB"), u("REP", a, b)) if "t" in OPT["nx"] else (ps, u("ZT"), u("EXP", a, b))])
+            a, b, ps = 512 * c, 512 * c + 512, u("p%d" % (c % 3))
+            mm(ps, (IDB, u("T", a, b)), (NIDB, u("REP", a, b)))
             act(u("SQ", a, b), ps, F.Square)
-        act(u("SQS"), e16(z), F.Square)
-        act(u("ZP"), e16(z), F.Identity, bias=128.0)
+        act(u("SQS"), s, F.Square)
+        act(u("ZP"), s, F.Identity, bias=128.0)
         k = u("p3", 128, 256)
-        mm([(k, u("ONEB"), u("KAb")), (k, u("PRE"), u("P20"))] + sums("p3", 128, "SQ", "w32"))
+        mm(k, (ONE, u("KAb")), (u("PRE"), u("P23")), *sums("p3", 128, "SQ", "w32"))
         scan(u("SB"), u("MS", 0, 128), k, A.mult, A.max)
         low(e16("ZB", 0, 128), e16("SB", 15), u("hb8"), 32)
-        tile("ZB", "HB", u("p4", 16, 24), -1, [(u("ID16"), u("CB"))])
+        tile("ZB", "HB", u("p4", 16, 24), -1, (IDB, u("CB")))
         cp(u("B16"), u("p4", 16, 24))
         act(u("XB"), ix(u("T"), u("B16")), F.Copy)
         act(u("SQB"), u("XB"), F.Square)
-        wv = u("p6", 288, 416)
-        if OPT["aw"]:
-            mm([(wv, e16(z), u("IDB")), (wv, u("XB"), u("NIDB"))])
-            copy(OPT["q"][4], u("WV"), wv)
-        else:
-            wv = u("p1", 0, 128)
-            mm([(wv, u("IDB"), e16(z)), (wv, u("NIDB"), u("XB"))])
-            for k in range(16):
-                tt(e16("AW", k), e16("T", k), wv, A.mult)
-        for c in range(4 * OPT["aw"]):
-            a, b = 512 * c, 512 * c + 512
-            ps = u("p%d" % (c % 2))
-            mm([(ps, u("WV"), u("EXP", a, b))])
+        mm(u("p6", 288, 416), (s, IDB), (u("XB"), NIDB))
+        act(u("WV"), u("p6", 288, 416), F.Copy)
+        for c in range(4):
+            a, b, ps = 512 * c, 512 * c + 512, u("p%d" % (c % 2))
+            mm(ps, (u("WV"), u("EXP", a, b)))
             tt(u("AW", a, b), u("T", a, b), ps, A.mult)
         lv = u("p7", 0, 128)
-        mm([(lv, u("ONEB"), u("K13")), (lv, u("N13"), u("PRE")), (lv, u("BD"), u("SQB")), (lv, u("NBD"), u("SQS"))]
-           + [(lv, u("Y2", 15 - k, 143 - k), e16("AW", k)) for k in range(16)])
-        ts(u("L1T"), lv, 0.0, A.is_lt)
-        pp = u("p7", 128, 384)
-        x = u("p2", 0, 256)
-        mm([(x, u("ONEB"), u("KAx")), (x, u("L1T"), u("BT1"))])
+        mm(lv, (ONE, u("K20")), (u("PRE"), u("N20")), (u("SQB"), BD), (u("SQS"), NBD), *sums("p7", 0, "AW", "w2"))
+        ts(u("LN", 0, 128), lv, 0.0, A.is_lt)
+        ts(u("LN", 128, 256), lv, 0.0, A.is_ge)
+        scan(u("XC"), u("MS", 0, 256), u("LN"), A.mult, A.add)
         for q in range(3):
-            act(u("XF", 256 * q, 256 * q + 256), x, F.Identity, scale=0.5 ** (q + 1), bias=159.5 + 0.5 ** (q + 2))
-        mm([(pp, u("ONEB"), u("KAp")), (pp, u("OWNH"), u("ID2")), (pp, u("L1T"), u("BTX"))]
-           + [(pp, u("RV%d" % q), u("XF", 256 * q, 256 * q + 256)) for q in range(3)])
+            ts(u("XF", 256 * q, 256 * q + 256), u("XC"), 0.5 ** (q + 1), A.mult, 159.5 + 0.5 ** (q + 2), A.add)
+        pp = u("p7", 128, 384)
+        mm(pp, (ONE, u("KAp")), (u("OWNH"), u("ID2")), (u("N20"), u("LN")), (u("P15"), u("XC")),
+           *[(u("RV%d" % q), u("XF", 256 * q, 256 * q + 256)) for q in range(3)])
         ts(u("Pa"), pp, 0.0, A.max)
-        TAG[0] = "shift%d" % t
-        for s in range(4):
-            a, b = ("Pa", "Pb") if s % 2 == 0 else ("Pb", "Pa")
-            th = 2.0 ** (15 - s)
-            if OPT["sh"] == "s":
-                act(u("Aa", 0, 256), u(a), F.Relu, bias=-th)
-            else:
-                ts(u("Aa", 0, 256), u(a), -th, A.add, 0.0, A.max)
-            if OPT["sg"][s] == "s":
-                act(u("p5", 0, 256), u(a), F.Relu, scale=2.0 ** 18, bias=(0.5 - th) * 2.0 ** 18)
-            else:
-                ts(u("p5", 0, 256), u(a), th, A.is_ge, 2 * th, A.mult)
+        for q in range(4):
+            a, b, th = "Pb" if q % 2 else "Pa", ("Pb", "Pa", "Pb", "SL")[q], 2.0 ** (15 - q)
+            act(u("Aa", 0, 256), u(a), F.Relu, bias=-th)
+            act(u("p5", 0, 256), u(a), F.Relu, scale=2.0 ** 18, bias=(0.5 - th) * 2.0 ** 18)
             tt(u("p5", 256, 512), u(a), u("p5", 0, 256), A.subtract)
-            tt(u(b if s < 3 else "SL"), u("p5", 256, 512), u("Aa", 1 << s, 256 + (1 << s)), A.max)
-        mm([(u("p6", 288, 416), u("SL", 0, 128), u("ID16")), (u("p6", 288, 416), u("NID16"), u("OWNH"))])
-        act(u("DS", 512, 640), u("p6", 288, 416), F.Copy)
+            tt(u(b), u("p5", 256, 512), u("Aa", 1 << q, 256 + (1 << q)), A.max)
+        mm(u("p6", 288, 416), (u("SL", 0, 128), IDB), (NIDB, u("OWNH")))
+        cp(u("DS", 512, 640), u("p6", 288, 416))
 
     def part_near(t):
-        TAG[0] = "near%d" % t
-        cl = t % 4
-        s1 = "S1" + "ab"[t % 2]
-        iota(e16("MINn"), [[0, 8]], 13 * 2 ** 20 + cl)
-        for h in range(2):
-            a, b = 1024 * h, 1024 * h + 1024
-            act(u("OG", a, b), ix(u("OT", 0, 2064), u("AN", 64 * h, 64 * h + 64)), F.Copy)
-        cuts = {2: (0, 64, 128), 3: (0, 56, 104, 128), 4: (0, 32, 64, 96, 128)}[OPT["nr"]]
-        for c in range(len(OPT["nc"]) - 1):
-            if "t" not in OPT["nx"]:
-                a, b = 16 * OPT["nc"][c], 16 * OPT["nc"][c + 1]
-                ps = u("p%d" % OPT["nb"][c], 0, b - a)
-                copy(OPT["nx"][c], u("AX", a, b), ix(win, u("AN", a // 16, b // 16)))
-                mm([(ps, u("ZT"), u("EXP", a, b)), (ps, u("IDB"), u("AX", a, b))])
-                act(u("DU", a, b), ps, F.Square)
-        for a, b in zip(cuts, cuts[1:]) if "t" in OPT["nx"] else ():
-            tt(u("AX", 16 * a, 16 * b), ix(win, u("AN", a, b)), u("REP", 16 * a, 16 * b), A.subtract)
+        iota(e16("MINn"), [[0, 8]], 13 * 2 ** 20 + t % 4)
+        for a in (0, 64):
+            act(u("OG", 16 * a, 16 * a + 1024), ix(OWNERS, u("AN", a, a + 64)), F.Copy)
+        for a, b in ((0, 56), (56, 104), (104, 128)):
+            tt(u("AX", 16 * a, 16 * b), ix(X, u("AN", a, b)), u("REP", 16 * a, 16 * b), A.subtract)
             act(u("DU", 16 * a, 16 * b), u("AX", 16 * a, 16 * b), F.Square)
         k = u("p3", 256, 384)
-        mm([(k, u("ONEB"), u("KAn")), (k, u("PRE"), u("N25"))] + sums("p3", 256, "OG", "og%d" % cl) + sums("p3", 256, "DU", "w8k"))
+        mm(k, (ONE, u("KAn")), (u("PRE"), u("N25")), *(sums("p3", 256, "OG", "og%d" % (t % 4)) + sums("p3", 256, "DU", "w8k")))
         scan(u("S2"), u("MINn"), k, A.max, A.min)
         cp(u("a8"), e16("S2", 15))
         ts(u("d8"), u("a8"), 511, A.bitwise_and)
         cp(e16("ZD", 0, 128), u("d8"))
-        tile("ZD", "HD", u("p4", 24, 32), 1, [])
+        tile("ZD", "HD", u("p4", 24, 32), 1)
         cp(u("D16"), u("p4", 24, 32))
-        TAG[0] = "partner%d" % t
-        lists = ix(u("W", 0, 512), u("D16"))
+
+    def part_partner(t):
+        lists = ix(LISTS, u("D16"))
         cp(u("DM"), lists)
-        gather("DT", "DM", OPT["DT"])
+        gather("DT", "DM", 80)
         act(u("PRD"), lists, F.Sign)
         cp(u("DMH"), lists)
+        codes = ix(u("CODE"), u("D16"))
+        codes = (codes[0], codes[1] + [("bit", 0, 9)]) + codes[2:]
         for q in range(4):
-            o, i, keep = u("CG", 128 * q, 128 * q + 128), ix(u("CODE"), u("D16")), u("KQ", 4 * q + cl, 4 * q + cl + 1)
-            i = (i[0], i[1] + [("bit", 0, 9)]) + i[2:]
-            if OPT["cg"][q] == "s":
-                act(o, i, F.Identity, scale=keep)
-            else:
-                ts(o, i, keep, A.mult)
+            act(u("CG", 128 * q, 128 * q + 128), codes, F.Identity, scale=u("KQ", 4 * q + t % 4, 4 * q + t % 4 + 1))
         for h in range(2):
             ps = "p%d" % h
-            items = [(u(ps), u("IDB"), u("PEN"))]
-            for q in range(4):
-                x = u("CG", 128 * q, 128 * q + 128, 1, (64 * h, 64 * h + 64))
-                items.append((u(ps, 128 * q, 128 * q + 128), x, x))
-            mm(items)
-            relu(OPT["eq"][h], u("EQ", 512 * h, 512 * h + 512), u(ps))
-        mm([(u("p6", 416, 424), u("PRE"), e16("BD")), (u("p6", 416, 424), u("PRD"), e16("BD"))])
+            parts = [u("CG", 128 * q, 128 * q + 128, 1, (64 * h, 64 * h + 64)) for q in range(4)]
+            mm(u(ps), (IDB, u("PEN")), *[(x, x, u(ps, 128 * q, 128 * q + 128)) for q, x in enumerate(parts)])
+            act(u("EQ", 512 * h, 512 * h + 512), u(ps), F.Relu)
+        mm(u("p6", 416, 424), (u("PRE"), e16("BD")), (u("PRD"), e16("BD")))
         act(u("SZ"), u("p6", 416, 424), F.Relu, scale=32.0, bias=-512.0)
-        k = u("p3", 384, 512)
-        cuts = (0, 16 * OPT["DT"], 2048) if OPT["dh"] else (0, 2048)
-        for a, b in zip(cuts, cuts[1:]):
-            copy(OPT["q"][5], u("DT", a + 15, b, 16), u("US", a + 15, b, 16))
+        for a, b in ((0, 1280), (1280, 2048)):
+            cp(u("DT", a + 15, b, 16), u("US", a + 15, b, 16))
             scan(u("AX", a, b), u("MS", a, b), u("DT", a, b), A.mult, A.max)
-        mm([(k, u("ONEB"), u("KAd")), (k, u("PRD"), u("N24")), (e16("p3", 399), u("IDF"), e16(s1, 15))] + sums("p3", 384, "DT", "w64k")[:15])
-        th = u("p4", 96, 104)
-        mm([(th, u("ONEB"), u("THN")), (th, u("ONEB"), u("THZ")), (th, u("P25"), u("SZ"))]
-           + [(u("p4", 96 + q, 97 + q), u("EQ", 128 * q, 128 * q + 128), u("C25", 0, 1)) for q in range(8)] + [(th, e16("AX", 15), u("w64k"))])
+        k = u("p3", 384, 512)
+        mm(k, (ONE, u("KAd")), (u("PRD"), u("N27")), (u("IDF"), e16("S1%d" % (t % 2), 15), e16("p3", 399)), *sums("p3", 384, "DT", "w64k")[:15])
+        mm(u("p4", 96, 104), (ONE, u("THN")), (ONE, u("THZ")), (u("P23"), u("SZ")),
+           *[(u("EQ", 128 * q, 128 * q + 128), u("C25", 0, 1), u("p4", 96 + q, 97 + q)) for q in range(8)], (e16("AX", 15), u("w64k")))
         scan(u("S3"), u("MIN"), k, A.max, A.min)
-        for c, (src, step, out) in enumerate((("DMH", 1, "D1"), ("DM2", 4, "DS"))):
+        for src, step, out in (("DMH", 1, "D1"), ("DM2", 4, "DS")):
             for q in range(4):
-                s = step * q
-                mm([(u("p2", 128 * q, 128 * q + 128), u("SH", 128 * s, 128 * s + 128) if s else u("IDB"), u(src))])
-            copy(OPT["ds"][c], u(out, 0, 512), u("p2"))
-            if c == 0:
+                mm(u("p2", 128 * q, 128 * q + 128), (u("SH", 128 * step * q, 128 * step * q + 128) if q else IDB, u(src)))
+            act(u(out, 0, 512), u("p2"), F.Copy)
+            if step == 1:
                 cp(u("DM2"), ix(u("D1"), u("BT16")))
 
     def part_finish(t):
-        TAG[0] = "fin%d" % t
-        cl = t % 4
-        z, rk = "Z%d" % (t % 2), "RK" + "ab"[t % 2]
+        cl, rk, ev = t % 4, "RK%d" % (t % 2), e16("ZE")
+        MR, WR, SR = u("MR"), u("WR"), u("SR")
         tt(e16("ZM"), e16("S3", 15), u("p4", 96, 104), A.is_ge)
         tt(e16("ZW"), u("wp8"), e16("ZM"), A.is_gt)
         scan(u("MWR"), u("MS", 0, 256), u("ZMW"), A.mult, A.add)
-        k0, k1 = u("p7", 384, 512), u("p5", 0, 128)
-        mm([(k0, u("ONEB"), u("K9")), (k0, u("ONEF"), u("NFF")), (k0, u("TRIm"), u("WR"))])
-        mm([(k1, u("ONEB"), u("K12")), (k1, u("TRIm"), u("WR"))] if OPT["k1"] else [])
-        ts(u("SR"), k0, 0.0, A.is_lt)
+        k0, k1, k2 = u("p7", 384, 512), u("p5", 0, 128), u("p7", 0, 128)
+        mm(k0, (ONE, u("K9")), (u("ONEF"), u("NFF")), (u("TRIm"), WR))
+        mm(k1, (ONE, u("K11")), (u("TRIm"), WR))
+        ts(SR, k0, 0.0, A.is_lt)
         tt(u("KR", 128, 256), k1, u("CMK%d" % cl), A.min)
-        k2 = u("p7", 0, 128)
-        mm([(k2, u("ONEB"), u("K12")), (k2, u("TRIm"), u("LR")), (k2, u("NTRIm"), u("MR")), (k2, u("NTRIm"), u("SR"))])
+        mm(u("p4", 112, 120), (u("KR", 128, 256), u("blk")))
+        cp(u(rk, 8, 16), u("p4", 112, 120))
+        mm(k2, (ONE, u("K11")), (u("TRIm"), u("LR")), (u("NTRIm"), MR), (u("NTRIm"), SR))
         tt(u("KR", 0, 128), k2, u("CMR"), A.min)
-        if OPT["rk"]:
-            mm([(u("p4", 104, 112), u("KR", 0, 128), u("blk"))])
-            mm([(u("p4", 112, 120), u("KR", 128, 256), u("blk"))])
-            cp(u(rk), u("p4", 104, 120))
-        else:
-            mm([(u("p4", 112, 120), u("KR", 128, 256), u("blk"))])
-            cp(u(rk, 8, 16), u("p4", 112, 120))
-            mm([(u("p4", 104, 112), u("KR", 0, 128), u("blk"))])
-            cp(u(rk, 0, 8), u("p4", 104, 112))
-        xv = "XV%d" % t
-        cp(ix(u(xv), u(rk, 0, 8)), u("ZP"))
-        send(T.cores[(rank + 1 + t % 7) % 8], u(xv, 0, 32), "QI%d" % t, "rq%d" % t, "fq%d" % t, "lq%d" % t, 0, T.cores[(rank - 1 - t % 7) % 8])
-        q = u("p6", 0, 256)
-        mm([(q, u("ID16"), u("CNT")), (u("p6", 0, 128), u("PRE"), u("A4n")), (u("p6", 0, 128), u("P12"), u("MR")), (u("p6", 128, 256), u("P12"), u("SR"))])
-        relu(OPT["q"][0], u("QN"), q)
-        nt = u("p4", 120, 128)
-        mm([(nt, u("ID16"), u("CT")), (nt, u("QN", 0, 128), u("nblkb")), (nt, u("QN", 128, 256), u("nblkb"))])
-        ts(u("NT16"), nt, 640.0, A.add)
+        mm(u("p4", 104, 112), (u("KR", 0, 128), u("blk")))
+        cp(u(rk, 0, 8), u("p4", 104, 112))
+        cp(ix(u("XV%d" % t), u(rk, 0, 8)), u("ZP"))
+        send(T.cores[(rank + 1 + t % 7) % 8], u("XV%d" % t, 0, 32), "QI%d" % t, "rq%d" % t, "fq%d" % t, "lq%d" % t, T.cores[(rank - 1 - t % 7) % 8])
+        a, b = u("p6", 0, 128), u("p6", 128, 256)
+        mm(u("p6", 0, 256), (IDB, u("CNT")), (u("PRE"), u("A4n"), a), (u("P11"), MR, a), (u("P11"), SR, b))
+        act(u("QN"), u("p6", 0, 256), F.Relu)
+        mm(u("p4", 120, 128), (IDB, u("CT")), (u("QN", 0, 128), u("nblk")), (u("QN", 128, 256), u("nblk")))
+        ts(u("NT16"), u("p4", 120, 128), 640.0, A.add)
         tt(u("W", cl, 512, 4), ix(u("DS"), u("NT16")), u("OWNH"), A.add)
-        copy(OPT["q"][3], e16("ZE"), ix(u("FREE"), u(rk, 8, 16)))
-        q = u("p0", 0, 256)
-        mm([(q, u("ID16"), u("CTG")), (u("p0", 0, 128), u("NID16"), u("HD", 0, 128)), (u("p0", 0, 128), u("P11"), u("MR")),
-            (u("p0", 128, 256), u("P11"), u("SR")), (u("p0", 128, 256), e16("ZE"), u("HWN"))])
-        relu(OPT["q"][1], u("QR", 0, 256), q)
-        tg = u("p4", 128, 136)
-        mm([(tg, u("ID16"), u("CT")), (tg, u("QR", 0, 128), u("nblkf")), (tg, u("QR", 128, 256), u("nblkf"))])
-        ts(u("TG16"), tg, 512.0, A.add)
-        el = u("p1", 0, 128)
-        mm([(el, u("SL", 128, 256), u("ID16")), (el, u("MR"), u("N13"))])
-        relu(OPT["q"][2], u("ELS"), el)
+        act(ev, ix(u("FREE"), u(rk, 8, 16)), F.Copy)
+        a, b = u("p0", 0, 128), u("p0", 128, 256)
+        mm(u("p0", 0, 256), (IDB, u("CTG")), (NIDB, u("HD", 0, 128), a), (u("P11"), MR, a), (u("P11"), SR, b), (ev, u("HWN"), b))
+        act(u("QR", 0, 256), u("p0", 0, 256), F.Relu)
+        mm(u("p4", 128, 136), (IDB, u("CT")), (u("QR", 0, 128), u("nblkf")), (u("QR", 128, 256), u("nblkf")))
+        ts(u("TG16"), u("p4", 128, 136), 512.0, A.add)
+        mm(u("p1", 0, 128), (u("SL", 128, 256), IDB), (MR, u("N20")))
+        ts(u("ELS"), u("p1", 0, 128), 0.0, A.max)
         cp(ix(u("W"), u("TG16")), u("ELS"))
-        if t in OPT["alt"]:
-            copy(OPT["q"][6], u("ALT", cl, 512, 4), e16("ZE"))
-            cp(ix(u("ALT"), u("TG16")), e16("ZE"))
-        else:
-            part_move(t)
-        if t + 1 < RO:
-            mm([(u("p6", 424, 432), u("ONEB"), e16("ZM"))])
-            act(u("z8"), u("p6", 424, 432), F.Identity, bias=-0.9375, acc=u("mc", 4, 5))
-            c = 1.5 * 2.0 ** 27
-            ts(u("mc", 5, 6), u("mc", 4, 5), c, A.add, c, A.subtract)
-            ts(u("mc", 6, 7), u("mc", 4, 5), u("mc", 5, 6), A.subtract, 7.5, A.add)
-            act(u("THZ"), u("ROW1"), F.Identity, scale=u("mc", 6, 7))
-        if t in OPT["alt"] and t + 1 < RO:
-            part_movers(t)
-
-    def part_movers(t):
+        if t + 1 == RO:
+            act(u("ALT", cl, 512, 4), ev, F.Copy)
+            cp(ix(u("ALT"), u("TG16")), ev)
+            return
         a, b = u("p7", 128, 256), u("p7", 256, 384)
-        mm([(a, u("ONEB"), u("K14")), (a, u("ID16"), u("DMH")), (a, u("N13"), u("PRD")), (a, u("MR"), u("N13"))])
-        mm([(b, u("ONEB"), u("K14")), (b, u("ID16"), u("OWNH")), (b, u("N13"), u("L1T")), (b, u("SR"), u("N13"))])
+        mm(a, (ONE, u("K21")), (IDB, u("DMH")), (u("N20"), u("PRD")), (MR, u("N20")))
+        mm(b, (ONE, u("K21")), (IDB, u("OWNH")), (u("LN", 0, 128), u("N20")), (SR, u("N20")))
         tt(u("m1"), a, u("DUM", 0, 128), A.min)
         tt(u("m2"), b, u("m1"), A.min)
         cp(u("MVO"), u("m2"))
-        if "s" in OPT["mv"]:
-            cp(u("EV"), e16("ZE"))
+        for a in range(0, 2048, 512):
+            scan(u("VE", a, a + 512), u("MS", a, a + 512), u("ZE", a, a + 512), A.mult, A.add)
+            act(ix(u("OT"), u("MVO", a // 16, a // 16 + 32)), u("VE", a, a + 512), F.Silu)
+        mm(u("p6", 424, 432), (ONE, e16("ZM")))
+        act(u("z8"), u("p6", 424, 432), F.Identity, bias=-0.9375, acc=u("mc", 0, 1))
+        ts(u("mc", 1, 2), u("mc", 0, 1), 1.5 * 2.0 ** 27, A.add, 1.5 * 2.0 ** 27, A.subtract)
+        ts(u("mc", 2, 3), u("mc", 0, 1), u("mc", 1, 2), A.subtract, 7.5, A.add)
+        act(u("THZ"), u("ROW1"), F.Identity, scale=u("mc", 2, 3))
 
-    def part_move(t):
-        TAG[0] = "move%d" % t
-        if t not in OPT["alt"]:
-            part_movers(t)
-        n = len(OPT["mv"])
-        for h in range(n):
-            a, b = 2048 // n * h, 2048 // n * (h + 1)
-            to = ix(u("OT"), u("MVO", a // 16, b // 16))
-            if OPT["mv"][h] == "s":
-                act(u("VE", a, b), ix(u("EV"), u("CREP", a // 16, b // 16)), F.Copy)
-                act(to, u("VE", a, b), F.Silu)
-            elif OPT["mv"][h] == "w":
-                scan(u("VE", a, b), u("MS", a, b), u("ZE", a, b), A.mult, A.add)
-                act(to, u("VE", a, b), F.Silu)
-            else:
-                scan(u("VB", a, b), u("MS", a, b), u("ZE", a, b), A.mult, A.add)
-                cp(to, u("VB", a, b))
+    def wrap(lo, *pairs):
+        mm(u("p4", lo, lo + 32), (IDB, u("PENW")), *pairs)
+        scan(u("WP"), u("MS", 0, 32), u("p4", lo, lo + 32), A.mult, A.min)
+        return e16("WP", 15)
 
     def part_serve(t):
-        TAG[0] = "serve%d" % t
-        src = T.cores[(rank - 1 - t % 7) % 8]
-        qi, sn = "QI%d" % t, "SN%d" % t
+        qi = u("QI%d" % t)
         if t + 1 < RO:
-            iota(u("XV%d" % (t + 1)), [[0, 256]], 128, after=u(qi))
-        if t + 2 == RO:
-            iota(u("ALT"), [[0, 640]], 0, after=u(qi))
-        if t == 1:
-            iota(u("IDT", 0, 1024), [[1, 1024]], 0, after=u(qi))
-        if t == 2:
-            iota(u("IDT", 1024, 2064), [[1, 1040]], 1024, after=u(qi))
-        a = u("p4", 136, 138)
-        mm([(a, u("WTn"), u("ONEB", 0, 2))] + [(a, u("WY", 15 - j, 143 - j), e16(qi, j)) for j in range(16)])
-        cp(u("VI"), a)
+            iota(u("XV%d" % (t + 1)), [[0, 256]], 128, after=qi)
+        for o, pat, base in {1: [(u("IDT", 0, 1024), 1, 0)], 2: [(u("IDT", 1024, 2064), 1, 1024)], 3: [(u("ALT"), 0, 0)]}.get(t, []):
+            iota(o, [[pat, o[2]]], base, after=qi)
+        ts(u("VI"), wrap(192, (u("WTn"), u("ONEB", 0, 32)), (u("WTm"), qi)), -1.0, A.mult)
         ts(u("VI2"), u("VI"), 2047, A.bitwise_and)
         ts(u("VV16"), u("VI2"), 1, A.add)
-        ts(e16("QZ"), u(qi), -128.0, A.add)
+        ts(e16("QZ"), qi, -128.0, A.add)
         scan(u("QRp"), u("MS", 0, 512), u("QZ"), A.mult, A.add)
-        copy(OPT["ho"], u("HO"), ix(u("OT", 0, 2064), u("VV16")))
-        a = u("p4", 138, 140)
-        mm([(a, u("HY", 15 - j, 143 - j), e16("HO", j)) for j in range(16)])
-        if t in OPT["alt"]:
-            ts(u("O16"), a, -512.0, A.add)
+        act(u("HO"), ix(OWNERS, u("VV16")), F.Copy)
+        host = wrap(224, (u("HWN"), u("HO")))
+        if t + 1 == RO:
+            ts(u("O16"), host, -1.0, A.mult, -512.0, A.add)
             act(u("VR"), ix(u("IDT"), u("VV16")), F.Copy)
             act(u("PA"), ix(u("ALT"), u("O16")), F.Copy)
-            tt(u("EH"), ix(u("W", 0, 512), u("O16")), u("VR"), A.is_equal)
-            mm([(u("p4", 160, 192), u("BD"), u("EH"))])
+            tt(u("EH"), ix(LISTS, u("O16")), u("VR"), A.is_equal)
+            mm(u("p4", 160, 192), (BD, u("EH")))
             tt(u("PD"), u("HO"), u("PA"), A.subtract)
             tt(u("PM"), u("PD"), u("p4", 160, 192), A.mult)
-            a = u("p4", 142, 144)
-            mm([(a, u("HY", 15 - j, 143 - j), e16(x, j)) for x in ("PA", "PM") for j in range(16)])
-            if t + 1 < RO:
-                part_move(t)
-            TAG[0] = "serve%d" % t
-        ts(u("H16"), a, -512.0, A.add)
-        cp(u("HL"), ix(u("W", 0, 512), u("H16")))
-        k = u("p5")
+            host = wrap(256, (u("HWN"), u("PA")), (u("HWN"), u("PM")))
+        ts(u("H16"), host, -1.0, A.mult, -512.0, A.add)
+        cp(u("HL"), ix(LISTS, u("H16")))
+        pairs = [(ONE, u("KQ5")), (u("ID2x"), u("QRp"))]
         for a, b in ((0, 256), (256, 512)):
-            tt(u("QD", a, b), ix(win, u("HL", a // 16, b // 16)), u("QRp", a, b), A.subtract)
+            tt(u("QD", a, b), ix(X, u("HL", a // 16, b // 16)), u("QRp", a, b), A.subtract)
             act(u("QS", a, b), u("QD", a, b), F.Square)
-            x = u("p5", a, b)
-            mm([(x, u("ONEB"), u("KQ5", a, b)), (x, u("ID2x"), u("QRp", a, b)), (x, u("IDB"), u("QD", a, b)), (x, u("B512"), u("QS", a, b))])
-        scan(u("QR"), u("MIN5"), k, A.max, A.min)
-        low(u(sn), e16("QR", 15), u("hs"), 32)
-        send(src, u(sn), "RS%d" % t, "rs%d" % t, "fs%d" % t, "ls%d" % t, 1, T.cores[(rank + 1 + t % 7) % 8])
+            pairs += [(IDB, u("QD", a, b), u("p5", a, b)), (u("B512"), u("QS", a, b), u("p5", a, b))]
+        mm(u("p5"), *pairs)
+        scan(u("QR"), u("MIN5"), u("p5"), A.max, A.min)
+        low(u("SN%d" % t), e16("QR", 15), u("hs"), 32)
+        send(T.cores[(rank - 1 - t % 7) % 8], u("SN%d" % t), "RS%d" % t, "rs%d" % t, "fs%d" % t, "ls%d" % t, T.cores[(rank + 1 + t % 7) % 8])
 
     def part_apply(t):
-        TAG[0] = "apply%d" % t
-        xv = "XV%d" % t
-        if OPT["ap"][0] == "s":
-            act(u(xv, 0, 32), u("RS%d" % t), F.Identity, scale=0.5, bias=135.25)
-        else:
-            ts(u(xv, 0, 32), u("RS%d" % t), 0.5, A.mult, 135.25, A.add)
-        if OPT["ap"][1] == "s":
-            act(u("NV"), ix(u(xv), u("RK" + "ab"[t % 2], 0, 8)), F.Identity, bias=-128.0)
-        else:
-            ts(u("NV"), ix(u(xv), u("RK" + "ab"[t % 2], 0, 8)), -128.0, A.add)
-        cp(ix(win, u("S16" + "ab"[t % 2])), u("NV"))
+        ts(u("XV%d" % t, 0, 32), u("RS%d" % t), 0.5, A.mult, 135.25, A.add)
+        ts(u("NV"), ix(u("XV%d" % t), u("RK%d" % (t % 2), 0, 8)), -128.0, A.add)
+        cp(ix(X, u("S16%d" % (t % 2))), u("NV"))
 
-    part_own(0)
-    part_vacant(0)
-    part_split(0)
     for t in range(RO):
+        part_own(t)
+        part_vacant()
+        part_split(t)
+        if t:
+            part_apply(t - 1)
         part_near(t)
+        part_partner(t)
         part_finish(t)
         if t + 1 == RO:
-            ts(u("t512a"), u("W", 0, 512), 0.0, A.is_equal, 2049.0, A.mult)
-            act(u("p1"), u("W", 0, 512), F.Identity, bias=-1.0)
+            ts(u("t512a"), LISTS, 0.0, A.is_equal, 2049.0, A.mult)
+            act(u("p1"), LISTS, F.Identity, bias=-1.0)
             tt(u("YM"), u("t512a"), u("p1"), A.add)
-            dma("y", ext(T.ym[:], "out_m"), u("YM"), "st0")
+            dma(mark("ym", ap=T.ym[:]), u("YM"), "st0")
         part_serve(t)
-        if t + 1 < RO:
-            part_own(t + 1)
-            part_vacant(t + 1)
-            part_split(t + 1)
-        part_apply(t)
-    dma("y", ext(T.yx[:], "out_x"), u("X", 1, 2049), "st1")
+    part_apply(RO - 1)
+    dma(mark("yx", ap=T.yx[:]), u("X", 1, 2049), "st1")
 
     if "o" not in _ORDER:
         _ORDER["o"] = _order(ops)
@@ -1120,63 +773,48 @@ def rank_program(g, core, T, topo):
     known = {e: {} for e in E}
     snap, log, total = {}, {}, {}
 
-    def need(e, reads, writes):
+    def wait(e, reads, writes):
         w = {}
         for kind, lst in ((0, reads), (1, writes)):
             for (b, lo, hi) in lst:
-                psum = _psum(b)
                 for (l2, h2, e2, sem, val, wr) in log.get(b, ()):
-                    if psum:
-                        if e2 == e and (e == "p" or not (lo < h2 and l2 < hi and (kind or wr))):
-                            continue
-                    elif not (lo < h2 and l2 < hi and (kind or wr)):
-                        continue
-                    if w.get(sem, 0) < val:
-                        w[sem] = val
-        return w
-
-    def wait(e, w):
-        for sem in w:
-            if known[e].get(sem, 0) < w[sem]:
-                E[e].wait_ge(T.sem[sem], w[sem])
-                known[e][sem] = w[sem]
-                for s2, v2 in snap.get((sem, w[sem]), {}).items():
-                    if known[e].get(s2, 0) < v2:
-                        known[e][s2] = v2
+                    clash = lo < h2 and l2 < hi and (kind or wr)
+                    if (e2 != e or (e != "p" and clash)) if _psum(b) else clash:
+                        w[sem] = max(w.get(sem, 0), val)
+        for sem, val in w.items():
+            if known[e].get(sem, 0) < val:
+                E[e].wait_ge(T.sem[sem], val)
+                known[e][sem] = val
+                for s2, v2 in snap.get((sem, val), {}).items():
+                    known[e][s2] = max(known[e].get(s2, 0), v2)
 
     def note(e, reads, writes, sem, val):
-        d = dict(known[e])
-        d[sem] = max(d.get(sem, 0), val)
-        snap[(sem, val)] = d
+        snap[(sem, val)] = dict(known[e])
         total[sem] = val
         for (b, lo, hi) in writes:
-            old = log.get(b, [])
-            log[b] = [x for x in old if not (lo <= x[0] and x[1] <= hi and (x[2] == e or not _psum(b)))] + [(lo, hi, e, sem, val, True)]
+            log[b] = [x for x in log.get(b, []) if not (lo <= x[0] and x[1] <= hi and (x[2] == e or not _psum(b)))] + [(lo, hi, e, sem, val, True)]
         for (b, lo, hi) in reads:
-            old = log.get(b, [])
-            log[b] = [x for x in old if not (x[2] == e and not x[5] and lo <= x[0] and x[1] <= hi and x[3] == sem)] + [(lo, hi, e, sem, val, False)]
+            log[b] = [x for x in log.get(b, []) if not (x[2] == e and not x[5] and lo <= x[0] and x[1] <= hi and x[3] == sem)] + [(lo, hi, e, sem, val, False)]
 
     for i in _ORDER["o"]:
         o = ops[i]
         e, rd, wr = o["e"], o["rd"], o["wr"]
-        TAG[0] = o["tag"]
-        if o["items"]:
-            wait(e, need(e, [], wr))
-            n = len(o["items"])
-            for j, (x, a, b) in enumerate(o["items"]):
-                wait(e, need(e, a[1] + b[1], []))
-                ins = g.tensor.matmul(x[0], a[0], b[0], j == 0, j == n - 1)
-        elif o["land"]:
-            sem, nb, loc, n = o["land"]
-            wait(e, need(e, rd, []))
+        if o["land"]:
+            sem, landed, loc, left = o["land"]
+            wait(e, rd, [])
             o["fn"]()
-            note(e, rd, [], loc, n)
-            snap[(loc, n)] = {}
-            log[wr[0][0]] = [(wr[0][1], wr[0][2], "far", sem, nb, True)]
-            total[sem] = nb
+            note(e, rd, [], loc, left)
+            snap[(loc, left)] = {}
+            log[wr[0][0]] = [(wr[0][1], wr[0][2], "far", sem, landed, True)]
+            total[sem] = landed
             continue
+        if o["items"]:
+            wait(e, [], wr)
+            for j, (x, a, b) in enumerate(o["items"]):
+                wait(e, a[1] + b[1], [])
+                ins = g.tensor.matmul(x[0], a[0], b[0], j == 0, j == len(o["items"]) - 1)
         else:
-            wait(e, need(e, rd, wr))
+            wait(e, rd, wr)
             ins = o["fn"]()
         if o["dma"]:
             ins.then_inc(T.sem[o["dma"]], 16)
@@ -1185,7 +823,6 @@ def rank_program(g, core, T, topo):
             cnt[e] += 1
             ins.then_inc(T.sem[e], 1)
             note(e, rd, wr, e, cnt[e])
-    for sem in total:
-        n = total[sem]
+    for sem, n in total.items():
         if known["k"].get(sem, 0) < n:
             g.wait_ge(T.sem[sem], n)

@@ -1,8 +1,10 @@
+import math
 from concourse.mybir import AluOpType as A, ActivationFunctionType as F
 
 RO = 5
 S, B, H, I, U = "float32", "bfloat16", "float16", "int32", "uint16"
 LOW = 1 - 2 ** 24
+TAU = 4096.0
 _BUF = []
 
 
@@ -12,67 +14,67 @@ def _sb(dtype, cols, names):
 
 _sb(B, 2304, "X")
 _sb(B, 2048, "T MS VB US REP SQ AX AW SH OG DT DU Z0 Z1 ZE EXP")
+_sb(B, 1920, "YL")
 _sb(B, 1024, "EQ")
 _sb(B, 768, "XF")
-_sb(B, 640, "ALT")
+_sb(B, 240, "J240")
 _sb(B, 512, "CODE QD OCC PEN QZ QRp QS CG KQ5")
-_sb(B, 256, "ID2 KAp QN LN XC ZMW MWR")
+_sb(B, 256, "ID2 KAp QN LN XC ZMW MWR EE PEN2 M32")
 _sb(B, 144, "Jb Y")
-_sb(B, 128, "J4b J15b b1 b2 R16 MC NIDB BD NBD BTI ONEB PRE PRD LR SR XB SQS SQB NV SEL0R TRIm NTRIm HWN N27 N25 N20 P23 P15 P11 "
-            "RV0 RV1 RV2 KAs KAb KAd KAn K9 K11 K20 K21 WV A4n B4 CN1 QB ZP WTm WTn ID2x B512")
-_sb(B, 32, "OCb HO PA EH PD PM PENW")
-_sb(B, 8, "blk nblk w64k w8k w32 w2 og0 og1 og2 og3 SEL0 L2N THN THZ ROW1 SZ wp8 C25")
-_sb(H, 256, "SL CNT CTG KR")
+_sb(B, 128, "J4b J15b b1 b2 R16 MC IDB BD NBD BTI ONEB PRE PRD LR SR XB SQS SQB SEL0R TRIm NTRIm HWN N27 N25 N20 P23 P20 P11 "
+            "RV0 RV1 RV2 RV3 ST KAs KAb KAd KAn KAr KAm K9 K11 K20 PRL WV A4n B4 CN1 QB ZP0 ZP1 WTp IDh B256 B512 N512 HO PA EH PENW WM")
+_sb(B, 32, "OCb")
+_sb(B, 8, "blk nblk w64k w8k w32 w2 og0 og1 og2 og3 SEL0 L2N THN THZ ROW1 SZ wp8 C25 PB")
+_sb(H, 256, "SL CNT CTG ES")
 _sb(H, 144, "ZS HS ZB HB ZD HD")
-_sb(H, 128, "OWNH DMH DM2 CMR CMK0 CMK1 CMK2 CMK3")
+_sb(H, 128, "OWNH DMH DM2 CMK0 CMK1 CMK2 CMK3 KR KV SS m1 m2")
 _sb(H, 32, "CIX")
 _sb(H, 8, "CB")
 _sb(S, 4112, "OT")
-_sb(S, 2064, "IDT")
 _sb(S, 2048, "VE VG")
 _sb(S, 1536, "FREE")
 _sb(S, 768, "DS")
-_sb(S, 640, "W")
-_sb(S, 512, "J2f J3f t512a t512b YM QR DUM D1 MIN5")
-_sb(S, 264, "Aa")
-_sb(S, 256, "Pa Pb")
-_sb(S, 128, "MINs MINn MIN S10 S11 S2 S3 SB ELS m1 m2 IDF ONEF NFF")
+_sb(S, 640, "W ALT")
+_sb(S, 512, "J2f J3f t512a t512b YM QR DUM D1 MIN5 EV")
+_sb(S, 264, "Pa Pb")
+_sb(S, 256, "WP")
+_sb(S, 128, "MINs MINn MIN S10 S11 S2 S3 SB ELS IDF ONEF NFF VH VR HLA HWF DUL")
 _sb(S, 64, "PC")
-_sb(S, 32, "CS r1 r2 C512 hs VR WP")
+_sb(S, 32, "CS r1 r2 C512 hs ht")
 _sb(S, 16, "E16 KQ")
-_sb(S, 8, "nblkf hi8 hb8 z8 mc kq G4 EP sp4 kp4")
+_sb(S, 8, "blkf nblkf hi8 hb8 z8 mc kq G4 EP sp4 kp4")
 _sb(I, 2192, "AC4")
 _sb(I, 512, "MI")
 _sb(I, 8, "PIi a8 d8")
-_sb(I, 2, "LI WI VI VI2")
+_sb(I, 2, "LI WI")
 _sb(U, 512, "INO")
 _sb(U, 128, "OWN AN DM MVO")
 _sb(U, 32, "F16 HL")
-_sb(U, 16, "RK0 RK1")
-_sb(U, 8, "S160 S161 B16 D16 NT16 TG16 BT16")
-_sb(U, 2, "VV16 H16 O16")
+_sb(U, 8, "RK S16 B16 D16 NT16 TG16 BT16 VV16 H16 O16")
+_sb(U, 2, "S32")
 _AT, _end = {}, {}
 for _n, _c, _d in _BUF:
     _AT[_n] = ("ar_" + _d, _end.get(_d, 0), _c, _d)
     _end[_d] = _end.get(_d, 0) + -(-_c // 16) * 16
 SCRATCH = {"ar_" + _d: ("sbuf", [128, _c], _d) for _d, _c in _end.items()}
-for _n, _m, _o, _c in (("IDB", "ID2", 0, 128), ("ZM", "ZMW", 0, 128), ("ZW", "ZMW", 128, 128), ("MR", "MWR", 0, 128), ("WR", "MWR", 128, 128),
+for _n, _m, _o, _c in (("NIDB", "ID2", 0, 128), ("ZM", "ZMW", 0, 128), ("ZW", "ZMW", 128, 128), ("MR", "MWR", 0, 128), ("WR", "MWR", 128, 128),
                        ("ZALL", "ZS", 0, 864), ("MIN3", "MINs", 0, 384), ("CT", "CIX", 0, 8)):
     _AT[_n] = (_AT[_m][0], _AT[_m][1] + _o, _c, _AT[_m][3])
 for _t in range(RO):
-    for _n, _c in (("XV", 256), ("QI", 32), ("SN", 32), ("RS", 32)):
-        SCRATCH["%s%d" % (_n, _t)] = ("sbuf", [128, _c], B)
-        _AT["%s%d" % (_n, _t)] = ("%s%d" % (_n, _t), 0, _c, B)
+    for _n, _c, _d in (("QA", 128, B), ("SE", 2, U), ("QI", 2, U), ("SN", 32, B), ("RS", 32, B)):
+        SCRATCH["%s%d" % (_n, _t)] = ("sbuf", [128, _c], _d)
+        _AT["%s%d" % (_n, _t)] = ("%s%d" % (_n, _t), 0, _c, _d)
 for _k in range(8):
     SCRATCH["p%d" % _k] = ("psum", [128, 512], S)
     _AT["p%d" % _k] = ("p%d" % _k, 0, 512, S)
 SEMAPHORES = ["v", "p", "s", "k", "st0", "st1"] + ["ld%d" % i for i in range(10)] + ["cd%d" % i for i in range(9)]
 for _t in range(RO):
-    SEMAPHORES += [n + str(_t) for n in ("rq", "rs", "lq", "ls", "fq", "fs", "mq", "ms")]
+    SEMAPHORES += [a + b + str(_t) for a in "rlfm" for b in "aqs"]
 
 CYC, PEC, GAT, SCA, WAKE, XWAKE, WAY, FIRST = 0.00085, 0.0005, 1.6, 3.7, 0.24, 0.12, 2.3, 2.5
 VIEWS = ((0.27, 0.09, 1.0, 0.92, 0.8), (0.21, 0.16, 1.0, 0.92, 0.8), (0.27, 0.1, 1.22, 1.4, 1.65))
 RULES = ((3, 2, 0.1), (5, 2, 0.1), (8, 2, 0.1), (3, 2, 0.05), (5, 2, 0.05), (8, 2, 0.05), (5, 0, 0.1), (5, 1, 0.08), (12, 1, 0.08), (2, 1, 0.08))
+TURNS, EASE = 16000, 0.08
 _ORDER = {}
 
 
@@ -85,7 +87,7 @@ def _relay(topo, a, b):
 def _relay_program(g, core, T, topo):
     used = []
     for t in range(RO):
-        for back, (buf, arr, fwd, loc) in enumerate((("QI", "rq", "fq", "mq"), ("RS", "rs", "fs", "ms"))):
+        for back, buf, arr, fwd, loc in ((0, "QA", "ra", "fa", "ma"), (0, "QI", "rq", "fq", "mq"), (1, "RS", "rs", "fs", "ms")):
             for r in range(8):
                 x, y = T.cores[r], T.cores[(r + 1 + t % 7) % 8]
                 x, y = (y, x) if back else (x, y)
@@ -130,6 +132,12 @@ def _order(ops):
                         early[(j, i)] = at
                         break
                     at += _cycles(a, b) * PEC
+    sends = [i for i in range(n) if ops[i]["land"]]
+    for j, i in zip(sends, sends[1:]):
+        if j not in pred[i]:
+            pred[i].add(j)
+            succ[j].append(i)
+            early[(j, i)] = ops[j]["lat"]
     eng, cost, lat = [o["e"] for o in ops], [o["cost"] for o in ops], [o["lat"] for o in ops]
     banks = [sorted(set(b for (b, _l, _h) in o["rd"] + o["wr"] if _psum(b))) for o in ops]
     way0 = [0.0] * n
@@ -149,7 +157,7 @@ def _order(ops):
                        + [t + XWAKE for b in banks[i] for e, t in bank.get(b, {}).items() if e != eng[i]])
 
         def done(a, s, j):
-            return s + cost[a] + (WAKE if eng[a] == eng[j] else XWAKE) + (0.0 if back else lat[a]) - early.get((j, a) if back else (a, j), 0.0)
+            return s + cost[a] + (XWAKE if eng[a] != eng[j] else 0.0 if eng[a] == "p" else WAKE) + (0.0 if back else lat[a]) - early.get((j, a) if back else (a, j), 0.0)
         for _i in range(n):
             st = {i: can(i) for lst in ready.values() for i in lst}
             soon, front = {}, st
@@ -199,54 +207,75 @@ def _order(ops):
     views = []
     for wake, xw, mul, gat, sca in VIEWS:
         c = [cost[i] * (mul, gat, sca)[ops[i]["how"]] for i in range(n)]
-        views.append((c, xw, [[(j, c[j] + lat[j] + (wake if eng[j] == eng[i] else xw) - mul * early.get((j, i), 0.0)) for j in pred[i]] for i in range(n)]))
+        views.append((c, xw, [[(j, c[j] + lat[j] + (xw if eng[j] != eng[i] else 0.0 if eng[i] == "p" else wake) - mul * early.get((j, i), 0.0)) for j in pred[i]] for i in range(n)]))
 
-    def clock(order):
-        total, pairs = 0.0, []
-        for c, xw, inc in views:
-            start, by, last, user = [0.0] * n, [None] * n, {}, {}
-            for a in order:
-                s, w = 0.0, None
+    queue = ["vpsky".index(e) for e in eng]
+    mine = [[3 * int(b[1]) + queue[i] for b in banks[i]] for i in range(n)]
+    others = [[3 * int(b[1]) + e for b in banks[i] for e in range(3) if e != queue[i]] for i in range(n)]
+
+    def clock(order, at, old):
+        total, new = 0.0, []
+        for k, (c, xw, inc) in enumerate(views):
+            if old:
+                start, by, kept = old[k][0][:], old[k][1][:], old[k][2][:at // 64]
+                last, user = old[k][2][at // 64][0][:], old[k][2][at // 64][1][:]
+            else:
+                start, by, kept, last, user = [0.0] * n, [-1] * n, [], [-1] * 5, [-1] * 24
+            for pos in range(at // 64 * 64, n):
+                if pos % 64 == 0:
+                    kept.append((last[:], user[:]))
+                a = order[pos]
+                s, w = 0.0, -1
                 for j, d in inc[a]:
-                    if start[j] + d > s:
-                        s, w = start[j] + d, j
-                j = last.get(eng[a])
-                if j is not None and start[j] + c[j] > s:
+                    d += start[j]
+                    if d > s:
+                        s, w = d, j
+                j = last[queue[a]]
+                if j >= 0 and start[j] + c[j] > s:
                     s, w = start[j] + c[j], j
-                last[eng[a]] = a
-                for b in banks[a]:
-                    for e, j in user.setdefault(b, {}).items():
-                        if e != eng[a] and start[j] + c[j] + xw > s:
-                            s, w = start[j] + c[j] + xw, j
-                    user[b][eng[a]] = a
+                last[queue[a]] = a
+                for q in others[a]:
+                    j = user[q]
+                    if j >= 0 and start[j] + c[j] + xw > s:
+                        s, w = start[j] + c[j] + xw, j
+                for q in mine[a]:
+                    user[q] = a
                 start[a], by[a] = s, w
             a = max(order[-60:], key=lambda i: start[i] + c[i] + lat[i])
             total += start[a] + c[a] + lat[a]
-            while by[a] is not None:
+            new.append((start, by, kept, a))
+        return total / len(views), new
+
+    def chain(state):
+        pairs = []
+        for _start, by, _kept, a in state:
+            while by[a] >= 0:
                 if by[a] not in pred[a]:
                     pairs.append((by[a], a))
                 a = by[a]
-        return total / len(views), pairs
+        return pairs
     order = best[1]
-    span, pairs = clock(order)
-    seed = 12345
-    for _turn in range(2500):
+    span, state = clock(order, 0, None)
+    pairs, best, seed = chain(state), (span, order), 12345
+    for turn in range(TURNS):
         seed = (seed * 1103515245 + 12345) % 2147483648
         b, a = pairs[(seed >> 8) % len(pairs)]
-        mid = order[order.index(b):order.index(a) + 1]
-        up = (seed >> 4) & 1
+        i = order.index(b)
+        mid = order[i:order.index(a) + 1]
+        up = bool((seed >> 4) & 1)
         take = {a if up else b}
         for x in reversed(mid) if up else mid:
             if any(y in take for y in (succ[x] if up else pred[x])):
                 take.add(x)
         if (b if up else a) in take:
             continue
-        i = order.index(b)
-        trial = order[:i] + [x for x in mid if (x in take) == bool(up)] + [x for x in mid if (x in take) != bool(up)] + order[i + len(mid):]
-        s2, p2 = clock(trial)
-        if s2 <= span:
-            order, span, pairs = trial, s2, p2
-    return order
+        trial = order[:i] + [x for x in mid if (x in take) == up] + [x for x in mid if (x in take) != up] + order[i + len(mid):]
+        s2, new = clock(trial, i, state)
+        seed = (seed * 1103515245 + 12345) % 2147483648
+        if s2 <= span - EASE * 0.125 ** (turn / TURNS) * math.log((seed + 1) / 2147483648):
+            order, span, state, pairs = trial, s2, new, chain(new)
+            best = min(best, (span, order))
+    return best[1]
 
 
 def rank_program(g, core, T, topo):
@@ -336,12 +365,14 @@ def rank_program(g, core, T, topo):
         (b1, l1, h1), (b2, l2, h2) = dst[1][0], src[1][0]
         op("y", lambda: g.sync.dma_start(T[b1][row:128:16, l1:h1], T[b2][src_row:128:16, l2:h2]), outs, ins, 0.1, dma=sem, lat=2.5)
 
-    def send(dst, src, buf, sem, fwd, loc, back):
+    def send(src, buf, kind, t, way):
+        dst, back = T.cores[(rank + way * (1 + t % 7)) % 8], T.cores[(rank - way * (1 + t % 7)) % 8]
+        buf, sem, fwd, loc = buf + str(t), "r%s%d" % (kind, t), "f%s%d" % (kind, t), "l%s%d" % (kind, t)
         to, via = _relay(topo, core, dst), _relay(topo, back, core)
         d = dst if to is None else to
         rid, pid = topo.addr(d, core)
         op("k", lambda: g.remote_dma(T[buf][:], src[0], T.sem[sem if to is None else fwd], T.sem[loc], pid, rid, topo.mask(core, d)),
-           [u(buf)], [src], 0.3, lat=(WAY + (FIRST if buf == "QI0" else 0)) * (1 if to is None else 2),
+           [u(buf)], [src], 0.3, lat=(WAY + (FIRST if buf == "QA0" else 0)) * (1 if to is None else 2),
            land=(sem, len(topo.engines(back if via is None else via, core)), loc, len(topo.engines(core, d))))
 
     def sums(ps, base, src, w):
@@ -388,7 +419,7 @@ def rank_program(g, core, T, topo):
     iota(u("PC", 4, 8), [[1, 4]], 1024, 4)
     iota(u("PC", 8, 10), [[512, 2]], 8192 - 1536, 1)
     iota(u("PC", 10, 11), [[0, 1]], 128, 1)
-    for o, val in ((u("FREE", 0, 1024), 0), (u("Z1"), 0), (u("QZ"), 0), (u("DS", 640, 768), 0), (u("XV0"), 128), (u("MIN5"), LOW), (e16("MIN5"), -LOW)):
+    for o, val in ((u("FREE", 0, 1024), 0), (u("Z1"), 0), (u("QZ"), 0), (u("DS", 640, 768), 0), (u("ALT"), 0), (u("MIN5"), LOW), (e16("MIN5"), -LOW)):
         iota(o, [[0, o[2]]], val)
     for o, val in ((u("MS"), 1.0), (e16("MS"), 0.0), (u("ZE"), 0.0), (u("Z0"), 0.0), (u("OT", 0, 8), 0.0), (u("OT", 2048, 2064), 0.0), (u("W", 512, 640), 0.0)):
         fill(o, val)
@@ -435,30 +466,43 @@ def rank_program(g, core, T, topo):
     for name, src, val in (("nblk", "blk", -1.0), ("nblkf", "blk", -1.0), ("w64k", "blk", 65536.0), ("w8k", "blk", 8192.0), ("w32", "blk", 32.0),
                            ("NBD", "BD", -1.0), ("IDF", "IDB", 1.0), ("SEL0R", "BD", row0), ("SEL0", "blk", row0), ("N25", "SEL0R", -2.0 ** 25),
                            ("NIDB", "IDB", -1.0), ("N27", "IDB", -2.0 ** 27), ("N20", "IDB", -2.0 ** 20), ("P23", "IDB", 2.0 ** 23),
-                           ("P11", "IDB", 2.0 ** 11), ("RV0", "IDB", -49152.0), ("RV1", "IDB", -24576.0), ("RV2", "IDB", -12288.0)):
+                           ("P11", "IDB", 2.0 ** 11), ("RV0", "IDB", 90.0 * TAU), ("RV1", "IDB", 30.0 * TAU), ("RV2", "IDB", 10.0 * TAU),
+                           ("RV3", "IDB", -54.0 * TAU), ("P20", "IDB", 2.0 ** 20)):
         act(u(name), u(src), F.Identity, scale=val)
     act(u("CN1"), u("R16"), F.Identity, scale=8192.0, bias=-8192.0)
-    act(u("ID2", 128, 256), IDB, F.Identity)
+    act(u("ID2", 128, 256), IDB, F.Identity, scale=-1.0)
     first[0] = 0
     ts(u("MC"), J15, P15, A.is_le)
     fill(e16("MC"), 0.0)
     fill(ONE, 1.0)
     ts(u("ZALL"), u("MS", 0, 864), 0.0, A.mult)
-    for name, slope, c1, c2 in (("KAs", 4096.0, 2.0 ** 27, -1088.0), ("KAb", -1.0, -2.0 ** 23, 7.0), ("KAn", 512.0, 2.0 ** 24, 0.0), ("KQ5", 32.0, -15.0, 0.0)):
+    for name, slope, c1, c2 in (("KAs", 4096.0, 2.0 ** 27, -1088.0), ("KAb", -1.0, -2.0 ** 23, 7.0), ("KAn", 512.0, 2.0 ** 24, 0.0), ("KQ5", 16.0, -7.25, 0.0),
+                                ("KAr", -1.0, 2048.0, 0.0), ("KAm", 0.0, 2.0 ** 21, -1536.0)):
         b = col(u("EP", 1, 2), c1, A.mult)
         if c2:
             ts(b, u("EP", 2, 3), c2, A.mult, b, A.add)
         ts(u(name, 0, 128), J15, col(u("EP", 0, 1), slope, A.mult), A.mult, b, A.add)
+    b = col(u("EP", 1, 2), -128.0 * 160 * TAU, A.mult)
+    ts(b, u("EP", 2, 3), -2.0 * 160 * TAU, A.mult, b, A.add)
+    ts(b, u("EP", 3, 4), 81.0 * TAU, A.mult, b, A.add)
+    ts(u("KAp"), u("MS", 0, 256), 0.0, A.mult, b, A.add)
     cp(u("KQ5", 128, 256), u("KQ5", 0, 128))
     cp(u("KQ5", 256, 512), u("KQ5", 0, 256))
-    for o, val in ((u("KAd"), 2 ** 20), (u("K11"), 2 ** 4), (u("K20"), 2 ** 13), (u("K21"), 2 ** 14), (u("THZ"), 0), (u("MIN3"), LOW), (u("ZMW"), 0),
-                   (u("K9"), 12), (u("ONEF"), 1), (u("KAp"), 21 * 32 * 160), (e16("KAd", 15), 0), (u("Aa", 256, 264), 0), (e16("MIN"), -LOW), (u("CODE"), 0)):
+    for o, val in ((u("KAd"), 2 ** 20), (u("K11"), 2 ** 4), (u("K20"), 2 ** 13), (u("THZ"), 0), (u("MIN3"), LOW), (u("ZMW"), 0),
+                   (u("K9"), 12), (u("ONEF"), 1), (e16("KAd", 15), 0), (u("Pa", 256, 264), 2 ** 20), (u("Pb", 256, 264), 2 ** 20), (e16("MIN"), -LOW), (u("CODE"), 0)):
         iota(o, [[0, o[2]]], val)
     fill(u("C25"), 2.0 ** 25)
     iota(e16("MINs"), [[0, 8]], 255 * 65536 + 2049 - 1088, 1)
     hw = col(P15, 4.0, A.is_lt, P15, A.mult)
     ts(hw, hw, 1.0 / 64, A.mult, col(row4, 4.0, A.mult), A.add)
     ts(u("HWN"), NBD, hw, A.mult)
+    ts(u("HWF"), NBD, hw, A.mult)
+    iota(u("DUL"), [[0, 16], [128, 8]], 2064 - 1536, 1)
+    iota(u("J240"), [[1, 240]], 0)
+    cp(u("blkf"), u("blk"))
+    at = col(P15, 112.0, A.add)
+    for j in range(8):
+        ts(u("YL", 240 * j, 240 * j + 240), u("J240"), at, A.is_equal, u("blkf", j, j + 1), A.mult)
     ts(u("kq", 0, 4), u("E16", 0, 4), 2.0 ** 19, A.mult, hw, A.add)
     for c in range(4):
         ts(u("og%d" % c), u("blk"), u("kq", c, c + 1), A.mult)
@@ -474,15 +518,26 @@ def rank_program(g, core, T, topo):
     tt(u("PEN", 0, 128), u("b1"), u("b2"), A.add)
     cp(u("PEN", 128, 256), u("PEN", 0, 128))
     cp(u("PEN", 256, 512), u("PEN", 0, 256))
-    for name, src, val in (("P15", IDB, 32768.0), ("w2", u("blk"), 2.0), ("ID2x", IDB, 2.0), ("B512", BD, 512.0)):
+    for name, src, val in (("w2", u("blk"), 2.0), ("IDh", IDB, 0.5), ("B256", BD, 256.0), ("B512", BD, 512.0), ("N512", BD, -512.0)):
         ts(u(name), src, val, A.mult)
-    ts(u("CMR"), u("R16"), u("PC", 10, 11), A.mult)
     for c in range(4):
         ts(u("CMK%d" % c), u("R16"), u("PC", 4 + c, 5 + c), A.mult)
     for q, val in enumerate((640 - 2048, 128 - 2048)):
         ts(u("CNT", 128 * q, 128 * q + 128), u("R16"), 8192.0 + val, A.mult, -8192.0, A.add)
         ts(u("CTG", 128 * q, 128 * q + 128), u("R16"), u("PC", 8 + q, 9 + q), A.mult, -8192.0, A.add)
-    ts(u("PENW"), u("R16", 0, 32), -2.0 ** 17, A.mult, 2.0 ** 17, A.add)
+    ts(u("PENW"), u("R16"), -2.0 ** 17, A.mult, 2.0 ** 17, A.add)
+    ts(u("PEN2", 0, 256, 2), u("R16"), 512 - 2.0 ** 17, A.mult, 2.0 ** 17, A.add)
+    cp(u("PEN2", 1, 256, 2), u("PENW"))
+    iota(u("M32"), [[0, 256]], 1)
+    iota(u("M32", 0, 256, 32), [[0, 8]], 0)
+    ts(u("b1"), J15, col(P15, 1.0, A.add), A.is_equal, 4096.0, A.mult)
+    ts(u("b2"), u("R16"), -2.0 ** 20, A.mult)
+    tt(u("WM"), u("b1"), u("b2"), A.add)
+    held = col(P15, 15.0, A.is_lt, 4096.0, A.mult)
+    spare = [col(P15, 2177.0 + 16 * q, A.add) for q in range(2)]
+    cp(u("PB", 0, 1), P)
+    fill(u("PB", 1, 2), 1088.0 - 4096.0)
+    ts(u("KV"), J, 0.0, A.mult, -1023.5, A.add)
     ts(u("CIX"), u("Jb", 0, 32), 16.0, A.mult, P15, A.add)
     ts(u("CB"), u("CT"), 16.0, A.mult, 7.0, A.add)
     ts(u("C512"), u("CIX"), 512.0, A.add)
@@ -500,8 +555,7 @@ def rank_program(g, core, T, topo):
         ts(u("KQ", 4 * q, 4 * q + 4), u("kp4", 0, 4), u("G4", q, q + 1), A.mult)
     ts(u("PC", 12, 14), u("LI"), -65536.0, A.mult)
     wt = col(u("WI", 0, 1), 1.0, A.mult)
-    ts(u("WTm"), NBD, wt, A.mult)
-    ts(u("WTn"), BD, wt, A.mult, 128.0, A.mult)
+    ts(u("WTp"), BD, wt, A.mult)
     less = col(u("EP", 1, 2), -2048.0, A.mult)
     ts(u("L2N"), u("SEL0"), u("PC", 13, 14), A.mult, less, A.add)
     ts(u("THN"), u("SEL0"), u("PC", 12, 13), A.mult, less, A.add)
@@ -513,7 +567,7 @@ def rank_program(g, core, T, topo):
     ts(u("A4n"), BD, fourth, A.mult)
     ts(u("B4"), BD, col(fourth, 4.0, A.mult, 128.0, A.add), A.mult)
 
-    X, LISTS, OWNERS = u("X", 0, 2192), u("W", 0, 512), u("OT", 0, 2064)
+    X, LISTS, OWNERS = u("X", 0, 2224), u("W", 0, 512), u("OT", 0, 2064)
 
     def gather(out, off, cut):
         cp(u(out, 0, 16 * cut), ix(X, u(off, 0, cut)))
@@ -521,7 +575,7 @@ def rank_program(g, core, T, topo):
             act(u(out, 16 * cut, 2048), ix(X, u(off, cut, 128)), F.Copy)
 
     def part_own(t):
-        z, s1, s16 = "Z%d" % (t % 2), "S1%d" % (t % 2), "S16%d" % (t % 2)
+        z, s1, s16 = "Z%d" % (t % 2), "S1%d" % (t % 2), "S16"
         lanes = u("W", t % 4, 512, 4)
         cp(u("OWN"), lanes)
         gather("T", "OWN", 112 if t else 128)
@@ -537,6 +591,9 @@ def rank_program(g, core, T, topo):
         tile("ZS", "HS", u("p4", 0, 8), 1)
         ts(u(s16), u("p4", 0, 8), 1088.0, A.add)
         cp(e16(z), ix(X, u(s16)))
+        act(u("ZP%d" % (t % 2)), e16(z), F.Copy)
+        send(u("ZP%d" % (t % 2)), "QA", "a", t, 1)
+        scan(u("SS"), u("MS", 0, 128), u("ZS", 0, 128), A.mult, A.add)
         ts(u("AN"), ix(u("AC4"), u(s16)), 1, A.add)
         scan(u("REP"), u("MS"), u(z), A.mult, A.add)
         scan(u("US"), u("MS"), u("T"), A.mult, A.max)
@@ -564,12 +621,13 @@ def rank_program(g, core, T, topo):
 
     def part_split(t):
         s = e16("Z%d" % (t % 2))
+        mm(u("p6", 288, 416), (s, NIDB))
+        act(u("ST"), u("p6", 288, 416), F.Copy)
         for c in range(4):
             a, b, ps = 512 * c, 512 * c + 512, u("p%d" % (c % 3))
-            mm(ps, (IDB, u("T", a, b)), (NIDB, u("REP", a, b)))
+            mm(ps, (IDB, u("T", a, b)), (u("ST"), u("EXP", a, b)))
             act(u("SQ", a, b), ps, F.Square)
         act(u("SQS"), s, F.Square)
-        act(u("ZP"), s, F.Identity, bias=128.0)
         k = u("p3", 128, 256)
         mm(k, (ONE, u("KAb")), (u("PRE"), u("P23")), *sums("p3", 128, "SQ", "w32"))
         scan(u("SB"), u("MS", 0, 128), k, A.mult, A.max)
@@ -592,22 +650,24 @@ def rank_program(g, core, T, topo):
         for q in range(3):
             ts(u("XF", 256 * q, 256 * q + 256), u("XC"), 0.5 ** (q + 1), A.mult, 159.5 + 0.5 ** (q + 2), A.add)
         pp = u("p7", 128, 384)
-        mm(pp, (ONE, u("KAp")), (u("OWNH"), u("ID2")), (u("N20"), u("LN")), (u("P15"), u("XC")),
-           *[(u("RV%d" % q), u("XF", 256 * q, 256 * q + 256)) for q in range(3)])
-        ts(u("Pa"), pp, 0.0, A.max)
-        for q in range(4):
-            a, b, th = "Pb" if q % 2 else "Pa", ("Pb", "Pa", "Pb", "SL")[q], 2.0 ** (15 - q)
-            act(u("Aa", 0, 256), u(a), F.Relu, bias=-th)
-            act(u("p5", 0, 256), u(a), F.Relu, scale=2.0 ** 18, bias=(0.5 - th) * 2.0 ** 18)
-            tt(u("p5", 256, 512), u(a), u("p5", 0, 256), A.subtract)
-            tt(u(b), u("p5", 256, 512), u("Aa", 1 << q, 256 + (1 << q)), A.max)
-        mm(u("p6", 288, 416), (u("SL", 0, 128), IDB), (NIDB, u("OWNH")))
+        mm(pp, (ONE, u("KAp")), *[(u("RV%d" % q), u("XF", 256 * q, 256 * q + 256)) for q in range(3)],
+           (u("P20"), u("LN")), (u("RV3"), u("XC")), (u("OWNH"), u("ID2")))
+        act(u("Pa", 0, 256), pp, F.Abs, bias=-54.0 * TAU)
+        tt(u("Pa", 0, 255), u("p7", 129, 384), u("Pa", 0, 255), A.min)
+        for q, a, b in ((1, "Pa", "Pb"), (2, "Pb", "Pa"), (3, "Pa", "Pb")):
+            act(u("p5", 0, 256), u(a, 0, 256), F.Abs, bias=-2.0 * 3 ** (3 - q) * TAU)
+            tt(u(b, 0, 256), u("p5", 0, 256), u(a, 1 << q, 256 + (1 << q)), A.min)
+        ts(u("SL"), u("Pb", 0, 256), TAU, A.min, TAU, A.subtract)
+        mm(u("p6", 288, 416), (u("SL", 0, 128), NIDB), (NIDB, u("OWNH")))
         cp(u("DS", 512, 640), u("p6", 288, 416))
 
     def part_near(t):
         iota(e16("MINn"), [[0, 8]], 13 * 2 ** 20 + t % 4)
         for a in (0, 64):
-            act(u("OG", 16 * a, 16 * a + 1024), ix(OWNERS, u("AN", a, a + 64)), F.Copy)
+            if t:
+                act(u("OG", 16 * a, 16 * a + 1024), ix(OWNERS, u("AN", a, a + 64)), F.Copy)
+            else:
+                cp(u("OG", 16 * a, 16 * a + 1024), ix(OWNERS, u("AN", a, a + 64)))
         for a, b in ((0, 56), (56, 104), (104, 128)):
             tt(u("AX", 16 * a, 16 * b), ix(X, u("AN", a, b)), u("REP", 16 * a, 16 * b), A.subtract)
             act(u("DU", 16 * a, 16 * b), u("AX", 16 * a, 16 * b), F.Square)
@@ -653,7 +713,7 @@ def rank_program(g, core, T, topo):
                 cp(u("DM2"), ix(u("D1"), u("BT16")))
 
     def part_finish(t):
-        cl, rk, ev = t % 4, "RK%d" % (t % 2), e16("ZE")
+        cl, ev = t % 4, u("EV", 0, 128)
         MR, WR, SR = u("MR"), u("WR"), u("SR")
         tt(e16("ZM"), e16("S3", 15), u("p4", 96, 104), A.is_ge)
         tt(e16("ZW"), u("wp8"), e16("ZM"), A.is_gt)
@@ -662,92 +722,100 @@ def rank_program(g, core, T, topo):
         mm(k0, (ONE, u("K9")), (u("ONEF"), u("NFF")), (u("TRIm"), WR))
         mm(k1, (ONE, u("K11")), (u("TRIm"), WR))
         ts(SR, k0, 0.0, A.is_lt)
-        tt(u("KR", 128, 256), k1, u("CMK%d" % cl), A.min)
-        mm(u("p4", 112, 120), (u("KR", 128, 256), u("blk")))
-        cp(u(rk, 8, 16), u("p4", 112, 120))
-        mm(k2, (ONE, u("K11")), (u("TRIm"), u("LR")), (u("NTRIm"), MR), (u("NTRIm"), SR))
-        tt(u("KR", 0, 128), k2, u("CMR"), A.min)
-        mm(u("p4", 104, 112), (u("KR", 0, 128), u("blk")))
-        cp(u(rk, 0, 8), u("p4", 104, 112))
-        cp(ix(u("XV%d" % t), u(rk, 0, 8)), u("ZP"))
-        send(T.cores[(rank + 1 + t % 7) % 8], u("XV%d" % t, 0, 32), "QI%d" % t, "rq%d" % t, "fq%d" % t, "lq%d" % t, T.cores[(rank - 1 - t % 7) % 8])
+        tt(u("KR"), k1, u("CMK%d" % cl), A.min)
+        mm(u("p4", 112, 120), (u("KR"), u("blk")))
+        cp(u("RK"), u("p4", 112, 120))
+        mm(k2, (ONE, u("KAr")), (u("TRIm"), u("LR")), (u("NTRIm"), MR), (u("NTRIm"), SR))
+        for q in range(2):
+            ts(u("EE", 128 * q, 128 * q + 128), k2, 16.0 * q, A.is_equal)
+            mm(u("p4", 104 + q, 105 + q), (u("EE", 128 * q, 128 * q + 128), u("PB", 0, 1)))
+        cp(u("SE%d" % t), u("p4", 104, 106))
+        send(u("SE%d" % t), "QI", "q", t, 1)
+        for q in range(2):
+            e, ps = u("EE", 128 * q, 128 * q + 128), u("p4", 106 + q, 107 + q)
+            tt(u("ES", 128 * q, 128 * q + 128), e, u("SS"), A.mult)
+            mm(ps, (e, u("PB", 1, 2)), (u("ES", 128 * q, 128 * q + 128), u("ONEB", 0, 1)))
+            ts(u("S32", q, q + 1), ps, 4096.0, A.add, spare[q], A.min)
         a, b = u("p6", 0, 128), u("p6", 128, 256)
         mm(u("p6", 0, 256), (IDB, u("CNT")), (u("PRE"), u("A4n"), a), (u("P11"), MR, a), (u("P11"), SR, b))
         act(u("QN"), u("p6", 0, 256), F.Relu)
         mm(u("p4", 120, 128), (IDB, u("CT")), (u("QN", 0, 128), u("nblk")), (u("QN", 128, 256), u("nblk")))
         ts(u("NT16"), u("p4", 120, 128), 640.0, A.add)
         tt(u("W", cl, 512, 4), ix(u("DS"), u("NT16")), u("OWNH"), A.add)
-        act(ev, ix(u("FREE"), u(rk, 8, 16)), F.Copy)
+        act(ev, ix(u("FREE"), u("RK")), F.Copy)
         a, b = u("p0", 0, 128), u("p0", 128, 256)
-        mm(u("p0", 0, 256), (IDB, u("CTG")), (NIDB, u("HD", 0, 128), a), (u("P11"), MR, a), (u("P11"), SR, b), (ev, u("HWN"), b))
+        mm(u("p0", 0, 256), (IDB, u("CTG")), (NIDB, u("HD", 0, 128), a), (u("P11"), MR, a), (u("P11"), SR, b), (ev, u("HWF"), b))
         act(u("QR", 0, 256), u("p0", 0, 256), F.Relu)
         mm(u("p4", 128, 136), (IDB, u("CT")), (u("QR", 0, 128), u("nblkf")), (u("QR", 128, 256), u("nblkf")))
         ts(u("TG16"), u("p4", 128, 136), 512.0, A.add)
-        mm(u("p1", 0, 128), (u("SL", 128, 256), IDB), (MR, u("N20")))
+        mm(u("p1", 0, 128), (u("SL", 128, 256), NIDB), (MR, u("N20")))
         ts(u("ELS"), u("p1", 0, 128), 0.0, A.max)
         cp(ix(u("W"), u("TG16")), u("ELS"))
+        act(u("ALT", cl, 512, 4), ev, F.Copy)
+        cp(ix(u("ALT"), u("TG16")), ev)
         if t + 1 == RO:
-            act(u("ALT", cl, 512, 4), ev, F.Copy)
-            cp(ix(u("ALT"), u("TG16")), ev)
             return
         a, b = u("p7", 128, 256), u("p7", 256, 384)
-        mm(a, (ONE, u("K21")), (IDB, u("DMH")), (u("N20"), u("PRD")), (MR, u("N20")))
-        mm(b, (ONE, u("K21")), (IDB, u("OWNH")), (u("LN", 0, 128), u("N20")), (SR, u("N20")))
-        tt(u("m1"), a, u("DUM", 0, 128), A.min)
+        ts(u("PRL"), u("SL", 128, 256), 0.0, A.is_lt)
+        mm(a, (ONE, u("KAm")), (u("DMH"), IDB), (u("PRD"), u("N20")), (u("N20"), MR))
+        mm(b, (ONE, u("KAm")), (NIDB, u("SL", 128, 256)), (u("N20"), u("PRL")), (u("N20"), SR))
+        tt(u("m1"), a, u("DUL"), A.min)
         tt(u("m2"), b, u("m1"), A.min)
-        cp(u("MVO"), u("m2"))
-        for a in range(0, 2048, 512):
-            scan(u("VE", a, a + 512), u("MS", a, a + 512), u("ZE", a, a + 512), A.mult, A.add)
-            act(ix(u("OT"), u("MVO", a // 16, a // 16 + 32)), u("VE", a, a + 512), F.Silu)
+        for j in range(8):
+            mm(u("p1", 128 + j, 248, 8), *[(u("YL", 240 * j + 112 - 16 * q, 240 * j + 240 - 16 * q), u("m2", 16 * q, 16 * q + 15)) for q in range(8)])
+        ts(u("MVO", 0, 120), u("p1", 128, 248), 1536.0, A.add)
+        cp(u("EV", 128, 256), ev)
+        cp(u("EV", 256, 512), u("EV", 0, 256))
+        for a in range(0, 120, 32):
+            b = min(a + 32, 120)
+            act(ix(u("OT"), u("MVO", a, b)), u("EV", 0, 16 * (b - a)), F.Silu)
         mm(u("p6", 424, 432), (ONE, e16("ZM")))
         act(u("z8"), u("p6", 424, 432), F.Identity, bias=-0.9375, acc=u("mc", 0, 1))
         ts(u("mc", 1, 2), u("mc", 0, 1), 1.5 * 2.0 ** 27, A.add, 1.5 * 2.0 ** 27, A.subtract)
         ts(u("mc", 2, 3), u("mc", 0, 1), u("mc", 1, 2), A.subtract, 7.5, A.add)
         act(u("THZ"), u("ROW1"), F.Identity, scale=u("mc", 2, 3))
 
-    def wrap(lo, *pairs):
-        mm(u("p4", lo, lo + 32), (IDB, u("PENW")), *pairs)
-        scan(u("WP"), u("MS", 0, 32), u("p4", lo, lo + 32), A.mult, A.min)
-        return e16("WP", 15)
+    def part_look(t):
+        qa, a, b, c = u("QA%d" % t), u("p2", 0, 128), u("p2", 128, 256), u("p2", 256, 384)
+        mm(a, (IDB, u("KV")), (u("WTp"), qa))
+        mm(b, (IDB, ONE), (u("WTp"), qa))
+        ts(u("VH"), a, 1.5 * 2.0 ** 34, A.add, 1.5 * 2.0 ** 34, A.subtract)
+        tt(u("VR"), b, u("VH"), A.subtract)
+        scan(u("WP", 0, 128), u("WM"), u("VR"), A.add, A.max)
+        ts(u("VV16"), e16("WP", 15, 128), held, A.subtract)
+        act(u("HO"), ix(OWNERS, u("VV16")), F.Copy)
+        mm(c, (IDB, u("PENW")), (u("HWN"), u("HO")))
+        scan(u("WP", 0, 128), u("MS", 0, 128), c, A.mult, A.min)
+        ts(u("O16"), e16("WP", 15, 128), -1.0, A.mult, -512.0, A.add)
+
+    def part_host(t):
+        act(u("PA"), ix(u("ALT"), u("O16")), F.Copy)
+        tt(u("EH"), ix(LISTS, u("O16")), u("VR"), A.is_equal)
+        a, b = u("p2", 0, 256, 2), u("p2", 1, 256, 2)
+        mm(u("p2", 0, 256), (IDB, u("PEN2")), (u("HWN"), u("HO"), a), (u("HWN"), u("PA"), b), (u("N512"), u("EH"), a), (u("B512"), u("EH"), b))
+        scan(u("WP"), u("M32"), u("p2", 0, 256), A.mult, A.min)
+        ts(u("H16"), u("WP", 31, 256, 32), -1.0, A.mult, -512.0, A.add)
+        cp(u("HLA"), ix(LISTS, u("H16")))
 
     def part_serve(t):
         qi = u("QI%d" % t)
-        if t + 1 < RO:
-            iota(u("XV%d" % (t + 1)), [[0, 256]], 128, after=qi)
-        for o, pat, base in {1: [(u("IDT", 0, 1024), 1, 0)], 2: [(u("IDT", 1024, 2064), 1, 1024)], 3: [(u("ALT"), 0, 0)]}.get(t, []):
-            iota(o, [[pat, o[2]]], base, after=qi)
-        ts(u("VI"), wrap(192, (u("WTn"), u("ONEB", 0, 32)), (u("WTm"), qi)), -1.0, A.mult)
-        ts(u("VI2"), u("VI"), 2047, A.bitwise_and)
-        ts(u("VV16"), u("VI2"), 1, A.add)
-        ts(e16("QZ"), qi, -128.0, A.add)
-        scan(u("QRp"), u("MS", 0, 512), u("QZ"), A.mult, A.add)
-        act(u("HO"), ix(OWNERS, u("VV16")), F.Copy)
-        host = wrap(224, (u("HWN"), u("HO")))
-        if t + 1 == RO:
-            ts(u("O16"), host, -1.0, A.mult, -512.0, A.add)
-            act(u("VR"), ix(u("IDT"), u("VV16")), F.Copy)
-            act(u("PA"), ix(u("ALT"), u("O16")), F.Copy)
-            tt(u("EH"), ix(LISTS, u("O16")), u("VR"), A.is_equal)
-            mm(u("p4", 160, 192), (BD, u("EH")))
-            tt(u("PD"), u("HO"), u("PA"), A.subtract)
-            tt(u("PM"), u("PD"), u("p4", 160, 192), A.mult)
-            host = wrap(256, (u("HWN"), u("PA")), (u("HWN"), u("PM")))
-        ts(u("H16"), host, -1.0, A.mult, -512.0, A.add)
-        cp(u("HL"), ix(LISTS, u("H16")))
-        pairs = [(ONE, u("KQ5")), (u("ID2x"), u("QRp"))]
+        cp(e16("QZ"), ix(u("QA%d" % t), qi))
+        cp(u("HL"), ix(u("HLA"), qi))
+        pairs = [(ONE, u("KQ5"))]
         for a, b in ((0, 256), (256, 512)):
+            scan(u("QRp", a, b), u("MS", a, b), u("QZ", a, b), A.mult, A.add)
             tt(u("QD", a, b), ix(X, u("HL", a // 16, b // 16)), u("QRp", a, b), A.subtract)
             act(u("QS", a, b), u("QD", a, b), F.Square)
-            pairs += [(IDB, u("QD", a, b), u("p5", a, b)), (u("B512"), u("QS", a, b), u("p5", a, b))]
+            pairs += [(IDB, u("QRp", a, b), u("p5", a, b)), (u("IDh"), u("QD", a, b), u("p5", a, b)), (u("B256"), u("QS", a, b), u("p5", a, b))]
         mm(u("p5"), *pairs)
         scan(u("QR"), u("MIN5"), u("p5"), A.max, A.min)
-        low(u("SN%d" % t), e16("QR", 15), u("hs"), 32)
-        send(T.cores[(rank - 1 - t % 7) % 8], u("SN%d" % t), "RS%d" % t, "rs%d" % t, "fs%d" % t, "ls%d" % t, T.cores[(rank + 1 + t % 7) % 8])
+        ts(u("hs"), e16("QR", 15), 1.5 * 2.0 ** 27, A.add, 1.5 * 2.0 ** 27, A.subtract)
+        ts(u("ht"), e16("QR", 15), 1.5 * 2.0 ** 23, A.add, 1.5 * 2.0 ** 23 - 7, A.subtract)
+        tt(u("SN%d" % t), u("ht"), u("hs"), A.subtract)
+        send(u("SN%d" % t), "RS", "s", t, -1)
 
     def part_apply(t):
-        ts(u("XV%d" % t, 0, 32), u("RS%d" % t), 0.5, A.mult, 135.25, A.add)
-        ts(u("NV"), ix(u("XV%d" % t), u("RK%d" % (t % 2), 0, 8)), -128.0, A.add)
-        cp(ix(X, u("S16%d" % (t % 2))), u("NV"))
+        cp(ix(X, u("S32")), u("RS%d" % t))
 
     for t in range(RO):
         part_own(t)
@@ -757,7 +825,9 @@ def rank_program(g, core, T, topo):
             part_apply(t - 1)
         part_near(t)
         part_partner(t)
+        part_look(t)
         part_finish(t)
+        part_host(t)
         if t + 1 == RO:
             ts(u("t512a"), LISTS, 0.0, A.is_equal, 2049.0, A.mult)
             act(u("p1"), LISTS, F.Identity, bias=-1.0)

@@ -13,36 +13,43 @@ def _sb(dtype, cols, names):
 
 
 _sb(B, 2304, "X")
-_sb(B, 2048, "T MS VB US REP SQ AX AW SH OG DT DU Z0 Z1 ZE EXP")
+_sb(B, 2048, "T MS US SQ AX AW SH OG DT DU EXP EXA REP Z0")
+_sb(H, 1024, "RH")
+_sb(S, 16, "two")
+_sb(B, 128, "MC2 WD")
+_sb(H, 128, "KD")
+_sb(B, 8, "blk2 nblk2")
 _sb(B, 1920, "YL")
 _sb(B, 1024, "EQ")
 _sb(B, 768, "XF")
-_sb(B, 240, "J240")
-_sb(B, 512, "CODE QD OCC PEN QZ QRp QS CG KQ5")
-_sb(B, 256, "ID2 KAp QN LN XC ZMW MWR EE PEN2 M32")
-_sb(B, 144, "Jb Y")
-_sb(B, 128, "J4b J15b b1 b2 R16 MC IDB BD NBD BTI ONEB PRE PRD LR SR XB SQS SQB SEL0R TRIm NTRIm HWN N27 N25 N20 P23 P20 P11 "
+_sb(B, 512, "CODE QD OCC QZ QRp QS KQ5")
+_sb(B, 256, "PEN CG ID2 KAp QN LN XC ZMW MWR EE PEN2 M32")
+_sb(B, 144, "Jb Y w8k og0 og1 og2 og3")
+_sb(B, 128, "J4b J15b b1 b2 R16 MC IDB BD NBD BTI ONEB PRE PRD LR SR XB SQS SQB SEL0R TRIm NTRIm HWN N27 N20 P23 P20 P11 "
             "RV0 RV1 RV2 RV3 ST KAs KAb KAd KAn KAr KAm K9 K11 K20 PRL WV A4n B4 CN1 QB ZP0 ZP1 WTp IDh B256 B512 N512 HO PA EH PENW WM")
 _sb(B, 32, "OCb")
-_sb(B, 8, "blk nblk w64k w8k w32 w2 og0 og1 og2 og3 SEL0 L2N THN THZ ROW1 SZ wp8 C25 PB")
-_sb(H, 256, "SL CNT CTG ES")
-_sb(H, 144, "ZS HS ZB HB ZD HD")
-_sb(H, 128, "OWNH DMH DM2 CMK0 CMK1 CMK2 CMK3 KR KV SS m1 m2")
+_sb(B, 16, "THN THZ ROW1 SZ w64d PENB")
+_sb(B, 8, "blk nblk w64k w32 w2 SEL0 L2N wp8 C25 PB C3K")
+_sb(H, 256, "SL CNT CTG QH")
+_sb(H, 144, "ZS HS ZB HB HD")
+_sb(H, 128, "OWNH DMH DM2 CMK0 CMK1 CMK2 CMK3 KR KV m1 m2")
 _sb(H, 32, "CIX")
 _sb(H, 8, "CB")
 _sb(S, 4112, "OT")
 _sb(S, 2048, "VE VG")
 _sb(S, 1536, "FREE")
 _sb(S, 768, "DS")
-_sb(S, 640, "W ALT")
-_sb(S, 512, "J2f J3f t512a t512b YM QR DUM D1 MIN5 EV")
+_sb(B, 640, "ALT")
+_sb(B, 128, "EVB N40")
+_sb(S, 640, "W")
+_sb(S, 512, "J2f J3f t512a t512b YM QR D1 MIN5 EV")
 _sb(S, 264, "Pa Pb")
 _sb(S, 256, "WP")
-_sb(S, 128, "MINs MINn MIN S10 S11 S2 S3 SB ELS IDF ONEF NFF VH VR HLA HWF DUL")
-_sb(S, 64, "PC")
+_sb(S, 128, "MINs MINn MIN S10 S11 S2 S3 SB ELS IDF ONEF NFF VH VR HLA DUL DUM")
+_sb(S, 80, "PC")
 _sb(S, 32, "CS r1 r2 C512 hs ht")
-_sb(S, 16, "E16 KQ")
-_sb(S, 8, "blkf nblkf hi8 hb8 z8 mc kq G4 EP sp4 kp4")
+_sb(S, 16, "E16 KQ SV")
+_sb(S, 8, "blkf hi8 hb8 z8 mc kq G4 EP sp4 kp4")
 _sb(I, 2192, "AC4")
 _sb(I, 512, "MI")
 _sb(I, 8, "PIi a8 d8")
@@ -50,7 +57,7 @@ _sb(I, 2, "LI WI")
 _sb(U, 512, "INO")
 _sb(U, 128, "OWN AN DM MVO")
 _sb(U, 32, "F16 HL")
-_sb(U, 8, "RK S16 B16 D16 NT16 TG16 BT16 VV16 H16 O16")
+_sb(U, 8, "RK S16 A16 B16 D16 NT16 TG16 BT16 VV16 H16 O16")
 _sb(U, 2, "S32")
 _AT, _end = {}, {}
 for _n, _c, _d in _BUF:
@@ -58,7 +65,7 @@ for _n, _c, _d in _BUF:
     _end[_d] = _end.get(_d, 0) + -(-_c // 16) * 16
 SCRATCH = {"ar_" + _d: ("sbuf", [128, _c], _d) for _d, _c in _end.items()}
 for _n, _m, _o, _c in (("NIDB", "ID2", 0, 128), ("ZM", "ZMW", 0, 128), ("ZW", "ZMW", 128, 128), ("MR", "MWR", 0, 128), ("WR", "MWR", 128, 128),
-                       ("ZALL", "ZS", 0, 864), ("MIN3", "MINs", 0, 384), ("CT", "CIX", 0, 8)):
+                       ("ZALL", "ZS", 0, 720), ("MIN3", "MINs", 0, 384), ("CT", "CIX", 0, 8)):
     _AT[_n] = (_AT[_m][0], _AT[_m][1] + _o, _c, _AT[_m][3])
 for _t in range(RO):
     for _n, _c, _d in (("QA", 128, B), ("SE", 2, U), ("QI", 2, U), ("SN", 32, B), ("RS", 32, B)):
@@ -67,14 +74,18 @@ for _t in range(RO):
 for _k in range(8):
     SCRATCH["p%d" % _k] = ("psum", [128, 512], S)
     _AT["p%d" % _k] = ("p%d" % _k, 0, 512, S)
-SEMAPHORES = ["v", "p", "s", "k", "st0", "st1"] + ["ld%d" % i for i in range(10)] + ["cd%d" % i for i in range(9)]
+SEMAPHORES = ["v", "p", "s", "k", "st0", "st1"] + ["ld%d" % i for i in range(8)]
+SEMAPHORES += [n + str(i) for n in ("va", "vb") for i in range(4)] + ["ev%d" % i for i in range(3 * RO - 3)]
 for _t in range(RO):
     SEMAPHORES += [a + b + str(_t) for a in "rlfm" for b in "aqs"]
 
 CYC, PEC, GAT, SCA, WAKE, XWAKE, WAY, FIRST = 0.00085, 0.0005, 1.6, 3.7, 0.24, 0.12, 2.3, 2.5
-VIEWS = ((0.27, 0.09, 1.0, 0.92, 0.8), (0.21, 0.16, 1.0, 0.92, 0.8), (0.27, 0.1, 1.22, 1.4, 1.65))
-RULES = ((3, 2, 0.1), (5, 2, 0.1), (8, 2, 0.1), (3, 2, 0.05), (5, 2, 0.05), (8, 2, 0.05), (5, 0, 0.1), (5, 1, 0.08), (12, 1, 0.08), (2, 1, 0.08))
-TURNS, EASE = 16000, 0.08
+VIEWS = ((0.26, 0.11, 1.0, 0.92, 0.8), (0.21, 0.17, 1.0, 0.75, 0.55), (0.27, 0.14, 1.22, 1.4, 1.65))
+PLAN, PASSES = (0.24, 0.14, 1.0, 0.92, 0.8), 8
+TURNS, AGAIN, EASE = 27000, 600, 0.15
+MOVERS = 16
+BANK_A, SPREAD, CUT_A = (0, 1, 2, 0), False, (56, 104)
+CUT_T, CUT_D, CUT_O, CUT_S = (32, 64, 96), (32, 64, 96), (32, 64, 96), 512
 _ORDER = {}
 
 
@@ -140,142 +151,174 @@ def _order(ops):
             early[(j, i)] = ops[j]["lat"]
     eng, cost, lat = [o["e"] for o in ops], [o["cost"] for o in ops], [o["lat"] for o in ops]
     banks = [sorted(set(b for (b, _l, _h) in o["rd"] + o["wr"] if _psum(b))) for o in ops]
-    way0 = [0.0] * n
-    for i in range(n - 1, -1, -1):
-        way0[i] = cost[i] + lat[i] + max([way0[j] + WAKE for j in succ[i]] + [0.0])
+    views = [([0.0] * n, x[1], [None] * n) for x in VIEWS]
+    queue, mine, others, other = [0] * n, [None] * n, [None] * n, [o["alt"] and (o["alt"][0], o["alt"][2]) for o in ops]
 
-    def run(before, after, rank, back, rule):
-        haste, look, slip = rule
-        left, base, start = [len(p) for p in before], [0.0] * n, [0.0] * n
-        free, bank, ready, order = {}, {}, {}, []
-        for i in range(n):
-            if not left[i]:
-                ready.setdefault(eng[i], []).append(i)
+    def settle(calls, after):
+        for i in calls:
+            queue[i] = "vpsky".index(eng[i])
+            mine[i] = [3 * int(b[1]) + queue[i] for b in banks[i]]
+            others[i] = [3 * int(b[1]) + e for b in banks[i] for e in range(3) if e != queue[i]]
+        for (c, xw, inc), (wake, _xw, mul, gat, sca) in zip(views, VIEWS):
+            for i in calls:
+                c[i] = cost[i] * (mul, gat, sca)[ops[i]["how"]]
+            for i in after:
+                inc[i] = [(j, c[j] + lat[j] + (xw if eng[j] != eng[i] else 0.0 if eng[i] == "p" else wake) - mul * early.get((j, i), 0.0)) for j in pred[i]]
 
-        def can(i):
-            return max([base[i] + (lat[i] if back else 0.0), free.get(eng[i], 0.0)]
-                       + [t + XWAKE for b in banks[i] for e, t in bank.get(b, {}).items() if e != eng[i]])
+    def move(i):
+        other[i], (eng[i], cost[i]) = (eng[i], cost[i]), other[i]
+        settle([i], [i] + succ[i])
+    settle(range(n), range(n))
 
-        def done(a, s, j):
-            return s + cost[a] + (XWAKE if eng[a] != eng[j] else 0.0 if eng[a] == "p" else WAKE) + (0.0 if back else lat[a]) - early.get((j, a) if back else (a, j), 0.0)
-        for _i in range(n):
-            st = {i: can(i) for lst in ready.values() for i in lst}
-            soon, front = {}, st
-            for _d in range(look):
-                nxt, seen = {}, {}
-                for a, s in front.items():
-                    for j in after[a]:
-                        seen[j] = seen.get(j, 0) + 1
-                        nxt[j] = max(nxt.get(j, base[j]), done(a, s, j))
-                front = {j: max(s, free.get(eng[j], 0.0)) for j, s in nxt.items() if seen[j] == left[j]}
-                for j, s in front.items():
-                    soon.setdefault(eng[j], []).append((j, s))
-            pick = held = None
-            for e, lst in ready.items():
-                if lst:
-                    a = max(lst, key=lambda i: rank[i] - haste * st[i])
-                    wait = [s for j, s in soon.get(e, ()) if rank[j] - 2 * s > rank[a] - 2 * st[a] and s < st[a] + cost[a] - slip]
-                    fit = [i for i in lst if st[i] + cost[i] <= (wait[0] if wait else st[a]) + slip]
-                    if wait and (held is None or st[a] < held[0]):
-                        held = (st[a], a)
-                    a = max(fit, key=lambda i: rank[i]) if fit else None if wait else a
-                    if a is not None and (pick is None or st[a] < pick[0]):
-                        pick = (st[a], a)
-            s, a = pick or held
-            ready[eng[a]].remove(a)
-            order.append(a)
-            start[a], free[eng[a]] = s, s + cost[a]
-            for b in banks[a]:
-                bank.setdefault(b, {})[eng[a]] = s + cost[a]
-            for j in after[a]:
-                base[j] = max(base[j], done(a, s, j))
-                left[j] -= 1
-                if not left[j]:
-                    ready.setdefault(eng[j], []).append(j)
-        return order, [start[i] + cost[i] + (0.0 if back else lat[i]) for i in range(n)]
-    best = None
-    for rule in RULES:
-        way = way0
-        for _turn in range(4):
-            way = [x + o["first"] for x, o in zip(way, ops)]
-            for i in range(n - 1, -1, -1):
-                way[i] = max([way[i]] + [way[j] + 0.01 for j in succ[i]])
-            order, end = run(pred, succ, way, False, rule)
-            if best is None or max(end) < best[0]:
-                best = (max(end), order)
-            way = run(succ, pred, end, True, rule)[1]
-    views = []
-    for wake, xw, mul, gat, sca in VIEWS:
-        c = [cost[i] * (mul, gat, sca)[ops[i]["how"]] for i in range(n)]
-        views.append((c, xw, [[(j, c[j] + lat[j] + (xw if eng[j] != eng[i] else 0.0 if eng[i] == "p" else wake) - mul * early.get((j, i), 0.0)) for j in pred[i]] for i in range(n)]))
+    def times(k, order, lo, hi, start, by, kept, last, user):
+        c, xw, inc = views[k]
+        for pos in range(lo, hi):
+            if pos % 32 == 0:
+                kept.append((last[:], user[:]))
+            a = order[pos]
+            s, w = 0.0, -1
+            for j, d in inc[a]:
+                d += start[j]
+                if d > s:
+                    s, w = d, j
+            j = last[queue[a]]
+            if j >= 0 and start[j] + c[j] > s:
+                s, w = start[j] + c[j], j
+            last[queue[a]] = a
+            for q in others[a]:
+                j = user[q]
+                if j >= 0 and start[j] + c[j] + xw > s:
+                    s, w = start[j] + c[j] + xw, j
+            for q in mine[a]:
+                user[q] = a
+            start[a], by[a] = s, w
 
-    queue = ["vpsky".index(e) for e in eng]
-    mine = [[3 * int(b[1]) + queue[i] for b in banks[i]] for i in range(n)]
-    others = [[3 * int(b[1]) + e for b in banks[i] for e in range(3) if e != queue[i]] for i in range(n)]
-
-    def clock(order, at, old):
-        total, new = 0.0, []
-        for k, (c, xw, inc) in enumerate(views):
+    def clock(order, lo, hi, old, loss):
+        work, late = [], 0.0
+        for k in range(len(views)):
             if old:
-                start, by, kept = old[k][0][:], old[k][1][:], old[k][2][:at // 64]
-                last, user = old[k][2][at // 64][0][:], old[k][2][at // 64][1][:]
+                start, by, kept, on = old[k]
+                w = (start[:], by[:], kept[:lo // 32], kept[lo // 32][0][:], kept[lo // 32][1][:])
+                at = next((pos for pos in range(hi, n) if order[pos] in on), n - 1) + 1
+                times(k, order, lo // 32 * 32, at, *w)
+                late += w[0][order[at - 1]] - start[order[at - 1]] if order[at - 1] in on else -1e9
             else:
-                start, by, kept, last, user = [0.0] * n, [-1] * n, [], [-1] * 5, [-1] * 24
-            for pos in range(at // 64 * 64, n):
-                if pos % 64 == 0:
-                    kept.append((last[:], user[:]))
-                a = order[pos]
-                s, w = 0.0, -1
-                for j, d in inc[a]:
-                    d += start[j]
-                    if d > s:
-                        s, w = d, j
-                j = last[queue[a]]
-                if j >= 0 and start[j] + c[j] > s:
-                    s, w = start[j] + c[j], j
-                last[queue[a]] = a
-                for q in others[a]:
-                    j = user[q]
-                    if j >= 0 and start[j] + c[j] + xw > s:
-                        s, w = start[j] + c[j] + xw, j
-                for q in mine[a]:
-                    user[q] = a
-                start[a], by[a] = s, w
+                w, at = ([0.0] * n, [-1] * n, [], [-1] * 5, [-1] * 24), 0
+            work.append((w, at))
+        if late > loss * len(views):
+            return None, None
+        total, new = 0.0, []
+        for k, (w, at) in enumerate(work):
+            times(k, order, at, n, *w)
+            start, by, c = w[0], w[1], views[k][0]
             a = max(order[-60:], key=lambda i: start[i] + c[i] + lat[i])
             total += start[a] + c[a] + lat[a]
-            new.append((start, by, kept, a))
+            on = {a}
+            while by[a] >= 0:
+                a = by[a]
+                on.add(a)
+            new.append((start, by, w[2], on))
         return total / len(views), new
 
     def chain(state):
         pairs = []
-        for _start, by, _kept, a in state:
-            while by[a] >= 0:
-                if by[a] not in pred[a]:
+        for start, by, _kept, on in state:
+            way = sorted(on, key=lambda i: (start[i], i))
+            for k, a in enumerate(way):
+                if by[a] >= 0 and by[a] not in pred[a]:
                     pairs.append((by[a], a))
-                a = by[a]
+                    pairs += [(way[k - d], a) for d in (4, 16) if k >= d and queue[way[k - d]] == queue[a]]
         return pairs
+
+    def place(rank, back, choose):
+        wake, xw, mul, gat, sca = PLAN
+        before, after = (succ, pred) if back else (pred, succ)
+        left, start, end, busy = [len(x) for x in before], [0.0] * n, [0.0] * n, {}
+        ready = sorted((rank[i], i) for i in range(n) if not left[i])
+        while ready:
+            a = ready.pop()[1]
+            found = None
+            for e, c in [(eng[a], cost[a])] + ([other[a]] if choose and other[a] else []):
+                c *= (mul, gat, sca)[ops[a]["how"]]
+                s = lat[a] if back else 0.0
+                for j in before[a]:
+                    w = xw if eng[j] != e else 0.0 if e == "p" else wake
+                    s = max(s, end[j] + w + lat[a if back else j] - mul * early.get((a, j) if back else (j, a), 0.0))
+                moved = True
+                while moved:
+                    moved = False
+                    for key, gap in [(e, 0.0)] + [(b, xw) for b in banks[a]]:
+                        for lo, hi, e2 in busy.get(key, ()):
+                            if (key == e or e2 != e) and lo < s + c + gap and s < hi + gap:
+                                s, moved = hi + gap, True
+                if found is None or s + 2 * c < found[3] - 0.02:
+                    found = (s + c, s, e, s + 2 * c)
+            if found[2] != eng[a]:
+                move(a)
+            end[a], start[a] = found[:2]
+            for key in [eng[a]] + banks[a]:
+                busy.setdefault(key, []).append((start[a], end[a], eng[a]))
+            for j in after[a]:
+                left[j] -= 1
+                if not left[j]:
+                    ready.append((rank[j], j))
+            ready.sort()
+        return start, [end[i] + (0.0 if back else lat[i]) for i in range(n)]
+
+    def sort(start):
+        at = [0.0] * n
+        for i in range(n):
+            at[i] = max([start[i]] + [at[j] + 1e-6 for j in pred[i]])
+        return sorted(range(n), key=lambda i: at[i])
+    way, best, seed = [0.0] * n, None, 12345
+    for i in range(n - 1, -1, -1):
+        way[i] = cost[i] + lat[i] + max([way[j] + PLAN[0] for j in succ[i]] + [0.0])
+    for turn in range(PASSES):
+        start, end = place(way, False, True)
+        order = sort(start)
+        span = clock(order, 0, n, None, 0.0)[0]
+        if best is None or span < best[0]:
+            best = (span, order, eng[:])
+        way = place(end, True, False)[1]
+    for i in range(n):
+        if eng[i] != best[2][i]:
+            move(i)
     order = best[1]
-    span, state = clock(order, 0, None)
-    pairs, best, seed = chain(state), (span, order), 12345
+    span, state = clock(order, 0, n, None, 0.0)
+    pairs = chain(state)
     for turn in range(TURNS):
+        if turn % AGAIN == AGAIN - 1:
+            way = place([state[0][0][i] + views[0][0][i] + lat[i] for i in range(n)], True, False)[1]
+            trial = sort(place(way, False, False)[0])
+            s2, new = clock(trial, 0, n, None, 0.0)
+            if s2 < span:
+                order, span, state, pairs = trial, s2, new, chain(new)
         seed = (seed * 1103515245 + 12345) % 2147483648
         b, a = pairs[(seed >> 8) % len(pairs)]
-        i = order.index(b)
-        mid = order[i:order.index(a) + 1]
         up = bool((seed >> 4) & 1)
-        take = {a if up else b}
-        for x in reversed(mid) if up else mid:
-            if any(y in take for y in (succ[x] if up else pred[x])):
-                take.add(x)
-        if (b if up else a) in take:
-            continue
-        trial = order[:i] + [x for x in mid if (x in take) == up] + [x for x in mid if (x in take) != up] + order[i + len(mid):]
-        s2, new = clock(trial, i, state)
+        moved = (a if up else b) if (seed >> 5) % 3 == 0 and other[a if up else b] else None
+        if moved is not None:
+            move(moved)
+            trial, i, mid = order, order.index(moved), [moved]
+        else:
+            i = order.index(b)
+            mid = order[i:order.index(a) + 1]
+            take = {a if up else b}
+            for x in reversed(mid) if up else mid:
+                if any(y in take for y in (succ[x] if up else pred[x])):
+                    take.add(x)
+            if (b if up else a) in take:
+                continue
+            trial = order[:i] + [x for x in mid if (x in take) == up] + [x for x in mid if (x in take) != up] + order[i + len(mid):]
         seed = (seed * 1103515245 + 12345) % 2147483648
-        if s2 <= span - EASE * 0.125 ** (turn / TURNS) * math.log((seed + 1) / 2147483648):
+        loss = -EASE * 0.125 ** (turn / TURNS) * math.log((seed + 1) / 2147483648)
+        s2, new = clock(trial, i, i + len(mid), state, loss)
+        if new and s2 <= span + loss:
             order, span, state, pairs = trial, s2, new, chain(new)
-            best = min(best, (span, order))
-    return best[1]
+            best = min(best, (span, order, eng[:]))
+        elif moved is not None:
+            move(moved)
+    return best[1:]
 
 
 def rank_program(g, core, T, topo):
@@ -303,10 +346,10 @@ def rank_program(g, core, T, topo):
     def mark(name, lo=0, hi=1, ap=None):
         return (ap, [(name, lo, hi)], 0, None, None)
 
-    def op(e, fn, outs, ins, cost, dma=None, lat=0.0, items=None, land=None):
+    def op(e, fn, outs, ins, cost, dma=None, lat=0.0, items=None, land=None, alt=None):
         rd = [r for x in ins for r in x[1]] + [r for x in outs if x[4] for r in x[1][1:]]
         wr = [r for x in outs for r in (x[1][:1] if x[4] else x[1])]
-        ops.append({"e": e, "fn": fn, "rd": rd, "wr": wr, "cost": cost, "dma": dma, "lat": lat, "items": items, "land": land, "first": first[0],
+        ops.append({"e": e, "fn": fn, "rd": rd, "wr": wr, "cost": cost, "dma": dma, "lat": lat, "items": items, "land": land, "first": first[0], "alt": alt,
                     "how": 2 if outs[0][4] else 1 if ins and ins[0][4] else 0})
 
     def _c(x):
@@ -322,14 +365,21 @@ def rank_program(g, core, T, topo):
             per = 1.0
         return 0.005 + max(64, o[2] * per) * CYC
 
+    def scalar(o, i, f, **kw):
+        if o[3] in (S, B) and i[3] in (S, B) and not o[4]:
+            return ("s", lambda: sc.activation(o[0], i[0], f, **kw), cost(o, [i], 1.0) + 0.02)
+
     def cp(o, i):
-        op("v", lambda: v.tensor_copy(o[0], i[0]), [o], [i], cost(o, [i], 0.5))
+        op("v", lambda: v.tensor_copy(o[0], i[0]), [o], [i], cost(o, [i], 0.5), alt=scalar(o, i, F.Copy))
 
     def ts(o, i, s1, o1, s2=None, o2=None):
         if o2 is None:
-            op("v", lambda: v.tensor_scalar(o[0], i[0], _c(s1), None, o1), [o], [i] + _r(s1), cost(o, [i], 0.5))
+            alt = (scalar(o, i, F.Identity, scale=_c(s1)) if o1 == A.mult else scalar(o, i, F.Identity, bias=_c(s1)) if o1 == A.add
+                   else scalar(o, i, F.Relu) if o1 == A.max and s1 == 0.0 else None)
+            op("v", lambda: v.tensor_scalar(o[0], i[0], _c(s1), None, o1), [o], [i] + _r(s1), cost(o, [i], 0.5), alt=alt)
         else:
-            op("v", lambda: v.tensor_scalar(o[0], i[0], _c(s1), _c(s2), o1, o2), [o], [i] + _r(s1, s2), cost(o, [i], 0.5))
+            alt = scalar(o, i, F.Identity, scale=_c(s1), bias=_c(s2)) if (o1, o2) == (A.mult, A.add) else None
+            op("v", lambda: v.tensor_scalar(o[0], i[0], _c(s1), _c(s2), o1, o2), [o], [i] + _r(s1, s2), cost(o, [i], 0.5), alt=alt)
 
     def tt(o, a, b, o1):
         per = 1.0 if _psum(a[1][0][0]) or _psum(b[1][0][0]) else 2.0
@@ -339,31 +389,45 @@ def rank_program(g, core, T, topo):
         op("v", lambda: v.tensor_tensor_scan(o[0], a[0], b[0], 0.0, o1, o2), [o], [a, b], cost(o, [a, b], 0.5))
 
     def fill(o, c):
-        op("v", lambda: v.memset(o[0], c), [o], [], cost(o, [], 0.5))
+        kw = {} if o[3] == I else {"allow_small_or_imprecise_dtypes": True}
+        alt = ("k", lambda: g.iota(o[0], [[0, o[2]]], int(c), 0, **kw), 0.13 + 2 * o[2] * CYC) if c == int(c) and abs(c) < 2 ** 24 else None
+        op("v", lambda: v.memset(o[0], c), [o], [], cost(o, [], 0.5), alt=alt)
 
     def act(o, i, f, scale=None, bias=None, acc=None):
         kw = {k: _c(x) for k, x in (("scale", scale), ("bias", bias), ("accum_out", acc)) if x is not None}
-        op("s", lambda: sc.activation(o[0], i[0], f, **kw), [o] + _r(acc), [i] + _r(scale, bias), cost(o, [i], 1.0) + 0.02)
+        fn, per = None, 0.5
+        if f in (F.Copy, F.Silu):
+            fn = lambda: v.tensor_copy(o[0], i[0])
+        elif f == F.Identity and acc is None:
+            fn = lambda: v.tensor_scalar(o[0], i[0], kw.get("scale", 1.0), kw.get("bias", 0.0), A.mult, A.add)
+        elif f in (F.Relu, F.Sign) and not kw:
+            fn = lambda: v.tensor_scalar(o[0], i[0], 0.0, None, A.max if f == F.Relu else A.is_gt)
+        elif f == F.Square and not _psum(i[1][0][0]):
+            fn, per = lambda: v.tensor_tensor(o[0], i[0], i[0], A.mult), 2.0
+        op("s", lambda: sc.activation(o[0], i[0], f, **kw), [o] + _r(acc), [i] + _r(scale, bias), cost(o, [i], 1.0) + 0.02,
+           alt=fn and ("v", fn, cost(o, [i], per)))
 
     def iota(o, pat, base, cm=0, after=None):
         kw = {} if o[3] == I else {"allow_small_or_imprecise_dtypes": True}
-        op("k", lambda: g.iota(o[0], pat, base, cm, **kw), [o], _r(after), 0.13 + 2 * o[2] * CYC)
+        alt = ("v", lambda: v.memset(o[0], base if o[3] == I else float(base)), cost(o, [], 0.5)) if pat == [[0, o[2]]] and not cm else None
+        op("k", lambda: g.iota(o[0], pat, base, cm, **kw), [o], _r(after), 0.13 + 2 * o[2] * CYC, alt=alt)
 
     def select(o, i, pat, test, other, base, cm):
         op("k", lambda: g.affine_select(o[0], i[0], pat, test, other, base, cm), [o], [i], 0.2 + 2 * o[2] * CYC)
 
-    def mm(out, *pairs):
+    def mm(out, *pairs, ends=(True, True)):
         items = [(x[2] if len(x) > 2 else out, x[0], x[1]) for x in pairs]
-        op("p", None, [x[0] for x in items], [y for x in items for y in x[1:]], sum(_cycles(a, b) for _o, a, b in items) * PEC, items=items)
+        keys = [mark("keys")] if out[1][0][0] == "p3" else []
+        op("p", ends, [x[0] for x in items] + keys, [y for x in items for y in x[1:]], sum(_cycles(a, b) for _o, a, b in items) * PEC, items=items)
 
-    def dma(o, i, sem):
-        first[0] = 50
-        op("y", lambda: g.sync.dma_start(o[0], i[0]), [o], [i], 0.1, dma=sem, lat=4.0)
+    def dma(o, i, sem, haste=50, lat=4.0):
+        first[0] = haste
+        op("y", lambda: g.sync.dma_start(o[0], i[0]), [o], [i], 0.1, dma=sem, lat=lat)
         first[0] = 0
 
     def rows(dst, row, src, src_row, outs, ins, sem):
         (b1, l1, h1), (b2, l2, h2) = dst[1][0], src[1][0]
-        op("y", lambda: g.sync.dma_start(T[b1][row:128:16, l1:h1], T[b2][src_row:128:16, l2:h2]), outs, ins, 0.1, dma=sem, lat=2.5)
+        op("y", lambda: g.sync.dma_start(T[b1][row:128:16, l1:h1], T[b2][src_row:128:16, l2:h2]), outs, ins, 0.1, dma=sem, lat=3.0)
 
     def send(src, buf, kind, t, way):
         dst, back = T.cores[(rank + way * (1 + t % 7)) % 8], T.cores[(rank - way * (1 + t % 7)) % 8]
@@ -378,9 +442,8 @@ def rank_program(g, core, T, topo):
     def sums(ps, base, src, w):
         return [(e16(src, k), u(w), u(ps, base + k, base + 128, 16)) for k in range(16)]
 
-    def tile(z, h, ps, sign, *more):
-        scan(u(h, 0, 128), u("MC"), u(z, 0, 128), A.mult, A.add)
-        a, b = ("blk", "nblk") if sign > 0 else ("nblk", "blk")
+    def tile(z, h, ps, a, b, mask, *more):
+        scan(u(h, 0, 128), u(mask), u(z, 0, 128), A.mult, A.add)
         mm(ps, (u(h, 0, 128), u(a)), (u(h, 1, 129), u(b)), (u(z, 1, 129), u(a)), *more)
 
     def low(z, key, hi, step):
@@ -391,8 +454,8 @@ def rank_program(g, core, T, topo):
     fill(u("X", 0, 16), -64.0)
     fill(u("X", 2048, 2304), 0.0)
     fill(u("AC4", 0, 8), 0)
-    fill(u("AC4", 2048, 2192), 0)
-    dma(u("MI"), mark("ml", ap=T.ml[:]), "ld0")
+    fill(u("AC4", 2048, 2192), 2048)
+    dma(u("MI"), mark("ml", ap=T.ml[:]), "ld0", 70)
     dma(u("X", 1, 2049), mark("x0", ap=T.x0[:]), "ld1")
     dma(u("LI"), mark("lims", ap=T.lims[:]), "ld2")
     dma(u("WI", 0, 1), mark("wt", ap=T.wt[:]), "ld3")
@@ -412,59 +475,72 @@ def rank_program(g, core, T, topo):
     iota(J144, [[1, 144]], 0)
     iota(J15, [[0, 8], [1, 16]], 0)
     iota(J4, [[1, 8], [0, 16]], 0)
-    for a, b in ((0, 128), (128, 512)):
-        iota(u("J2f", a, b), [[1, (b - a) // 4], [0, 4]], a // 4)
-        iota(u("J3f", a, b), [[0, (b - a) // 4], [1, 4]], 0)
-        iota(u("DUM", a, b), [[0, (b - a) // 128], [16, 128]], 2064)
+    first[0] = 40
+    iota(u("DUM"), [[16, 128]], 2064)
+    for a in (0, 1024):
+        iota(u("SQ", a, a + 1024), [[1, 64], [0, 16]], 128 + a // 16)
+    first[0] = 0
+    iota(u("J2f"), [[1, 128], [0, 4]], 0)
+    iota(u("J3f"), [[0, 128], [1, 4]], 0)
     iota(u("PC", 4, 8), [[1, 4]], 1024, 4)
     iota(u("PC", 8, 10), [[512, 2]], 8192 - 1536, 1)
     iota(u("PC", 10, 11), [[0, 1]], 128, 1)
-    for o, val in ((u("FREE", 0, 1024), 0), (u("Z1"), 0), (u("QZ"), 0), (u("DS", 640, 768), 0), (u("ALT"), 0), (u("MIN5"), LOW), (e16("MIN5"), -LOW)):
+    for o, val in ((u("FREE", 0, 1024), 0), (u("QZ"), 0), (u("DS", 640, 768), 0), (u("ALT"), 0), (u("MIN5"), LOW), (e16("MIN5"), -LOW)):
         iota(o, [[0, o[2]]], val)
-    for o, val in ((u("MS"), 1.0), (e16("MS"), 0.0), (u("ZE"), 0.0), (u("Z0"), 0.0), (u("OT", 0, 8), 0.0), (u("OT", 2048, 2064), 0.0), (u("W", 512, 640), 0.0)):
+    for o, val in ((u("MS"), 1.0), (e16("MS"), 0.0), (u("W", 512, 640), 0.0)):
         fill(o, val)
     ts(u("PIi", 1, 2), u("PIi", 0, 1), 4, A.logical_shift_right)
     ts(u("PIi", 2, 3), u("PIi", 0, 1), 15, A.bitwise_and)
     cp(u("PC", 0, 3), u("PIi", 0, 3))
     ts(u("E16"), u("J15b", 0, 16), P15, A.is_equal)
     ts(u("EP", 0, 4), u("Jb", 0, 4), P, A.is_equal)
-    row0, row4, row10 = u("E16", 0, 1), u("E16", 4, 5), u("E16", 10, 11)
+    row0, row4 = u("E16", 0, 1), u("E16", 4, 5)
     V0 = u("FREE", 1024, 1536)
-    slope = col(row4, row10, A.add)
-    base = col(slope, 128.0, A.mult)
-    tt(base, base, col(row10, 64.0, A.mult), A.add)
-    for a, b in ((0, 128), (128, 512)):
-        ps = u("p4" if a else "p3", a, b)
-        ts(u("DUM", a, b), u("DUM", a, b), P15, A.add)
-        act(ps, u("J2f", a, b), F.Identity, scale=slope, bias=base)
-        ts(u("t512b", a, b), u("J3f", a, b), P15, A.is_equal, 64.0, A.mult)
-        tt(u("FREE", 1024 + a, 1024 + b), u("t512b", a, b), ps, A.add)
-    for a, b in ((0, 128), (128, 512)):
-        ts(u("p6", a, b), u("MI", a, b), 2048, A.is_equal, 8192.0, A.mult)
-        ts(u("t512a", a, b), u("MI", a, b), 1, A.add)
-        tt(u("p5", a, b), u("t512a", a, b), u("p6", a, b), A.add)
-        tt(u("YM", a, b), u("DUM", a, b), u("p5", a, b), A.min)
-        cp(u("INO", a, b), u("YM", a, b))
-        tt(u("p5", a, b), u("t512a", a, b), u("p6", a, b), A.subtract)
-        ts(u("W", a, b), u("p5", a, b), 0.0, A.max)
-    for c in range(4):
-        ve = "VG" if c % 2 else "VE"
-        if c >= 2:
-            rows(u(ve), 4, u(ve), 10, [u(ve)], [], "ld%d" % (6 + c))
-        for a in (0, 1024) if c < 2 else ():
-            cp(u("ZE", a, a + 1024, 16), u("FREE", 1024 + 128 * c + a // 16, 1088 + 128 * c + a // 16))
-            scan(u(ve, a, a + 1024), u("MS", a, a + 1024), u("ZE", a, a + 1024), A.mult, A.add)
-        first[0] = 14
-        for a in (0, 1024):
-            act(ix(u("OT"), u("INO", 128 * c + a // 16, 128 * c + a // 16 + 64)), u(ve, a, a + 1024), F.Silu)
-        first[0] = 0
-    first[0] = 30
+    base = col(row4, 128.0, A.mult)
+    act(u("p4"), u("J2f"), F.Identity, scale=row4, bias=base)
+    ts(u("t512b"), u("J3f"), P15, A.is_equal, 64.0, A.mult)
+    tt(V0, u("t512b"), u("p4"), A.add)
+    first[0] = 40
+    ts(u("DUM"), u("DUM"), P15, A.add)
+    zero = col(row0, 64.0, A.mult, base, A.add)
+    one, two = [col(u("E16", c, c + 1), u("E16", 5, 6), A.add, 64.0, A.mult) for c in (1, 2)]
+    for a in (0, 1024):
+        act(u("VE", a, a + 1024), u("SQ", a, a + 1024), F.Identity, scale=row4, bias=one)
+        act(u("VG", a, a + 1024), u("SQ", a, a + 1024), F.Identity, scale=row4, bias=two)
+        act(u("OT", a, a + 1024), u("MS", a, a + 1024), F.Identity, scale=0.0, bias=zero)
+    act(u("OT", 2048, 2049), u("MS", 0, 1), F.Identity, scale=0.0, bias=zero)
+    every = col(P15, 4.0, A.is_lt, 64.0, A.mult)
+    act(u("OT", 2049, 2064), u("MS", 0, 15), F.Identity, scale=0.0, bias=col(every, base, A.add))
+
+    def owners(c):
+        for h in range(2):
+            ve, at = u("VE" if c % 2 else "VG", 1024 * h, 1024 * h + 1024), 4 * (c % 2) + 2 * h
+            both = [("row", at, at + 2)]
+            if c in (0, 3):
+                rows(ve, c, ve, 5, [mark("row", at, at + 1)], [ve], "va%d" % (at // 2))
+                rows(ve, (c - 2) % 4, ve, 6, [mark("row", at + 1, at + 2)], [ve], "vb%d" % (at // 2))
+            act(ix(u("OT"), u("INO", 128 * c + 64 * h, 128 * c + 64 * h + 64)), (ve[0], ve[1] + both) + ve[2:], F.Silu)
+    for c in (1, 0, 2, 3):
+        first[0] = 40 if c == 1 else 25
+        a, b, ml = 128 * c, 128 * c + 128, u("MI", c, 512, 4)
+        ts(u("p6", a, b), ml, 2048, A.is_lt, 8192.0, A.mult)
+        ts(u("t512a", a, b), ml, 1, A.add)
+        tt(u("p5", a, b), u("DUM"), u("p6", a, b), A.subtract)
+        tt(u("YM", a, b), u("t512a", a, b), u("p6", a, b), A.min)
+        tt(u("t512a", a, b), u("YM", a, b), u("p5", a, b), A.max)
+        cp(u("INO", a, b), u("t512a", a, b))
+        cp(u("W", c, 512, 4), u("YM", a, b))
+        first[0] = 30
+        if c:
+            owners(c)
+    first[0] = 0
+    first[0] = 10
     ts(IDB, J, P, A.is_equal)
     ts(BD, J4, P4, A.is_equal)
     ts(u("blk"), J8, P4, A.is_equal)
     ts(u("R16"), J15, P15, A.is_equal)
-    for name, src, val in (("nblk", "blk", -1.0), ("nblkf", "blk", -1.0), ("w64k", "blk", 65536.0), ("w8k", "blk", 8192.0), ("w32", "blk", 32.0),
-                           ("NBD", "BD", -1.0), ("IDF", "IDB", 1.0), ("SEL0R", "BD", row0), ("SEL0", "blk", row0), ("N25", "SEL0R", -2.0 ** 25),
+    for name, src, val in (("nblk", "blk", -1.0), ("N40", "IDB", -2.0 ** 40), ("w64k", "blk", 65536.0), ("w32", "blk", 32.0),
+                           ("NBD", "BD", -1.0), ("IDF", "IDB", 1.0), ("SEL0R", "BD", row0), ("SEL0", "blk", row0),
                            ("NIDB", "IDB", -1.0), ("N27", "IDB", -2.0 ** 27), ("N20", "IDB", -2.0 ** 20), ("P23", "IDB", 2.0 ** 23),
                            ("P11", "IDB", 2.0 ** 11), ("RV0", "IDB", 90.0 * TAU), ("RV1", "IDB", 30.0 * TAU), ("RV2", "IDB", 10.0 * TAU),
                            ("RV3", "IDB", -54.0 * TAU), ("P20", "IDB", 2.0 ** 20)):
@@ -475,8 +551,8 @@ def rank_program(g, core, T, topo):
     ts(u("MC"), J15, P15, A.is_le)
     fill(e16("MC"), 0.0)
     fill(ONE, 1.0)
-    ts(u("ZALL"), u("MS", 0, 864), 0.0, A.mult)
-    for name, slope, c1, c2 in (("KAs", 4096.0, 2.0 ** 27, -1088.0), ("KAb", -1.0, -2.0 ** 23, 7.0), ("KAn", 512.0, 2.0 ** 24, 0.0), ("KQ5", 16.0, -7.25, 0.0),
+    ts(u("ZALL"), u("MS", 0, 720), 0.0, A.mult)
+    for name, slope, c1, c2 in (("KAs", 4096.0, 2.0 ** 27, -1088.0), ("KAb", -1.0, -2.0 ** 23, 7.0), ("KAn", 512.0, -2.0 ** 24, 0.0), ("KQ5", 16.0, -7.25, 0.0),
                                 ("KAr", -1.0, 2048.0, 0.0), ("KAm", 0.0, 2.0 ** 21, -1536.0)):
         b = col(u("EP", 1, 2), c1, A.mult)
         if c2:
@@ -489,24 +565,21 @@ def rank_program(g, core, T, topo):
     cp(u("KQ5", 128, 256), u("KQ5", 0, 128))
     cp(u("KQ5", 256, 512), u("KQ5", 0, 256))
     for o, val in ((u("KAd"), 2 ** 20), (u("K11"), 2 ** 4), (u("K20"), 2 ** 13), (u("THZ"), 0), (u("MIN3"), LOW), (u("ZMW"), 0),
-                   (u("K9"), 12), (u("ONEF"), 1), (e16("KAd", 15), 0), (u("Pa", 256, 264), 2 ** 20), (u("Pb", 256, 264), 2 ** 20), (e16("MIN"), -LOW), (u("CODE"), 0)):
+                   (u("K9"), 12), (u("ONEF"), 1), (e16("KAd", 15), 0), (u("Pa", 256, 264), 2 ** 20), (u("Pb", 256, 264), 2 ** 20), (e16("MIN"), -LOW)):
         iota(o, [[0, o[2]]], val)
     fill(u("C25"), 2.0 ** 25)
     iota(e16("MINs"), [[0, 8]], 255 * 65536 + 2049 - 1088, 1)
     hw = col(P15, 4.0, A.is_lt, P15, A.mult)
     ts(hw, hw, 1.0 / 64, A.mult, col(row4, 4.0, A.mult), A.add)
     ts(u("HWN"), NBD, hw, A.mult)
-    ts(u("HWF"), NBD, hw, A.mult)
     iota(u("DUL"), [[0, 16], [128, 8]], 2064 - 1536, 1)
-    iota(u("J240"), [[1, 240]], 0)
-    cp(u("blkf"), u("blk"))
-    at = col(P15, 112.0, A.add)
+    iota(u("YL"), [[0, 1920]], 0)
     for j in range(8):
-        ts(u("YL", 240 * j, 240 * j + 240), u("J240"), at, A.is_equal, u("blkf", j, j + 1), A.mult)
+        select(u("YL", 240 * j + 112, 240 * j + 128), u("ONEB", 0, 16), [[1, 16]], A.is_equal, 0.0, 16 * j, -1)
     ts(u("kq", 0, 4), u("E16", 0, 4), 2.0 ** 19, A.mult, hw, A.add)
-    for c in range(4):
-        ts(u("og%d" % c), u("blk"), u("kq", c, c + 1), A.mult)
-    ts(u("Y"), J144, col(P4, 16.0, A.mult, 15.0, A.add), A.is_equal, row0, A.mult)
+    at = col(P4, 16.0, A.mult, 15.0, A.add)
+    for name, w in [("og%d" % c, u("kq", c, c + 1)) for c in range(4)] + [("w8k", 8192.0), ("Y", row0)]:
+        ts(u(name), J144, at, A.is_equal, w, A.mult)
     ts(u("b1"), J, P, A.is_gt)
     tt(u("TRIm"), u("b1"), u("P11"), A.subtract)
     ts(u("NTRIm"), u("TRIm"), -1.0, A.mult)
@@ -517,7 +590,6 @@ def rank_program(g, core, T, topo):
     ts(u("b1"), u("b1"), -56.0, A.mult, -8.0, A.add)
     tt(u("PEN", 0, 128), u("b1"), u("b2"), A.add)
     cp(u("PEN", 128, 256), u("PEN", 0, 128))
-    cp(u("PEN", 256, 512), u("PEN", 0, 256))
     for name, src, val in (("w2", u("blk"), 2.0), ("IDh", IDB, 0.5), ("B256", BD, 256.0), ("B512", BD, 512.0), ("N512", BD, -512.0)):
         ts(u(name), src, val, A.mult)
     for c in range(4):
@@ -536,49 +608,74 @@ def rank_program(g, core, T, topo):
     held = col(P15, 15.0, A.is_lt, 4096.0, A.mult)
     spare = [col(P15, 2177.0 + 16 * q, A.add) for q in range(2)]
     cp(u("PB", 0, 1), P)
-    fill(u("PB", 1, 2), 1088.0 - 4096.0)
+    fill(u("C3K"), 1088.0 - 4096.0)
     ts(u("KV"), J, 0.0, A.mult, -1023.5, A.add)
     ts(u("CIX"), u("Jb", 0, 32), 16.0, A.mult, P15, A.add)
     ts(u("CB"), u("CT"), 16.0, A.mult, 7.0, A.add)
     ts(u("C512"), u("CIX"), 512.0, A.add)
     ts(u("sp4", 0, 4), u("Jb", 0, 4), col(P15, -9.0, A.add), A.is_equal, 4.0, A.mult)
-    cp(u("CODE", 0, 4), u("sp4", 0, 4))
-    for b in range(9):
-        src = u("VB" if b < 4 else "DT" if b < 8 else "QS", 512 * (b % 4), 512 * (b % 4) + 512)
-        iota(src, [x for x in ([0, 256 >> b], [2, 2], [0, 1 << b]) if x[1] > 1], -1)
-        rows(u("CODE"), b, src, b, [mark("bit", b, b + 1)], [src, u("CODE")], "cd%d" % b)
-    ts(u("PIi", 3, 4), u("PIi", 1, 2), 3, A.bitwise_and)
+    nine = col(P15, 9.0, A.is_lt)
+    fill(u("two"), 2.0)
+    scan(u("two"), u("two"), u("E16"), A.mult, A.add)
+    half = col(u("two", 15, 16), 2.0 ** -16, A.mult)
+    iota(u("QR"), [[1, 512]], 0)
+    for q in range(2):
+        ts(u("RH", 512 * q, 512 * q + 512), u("QR"), half, A.mult, 1536 + 2.0 ** -11 - 0.5 * q, A.add)
+    scan(u("OCC"), u("RH", 0, 512), u("RH", 512, 1024), A.max, A.subtract)
+    ts(u("CODE"), u("OCC"), col(nine, 2.0, A.mult), A.mult, col(nine, -1.0, A.mult), A.add)
+    tt(u("CODE", 0, 4), u("CODE", 0, 4), u("sp4", 0, 4), A.add)
+    fill(u("two"), 0.5)
+    scan(u("two"), u("two"), u("E16"), A.mult, A.add)
+    ts(u("WD"), NBD, col(u("two", 15, 16), 2.0 ** 14, A.mult, nine, A.mult), A.mult)
+    ts(u("KD"), J, 0.0, A.mult, -255.5, A.add)
+    ts(u("PIi", 3, 4), u("PIi", 1, 2), 1, A.bitwise_and)
     ts(u("PIi", 4, 5), u("PIi", 0, 1), 3, A.bitwise_and)
-    ts(u("G4", 0, 4), u("Jb", 0, 4), col(u("PIi", 3, 4), 1.0, A.mult), A.is_equal)
-    ts(u("kp4", 0, 4), u("sp4", 0, 4), 0.25, A.mult, col(P15, 9.0, A.is_lt), A.add)
-    for q in range(4):
+    ts(u("PIi", 5, 6), u("PIi", 0, 1), 1, A.bitwise_and)
+    ts(u("G4", 0, 2), u("Jb", 0, 2), col(u("PIi", 3, 4), 1.0, A.mult), A.is_equal)
+    ts(u("kp4", 0, 4), u("sp4", 0, 4), 0.25, A.mult, nine, A.add)
+    for q in range(2):
         ts(u("KQ", 4 * q, 4 * q + 4), u("kp4", 0, 4), u("G4", q, q + 1), A.mult)
+    odd = col(u("PIi", 5, 6), 1.0, A.mult)
+    ts(u("MC2"), J15, col(odd, 8.0, A.mult, P4, A.add), A.is_le)
+    fill(e16("MC2"), 0.0)
+    ts(u("blk2"), J8, col(P15, odd, A.subtract, 0.5, A.mult), A.is_equal)
+    ts(u("nblk2"), u("blk2"), -1.0, A.mult)
+    at = col(P15, 8.0, A.mult, P4, A.add)
+    if SPREAD:
+        ts(u("EXA"), u("SQ"), col(at, 128.0, A.add), A.is_equal)
+    else:
+        fill(u("Z0"), 0.0)
+    ts(u("EXP"), u("SQ"), col(P, 128.0, A.add), A.is_equal)
     ts(u("PC", 12, 14), u("LI"), -65536.0, A.mult)
     wt = col(u("WI", 0, 1), 1.0, A.mult)
     ts(u("WTp"), BD, wt, A.mult)
     less = col(u("EP", 1, 2), -2048.0, A.mult)
     ts(u("L2N"), u("SEL0"), u("PC", 13, 14), A.mult, less, A.add)
-    ts(u("THN"), u("SEL0"), u("PC", 12, 13), A.mult, less, A.add)
-    ts(u("ROW1"), J8, 0.0, A.mult, col(less, 32.0, A.mult), A.add)
+    ts(u("THN"), u("SEL0R", 0, 128, 8), u("PC", 12, 13), A.mult, less, A.add)
+    ts(u("ROW1"), u("Jb", 0, 16), 0.0, A.mult, col(less, 32.0, A.mult), A.add)
+    ts(u("w64d"), u("BD", 0, 128, 8), 65536.0, A.mult)
+    for q in range(2):
+        ts(u("PENB", 8 * q, 8 * q + 8), u("blk"), -2.0 ** 17, A.mult, 2.0 ** 17, A.add)
     for s in (1, 2, 3, 4, 8, 12):
         select(u("SH", 128 * s, 128 * s + 128), BD, [[1, 128]], A.is_equal, 0.0, -s, -1)
-    select(u("EXP"), u("Z1"), [[-1, 128], [0, 16]], A.not_equal, 1.0, 0, 1)
     fourth = col(u("PIi", 4, 5), 3.0, A.is_equal, -128.0, A.mult)
     ts(u("A4n"), BD, fourth, A.mult)
     ts(u("B4"), BD, col(fourth, 4.0, A.mult, 128.0, A.add), A.mult)
 
     X, LISTS, OWNERS = u("X", 0, 2224), u("W", 0, 512), u("OT", 0, 2064)
 
-    def gather(out, off, cut):
-        cp(u(out, 0, 16 * cut), ix(X, u(off, 0, cut)))
-        if cut < 128:
-            act(u(out, 16 * cut, 2048), ix(X, u(off, cut, 128)), F.Copy)
+    def gather(out, win, off, cuts, many):
+        for k, (a, b) in enumerate(zip((0,) + cuts, cuts + (128,))):
+            if k < many:
+                cp(u(out, 16 * a, 16 * b), ix(win, u(off, a, b)))
+            else:
+                act(u(out, 16 * a, 16 * b), ix(win, u(off, a, b)), F.Copy)
 
     def part_own(t):
-        z, s1, s16 = "Z%d" % (t % 2), "S1%d" % (t % 2), "S16"
+        s1 = "S1%d" % (t % 2)
         lanes = u("W", t % 4, 512, 4)
         cp(u("OWN"), lanes)
-        gather("T", "OWN", 112 if t else 128)
+        gather("T", X, "OWN", CUT_T, 2 if t else 3)
         if t:
             act(u("PRE"), lanes, F.Sign)
         else:
@@ -588,17 +685,21 @@ def rank_program(g, core, T, topo):
         mm(k, (ONE, u("KAs")), (u("PRE"), u("N27")), (u("OWNH"), IDB), *sums("p3", 0, "T", "w64k"))
         scan(u(s1), u("MINs"), k, A.max, A.min)
         low(e16("ZS", 0, 128), e16(s1, 15), u("hi8"), 4096)
-        tile("ZS", "HS", u("p4", 0, 8), 1)
-        ts(u(s16), u("p4", 0, 8), 1088.0, A.add)
-        cp(e16(z), ix(X, u(s16)))
-        act(u("ZP%d" % (t % 2)), e16(z), F.Copy)
+        tile("ZS", "HS", u("p4", 0, 8), "blk", "nblk", "MC")
+        ts(u("S16"), u("p4", 0, 8), 1088.0, A.add)
+        cp(u("ZP%d" % (t % 2)), ix(X, u("S16")))
         send(u("ZP%d" % (t % 2)), "QA", "a", t, 1)
-        scan(u("SS"), u("MS", 0, 128), u("ZS", 0, 128), A.mult, A.add)
-        ts(u("AN"), ix(u("AC4"), u(s16)), 1, A.add)
-        scan(u("REP"), u("MS"), u(z), A.mult, A.add)
-        scan(u("US"), u("MS"), u("T"), A.mult, A.max)
+        tile("ZS", "HD", u("p4", 24, 32), "blk2", "nblk2", "MC2")
+        ts(u("A16"), u("p4", 24, 32), 1088.0, A.add)
+        ts(u("AN"), ix(u("AC4"), u("A16")), 1, A.add)
+        if not SPREAD:
+            cp(e16("Z0"), ix(X, u("A16")))
+        for a in range(0, 2048, CUT_S):
+            if not SPREAD:
+                scan(u("REP", a, a + CUT_S), u("MS", a, a + CUT_S), u("Z0", a, a + CUT_S), A.mult, A.add)
+            scan(u("US", a, a + CUT_S), u("MS", a, a + CUT_S), u("T", a, a + CUT_S), A.mult, A.max)
         mm(u("p4", 8, 16), (ONE, u("L2N")), (e16("US", 15), u("w64k")))
-        tt(u("wp8"), e16(s1, 15), u("p4", 8, 16), A.is_lt)
+        tt(u("wp8"), e16(s1, 15), u("p4", 8, 16), A.is_ge)
         mm(u("p6", 0, 128), (u("PRE"), u("SEL0R")))
         act(u("LR"), u("p6", 0, 128), F.Copy)
         mm(u("p6", 160, 288), (IDB, u("CN1")), (u("PRE"), u("B4")))
@@ -620,7 +721,7 @@ def rank_program(g, core, T, topo):
         act(u("NFF"), u("SEL0R"), F.Identity, scale=u("CS", 31, 32))
 
     def part_split(t):
-        s = e16("Z%d" % (t % 2))
+        s = u("ZP%d" % (t % 2))
         mm(u("p6", 288, 416), (s, NIDB))
         act(u("ST"), u("p6", 288, 416), F.Copy)
         for c in range(4):
@@ -632,7 +733,7 @@ def rank_program(g, core, T, topo):
         mm(k, (ONE, u("KAb")), (u("PRE"), u("P23")), *sums("p3", 128, "SQ", "w32"))
         scan(u("SB"), u("MS", 0, 128), k, A.mult, A.max)
         low(e16("ZB", 0, 128), e16("SB", 15), u("hb8"), 32)
-        tile("ZB", "HB", u("p4", 16, 24), -1, (IDB, u("CB")))
+        tile("ZB", "HB", u("p4", 16, 24), "nblk", "blk", "MC", (IDB, u("CB")))
         cp(u("B16"), u("p4", 16, 24))
         act(u("XB"), ix(u("T"), u("B16")), F.Copy)
         act(u("SQB"), u("XB"), F.Square)
@@ -663,47 +764,48 @@ def rank_program(g, core, T, topo):
 
     def part_near(t):
         iota(e16("MINn"), [[0, 8]], 13 * 2 ** 20 + t % 4)
-        for a in (0, 64):
-            if t:
-                act(u("OG", 16 * a, 16 * a + 1024), ix(OWNERS, u("AN", a, a + 64)), F.Copy)
-            else:
-                cp(u("OG", 16 * a, 16 * a + 1024), ix(OWNERS, u("AN", a, a + 64)))
-        for a, b in ((0, 56), (56, 104), (104, 128)):
-            tt(u("AX", 16 * a, 16 * b), ix(X, u("AN", a, b)), u("REP", 16 * a, 16 * b), A.subtract)
-            act(u("DU", 16 * a, 16 * b), u("AX", 16 * a, 16 * b), F.Square)
+        gather("OG", OWNERS, "AN", CUT_O, 0 if t else 2)
         k = u("p3", 256, 384)
-        mm(k, (ONE, u("KAn")), (u("PRE"), u("N25")), *(sums("p3", 256, "OG", "og%d" % (t % 4)) + sums("p3", 256, "DU", "w8k")))
+        mm(k, (ONE, u("KAn")), *[(u("og%d" % (t % 4), 15 - r, 143 - r), u("OG", 128 * r, 128 * r + 128)) for r in range(16)], ends=(True, False))
+        if SPREAD:
+            gather("AX", X, "AN", (32, 64, 96), 3)
+        for c, (a, b) in enumerate(zip((0,) + CUT_A, CUT_A + (128,))):
+            if SPREAD:
+                ps = u("p%d" % BANK_A[c], 0, 16 * (b - a))
+                mm(ps, (u("ST"), u("EXA", 16 * a, 16 * b)), (IDB, u("AX", 16 * a, 16 * b)))
+                act(u("DU", 16 * a, 16 * b), ps, F.Square)
+            else:
+                tt(u("AX", 16 * a, 16 * b), ix(X, u("AN", a, b)), u("REP", 16 * a, 16 * b), A.subtract)
+                act(u("DU", 16 * a, 16 * b), u("AX", 16 * a, 16 * b), F.Square)
+            mm(k, *[(u("w8k", 15 - r, 143 - r), u("DU", 128 * r, 128 * r + 128)) for r in range(a // 8, b // 8)], ends=(False, b == 128))
         scan(u("S2"), u("MINn"), k, A.max, A.min)
         cp(u("a8"), e16("S2", 15))
         ts(u("d8"), u("a8"), 511, A.bitwise_and)
-        cp(e16("ZD", 0, 128), u("d8"))
-        tile("ZD", "HD", u("p4", 24, 32), 1)
-        cp(u("D16"), u("p4", 24, 32))
+        cp(u("D16"), u("d8"))
 
     def part_partner(t):
         lists = ix(LISTS, u("D16"))
         cp(u("DM"), lists)
-        gather("DT", "DM", 80)
-        act(u("PRD"), lists, F.Sign)
+        gather("DT", X, "DM", CUT_D, 2)
         cp(u("DMH"), lists)
+        ts(u("PRD"), u("DMH"), 0.0, A.is_gt)
         codes = ix(u("CODE"), u("D16"))
-        codes = (codes[0], codes[1] + [("bit", 0, 9)]) + codes[2:]
-        for q in range(4):
+        for q in range(2):
             act(u("CG", 128 * q, 128 * q + 128), codes, F.Identity, scale=u("KQ", 4 * q + t % 4, 4 * q + t % 4 + 1))
-        for h in range(2):
-            ps = "p%d" % h
-            parts = [u("CG", 128 * q, 128 * q + 128, 1, (64 * h, 64 * h + 64)) for q in range(4)]
-            mm(u(ps), (IDB, u("PEN")), *[(x, x, u(ps, 128 * q, 128 * q + 128)) for q, x in enumerate(parts)])
-            act(u("EQ", 512 * h, 512 * h + 512), u(ps), F.Relu)
-        mm(u("p6", 416, 424), (u("PRE"), e16("BD")), (u("PRD"), e16("BD")))
-        act(u("SZ"), u("p6", 416, 424), F.Relu, scale=32.0, bias=-512.0)
-        for a, b in ((0, 1280), (1280, 2048)):
+        for h, ps in enumerate(("p0", "p1", "p2", "p6")):
+            parts = [u("CG", 128 * q, 128 * q + 128, 1, (32 * h, 32 * h + 32)) for q in range(2)]
+            mm(u(ps, 0, 256), (IDB, u("PEN")), *[(x, x, u(ps, 128 * q, 128 * q + 128)) for q, x in enumerate(parts)])
+            act(u("EQ", 256 * h, 256 * h + 256), u(ps, 0, 256), F.Relu)
+        mm(u("p6", 416, 432), (u("PRE"), u("BD", 0, 128, 8)), (u("PRD"), u("BD", 0, 128, 8)))
+        act(u("SZ"), u("p6", 416, 432), F.Relu, scale=32.0, bias=-512.0)
+        for a, b in zip((0,) + CUT_D, CUT_D + (128,)):
+            a, b = 16 * a, 16 * b
             cp(u("DT", a + 15, b, 16), u("US", a + 15, b, 16))
             scan(u("AX", a, b), u("MS", a, b), u("DT", a, b), A.mult, A.max)
         k = u("p3", 384, 512)
         mm(k, (ONE, u("KAd")), (u("PRD"), u("N27")), (u("IDF"), e16("S1%d" % (t % 2), 15), e16("p3", 399)), *sums("p3", 384, "DT", "w64k")[:15])
-        mm(u("p4", 96, 104), (ONE, u("THN")), (ONE, u("THZ")), (u("P23"), u("SZ")),
-           *[(u("EQ", 128 * q, 128 * q + 128), u("C25", 0, 1), u("p4", 96 + q, 97 + q)) for q in range(8)], (e16("AX", 15), u("w64k")))
+        mm(u("p4", 160, 176), (ONE, u("THN")), (ONE, u("THZ")), (u("N40"), u("wp8"), u("p4", 161, 176, 2)), (u("P23"), u("SZ")),
+           *[(u("EQ", 128 * q, 128 * q + 128), u("C25", 0, 2), u("p4", 160 + 2 * q, 162 + 2 * q)) for q in range(8)], (e16("AX", 15), u("w64d")))
         scan(u("S3"), u("MIN"), k, A.max, A.min)
         for src, step, out in (("DMH", 1, "D1"), ("DM2", 4, "DS")):
             for q in range(4):
@@ -713,10 +815,10 @@ def rank_program(g, core, T, topo):
                 cp(u("DM2"), ix(u("D1"), u("BT16")))
 
     def part_finish(t):
-        cl, ev = t % 4, u("EV", 0, 128)
+        cl, ev = t % 4, u("EVB")
         MR, WR, SR = u("MR"), u("WR"), u("SR")
-        tt(e16("ZM"), e16("S3", 15), u("p4", 96, 104), A.is_ge)
-        tt(e16("ZW"), u("wp8"), e16("ZM"), A.is_gt)
+        tt(e16("ZM"), e16("S3", 15), u("p4", 160, 176, 2), A.is_ge)
+        tt(e16("ZW"), e16("S3", 15), u("p4", 161, 176, 2), A.is_lt)
         scan(u("MWR"), u("MS", 0, 256), u("ZMW"), A.mult, A.add)
         k0, k1, k2 = u("p7", 384, 512), u("p5", 0, 128), u("p7", 0, 128)
         mm(k0, (ONE, u("K9")), (u("ONEF"), u("NFF")), (u("TRIm"), WR))
@@ -731,11 +833,11 @@ def rank_program(g, core, T, topo):
             mm(u("p4", 104 + q, 105 + q), (u("EE", 128 * q, 128 * q + 128), u("PB", 0, 1)))
         cp(u("SE%d" % t), u("p4", 104, 106))
         send(u("SE%d" % t), "QI", "q", t, 1)
+        mm(u("p4", 176, 192), (IDB, u("PENB")), *[(u("EE", 128 * q, 128 * q + 128), x, u("p4", 176 + 8 * q, 184 + 8 * q))
+                                                  for q in range(2) for x in (u("C3K"), e16("ZS", 0, 128))])
+        scan(u("SV"), u("MS", 0, 32, 2), u("p4", 176, 192), A.mult, A.min)
         for q in range(2):
-            e, ps = u("EE", 128 * q, 128 * q + 128), u("p4", 106 + q, 107 + q)
-            tt(u("ES", 128 * q, 128 * q + 128), e, u("SS"), A.mult)
-            mm(ps, (e, u("PB", 1, 2)), (u("ES", 128 * q, 128 * q + 128), u("ONEB", 0, 1)))
-            ts(u("S32", q, q + 1), ps, 4096.0, A.add, spare[q], A.min)
+            ts(u("S32", q, q + 1), u("SV", 8 * q + 7, 8 * q + 8), 4096.0, A.add, spare[q], A.min)
         a, b = u("p6", 0, 128), u("p6", 128, 256)
         mm(u("p6", 0, 256), (IDB, u("CNT")), (u("PRE"), u("A4n"), a), (u("P11"), MR, a), (u("P11"), SR, b))
         act(u("QN"), u("p6", 0, 256), F.Relu)
@@ -744,9 +846,9 @@ def rank_program(g, core, T, topo):
         tt(u("W", cl, 512, 4), ix(u("DS"), u("NT16")), u("OWNH"), A.add)
         act(ev, ix(u("FREE"), u("RK")), F.Copy)
         a, b = u("p0", 0, 128), u("p0", 128, 256)
-        mm(u("p0", 0, 256), (IDB, u("CTG")), (NIDB, u("HD", 0, 128), a), (u("P11"), MR, a), (u("P11"), SR, b), (ev, u("HWF"), b))
-        act(u("QR", 0, 256), u("p0", 0, 256), F.Relu)
-        mm(u("p4", 128, 136), (IDB, u("CT")), (u("QR", 0, 128), u("nblkf")), (u("QR", 128, 256), u("nblkf")))
+        mm(u("p0", 0, 256), (IDB, u("CTG")), (IDB, u("KD"), a), (u("CG", 0, 128), u("WD"), a), (u("CG", 128, 256), u("WD"), a), (u("P11"), MR, a), (u("P11"), SR, b), (ev, u("HWN"), b))
+        ts(u("QH"), u("p0", 0, 256), 0.0, A.max)
+        mm(u("p4", 128, 136), (IDB, u("CT")), (u("QH", 0, 128), u("nblk")), (u("QH", 128, 256), u("nblk")))
         ts(u("TG16"), u("p4", 128, 136), 512.0, A.add)
         mm(u("p1", 0, 128), (u("SL", 128, 256), NIDB), (MR, u("N20")))
         ts(u("ELS"), u("p1", 0, 128), 0.0, A.max)
@@ -756,21 +858,25 @@ def rank_program(g, core, T, topo):
         if t + 1 == RO:
             return
         a, b = u("p7", 128, 256), u("p7", 256, 384)
-        ts(u("PRL"), u("SL", 128, 256), 0.0, A.is_lt)
         mm(a, (ONE, u("KAm")), (u("DMH"), IDB), (u("PRD"), u("N20")), (u("N20"), MR))
-        mm(b, (ONE, u("KAm")), (NIDB, u("SL", 128, 256)), (u("N20"), u("PRL")), (u("N20"), SR))
+        if MOVERS == 15:
+            ts(u("PRL"), u("SL", 128, 256), 0.0, A.is_lt)
+            mm(b, (ONE, u("KAm")), (NIDB, u("SL", 128, 256)), (u("N20"), u("PRL")), (u("N20"), SR))
+        else:
+            mm(b, (ONE, u("KAm")), (u("OWNH"), IDB), (u("N20"), u("LN", 0, 128)), (u("N20"), SR))
         tt(u("m1"), a, u("DUL"), A.min)
         tt(u("m2"), b, u("m1"), A.min)
         for j in range(8):
-            mm(u("p1", 128 + j, 248, 8), *[(u("YL", 240 * j + 112 - 16 * q, 240 * j + 240 - 16 * q), u("m2", 16 * q, 16 * q + 15)) for q in range(8)])
-        ts(u("MVO", 0, 120), u("p1", 128, 248), 1536.0, A.add)
-        cp(u("EV", 128, 256), ev)
-        cp(u("EV", 256, 512), u("EV", 0, 256))
-        for a in range(0, 120, 32):
-            b = min(a + 32, 120)
+            mm(u("p1", 128 + j, 128 + 8 * MOVERS, 8), *[(u("YL", 240 * j + 112 - 16 * q, 240 * j + 240 - 16 * q), u("m2", 16 * q, 16 * q + MOVERS)) for q in range(8)])
+        ts(u("MVO", 0, 8 * MOVERS), u("p1", 128, 128 + 8 * MOVERS), 1536.0, A.add)
+        cp(u("EV", 0, 128), ev)
+        for q in range(1, 4):
+            dma(u("EV", 128 * q, 128 * q + 128), u("EV", 0, 128), "ev%d" % (3 * t + q - 1), 0, 3.0)
+        for a in range(0, 8 * MOVERS, 32):
+            b = min(a + 32, 8 * MOVERS)
             act(ix(u("OT"), u("MVO", a, b)), u("EV", 0, 16 * (b - a)), F.Silu)
-        mm(u("p6", 424, 432), (ONE, e16("ZM")))
-        act(u("z8"), u("p6", 424, 432), F.Identity, bias=-0.9375, acc=u("mc", 0, 1))
+        mm(u("p6", 432, 440), (ONE, e16("ZM")))
+        act(u("z8"), u("p6", 432, 440), F.Identity, bias=-0.9375, acc=u("mc", 0, 1))
         ts(u("mc", 1, 2), u("mc", 0, 1), 1.5 * 2.0 ** 27, A.add, 1.5 * 2.0 ** 27, A.subtract)
         ts(u("mc", 2, 3), u("mc", 0, 1), u("mc", 1, 2), A.subtract, 7.5, A.add)
         act(u("THZ"), u("ROW1"), F.Identity, scale=u("mc", 2, 3))
@@ -824,6 +930,8 @@ def rank_program(g, core, T, topo):
         if t:
             part_apply(t - 1)
         part_near(t)
+        if not t:
+            owners(0)
         part_partner(t)
         part_look(t)
         part_finish(t)
@@ -866,8 +974,11 @@ def rank_program(g, core, T, topo):
         for (b, lo, hi) in reads:
             log[b] = [x for x in log.get(b, []) if not (x[2] == e and not x[5] and lo <= x[0] and x[1] <= hi and x[3] == sem)] + [(lo, hi, e, sem, val, False)]
 
-    for i in _ORDER["o"]:
+    order, queues = _ORDER["o"]
+    for i in order:
         o = ops[i]
+        if o["e"] != queues[i]:
+            o["e"], o["fn"], o["cost"] = o["alt"]
         e, rd, wr = o["e"], o["rd"], o["wr"]
         if o["land"]:
             sem, landed, loc, left = o["land"]
@@ -879,10 +990,11 @@ def rank_program(g, core, T, topo):
             total[sem] = landed
             continue
         if o["items"]:
+            wr = [x for x in wr if _psum(x[0])]
             wait(e, [], wr)
             for j, (x, a, b) in enumerate(o["items"]):
                 wait(e, a[1] + b[1], [])
-                ins = g.tensor.matmul(x[0], a[0], b[0], j == 0, j == len(o["items"]) - 1)
+                ins = g.tensor.matmul(x[0], a[0], b[0], j == 0 and o["fn"][0], j == len(o["items"]) - 1 and o["fn"][1])
         else:
             wait(e, rd, wr)
             ins = o["fn"]()

@@ -5,6 +5,7 @@ RO = 5
 S, B, H, I, U = "float32", "bfloat16", "float16", "int32", "uint16"
 LOW = 1 - 2 ** 24
 TAU = 4096.0
+SCAN_I = True
 _BUF = []
 
 
@@ -13,39 +14,53 @@ def _sb(dtype, cols, names):
 
 
 _sb(B, 2304, "X")
-_sb(B, 2048, "T MS US SQ AX AW SH OG DT DU EXP EXA REP Z0")
+_sb(B, 2048, "T US SQ AX AW SH OG DT DU EXP EXA REP Z0")
+_sb(B, 512, "MS PR5")
+_sb(H, 512, "PF LT")
+_sb(B, 256, "YO")
+_sb(B, 144, "YH YK")
+_sb(B, 128, "UP UP11 N11 H15")
+_sb(H, 128, "PA")
+_sb(S, 1024, "SO")
+_sb(S, 512, "V0P MK")
+_sb(I, 256, "MT")
+_sb(S, 256, "DUM")
 _sb(H, 1024, "RH")
 _sb(S, 16, "two")
 _sb(B, 128, "MC2 WD")
-_sb(H, 128, "KD")
+_sb(B, 2048, "UD")
+_sb(B, 128, "P768")
+_sb(S, 256, "TGS MAXT")
+_sb(S, 128, "KR MINR")
+_sb(I, 128, "S2i")
 _sb(B, 8, "blk2 nblk2")
-_sb(B, 1920, "YL")
 _sb(B, 1024, "EQ")
 _sb(B, 768, "XF")
-_sb(B, 512, "CODE QD OCC QZ QRp QS KQ5")
+_sb(B, 512, "CODE QD OCC QZ QRp QS")
+_sb(B, 256, "KQ5")
+_sb(S, 256, "MIN5")
+_sb(I, 512, "QRi")
 _sb(B, 256, "PEN CG ID2 KAp QN LN XC ZMW MWR EE PEN2 M32")
 _sb(B, 144, "Jb Y w8k og0 og1 og2 og3")
 _sb(B, 128, "J4b J15b b1 b2 R16 MC IDB BD NBD BTI ONEB PRE PRD LR SR XB SQS SQB SEL0R TRIm NTRIm HWN N27 N20 P23 P20 P11 "
-            "RV0 RV1 RV2 RV3 ST KAs KAb KAd KAn KAr KAm K9 K11 K20 PRL WV A4n B4 CN1 QB ZP0 ZP1 WTp IDh B256 B512 N512 HO PA EH PENW WM")
+            "RV0 RV1 RV2 RV3 ST KAs KAb KAd KAn KAr KAm PENK PRL WV A4n B4 CN1 QB ZP0 ZP1 WTp IDh B256 B512 N512 HO EH PENW WM")
 _sb(B, 32, "OCb")
 _sb(B, 16, "THN THZ ROW1 SZ w64d PENB")
 _sb(B, 8, "blk nblk w64k w32 w2 SEL0 L2N wp8 C25 PB C3K")
-_sb(H, 256, "SL CNT CTG QH")
+_sb(H, 256, "SL CNT CTG")
 _sb(H, 144, "ZS HS ZB HB HD")
-_sb(H, 128, "OWNH DMH DM2 CMK0 CMK1 CMK2 CMK3 KR KV m1 m2")
+_sb(H, 128, "OWNH DMH DM2 KV m1 m2 NFF")
 _sb(H, 32, "CIX")
 _sb(H, 8, "CB")
 _sb(S, 4112, "OT")
-_sb(S, 2048, "VE VG")
 _sb(S, 1536, "FREE")
 _sb(S, 768, "DS")
-_sb(B, 640, "ALT")
 _sb(B, 128, "EVB N40")
 _sb(S, 640, "W")
-_sb(S, 512, "J2f J3f t512a t512b YM QR D1 MIN5 EV")
+_sb(S, 512, "J2f J3f t512a t512b YM QR D1 EV")
 _sb(S, 264, "Pa Pb")
 _sb(S, 256, "WP")
-_sb(S, 128, "MINs MINn MIN S10 S11 S2 S3 SB ELS IDF ONEF NFF VH VR HLA DUL DUM")
+_sb(S, 128, "MINs MINn MIN S10 S11 S2 S3 SB ELS IDF VH VR HLA DUL")
 _sb(S, 80, "PC")
 _sb(S, 32, "CS r1 r2 C512 hs ht")
 _sb(S, 16, "E16 KQ SV")
@@ -54,7 +69,7 @@ _sb(I, 2192, "AC4")
 _sb(I, 512, "MI")
 _sb(I, 8, "PIi a8 d8")
 _sb(I, 2, "LI WI")
-_sb(U, 512, "INO")
+_sb(U, 576, "INO")
 _sb(U, 128, "OWN AN DM MVO")
 _sb(U, 32, "F16 HL")
 _sb(U, 8, "RK S16 A16 B16 D16 NT16 TG16 BT16 VV16 H16 O16")
@@ -68,23 +83,26 @@ for _n, _m, _o, _c in (("NIDB", "ID2", 0, 128), ("ZM", "ZMW", 0, 128), ("ZW", "Z
                        ("ZALL", "ZS", 0, 720), ("MIN3", "MINs", 0, 384), ("CT", "CIX", 0, 8)):
     _AT[_n] = (_AT[_m][0], _AT[_m][1] + _o, _c, _AT[_m][3])
 for _t in range(RO):
-    for _n, _c, _d in (("QA", 128, B), ("SE", 2, U), ("QI", 2, U), ("SN", 32, B), ("RS", 32, B)):
+    for _n, _c, _d in (("QA", 128, B), ("SE", 2, U), ("QI", 2, U), ("SN", 32, I if SCAN_I else B), ("RS", 32, I if SCAN_I else B)):
         SCRATCH["%s%d" % (_n, _t)] = ("sbuf", [128, _c], _d)
         _AT["%s%d" % (_n, _t)] = ("%s%d" % (_n, _t), 0, _c, _d)
 for _k in range(8):
     SCRATCH["p%d" % _k] = ("psum", [128, 512], S)
     _AT["p%d" % _k] = ("p%d" % _k, 0, 512, S)
-SEMAPHORES = ["v", "p", "s", "k", "st0", "st1"] + ["ld%d" % i for i in range(8)]
-SEMAPHORES += [n + str(i) for n in ("va", "vb") for i in range(4)] + ["ev%d" % i for i in range(3 * RO - 3)]
+SEMAPHORES = ["v", "p", "s", "k", "st0", "st1"] + ["ld%d" % i for i in range(11)] + ["ev%d" % i for i in range(RO - 1)]
 for _t in range(RO):
     SEMAPHORES += [a + b + str(_t) for a in "rlfm" for b in "aqs"]
 
-CYC, PEC, GAT, SCA, WAKE, XWAKE, WAY, FIRST = 0.00085, 0.0005, 1.6, 3.7, 0.24, 0.12, 2.3, 2.5
-VIEWS = ((0.26, 0.11, 1.0, 0.92, 0.8), (0.21, 0.17, 1.0, 0.75, 0.55), (0.27, 0.14, 1.22, 1.4, 1.65))
+CYC, PEC, GAT, SCA, WAY, FIRST = 0.00085, 0.0005, 1.6, 3.7, 2.3, 2.5
+START, PERKB = 2.2, 0.005
+VIEWS = ((0.23, 0.14, 1.0, 0.8, 0.62), (0.26, 0.13, 1.15, 1.2, 1.3))
 PLAN, PASSES = (0.24, 0.14, 1.0, 0.92, 0.8), 8
-TURNS, AGAIN, EASE = 27000, 600, 0.15
-MOVERS = 16
-BANK_A, SPREAD, CUT_A = (0, 1, 2, 0), False, (56, 104)
+TURNS, AGAIN, EASE = 50000, 800, 0.15
+MOVERS = 15
+RANKS = [-(-(2048 // (_k + 1)) // 16) * 16 for _k in range(16)]
+CUT_A, BY_PE, BANK_Q, BANK_A = (32, 64, 104), (0, 1), "p0", ("p2", "p2", "p2", "p2")
+BANK_E, BANK_D, BANK_B = (("p0", 0), ("p1", 0), ("p2", 0), ("p6", 0)), "p2", ("p7", 0)
+PLAIN = 5
 CUT_T, CUT_D, CUT_O, CUT_S = (32, 64, 96), (32, 64, 96), (32, 64, 96), 512
 _ORDER = {}
 
@@ -152,7 +170,7 @@ def _order(ops):
     eng, cost, lat = [o["e"] for o in ops], [o["cost"] for o in ops], [o["lat"] for o in ops]
     banks = [sorted(set(b for (b, _l, _h) in o["rd"] + o["wr"] if _psum(b))) for o in ops]
     views = [([0.0] * n, x[1], [None] * n) for x in VIEWS]
-    queue, mine, others, other = [0] * n, [None] * n, [None] * n, [o["alt"] and (o["alt"][0], o["alt"][2]) for o in ops]
+    queue, mine, others, ways = [0] * n, [None] * n, [None] * n, [o["ways"] for o in ops]
 
     def settle(calls, after):
         for i in calls:
@@ -165,8 +183,8 @@ def _order(ops):
             for i in after:
                 inc[i] = [(j, c[j] + lat[j] + (xw if eng[j] != eng[i] else 0.0 if eng[i] == "p" else wake) - mul * early.get((j, i), 0.0)) for j in pred[i]]
 
-    def move(i):
-        other[i], (eng[i], cost[i]) = (eng[i], cost[i]), other[i]
+    def move(i, e):
+        eng[i], cost[i] = e, ways[i][e][1]
         settle([i], [i] + succ[i])
     settle(range(n), range(n))
 
@@ -238,7 +256,7 @@ def _order(ops):
         while ready:
             a = ready.pop()[1]
             found = None
-            for e, c in [(eng[a], cost[a])] + ([other[a]] if choose and other[a] else []):
+            for e, c in [(eng[a], cost[a])] + [(e2, x[1]) for e2, x in ways[a].items() if choose and e2 != eng[a]]:
                 c *= (mul, gat, sca)[ops[a]["how"]]
                 s = lat[a] if back else 0.0
                 for j in before[a]:
@@ -254,7 +272,7 @@ def _order(ops):
                 if found is None or s + 2 * c < found[3] - 0.02:
                     found = (s + c, s, e, s + 2 * c)
             if found[2] != eng[a]:
-                move(a)
+                move(a, found[2])
             end[a], start[a] = found[:2]
             for key in [eng[a]] + banks[a]:
                 busy.setdefault(key, []).append((start[a], end[a], eng[a]))
@@ -282,7 +300,7 @@ def _order(ops):
         way = place(end, True, False)[1]
     for i in range(n):
         if eng[i] != best[2][i]:
-            move(i)
+            move(i, best[2][i])
     order = best[1]
     span, state = clock(order, 0, n, None, 0.0)
     pairs = chain(state)
@@ -296,9 +314,11 @@ def _order(ops):
         seed = (seed * 1103515245 + 12345) % 2147483648
         b, a = pairs[(seed >> 8) % len(pairs)]
         up = bool((seed >> 4) & 1)
-        moved = (a if up else b) if (seed >> 5) % 3 == 0 and other[a if up else b] else None
+        moved = (a if up else b) if (seed >> 5) % 3 == 0 and len(ways[a if up else b]) > 1 else None
         if moved is not None:
-            move(moved)
+            was = eng[moved]
+            to = [e for e in ways[moved] if e != was]
+            move(moved, to[(seed >> 20) % len(to)])
             trial, i, mid = order, order.index(moved), [moved]
         else:
             i = order.index(b)
@@ -317,7 +337,7 @@ def _order(ops):
             order, span, state, pairs = trial, s2, new, chain(new)
             best = min(best, (span, order, eng[:]))
         elif moved is not None:
-            move(moved)
+            move(moved, was)
     return best[1:]
 
 
@@ -349,7 +369,10 @@ def rank_program(g, core, T, topo):
     def op(e, fn, outs, ins, cost, dma=None, lat=0.0, items=None, land=None, alt=None):
         rd = [r for x in ins for r in x[1]] + [r for x in outs if x[4] for r in x[1][1:]]
         wr = [r for x in outs for r in (x[1][:1] if x[4] else x[1])]
-        ops.append({"e": e, "fn": fn, "rd": rd, "wr": wr, "cost": cost, "dma": dma, "lat": lat, "items": items, "land": land, "first": first[0], "alt": alt,
+        ways = {e: (fn, cost)}
+        if alt:
+            ways[alt[0]] = alt[1:]
+        ops.append({"e": e, "fn": fn, "rd": rd, "wr": wr, "cost": cost, "dma": dma, "lat": lat, "items": items, "land": land, "ways": ways,
                     "how": 2 if outs[0][4] else 1 if ins and ins[0][4] else 0})
 
     def _c(x):
@@ -385,8 +408,8 @@ def rank_program(g, core, T, topo):
         per = 1.0 if _psum(a[1][0][0]) or _psum(b[1][0][0]) else 2.0
         op("v", lambda: v.tensor_tensor(o[0], a[0], b[0], o1), [o], [a, b], cost(o, [a, b], per))
 
-    def scan(o, a, b, o1, o2):
-        op("v", lambda: v.tensor_tensor_scan(o[0], a[0], b[0], 0.0, o1, o2), [o], [a, b], cost(o, [a, b], 0.5))
+    def scan(o, a, b, o1, o2, init=0.0):
+        op("v", lambda: v.tensor_tensor_scan(o[0], a[0], b[0], _c(init), o1, o2), [o], [a, b] + _r(init), cost(o, [a, b], 0.5))
 
     def fill(o, c):
         kw = {} if o[3] == I else {"allow_small_or_imprecise_dtypes": True}
@@ -404,7 +427,7 @@ def rank_program(g, core, T, topo):
             fn = lambda: v.tensor_scalar(o[0], i[0], 0.0, None, A.max if f == F.Relu else A.is_gt)
         elif f == F.Square and not _psum(i[1][0][0]):
             fn, per = lambda: v.tensor_tensor(o[0], i[0], i[0], A.mult), 2.0
-        op("s", lambda: sc.activation(o[0], i[0], f, **kw), [o] + _r(acc), [i] + _r(scale, bias), cost(o, [i], 1.0) + 0.02,
+        op("s", lambda: sc.activation(o[0], i[0], f, **kw), [o] + _r(acc), [i] + _r(scale, bias) + [mark("silu")] * (f == F.Silu), cost(o, [i], 1.0) + 0.02,
            alt=fn and ("v", fn, cost(o, [i], per)))
 
     def iota(o, pat, base, cm=0, after=None):
@@ -415,19 +438,33 @@ def rank_program(g, core, T, topo):
     def select(o, i, pat, test, other, base, cm):
         op("k", lambda: g.affine_select(o[0], i[0], pat, test, other, base, cm), [o], [i], 0.2 + 2 * o[2] * CYC)
 
-    def mm(out, *pairs, ends=(True, True)):
+    def mm(out, *pairs, ends=(True, True), size=0):
         items = [(x[2] if len(x) > 2 else out, x[0], x[1]) for x in pairs]
         keys = [mark("keys")] if out[1][0][0] == "p3" else []
-        op("p", ends, [x[0] for x in items] + keys, [y for x in items for y in x[1:]], sum(_cycles(a, b) for _o, a, b in items) * PEC, items=items)
+        size = size or len(items)
+        flags = [(j % size == 0 and ends[0], j % size == size - 1 and ends[1]) for j in range(len(items))]
+        op("p", flags, [x[0] for x in items] + keys, [y for x in items for y in x[1:]], sum(_cycles(a, b) for _o, a, b in items) * PEC, items=items)
 
-    def dma(o, i, sem, haste=50, lat=4.0):
-        first[0] = haste
-        op("y", lambda: g.sync.dma_start(o[0], i[0]), [o], [i], 0.1, dma=sem, lat=lat)
-        first[0] = 0
+    def dma(pairs, sem, kb):
+        op("y", lambda: [g.sync.dma_start(o[0], i[0]) for o, i in pairs], [o for o, i in pairs], [i for o, i in pairs],
+           max(0.1 * len(pairs), kb * PERKB), dma=sem, lat=START)
 
-    def rows(dst, row, src, src_row, outs, ins, sem):
-        (b1, l1, h1), (b2, l2, h2) = dst[1][0], src[1][0]
-        op("y", lambda: g.sync.dma_start(T[b1][row:128:16, l1:h1], T[b2][src_row:128:16, l2:h2]), outs, ins, 0.1, dma=sem, lat=3.0)
+    def row(x, k):
+        b, lo, hi = x[1][0]
+        return (T[b][k:128:16, lo:hi],) + x[1:]
+
+    def times_id(name, val):
+        o = u(name) if isinstance(name, str) else name
+        act(o, IDB, F.Identity, scale=val)
+        ops[-1]["ways"]["k"] = (lambda: g.affine_select(o[0], IDB[0], [[-1, 128]], A.not_equal, val, 0, 1), 0.2 + 256 * CYC)
+
+    def unfold(ps, first, step, src, at, j, n, rows=128):
+        pairs = []
+        for h in range(4):
+            for m, w, lo, q in ((32, "YO", 32 * j, 1), (16, "IDB", 16 * j, 0)):
+                pairs.append((u(w, lo, lo + m, 1, (0, rows)), u(src, at + 32 * h + 16 * q, at + 32 * h + 16 * q + n, 1, (0, rows)),
+                              u(ps, first, first + step * (n - 1) + 1, step, (32 * h, 32 * h + m))))
+        mm(pairs[0][2], *pairs, size=2)
 
     def send(src, buf, kind, t, way):
         dst, back = T.cores[(rank + way * (1 + t % 7)) % 8], T.cores[(rank - way * (1 + t % 7)) % 8]
@@ -452,15 +489,15 @@ def rank_program(g, core, T, topo):
         tt(z, key, hi, A.subtract)
 
     fill(u("X", 0, 16), -64.0)
-    fill(u("X", 2048, 2304), 0.0)
+    fill(u("X", 2048, 2216), 0.0)
+    fill(u("X", 2216, 2224), 64.0)
     fill(u("AC4", 0, 8), 0)
     fill(u("AC4", 2048, 2192), 2048)
-    dma(u("MI"), mark("ml", ap=T.ml[:]), "ld0", 70)
-    dma(u("X", 1, 2049), mark("x0", ap=T.x0[:]), "ld1")
-    dma(u("LI"), mark("lims", ap=T.lims[:]), "ld2")
-    dma(u("WI", 0, 1), mark("wt", ap=T.wt[:]), "ld3")
-    for q in range(4):
-        dma(u("AC4", 1 + 512 * q, 513 + 512 * q), mark("ac", ap=T.ac[:]), "ld%d" % (4 + q))
+    dma([(u("MI"), mark("ml", ap=T.ml[:]))], "ld0", 256)
+    dma([(u("MT", 32 * k, 32 * k + 32), mark("ml", ap=T.ml[k:128:16, :])) for k in range(PLAIN)], "ld4", 50 * PLAIN)
+    dma([(u("X", 1, 2049), mark("x0", ap=T.x0[:]))], "ld1", 512)
+    dma([(u("LI"), mark("lims", ap=T.lims[:])), (u("WI", 0, 1), mark("wt", ap=T.wt[:]))], "ld2", 60)
+    dma([(u("AC4", 1 + 512 * q, 513 + 512 * q), mark("ac", ap=T.ac[:])) for q in range(4)], "ld3", 1024)
     J, J4, J15, J144, J8 = u("Jb", 0, 128), u("J4b"), u("J15b"), u("Jb"), u("Jb", 0, 8)
     P, P4, P15 = u("PC", 0, 1), u("PC", 1, 2), u("PC", 2, 3)
     IDB, NIDB, ONE, BD, NBD = u("IDB"), u("NIDB"), u("ONEB"), u("BD"), u("NBD")
@@ -475,18 +512,19 @@ def rank_program(g, core, T, topo):
     iota(J144, [[1, 144]], 0)
     iota(J15, [[0, 8], [1, 16]], 0)
     iota(J4, [[1, 8], [0, 16]], 0)
-    first[0] = 40
-    iota(u("DUM"), [[16, 128]], 2064)
-    for a in (0, 1024):
-        iota(u("SQ", a, a + 1024), [[1, 64], [0, 16]], 128 + a // 16)
-    first[0] = 0
-    iota(u("J2f"), [[1, 128], [0, 4]], 0)
+    iota(u("DUM", 0, 32 * PLAIN), [[0, PLAIN], [16, 32]], 2063, 1)
+    iota(u("J2f"), [[1, 128], [0, 4]], 128)
     iota(u("J3f"), [[0, 128], [1, 4]], 0)
-    iota(u("PC", 4, 8), [[1, 4]], 1024, 4)
-    iota(u("PC", 8, 10), [[512, 2]], 8192 - 1536, 1)
-    iota(u("PC", 10, 11), [[0, 1]], 128, 1)
-    for o, val in ((u("FREE", 0, 1024), 0), (u("QZ"), 0), (u("DS", 640, 768), 0), (u("ALT"), 0), (u("MIN5"), LOW), (e16("MIN5"), -LOW)):
+    iota(u("t512a"), [[1, 8], [0, 4], [8, 16]], 128)
+    iota(u("t512b"), [[0, 8], [1, 4], [0, 16]], 0)
+    for o, val in ((u("QZ"), 0), (u("DS", 640, 768), 0), (u("MIN5"), LOW), (e16("MIN5"), -LOW), (u("SO", 0, RANKS[PLAIN]), 256), (u("OT", 0, 1), 0)):
         iota(o, [[0, o[2]]], val)
+    FROM = 512 * len(BY_PE)
+    if FROM < 2048:
+        dma([(u("Z0", a, a + 512), u("QZ")) for a in range(FROM, 2048, 512)], "ld5", 512 - FROM // 4)
+    dma([(u("FREE", a, a + 512), u("J2f")) for a in (0, 512)], "ld6", 512)
+    fill(u("UD", 0, 512), 64.0)
+    dma([(u("UD", a, a + 512), u("UD", 0, 512)) for a in range(512, 2048, 512)], "ld10", 384)
     for o, val in ((u("MS"), 1.0), (e16("MS"), 0.0), (u("W", 512, 640), 0.0)):
         fill(o, val)
     ts(u("PIi", 1, 2), u("PIi", 0, 1), 4, A.logical_shift_right)
@@ -495,64 +533,31 @@ def rank_program(g, core, T, topo):
     ts(u("E16"), u("J15b", 0, 16), P15, A.is_equal)
     ts(u("EP", 0, 4), u("Jb", 0, 4), P, A.is_equal)
     row0, row4 = u("E16", 0, 1), u("E16", 4, 5)
-    V0 = u("FREE", 1024, 1536)
-    base = col(row4, 128.0, A.mult)
-    act(u("p4"), u("J2f"), F.Identity, scale=row4, bias=base)
-    ts(u("t512b"), u("J3f"), P15, A.is_equal, 64.0, A.mult)
-    tt(V0, u("t512b"), u("p4"), A.add)
-    first[0] = 40
-    ts(u("DUM"), u("DUM"), P15, A.add)
-    zero = col(row0, 64.0, A.mult, base, A.add)
-    one, two = [col(u("E16", c, c + 1), u("E16", 5, 6), A.add, 64.0, A.mult) for c in (1, 2)]
-    for a in (0, 1024):
-        act(u("VE", a, a + 1024), u("SQ", a, a + 1024), F.Identity, scale=row4, bias=one)
-        act(u("VG", a, a + 1024), u("SQ", a, a + 1024), F.Identity, scale=row4, bias=two)
-        act(u("OT", a, a + 1024), u("MS", a, a + 1024), F.Identity, scale=0.0, bias=zero)
-    act(u("OT", 2048, 2049), u("MS", 0, 1), F.Identity, scale=0.0, bias=zero)
+    V0, V0P = u("FREE", 1024, 1536), u("V0P")
+    for o, cls, high, sem in ((V0P, "t512b", "t512a", "ld7"), (V0, "J3f", "J2f", "ld8")):
+        ts(o, u(cls), P15, A.is_equal, 64.0, A.mult)
+        dma([(row(o, 4), row(u(high), 4))], sem, 40)
     every = col(P15, 4.0, A.is_lt, 64.0, A.mult)
-    act(u("OT", 2049, 2064), u("MS", 0, 15), F.Identity, scale=0.0, bias=col(every, base, A.add))
-
-    def owners(c):
-        for h in range(2):
-            ve, at = u("VE" if c % 2 else "VG", 1024 * h, 1024 * h + 1024), 4 * (c % 2) + 2 * h
-            both = [("row", at, at + 2)]
-            if c in (0, 3):
-                rows(ve, c, ve, 5, [mark("row", at, at + 1)], [ve], "va%d" % (at // 2))
-                rows(ve, (c - 2) % 4, ve, 6, [mark("row", at + 1, at + 2)], [ve], "vb%d" % (at // 2))
-            act(ix(u("OT"), u("INO", 128 * c + 64 * h, 128 * c + 64 * h + 64)), (ve[0], ve[1] + both) + ve[2:], F.Silu)
-    for c in (1, 0, 2, 3):
-        first[0] = 40 if c == 1 else 25
-        a, b, ml = 128 * c, 128 * c + 128, u("MI", c, 512, 4)
-        ts(u("p6", a, b), ml, 2048, A.is_lt, 8192.0, A.mult)
-        ts(u("t512a", a, b), ml, 1, A.add)
-        tt(u("p5", a, b), u("DUM"), u("p6", a, b), A.subtract)
-        tt(u("YM", a, b), u("t512a", a, b), u("p6", a, b), A.min)
-        tt(u("t512a", a, b), u("YM", a, b), u("p5", a, b), A.max)
-        cp(u("INO", a, b), u("t512a", a, b))
-        cp(u("W", c, 512, 4), u("YM", a, b))
-        first[0] = 30
-        if c:
-            owners(c)
-    first[0] = 0
-    first[0] = 10
+    act(u("OT", 2049, 2064), u("MS", 0, 15), F.Identity, scale=0.0, bias=col(row4, 128.0, A.mult, every, A.add))
     ts(IDB, J, P, A.is_equal)
     ts(BD, J4, P4, A.is_equal)
     ts(u("blk"), J8, P4, A.is_equal)
     ts(u("R16"), J15, P15, A.is_equal)
-    for name, src, val in (("nblk", "blk", -1.0), ("N40", "IDB", -2.0 ** 40), ("w64k", "blk", 65536.0), ("w32", "blk", 32.0),
-                           ("NBD", "BD", -1.0), ("IDF", "IDB", 1.0), ("SEL0R", "BD", row0), ("SEL0", "blk", row0),
-                           ("NIDB", "IDB", -1.0), ("N27", "IDB", -2.0 ** 27), ("N20", "IDB", -2.0 ** 20), ("P23", "IDB", 2.0 ** 23),
-                           ("P11", "IDB", 2.0 ** 11), ("RV0", "IDB", 90.0 * TAU), ("RV1", "IDB", 30.0 * TAU), ("RV2", "IDB", 10.0 * TAU),
-                           ("RV3", "IDB", -54.0 * TAU), ("P20", "IDB", 2.0 ** 20)):
+    for name, src, val in (("nblk", "blk", -1.0), ("w64k", "blk", 65536.0), ("w32", "blk", 32.0),
+                           ("NBD", "BD", -1.0), ("SEL0R", "BD", row0), ("SEL0", "blk", row0)):
         act(u(name), u(src), F.Identity, scale=val)
+    for name, val in (("N40", -2.0 ** 40), ("IDF", 1.0), ("NIDB", -1.0), ("N27", -2.0 ** 27), ("N20", -2.0 ** 20), ("P23", 2.0 ** 23),
+                      ("P768", 768.0), ("N11", -2.0 ** 11), ("RV0", 90.0 * TAU), ("RV1", 30.0 * TAU), ("RV2", 10.0 * TAU),
+                      ("RV3", -54.0 * TAU), ("P20", 2.0 ** 20), (u("ID2", 128, 256), -1.0), ("IDh", 0.5)):
+        times_id(name, val)
+    op("s", lambda: sc.activation(u("P11")[0], IDB[0], F.Silu, scale=2.0 ** 11), [u("P11"), mark("silu")], [IDB], 1.5)
     act(u("CN1"), u("R16"), F.Identity, scale=8192.0, bias=-8192.0)
-    act(u("ID2", 128, 256), IDB, F.Identity, scale=-1.0)
-    first[0] = 0
     ts(u("MC"), J15, P15, A.is_le)
     fill(e16("MC"), 0.0)
     fill(ONE, 1.0)
-    ts(u("ZALL"), u("MS", 0, 720), 0.0, A.mult)
-    for name, slope, c1, c2 in (("KAs", 4096.0, 2.0 ** 27, -1088.0), ("KAb", -1.0, -2.0 ** 23, 7.0), ("KAn", 512.0, -2.0 ** 24, 0.0), ("KQ5", 16.0, -7.25, 0.0),
+    for a in (0, 360):
+        ts(u("ZALL", a, a + 360), u("MS", 0, 360), 0.0, A.mult)
+    for name, slope, c1, c2 in (("KAs", 4096.0, 2.0 ** 27, -1088.0), ("KAb", -1.0, -2.0 ** 23, 7.0), ("KAn", 512.0, -2.0 ** 24, 0.0), ("KQ5", 16.0, -0.25 if SCAN_I else -7.25, 0.0),
                                 ("KAr", -1.0, 2048.0, 0.0), ("KAm", 0.0, 2.0 ** 21, -1536.0)):
         b = col(u("EP", 1, 2), c1, A.mult)
         if c2:
@@ -563,9 +568,7 @@ def rank_program(g, core, T, topo):
     ts(b, u("EP", 3, 4), 81.0 * TAU, A.mult, b, A.add)
     ts(u("KAp"), u("MS", 0, 256), 0.0, A.mult, b, A.add)
     cp(u("KQ5", 128, 256), u("KQ5", 0, 128))
-    cp(u("KQ5", 256, 512), u("KQ5", 0, 256))
-    for o, val in ((u("KAd"), 2 ** 20), (u("K11"), 2 ** 4), (u("K20"), 2 ** 13), (u("THZ"), 0), (u("MIN3"), LOW), (u("ZMW"), 0),
-                   (u("K9"), 12), (u("ONEF"), 1), (e16("KAd", 15), 0), (u("Pa", 256, 264), 2 ** 20), (u("Pb", 256, 264), 2 ** 20), (e16("MIN"), -LOW)):
+    for o, val in ((u("KAd"), 2 ** 20), (u("THZ"), 0), (u("MIN3"), LOW), (u("ZMW"), 0), (e16("KAd", 15), 0), (u("Pa", 256, 264), 2 ** 20), (u("Pb", 256, 264), 2 ** 20), (e16("MIN"), -LOW)):
         iota(o, [[0, o[2]]], val)
     fill(u("C25"), 2.0 ** 25)
     iota(e16("MINs"), [[0, 8]], 255 * 65536 + 2049 - 1088, 1)
@@ -573,16 +576,13 @@ def rank_program(g, core, T, topo):
     ts(hw, hw, 1.0 / 64, A.mult, col(row4, 4.0, A.mult), A.add)
     ts(u("HWN"), NBD, hw, A.mult)
     iota(u("DUL"), [[0, 16], [128, 8]], 2064 - 1536, 1)
-    iota(u("YL"), [[0, 1920]], 0)
-    for j in range(8):
-        select(u("YL", 240 * j + 112, 240 * j + 128), u("ONEB", 0, 16), [[1, 16]], A.is_equal, 0.0, 16 * j, -1)
+    select(u("YO"), u("QZ", 0, 256), [[16, 8], [200, 2], [1, 16]], A.not_equal, 1.0, -200, -1)
     ts(u("kq", 0, 4), u("E16", 0, 4), 2.0 ** 19, A.mult, hw, A.add)
     at = col(P4, 16.0, A.mult, 15.0, A.add)
-    for name, w in [("og%d" % c, u("kq", c, c + 1)) for c in range(4)] + [("w8k", 8192.0), ("Y", row0)]:
+    for name, w in [("og%d" % c, u("kq", c, c + 1)) for c in range(4)] + [("w8k", 8192.0), ("Y", row0), ("YH", hw), ("YK", col(P15, float(PLAIN), A.is_ge))]:
         ts(u(name), J144, at, A.is_equal, w, A.mult)
-    ts(u("b1"), J, P, A.is_gt)
-    tt(u("TRIm"), u("b1"), u("P11"), A.subtract)
-    ts(u("NTRIm"), u("TRIm"), -1.0, A.mult)
+    select(u("TRIm"), u("N11"), [[-1, 128]], A.is_ge, 1.0, 0, 1)
+    select(u("NTRIm"), u("P11"), [[-1, 128]], A.is_ge, -1.0, 0, 1)
     ts(u("b2"), IDB, -4.0, A.mult)
     ts(u("b1"), J, P, A.is_lt)
     tt(u("BTI"), u("b1"), BD, A.mult)
@@ -590,14 +590,13 @@ def rank_program(g, core, T, topo):
     ts(u("b1"), u("b1"), -56.0, A.mult, -8.0, A.add)
     tt(u("PEN", 0, 128), u("b1"), u("b2"), A.add)
     cp(u("PEN", 128, 256), u("PEN", 0, 128))
-    for name, src, val in (("w2", u("blk"), 2.0), ("IDh", IDB, 0.5), ("B256", BD, 256.0), ("B512", BD, 512.0), ("N512", BD, -512.0)):
+    for name, src, val in (("w2", u("blk"), 2.0), ("B256", BD, 256.0), ("B512", BD, 512.0), ("N512", BD, -512.0)):
         ts(u(name), src, val, A.mult)
-    for c in range(4):
-        ts(u("CMK%d" % c), u("R16"), u("PC", 4 + c, 5 + c), A.mult)
     for q, val in enumerate((640 - 2048, 128 - 2048)):
         ts(u("CNT", 128 * q, 128 * q + 128), u("R16"), 8192.0 + val, A.mult, -8192.0, A.add)
-        ts(u("CTG", 128 * q, 128 * q + 128), u("R16"), u("PC", 8 + q, 9 + q), A.mult, -8192.0, A.add)
+        ts(u("CTG", q, 256, 2), u("R16"), 8192.0 - (255.5 + 768, 256.0)[q], A.mult, -8192.0, A.add)
     ts(u("PENW"), u("R16"), -2.0 ** 17, A.mult, 2.0 ** 17, A.add)
+    ts(u("PENK"), u("R16"), 2048 - 2.0 ** 17, A.mult, 2.0 ** 17, A.add)
     ts(u("PEN2", 0, 256, 2), u("R16"), 512 - 2.0 ** 17, A.mult, 2.0 ** 17, A.add)
     cp(u("PEN2", 1, 256, 2), u("PENW"))
     iota(u("M32"), [[0, 256]], 1)
@@ -612,7 +611,11 @@ def rank_program(g, core, T, topo):
     ts(u("KV"), J, 0.0, A.mult, -1023.5, A.add)
     ts(u("CIX"), u("Jb", 0, 32), 16.0, A.mult, P15, A.add)
     ts(u("CB"), u("CT"), 16.0, A.mult, 7.0, A.add)
-    ts(u("C512"), u("CIX"), 512.0, A.add)
+    ts(u("C512"), u("CIX"), 500.0, A.add)
+    fill(u("MINR"), LOW)
+    ts(e16("MINR"), u("CT"), 4.0, A.mult, 1024.0, A.add)
+    fill(u("MAXT"), -LOW)
+    ts(u("MAXT", 0, 256, 32), u("CT"), -1.0, A.mult, -512.0, A.add)
     ts(u("sp4", 0, 4), u("Jb", 0, 4), col(P15, -9.0, A.add), A.is_equal, 4.0, A.mult)
     nine = col(P15, 9.0, A.is_lt)
     fill(u("two"), 2.0)
@@ -627,25 +630,25 @@ def rank_program(g, core, T, topo):
     fill(u("two"), 0.5)
     scan(u("two"), u("two"), u("E16"), A.mult, A.add)
     ts(u("WD"), NBD, col(u("two", 15, 16), 2.0 ** 14, A.mult, nine, A.mult), A.mult)
-    ts(u("KD"), J, 0.0, A.mult, -255.5, A.add)
     ts(u("PIi", 3, 4), u("PIi", 1, 2), 1, A.bitwise_and)
     ts(u("PIi", 4, 5), u("PIi", 0, 1), 3, A.bitwise_and)
     ts(u("PIi", 5, 6), u("PIi", 0, 1), 1, A.bitwise_and)
-    ts(u("G4", 0, 2), u("Jb", 0, 2), col(u("PIi", 3, 4), 1.0, A.mult), A.is_equal)
+    oddg = col(u("PIi", 3, 4), 1.0, A.mult)
     ts(u("kp4", 0, 4), u("sp4", 0, 4), 0.25, A.mult, nine, A.add)
-    for q in range(2):
-        ts(u("KQ", 4 * q, 4 * q + 4), u("kp4", 0, 4), u("G4", q, q + 1), A.mult)
+    row15 = u("E16", 15, 16)
+    ts(u("MK"), u("QR"), col(row15, -1.0, A.mult), A.mult, col(row15, -512.0, A.mult), A.add)
+    but15, top15 = col(P15, 15.0, A.is_lt), col(row15, 2216.0, A.mult)
+    fill(u("H15"), 0.0)
+    ts(e16("H15", 15), u("nblk"), hw, A.mult)
     odd = col(u("PIi", 5, 6), 1.0, A.mult)
     ts(u("MC2"), J15, col(odd, 8.0, A.mult, P4, A.add), A.is_le)
     fill(e16("MC2"), 0.0)
     ts(u("blk2"), J8, col(P15, odd, A.subtract, 0.5, A.mult), A.is_equal)
     ts(u("nblk2"), u("blk2"), -1.0, A.mult)
-    at = col(P15, 8.0, A.mult, P4, A.add)
-    if SPREAD:
-        ts(u("EXA"), u("SQ"), col(at, 128.0, A.add), A.is_equal)
-    else:
-        fill(u("Z0"), 0.0)
-    ts(u("EXP"), u("SQ"), col(P, 128.0, A.add), A.is_equal)
+    for a in range(0, 2048, 512):
+        select(u("EXP", a, a + 512), u("QZ"), [[1, 32], [0, 16]], A.not_equal, 1.0, a // 16, -1)
+        if a < FROM:
+            select(u("EXA", a, a + 512), u("QZ"), [[1, 4], [16, 8], [0, 16]], A.not_equal, 1.0, a // 128, -1)
     ts(u("PC", 12, 14), u("LI"), -65536.0, A.mult)
     wt = col(u("WI", 0, 1), 1.0, A.mult)
     ts(u("WTp"), BD, wt, A.mult)
@@ -664,6 +667,59 @@ def rank_program(g, core, T, topo):
 
     X, LISTS, OWNERS = u("X", 0, 2224), u("W", 0, 512), u("OT", 0, 2064)
 
+    def part_start():
+        ts(u("PR5"), u("MI"), 2048, A.is_lt)
+        ts(u("p6"), u("MI"), 1, A.add)
+        tt(LISTS, u("p6"), u("PR5"), A.mult)
+        w = 32 * PLAIN
+        ts(u("p7", 0, w), u("MT", 0, w), -2047.5, A.add, 8192.0, A.mult)
+        tt(u("p7", 256, 256 + w), u("DUM", 0, w), u("p7", 0, w), A.min)
+        tt(u("TGS", 0, w), u("MT", 0, w), u("p7", 256, 256 + w), A.max)
+        ts(u("INO", 0, w), u("TGS", 0, w), 1.0, A.add)
+        for k in range(PLAIN):
+            act(ix(u("OT"), u("INO", 32 * k, 32 * k + 32)), V0P, F.Silu)
+        up = col(P15, 0.0, A.is_gt, -1.0, A.mult)
+        ts(u("UP"), J, col(P, -1.0, A.add), A.is_equal, up, A.mult)
+        ts(u("UP11"), u("UP"), -2048.0, A.mult)
+        scan(u("PF"), u("PR5"), u("PR5"), A.add, A.max)
+        mm(u("p6", 440, 441), (u("UP"), u("PF", 511, 512)))
+        mm(u("p5"), (IDB, u("PF")), (u("UP"), u("PF")), (u("N11"), u("PR5")), (u("UP11"), u("PR5")))
+        ts(u("PF"), u("p5"), u("p6", 440, 441), A.subtract, 0.0, A.min)
+        mm(u("p6", 448, 480), *[(u("YK", 15 - r, 143 - r), u("PF", 32 * r, 32 * r + 32)) for r in range(16)])
+        ts(u("r1"), u("CIX"), -1535.0, A.add)
+        tt(u("r2"), u("p6", 448, 480), u("r1"), A.min)
+        ts(u("F16"), u("r2"), 2047.0, A.add)
+        act(ix(u("SO"), u("F16")), V0P, F.Silu)
+        dma([(u("EV", a, a + 128), u("SO", 0, 128)) for a in range(0, 512, 128)], "ld9", 256)
+        n, left = RANKS[PLAIN], 16 - PLAIN
+        wide = -(-(n - 128) // 32) * 2
+        cp(u("DU", 0, n), u("SO", 0, n))
+        mm(u("p6", 480, 480 + n // 16), *[(u("YH", 15 - r, 143 - r), u("DU", r, n, 16)) for r in range(16)])
+        ts(u("HL", 0, n // 16), u("p6", 480, 480 + n // 16), -512.0, A.add)
+        cp(u("PF", 0, n), ix(u("W"), u("HL", 0, n // 16)))
+        ts(u("PR5", 0, n), u("PF", 0, n), 0.0, A.is_gt)
+        iota(u("PC", 76, 80), [[128, 4]], 2064 - 1536, 1)
+        for q in range(0, n, 128):
+            m = min(128, n - q)
+            ps, full = u("p5", q, q + 128, 1, (0, m)), u("PR5", q, q + m)
+            mm(ps, (u("ONEB", 0, m), u("KAm")), (u("PF", q, q + m), IDB), (full, u("N20")), (full, u("N20")))
+            if q:
+                ts(u("LT", q, q + 128, 1, (0, m)), ps, u("PC", 76 + q // 128, 77 + q // 128, 1, (0, m)), A.min)
+            else:
+                tt(u("LT", 0, 128), ps, u("DUL"), A.min)
+            for j in range(m // 16):
+                unfold("p4", 296 + q // 16 - 8 + j if q else 200 + j, wide if q else 8, "LT", q + PLAIN, j, left, m)
+            if not q:
+                ts(u("INO", 256, 256 + 8 * left), u("p4", 200, 200 + 8 * left), 1536.0, A.add)
+                for a in range(0, 8 * left, 32):
+                    b = min(a + 32, 8 * left)
+                    act(ix(u("OT"), u("INO", 256 + a, 256 + b)), u("EV", 0, 16 * (b - a)), F.Silu)
+        if n % 32:
+            unfold("p4", 295 + wide, wide, "LT", PLAIN, 0, left)
+        ts(u("INO", 352, 352 + wide * left), u("p4", 296, 296 + wide * left), 1536.0, A.add)
+        for k, m in enumerate(RANKS[PLAIN:-1]):
+            act(ix(u("OT"), u("INO", 352 + wide * k, 344 + wide * k + m // 16)), u("SO", 128, m), F.Silu)
+
     def gather(out, win, off, cuts, many):
         for k, (a, b) in enumerate(zip((0,) + cuts, cuts + (128,))):
             if k < many:
@@ -676,11 +732,8 @@ def rank_program(g, core, T, topo):
         lanes = u("W", t % 4, 512, 4)
         cp(u("OWN"), lanes)
         gather("T", X, "OWN", CUT_T, 2 if t else 3)
-        if t:
-            act(u("PRE"), lanes, F.Sign)
-        else:
-            ts(u("PRE"), lanes, 0.0, A.is_gt)
-        cp(u("OWNH"), lanes)
+        ts(u("OWNH"), lanes, 0.0, A.max)
+        ts(u("PRE"), u("OWNH"), 0.0, A.is_gt)
         k = u("p3", 0, 128)
         mm(k, (ONE, u("KAs")), (u("PRE"), u("N27")), (u("OWNH"), IDB), *sums("p3", 0, "T", "w64k"))
         scan(u(s1), u("MINs"), k, A.max, A.min)
@@ -692,12 +745,13 @@ def rank_program(g, core, T, topo):
         tile("ZS", "HD", u("p4", 24, 32), "blk2", "nblk2", "MC2")
         ts(u("A16"), u("p4", 24, 32), 1088.0, A.add)
         ts(u("AN"), ix(u("AC4"), u("A16")), 1, A.add)
-        if not SPREAD:
-            cp(e16("Z0"), ix(X, u("A16")))
+        if FROM < 2048:
+            cp(u("Z0", FROM, 2048, 16), ix(X, u("A16", FROM // 256, 8)))
         for a in range(0, 2048, CUT_S):
-            if not SPREAD:
-                scan(u("REP", a, a + CUT_S), u("MS", a, a + CUT_S), u("Z0", a, a + CUT_S), A.mult, A.add)
-            scan(u("US", a, a + CUT_S), u("MS", a, a + CUT_S), u("T", a, a + CUT_S), A.mult, A.max)
+            if a >= FROM:
+                scan(u("REP", a, a + CUT_S), u("MS", 0, CUT_S), u("Z0", a, a + CUT_S), A.mult, A.add)
+            scan(u("US", a, a + CUT_S), u("MS", 0, CUT_S), u("T", a, a + CUT_S), A.mult, A.max)
+        cp(e16("UD"), e16("US", 15))
         mm(u("p4", 8, 16), (ONE, u("L2N")), (e16("US", 15), u("w64k")))
         tt(u("wp8"), e16(s1, 15), u("p4", 8, 16), A.is_ge)
         mm(u("p6", 0, 128), (u("PRE"), u("SEL0R")))
@@ -707,7 +761,7 @@ def rank_program(g, core, T, topo):
         mm(u("p4", 144, 152), (IDB, u("CT")), (u("QB"), u("blk")))
         cp(u("BT16"), u("p4", 144, 152))
 
-    def part_vacant():
+    def part_vacant(t):
         act(u("OCC"), LISTS, F.Sign)
         mm(u("p6", 128, 160), *[(u("Y", 15 - r, 143 - r), e16("OCC", r)) for r in range(16)])
         act(u("OCb"), u("p6", 128, 160), F.Copy)
@@ -716,9 +770,9 @@ def rank_program(g, core, T, topo):
         scan(u("CS"), u("ONEB", 0, 32), u("p4", 32, 64), A.mult, A.add)
         tt(u("r1"), u("p4", 64, 96), u("CS"), A.subtract)
         tt(u("r2"), u("r1"), u("C512"), A.min)
-        cp(u("F16"), u("r2"))
+        ts(u("F16"), u("r2"), float(t % 4), A.add)
         act(ix(u("FREE", 0, 1024), u("F16")), V0, F.Silu)
-        act(u("NFF"), u("SEL0R"), F.Identity, scale=u("CS", 31, 32))
+        ts(u("NFF"), u("SEL0R"), u("CS", 31, 32), A.mult)
 
     def part_split(t):
         s = u("ZP%d" % (t % 2))
@@ -729,8 +783,8 @@ def rank_program(g, core, T, topo):
             mm(ps, (IDB, u("T", a, b)), (u("ST"), u("EXP", a, b)))
             act(u("SQ", a, b), ps, F.Square)
         act(u("SQS"), s, F.Square)
-        k = u("p3", 128, 256)
-        mm(k, (ONE, u("KAb")), (u("PRE"), u("P23")), *sums("p3", 128, "SQ", "w32"))
+        k = u(BANK_B[0], BANK_B[1], BANK_B[1] + 128)
+        mm(k, (ONE, u("KAb")), (u("PRE"), u("P23")), *sums(BANK_B[0], BANK_B[1], "SQ", "w32"))
         scan(u("SB"), u("MS", 0, 128), k, A.mult, A.max)
         low(e16("ZB", 0, 128), e16("SB", 15), u("hb8"), 32)
         tile("ZB", "HB", u("p4", 16, 24), "nblk", "blk", "MC", (IDB, u("CB")))
@@ -744,73 +798,70 @@ def rank_program(g, core, T, topo):
             mm(ps, (u("WV"), u("EXP", a, b)))
             tt(u("AW", a, b), u("T", a, b), ps, A.mult)
         lv = u("p7", 0, 128)
-        mm(lv, (ONE, u("K20")), (u("PRE"), u("N20")), (u("SQB"), BD), (u("SQS"), NBD), *sums("p7", 0, "AW", "w2"))
-        ts(u("LN", 0, 128), lv, 0.0, A.is_lt)
-        ts(u("LN", 128, 256), lv, 0.0, A.is_ge)
+        mm(lv, (u("PRE"), u("N20")), (u("SQS"), NBD), (u("SQB"), BD), *sums("p7", 0, "AW", "w2"))
+        ts(u("LN", 0, 128), lv, -2.0 ** 20, A.is_lt)
+        ts(u("LN", 128, 256), lv, -2.0 ** 20, A.is_ge)
         scan(u("XC"), u("MS", 0, 256), u("LN"), A.mult, A.add)
         for q in range(3):
             ts(u("XF", 256 * q, 256 * q + 256), u("XC"), 0.5 ** (q + 1), A.mult, 159.5 + 0.5 ** (q + 2), A.add)
         pp = u("p7", 128, 384)
-        mm(pp, (ONE, u("KAp")), *[(u("RV%d" % q), u("XF", 256 * q, 256 * q + 256)) for q in range(3)],
-           (u("P20"), u("LN")), (u("RV3"), u("XC")), (u("OWNH"), u("ID2")))
+        mm(pp, (ONE, u("KAp")), (u("P20"), u("LN")), (u("RV3"), u("XC")),
+           *[(u("RV%d" % q), u("XF", 256 * q, 256 * q + 256)) for q in range(3)], (u("OWNH"), u("ID2")))
         act(u("Pa", 0, 256), pp, F.Abs, bias=-54.0 * TAU)
         tt(u("Pa", 0, 255), u("p7", 129, 384), u("Pa", 0, 255), A.min)
         for q, a, b in ((1, "Pa", "Pb"), (2, "Pb", "Pa"), (3, "Pa", "Pb")):
             act(u("p5", 0, 256), u(a, 0, 256), F.Abs, bias=-2.0 * 3 ** (3 - q) * TAU)
             tt(u(b, 0, 256), u("p5", 0, 256), u(a, 1 << q, 256 + (1 << q)), A.min)
         ts(u("SL"), u("Pb", 0, 256), TAU, A.min, TAU, A.subtract)
-        mm(u("p6", 288, 416), (u("SL", 0, 128), NIDB), (NIDB, u("OWNH")))
-        cp(u("DS", 512, 640), u("p6", 288, 416))
 
     def part_near(t):
         iota(e16("MINn"), [[0, 8]], 13 * 2 ** 20 + t % 4)
         gather("OG", OWNERS, "AN", CUT_O, 0 if t else 2)
         k = u("p3", 256, 384)
         mm(k, (ONE, u("KAn")), *[(u("og%d" % (t % 4), 15 - r, 143 - r), u("OG", 128 * r, 128 * r + 128)) for r in range(16)], ends=(True, False))
-        if SPREAD:
-            gather("AX", X, "AN", (32, 64, 96), 3)
         for c, (a, b) in enumerate(zip((0,) + CUT_A, CUT_A + (128,))):
-            if SPREAD:
-                ps = u("p%d" % BANK_A[c], 0, 16 * (b - a))
+            if c in BY_PE:
+                act(u("AX", 16 * a, 16 * b), ix(X, u("AN", a, b)), F.Copy)
+                ps = u(BANK_A[c], 0, 16 * (b - a))
                 mm(ps, (u("ST"), u("EXA", 16 * a, 16 * b)), (IDB, u("AX", 16 * a, 16 * b)))
                 act(u("DU", 16 * a, 16 * b), ps, F.Square)
             else:
                 tt(u("AX", 16 * a, 16 * b), ix(X, u("AN", a, b)), u("REP", 16 * a, 16 * b), A.subtract)
                 act(u("DU", 16 * a, 16 * b), u("AX", 16 * a, 16 * b), F.Square)
             mm(k, *[(u("w8k", 15 - r, 143 - r), u("DU", 128 * r, 128 * r + 128)) for r in range(a // 8, b // 8)], ends=(False, b == 128))
-        scan(u("S2"), u("MINn"), k, A.max, A.min)
-        cp(u("a8"), e16("S2", 15))
-        ts(u("d8"), u("a8"), 511, A.bitwise_and)
+        if SCAN_I:
+            scan(u("S2i"), u("MINn"), k, A.max, A.min)
+            ts(u("d8"), e16("S2i", 15), 511, A.bitwise_and)
+        else:
+            scan(u("S2"), u("MINn"), k, A.max, A.min)
+            cp(u("a8"), e16("S2", 15))
+            ts(u("d8"), u("a8"), 511, A.bitwise_and)
         cp(u("D16"), u("d8"))
 
     def part_partner(t):
         lists = ix(LISTS, u("D16"))
-        cp(u("DM"), lists)
+        ts(u("DM"), lists, but15, A.mult, top15, A.add)
         gather("DT", X, "DM", CUT_D, 2)
-        cp(u("DMH"), lists)
+        ts(u("DMH"), lists, 0.0, A.max)
         ts(u("PRD"), u("DMH"), 0.0, A.is_gt)
-        codes = ix(u("CODE"), u("D16"))
-        for q in range(2):
-            act(u("CG", 128 * q, 128 * q + 128), codes, F.Identity, scale=u("KQ", 4 * q + t % 4, 4 * q + t % 4 + 1))
-        for h, ps in enumerate(("p0", "p1", "p2", "p6")):
-            parts = [u("CG", 128 * q, 128 * q + 128, 1, (32 * h, 32 * h + 32)) for q in range(2)]
-            mm(u(ps, 0, 256), (IDB, u("PEN")), *[(x, x, u(ps, 128 * q, 128 * q + 128)) for q, x in enumerate(parts)])
-            act(u("EQ", 256 * h, 256 * h + 256), u(ps, 0, 256), F.Relu)
+        act(u("CG", 0, 128), ix(u("CODE"), u("D16")), F.Identity, scale=u("kp4", t % 4, t % 4 + 1))
+        ts(u("CG", 128, 256), u("CG", 0, 128), oddg, A.mult)
+        for h, (ps, a) in enumerate(BANK_E):
+            parts = [u("CG", 128 * q, 128 * q + 128, 1, (32 * h, 32 * h + 16 + 16 * q)) for q in range(2)]
+            mm(u(ps, a, a + 256), (IDB, u("PEN")), *[(x, x, u(ps, a + 128 * q, a + 128 * q + 128)) for q, x in enumerate(parts)])
+            act(u("EQ", 256 * h, 256 * h + 256), u(ps, a, a + 256), F.Relu)
         mm(u("p6", 416, 432), (u("PRE"), u("BD", 0, 128, 8)), (u("PRD"), u("BD", 0, 128, 8)))
         act(u("SZ"), u("p6", 416, 432), F.Relu, scale=32.0, bias=-512.0)
-        for a, b in zip((0,) + CUT_D, CUT_D + (128,)):
-            a, b = 16 * a, 16 * b
-            cp(u("DT", a + 15, b, 16), u("US", a + 15, b, 16))
-            scan(u("AX", a, b), u("MS", a, b), u("DT", a, b), A.mult, A.max)
+        for a in range(0, 2048, 512):
+            scan(u("AX", a, a + 512), u("UD", a, a + 512), u("DT", a, a + 512), A.min, A.max, 64.0)
         k = u("p3", 384, 512)
         mm(k, (ONE, u("KAd")), (u("PRD"), u("N27")), (u("IDF"), e16("S1%d" % (t % 2), 15), e16("p3", 399)), *sums("p3", 384, "DT", "w64k")[:15])
         mm(u("p4", 160, 176), (ONE, u("THN")), (ONE, u("THZ")), (u("N40"), u("wp8"), u("p4", 161, 176, 2)), (u("P23"), u("SZ")),
-           *[(u("EQ", 128 * q, 128 * q + 128), u("C25", 0, 2), u("p4", 160 + 2 * q, 162 + 2 * q)) for q in range(8)], (e16("AX", 15), u("w64d")))
+           *[(u("EQ", 128 * q, 128 * q + 128), u("C25", 0, 2), u("p4", 160 + 2 * q, 162 + 2 * q)) for q in range(8)], (e16("AX", 14), u("w64d")))
         scan(u("S3"), u("MIN"), k, A.max, A.min)
         for src, step, out in (("DMH", 1, "D1"), ("DM2", 4, "DS")):
-            for q in range(4):
-                mm(u("p2", 128 * q, 128 * q + 128), (u("SH", 128 * step * q, 128 * step * q + 128) if q else IDB, u(src)))
-            act(u(out, 0, 512), u("p2"), F.Copy)
+            mm(u(BANK_D), *[(u("SH", 128 * step * q, 128 * step * q + 128) if q else IDB, u(src), u(BANK_D, 128 * q, 128 * q + 128)) for q in range(4)], size=1)
+            act(u(out, 0, 512), u(BANK_D), F.Copy)
             if step == 1:
                 cp(u("DM2"), ix(u("D1"), u("BT16")))
 
@@ -820,13 +871,12 @@ def rank_program(g, core, T, topo):
         tt(e16("ZM"), e16("S3", 15), u("p4", 160, 176, 2), A.is_ge)
         tt(e16("ZW"), e16("S3", 15), u("p4", 161, 176, 2), A.is_lt)
         scan(u("MWR"), u("MS", 0, 256), u("ZMW"), A.mult, A.add)
-        k0, k1, k2 = u("p7", 384, 512), u("p5", 0, 128), u("p7", 0, 128)
-        mm(k0, (ONE, u("K9")), (u("ONEF"), u("NFF")), (u("TRIm"), WR))
-        mm(k1, (ONE, u("K11")), (u("TRIm"), WR))
-        ts(SR, k0, 0.0, A.is_lt)
-        tt(u("KR"), k1, u("CMK%d" % cl), A.min)
-        mm(u("p4", 112, 120), (u("KR"), u("blk")))
-        cp(u("RK"), u("p4", 112, 120))
+        k0, k1, k2 = u("p7", 384, 512), u("p0", 256, 384), u("p7", 0, 128)
+        mm(k0, (ONE, u("NFF")), (u("TRIm"), WR))
+        mm(k1, (IDB, u("PENK")), (WR, u("TRIm")))
+        ts(SR, k0, -1536.0, A.is_lt)
+        scan(u("KR"), u("MINR"), k1, A.max, A.min)
+        ts(u("RK"), e16("KR", 15), float(cl), A.add)
         mm(k2, (ONE, u("KAr")), (u("TRIm"), u("LR")), (u("NTRIm"), MR), (u("NTRIm"), SR))
         for q in range(2):
             ts(u("EE", 128 * q, 128 * q + 128), k2, 16.0 * q, A.is_equal)
@@ -843,18 +893,17 @@ def rank_program(g, core, T, topo):
         act(u("QN"), u("p6", 0, 256), F.Relu)
         mm(u("p4", 120, 128), (IDB, u("CT")), (u("QN", 0, 128), u("nblk")), (u("QN", 128, 256), u("nblk")))
         ts(u("NT16"), u("p4", 120, 128), 640.0, A.add)
-        tt(u("W", cl, 512, 4), ix(u("DS"), u("NT16")), u("OWNH"), A.add)
         act(ev, ix(u("FREE"), u("RK")), F.Copy)
-        a, b = u("p0", 0, 128), u("p0", 128, 256)
-        mm(u("p0", 0, 256), (IDB, u("CTG")), (IDB, u("KD"), a), (u("CG", 0, 128), u("WD"), a), (u("CG", 128, 256), u("WD"), a), (u("P11"), MR, a), (u("P11"), SR, b), (ev, u("HWN"), b))
-        ts(u("QH"), u("p0", 0, 256), 0.0, A.max)
-        mm(u("p4", 128, 136), (IDB, u("CT")), (u("QH", 0, 128), u("nblk")), (u("QH", 128, 256), u("nblk")))
-        ts(u("TG16"), u("p4", 128, 136), 512.0, A.add)
+        mm(u("p6", 288, 416), (u("SL", 0, 128), NIDB), (NIDB, u("OWNH")), (u("H15"), ev))
+        cp(u("DS", 512, 640), u("p6", 288, 416))
+        tt(u("W", cl, 512, 4), ix(u("DS"), u("NT16")), u("OWNH"), A.add)
+        a, b = u("p0", 0, 256, 2), u("p0", 1, 256, 2)
+        mm(u("p0", 0, 256), (IDB, u("CTG")), (u("WD"), u("CG", 0, 128), a), (MR, u("P768"), a), (SR, u("P768"), b), (u("HWN"), ev, b))
+        scan(u("TGS"), u("MAXT"), u("p0", 0, 256), A.min, A.max)
+        ts(u("TG16"), u("TGS", 31, 256, 32), -1.0, A.mult)
         mm(u("p1", 0, 128), (u("SL", 128, 256), NIDB), (MR, u("N20")))
-        ts(u("ELS"), u("p1", 0, 128), 0.0, A.max)
+        tt(u("ELS"), u("p1", 0, 128), u("MK", cl, 512, 4), A.max)
         cp(ix(u("W"), u("TG16")), u("ELS"))
-        act(u("ALT", cl, 512, 4), ev, F.Copy)
-        cp(ix(u("ALT"), u("TG16")), ev)
         if t + 1 == RO:
             return
         a, b = u("p7", 128, 256), u("p7", 256, 384)
@@ -867,11 +916,10 @@ def rank_program(g, core, T, topo):
         tt(u("m1"), a, u("DUL"), A.min)
         tt(u("m2"), b, u("m1"), A.min)
         for j in range(8):
-            mm(u("p1", 128 + j, 128 + 8 * MOVERS, 8), *[(u("YL", 240 * j + 112 - 16 * q, 240 * j + 240 - 16 * q), u("m2", 16 * q, 16 * q + MOVERS)) for q in range(8)])
+            unfold("p1", 128 + j, 8, "m2", 0, j, MOVERS)
         ts(u("MVO", 0, 8 * MOVERS), u("p1", 128, 128 + 8 * MOVERS), 1536.0, A.add)
         cp(u("EV", 0, 128), ev)
-        for q in range(1, 4):
-            dma(u("EV", 128 * q, 128 * q + 128), u("EV", 0, 128), "ev%d" % (3 * t + q - 1), 0, 3.0)
+        dma([(u("EV", 128 * q, 128 * q + 128), u("EV", 0, 128)) for q in range(1, 4)], "ev%d" % t, 192)
         for a in range(0, 8 * MOVERS, 32):
             b = min(a + 32, 8 * MOVERS)
             act(ix(u("OT"), u("MVO", a, b)), u("EV", 0, 16 * (b - a)), F.Silu)
@@ -882,7 +930,7 @@ def rank_program(g, core, T, topo):
         act(u("THZ"), u("ROW1"), F.Identity, scale=u("mc", 2, 3))
 
     def part_look(t):
-        qa, a, b, c = u("QA%d" % t), u("p2", 0, 128), u("p2", 128, 256), u("p2", 256, 384)
+        qa, a, b, c = u("QA%d" % t), u("p5", 256, 384), u("p5", 384, 512), u("p5", 256, 384)
         mm(a, (IDB, u("KV")), (u("WTp"), qa))
         mm(b, (IDB, ONE), (u("WTp"), qa))
         ts(u("VH"), a, 1.5 * 2.0 ** 34, A.add, 1.5 * 2.0 ** 34, A.subtract)
@@ -895,10 +943,10 @@ def rank_program(g, core, T, topo):
         ts(u("O16"), e16("WP", 15, 128), -1.0, A.mult, -512.0, A.add)
 
     def part_host(t):
-        act(u("PA"), ix(u("ALT"), u("O16")), F.Copy)
+        ts(u("PA"), ix(LISTS, u("O16")), 0.0, A.min)
         tt(u("EH"), ix(LISTS, u("O16")), u("VR"), A.is_equal)
         a, b = u("p2", 0, 256, 2), u("p2", 1, 256, 2)
-        mm(u("p2", 0, 256), (IDB, u("PEN2")), (u("HWN"), u("HO"), a), (u("HWN"), u("PA"), b), (u("N512"), u("EH"), a), (u("B512"), u("EH"), b))
+        mm(u("p2", 0, 256), (IDB, u("PEN2")), (u("HWN"), u("HO"), a), (BD, u("PA"), b), (u("N512"), u("EH"), a), (u("B512"), u("EH"), b))
         scan(u("WP"), u("M32"), u("p2", 0, 256), A.mult, A.min)
         ts(u("H16"), u("WP", 31, 256, 32), -1.0, A.mult, -512.0, A.add)
         cp(u("HLA"), ix(LISTS, u("H16")))
@@ -907,43 +955,43 @@ def rank_program(g, core, T, topo):
         qi = u("QI%d" % t)
         cp(e16("QZ"), ix(u("QA%d" % t), qi))
         cp(u("HL"), ix(u("HLA"), qi))
-        pairs = [(ONE, u("KQ5"))]
-        for a, b in ((0, 256), (256, 512)):
-            scan(u("QRp", a, b), u("MS", a, b), u("QZ", a, b), A.mult, A.add)
+        for a, b, ps in ((0, 256, u("p5", 0, 256)), (256, 512, u(BANK_Q, 256, 512))):
+            scan(u("QRp", a, b), u("MS", 0, 256), u("QZ", a, b), A.mult, A.add)
             tt(u("QD", a, b), ix(X, u("HL", a // 16, b // 16)), u("QRp", a, b), A.subtract)
             act(u("QS", a, b), u("QD", a, b), F.Square)
-            pairs += [(IDB, u("QRp", a, b), u("p5", a, b)), (u("IDh"), u("QD", a, b), u("p5", a, b)), (u("B256"), u("QS", a, b), u("p5", a, b))]
-        mm(u("p5"), *pairs)
-        scan(u("QR"), u("MIN5"), u("p5"), A.max, A.min)
-        ts(u("hs"), e16("QR", 15), 1.5 * 2.0 ** 27, A.add, 1.5 * 2.0 ** 27, A.subtract)
-        ts(u("ht"), e16("QR", 15), 1.5 * 2.0 ** 23, A.add, 1.5 * 2.0 ** 23 - 7, A.subtract)
-        tt(u("SN%d" % t), u("ht"), u("hs"), A.subtract)
+            mm(ps, (ONE, u("KQ5")), (IDB, u("QRp", a, b)), (u("IDh"), u("QD", a, b)), (u("B256"), u("QS", a, b)))
+            scan(u("QRi" if SCAN_I else "QR", a, b), u("MIN5"), ps, A.max, A.min)
+        if SCAN_I:
+            ts(u("SN%d" % t), e16("QRi", 15), 15, A.bitwise_and)
+        else:
+            ts(u("hs"), e16("QR", 15), 1.5 * 2.0 ** 27, A.add, 1.5 * 2.0 ** 27, A.subtract)
+            ts(u("ht"), e16("QR", 15), 1.5 * 2.0 ** 23, A.add, 1.5 * 2.0 ** 23 - 7, A.subtract)
+            tt(u("SN%d" % t), u("ht"), u("hs"), A.subtract)
         send(u("SN%d" % t), "RS", "s", t, -1)
 
     def part_apply(t):
         cp(ix(X, u("S32")), u("RS%d" % t))
 
+    part_start()
     for t in range(RO):
         part_own(t)
-        part_vacant()
+        part_vacant(t)
         part_split(t)
         if t:
             part_apply(t - 1)
         part_near(t)
-        if not t:
-            owners(0)
         part_partner(t)
         part_look(t)
         part_finish(t)
         part_host(t)
         if t + 1 == RO:
-            ts(u("t512a"), LISTS, 0.0, A.is_equal, 2049.0, A.mult)
+            ts(u("t512a"), LISTS, 0.0, A.is_le, 2048.0, A.mult)
             act(u("p1"), LISTS, F.Identity, bias=-1.0)
-            tt(u("YM"), u("t512a"), u("p1"), A.add)
-            dma(mark("ym", ap=T.ym[:]), u("YM"), "st0")
+            tt(u("YM"), u("t512a"), u("p1"), A.max)
+            dma([(mark("ym", ap=T.ym[:]), u("YM"))], "st0", 256)
         part_serve(t)
     part_apply(RO - 1)
-    dma(mark("yx", ap=T.yx[:]), u("X", 1, 2049), "st1")
+    dma([(mark("yx", ap=T.yx[:]), u("X", 1, 2049))], "st1", 512)
 
     if "o" not in _ORDER:
         _ORDER["o"] = _order(ops)
@@ -977,9 +1025,8 @@ def rank_program(g, core, T, topo):
     order, queues = _ORDER["o"]
     for i in order:
         o = ops[i]
-        if o["e"] != queues[i]:
-            o["e"], o["fn"], o["cost"] = o["alt"]
-        e, rd, wr = o["e"], o["rd"], o["wr"]
+        e, rd, wr = queues[i], o["rd"], o["wr"]
+        o["fn"] = o["ways"][e][0]
         if o["land"]:
             sem, landed, loc, left = o["land"]
             wait(e, rd, [])
@@ -994,13 +1041,14 @@ def rank_program(g, core, T, topo):
             wait(e, [], wr)
             for j, (x, a, b) in enumerate(o["items"]):
                 wait(e, a[1] + b[1], [])
-                ins = g.tensor.matmul(x[0], a[0], b[0], j == 0 and o["fn"][0], j == len(o["items"]) - 1 and o["fn"][1])
+                ins = g.tensor.matmul(x[0], a[0], b[0], *o["fn"][j])
         else:
             wait(e, rd, wr)
             ins = o["fn"]()
         if o["dma"]:
-            ins.then_inc(T.sem[o["dma"]], 16)
-            note(e, rd, wr, o["dma"], 16)
+            for x in ins:
+                x.then_inc(T.sem[o["dma"]], 16)
+            note(e, rd, wr, o["dma"], 16 * len(ins))
         else:
             cnt[e] += 1
             ins.then_inc(T.sem[e], 1)

@@ -5,6 +5,7 @@ RO = 5
 S, B, H, I, U = "float32", "bfloat16", "float16", "int32", "uint16"
 LOW = 1 - 2 ** 24
 TAU = 4096.0
+COLS = 144
 SCAN_I = True
 _BUF = []
 
@@ -14,17 +15,24 @@ def _sb(dtype, cols, names):
 
 
 _sb(B, 2304, "X")
-_sb(B, 2048, "T US SQ AX AW SH OG DT DU EXP EXA REP Z0")
+_sb(B, 2048, "T US SQ AX AW AB SH OG DT DU EXA REP Z0")
 _sb(B, 512, "MS PR5")
-_sb(H, 512, "PF LT")
+_sb(H, 512, "PF")
+_sb(H, COLS, "ZE")
+_sb(B, COLS, "JM")
+_sb(B, 8, "LL")
+_sb(S, 16 * COLS, "PAY")
+_sb(S, 1056, "TAB")
+_sb(U, COLS, "PO INO")
+_sb(U, 64, "HR")
+_sb(U, 16, "IX")
 _sb(B, 256, "YO")
 _sb(B, 144, "YH YK")
 _sb(B, 128, "UP UP11 N11 H15")
 _sb(H, 128, "PA")
-_sb(S, 1024, "SO")
+_sb(B, 1024, "SO")
 _sb(S, 512, "V0P MK")
-_sb(I, 256, "MT")
-_sb(S, 256, "DUM")
+_sb(S, COLS, "DUM")
 _sb(H, 1024, "RH")
 _sb(S, 16, "two")
 _sb(B, 128, "MC2 WD")
@@ -36,32 +44,40 @@ _sb(I, 128, "S2i")
 _sb(B, 8, "blk2 nblk2")
 _sb(B, 1024, "EQ")
 _sb(B, 768, "XF")
-_sb(B, 512, "CODE QD OCC QZ QRp QS")
+_sb(B, 512, "CODE QD QZ QRp QS")
+_sb(B, 128, "OCC")
 _sb(B, 256, "KQ5")
 _sb(S, 256, "MIN5")
 _sb(I, 512, "QRi")
 _sb(B, 256, "PEN CG ID2 KAp QN LN XC ZMW MWR EE PEN2 M32")
 _sb(B, 144, "Jb Y w8k og0 og1 og2 og3")
-_sb(B, 128, "J4b J15b b1 b2 R16 MC IDB BD NBD BTI ONEB PRE PRD LR SR XB SQS SQB SEL0R TRIm NTRIm HWN N27 N20 P23 P20 P11 "
-            "RV0 RV1 RV2 RV3 ST KAs KAb KAd KAn KAr KAm PENK PRL WV A4n B4 CN1 QB ZP0 ZP1 WTp IDh B256 B512 N512 HO EH PENW WM")
+_sb(B, 128, "J4b J15b b1 b2 R16 MC IDB BD NBD BTI ONEB PRE PRD LR SR XB SQS SQB SEL0R TRIm NTRIm HWN N27 P23 N20 P20 P11 "
+            "RV0 RV1 RV2 RV3 ST KAs KAb KAd KAn KAr KAm PENK PRL A4n B4 CN1 QB ZP0 ZP1 WTp IDh B256 B512 N512 HO EH PENW WM")
 _sb(B, 32, "OCb")
-_sb(B, 16, "THN THZ ROW1 SZ w64d PENB")
-_sb(B, 8, "blk nblk w64k w32 w2 SEL0 L2N wp8 C25 PB C3K")
+_sb(B, 16, "THN THZ ROW1 SZ w64d PENB w64")
+_sb(B, 8, "blk nblk w64k n64k w32 w2 SEL0 L2N wp8 C25 PB C3K")
 _sb(H, 256, "SL CNT CTG")
 _sb(H, 144, "ZS HS ZB HB HD")
 _sb(H, 128, "OWNH DMH DM2 KV m1 m2 NFF")
 _sb(H, 32, "CIX")
 _sb(H, 8, "CB")
-_sb(S, 4112, "OT")
-_sb(S, 1536, "FREE")
+_sb(S, 4496, "OT")
+_sb(S, 768, "FREE")
+_sb(S, 48, "PX")
+_sb(S, 128, "VB")
+_sb(B, 256, "MB")
+_sb(B, 128, "MJ BTU TR32 SG0 SG1 SF0 SF1 LW0 LW1 LW2")
+_sb(B, 32, "OCt")
+_sb(U, 8, "V16")
 _sb(S, 768, "DS")
 _sb(B, 128, "EVB N40")
 _sb(S, 640, "W")
-_sb(S, 512, "J2f J3f t512a t512b YM QR D1 EV")
+_sb(S, 512, "J2f J3f t512a t512b YM QR D1")
+_sb(S, 1024, "EV")
 _sb(S, 264, "Pa Pb")
 _sb(S, 256, "WP")
 _sb(S, 128, "MINs MINn MIN S10 S11 S2 S3 SB ELS IDF VH VR HLA DUL")
-_sb(S, 80, "PC")
+_sb(S, 128, "PC")
 _sb(S, 32, "CS r1 r2 C512 hs ht")
 _sb(S, 16, "E16 KQ SV")
 _sb(S, 8, "blkf hi8 hb8 z8 mc kq G4 EP sp4 kp4")
@@ -69,58 +85,63 @@ _sb(I, 2192, "AC4")
 _sb(I, 512, "MI")
 _sb(I, 8, "PIi a8 d8")
 _sb(I, 2, "LI WI")
-_sb(U, 576, "INO")
 _sb(U, 128, "OWN AN DM MVO")
 _sb(U, 32, "F16 HL")
 _sb(U, 8, "RK S16 A16 B16 D16 NT16 TG16 BT16 VV16 H16 O16")
-_sb(U, 2, "S32")
+_sb(U, 2, "S32 SE")
+_sb(I, 32, "SN")
+_sb(S, 32, "OCf")
+_sb(B, 32, "OCg")
 _AT, _end = {}, {}
 for _n, _c, _d in _BUF:
     _AT[_n] = ("ar_" + _d, _end.get(_d, 0), _c, _d)
     _end[_d] = _end.get(_d, 0) + -(-_c // 16) * 16
 SCRATCH = {"ar_" + _d: ("sbuf", [128, _c], _d) for _d, _c in _end.items()}
 for _n, _m, _o, _c in (("NIDB", "ID2", 0, 128), ("ZM", "ZMW", 0, 128), ("ZW", "ZMW", 128, 128), ("MR", "MWR", 0, 128), ("WR", "MWR", 128, 128),
-                       ("ZALL", "ZS", 0, 720), ("MIN3", "MINs", 0, 384), ("CT", "CIX", 0, 8)):
+                       ("ZALL", "ZS", 0, 720), ("MIN3", "MINs", 0, 384), ("CT", "CIX", 0, 8), ("EW", "EV", 0, 1024)):
     _AT[_n] = (_AT[_m][0], _AT[_m][1] + _o, _c, _AT[_m][3])
 for _t in range(RO):
-    for _n, _c, _d in (("QA", 128, B), ("SE", 2, U), ("QI", 2, U), ("SN", 32, I if SCAN_I else B), ("RS", 32, I if SCAN_I else B)):
+    for _n, _c, _d in (("QA", 128, B), ("XQ", 2064, B), ("HQ", 128, S)):
         SCRATCH["%s%d" % (_n, _t)] = ("sbuf", [128, _c], _d)
         _AT["%s%d" % (_n, _t)] = ("%s%d" % (_n, _t), 0, _c, _d)
 for _k in range(8):
     SCRATCH["p%d" % _k] = ("psum", [128, 512], S)
     _AT["p%d" % _k] = ("p%d" % _k, 0, 512, S)
-SEMAPHORES = ["v", "p", "s", "k", "st0", "st1"] + ["ld%d" % i for i in range(11)] + ["ev%d" % i for i in range(RO - 1)]
+SEMAPHORES = ["v", "p", "s", "k", "st0", "st1"] + ["ld%d" % i for i in range(11)] + ["ev%d" % i for i in range(RO - 1)] + ["oc%d" % i for i in range(RO)]
 for _t in range(RO):
-    SEMAPHORES += [a + b + str(_t) for a in "rlfm" for b in "aqs"]
+    SEMAPHORES += [a + b + str(_t) for a in "rlfm" for b in "axh"]
 
 CYC, PEC, GAT, SCA, WAY, FIRST = 0.00085, 0.0005, 1.6, 3.7, 2.3, 2.5
+LONG = 9.0
 START, PERKB = 2.2, 0.005
 VIEWS = ((0.23, 0.14, 1.0, 0.8, 0.62), (0.26, 0.13, 1.15, 1.2, 1.3))
-PLAN, PASSES = (0.24, 0.14, 1.0, 0.92, 0.8), 8
-TURNS, AGAIN, EASE = 50000, 800, 0.15
+PLAN, PASSES = (0.24, 0.14, 1.0, 0.92, 0.8), 4
+TURNS, AGAIN, EASE = 110000, 1500, 0.12
+SAME = 64
 MOVERS = 15
-RANKS = [-(-(2048 // (_k + 1)) // 16) * 16 for _k in range(16)]
-CUT_A, BY_PE, BANK_Q, BANK_A = (32, 64, 104), (0, 1), "p0", ("p2", "p2", "p2", "p2")
+CUT_A, BY_PE, BANK_Q, BANK_A = (32, 64, 104), (0, 1), "p0", ("p2", "p1")
 BANK_E, BANK_D, BANK_B = (("p0", 0), ("p1", 0), ("p2", 0), ("p6", 0)), "p2", ("p7", 0)
-PLAIN = 5
+BANK_L, BANK_S, BANK_V = ("p6", 128), ("p5", 0, 256), ("p0", 0)
+CUT_M = (2, 4, 8, 12)
+CUT_I = (48, 96)
 CUT_T, CUT_D, CUT_O, CUT_S = (32, 64, 96), (32, 64, 96), (32, 64, 96), 512
 _ORDER = {}
 
 
-def _relay(topo, a, b):
-    if topo.may_write(a, b):
+def _relay(topo, a, b, long):
+    if topo.may_write(a, b) and not long:
         return None
-    return min((h for h in topo.cores_of(a) if h != a and topo.may_write(h, b)), key=lambda h: (topo.die(h) != topo.die(a), h))
+    return min((h for h in topo.cores_of(a) if h != a and topo.may_write(h, b)), key=lambda h: (topo.die(h) != topo.die(a), -h if long else h))
 
 
 def _relay_program(g, core, T, topo):
     used = []
     for t in range(RO):
-        for back, buf, arr, fwd, loc in ((0, "QA", "ra", "fa", "ma"), (0, "QI", "rq", "fq", "mq"), (1, "RS", "rs", "fs", "ms")):
+        for back, buf, arr, fwd, loc in ((0, "QA", "ra", "fa", "ma"), (1, "XQ", "rx", "fx", "mx"), (1, "HQ", "rh", "fh", "mh")):
             for r in range(8):
                 x, y = T.cores[r], T.cores[(r + 1 + t % 7) % 8]
                 x, y = (y, x) if back else (x, y)
-                if _relay(topo, x, y) == core:
+                if _relay(topo, x, y, buf == "XQ") == core:
                     rid, pid = topo.addr(y, core)
                     g.wait_ge(T.sem["%s%d" % (fwd, t)], len(topo.engines(x, core)))
                     g.remote_dma(T["%s%d" % (buf, t)][:], T["%s%d" % (buf, t)][:], T.sem["%s%d" % (arr, t)],
@@ -161,8 +182,8 @@ def _order(ops):
                         early[(j, i)] = at
                         break
                     at += _cycles(a, b) * PEC
-    sends = [i for i in range(n) if ops[i]["land"]]
-    for j, i in zip(sends, sends[1:]):
+    sends = [[i for i in range(n) if ops[i]["land"] and (ops[i]["land"][0][1] == "x") == long] for long in (0, 1)]
+    for j, i in [x for y in sends for x in zip(y, y[1:])]:
         if j not in pred[i]:
             pred[i].add(j)
             succ[j].append(i)
@@ -188,10 +209,18 @@ def _order(ops):
         settle([i], [i] + succ[i])
     settle(range(n), range(n))
 
-    def times(k, order, lo, hi, start, by, kept, last, user):
+    def times(k, order, lo, hi, start, by, kept, last, user, old=None):
         c, xw, inc = views[k]
         for pos in range(lo, hi):
             if pos % 32 == 0:
+                if old and pos >= lo + SAME:
+                    was = old[0]
+                    d = start[order[pos - 1]] - was[order[pos - 1]]
+                    if all(-1e-7 < start[x] - was[x] - d < 1e-7 for x in order[pos - SAME:pos]):
+                        for x in order[pos:]:
+                            start[x] = was[x] + d
+                        kept += old[2][pos // 32:]
+                        return
                 kept.append((last[:], user[:]))
             a = order[pos]
             s, w = 0.0, -1
@@ -227,25 +256,25 @@ def _order(ops):
             return None, None
         total, new = 0.0, []
         for k, (w, at) in enumerate(work):
-            times(k, order, at, n, *w)
+            times(k, order, at, n, *w, old and old[k])
             start, by, c = w[0], w[1], views[k][0]
-            a = max(order[-60:], key=lambda i: start[i] + c[i] + lat[i])
+            a = max(order[-16:], key=lambda i: start[i] + c[i] + lat[i])
             total += start[a] + c[a] + lat[a]
-            on = {a}
+            on = {a: 0}
             while by[a] >= 0:
                 a = by[a]
-                on.add(a)
+                on[a] = 0
             new.append((start, by, w[2], on))
         return total / len(views), new
 
     def chain(state):
         pairs = []
-        for start, by, _kept, on in state:
-            way = sorted(on, key=lambda i: (start[i], i))
-            for k, a in enumerate(way):
-                if by[a] >= 0 and by[a] not in pred[a]:
-                    pairs.append((by[a], a))
-                    pairs += [(way[k - d], a) for d in (4, 16) if k >= d and queue[way[k - d]] == queue[a]]
+        for _start, _by, _kept, on in state:
+            way = list(on)
+            for k, a in enumerate(way[:-1]):
+                if way[k + 1] not in pred[a]:
+                    pairs.append((way[k + 1], a))
+                    pairs += [(b, a) for b in way[k + 4:k + 17:12] if queue[b] == queue[a]]
         return pairs
 
     def place(rank, back, choose):
@@ -348,7 +377,7 @@ def rank_program(g, core, T, topo):
         return
     E = {"v": g.vector, "p": g.tensor, "s": g.scalar, "k": g, "y": g.sync}
     v, sc = g.vector, g.scalar
-    ops, first = [], [0]
+    ops = []
 
     def u(name, lo=0, hi=None, st=1, p=None):
         buf, o, n, d = _AT[name]
@@ -408,8 +437,21 @@ def rank_program(g, core, T, topo):
         per = 1.0 if _psum(a[1][0][0]) or _psum(b[1][0][0]) else 2.0
         op("v", lambda: v.tensor_tensor(o[0], a[0], b[0], o1), [o], [a, b], cost(o, [a, b], per))
 
-    def scan(o, a, b, o1, o2, init=0.0):
-        op("v", lambda: v.tensor_tensor_scan(o[0], a[0], b[0], _c(init), o1, o2), [o], [a, b] + _r(init), cost(o, [a, b], 0.5))
+    def scan(o, a, b, o1, o2, init=0.0, alt=None):
+        op("v", lambda: v.tensor_tensor_scan(o[0], a[0], b[0], _c(init), o1, o2), [o], [a, b] + _r(init), cost(o, [a, b], 0.5), alt=alt)
+
+    def times(o, a, b):
+        scan(o, a, b, A.min if a is b else A.max, A.mult, alt=scalar(o, a, F.Square) if a is b else None)
+
+    def by_slot(o, a, many):
+        for k in range(0, 16, many):
+            for j in range(k, k + many):
+                times(u(o, 128 * j, 128 * j + 128), a, e16("T", j))
+            part = [ops.pop() for _ in range(many)][::-1]
+            op("v", lambda part=part: [x["fn"]() for x in part], [u(o, 128 * k, 128 * (k + many))], [a, u("T")], sum(x["cost"] for x in part))
+
+    def turn(o, i):
+        op("v", lambda: v.transpose(o[0], i[0]), [o], [i], cost(o, [i], 0.5))
 
     def fill(o, c):
         kw = {} if o[3] == I else {"allow_small_or_imprecise_dtypes": True}
@@ -469,15 +511,15 @@ def rank_program(g, core, T, topo):
     def send(src, buf, kind, t, way):
         dst, back = T.cores[(rank + way * (1 + t % 7)) % 8], T.cores[(rank - way * (1 + t % 7)) % 8]
         buf, sem, fwd, loc = buf + str(t), "r%s%d" % (kind, t), "f%s%d" % (kind, t), "l%s%d" % (kind, t)
-        to, via = _relay(topo, core, dst), _relay(topo, back, core)
+        to, via = _relay(topo, core, dst, kind == "x"), _relay(topo, back, core, kind == "x")
         d = dst if to is None else to
         rid, pid = topo.addr(d, core)
         op("k", lambda: g.remote_dma(T[buf][:], src[0], T.sem[sem if to is None else fwd], T.sem[loc], pid, rid, topo.mask(core, d)),
-           [u(buf)], [src], 0.3, lat=(WAY + (FIRST if buf == "QA0" else 0)) * (1 if to is None else 2),
+           [u(buf)], [src], 0.3, lat=(WAY + (FIRST if t == 0 and kind != "h" else 0)) * (1 if to is None else 2) + LONG * (kind == "x"),
            land=(sem, len(topo.engines(back if via is None else via, core)), loc, len(topo.engines(core, d))))
 
-    def sums(ps, base, src, w):
-        return [(e16(src, k), u(w), u(ps, base + k, base + 128, 16)) for k in range(16)]
+    def sums(ps, base, src, w, by_slot=False):
+        return [(u(src, 128 * k, 128 * k + 128) if by_slot else e16(src, k), w, u(ps, base + k, base + 128, 16)) for k in range(16)]
 
     def tile(z, h, ps, a, b, mask, *more):
         scan(u(h, 0, 128), u(mask), u(z, 0, 128), A.mult, A.add)
@@ -488,13 +530,12 @@ def rank_program(g, core, T, topo):
         ts(hi, key, c, A.add, c, A.subtract)
         tt(z, key, hi, A.subtract)
 
-    fill(u("X", 0, 16), -64.0)
+    fill(u("X", 0, 16), 0.0)
     fill(u("X", 2048, 2216), 0.0)
     fill(u("X", 2216, 2224), 64.0)
     fill(u("AC4", 0, 8), 0)
     fill(u("AC4", 2048, 2192), 2048)
     dma([(u("MI"), mark("ml", ap=T.ml[:]))], "ld0", 256)
-    dma([(u("MT", 32 * k, 32 * k + 32), mark("ml", ap=T.ml[k:128:16, :])) for k in range(PLAIN)], "ld4", 50 * PLAIN)
     dma([(u("X", 1, 2049), mark("x0", ap=T.x0[:]))], "ld1", 512)
     dma([(u("LI"), mark("lims", ap=T.lims[:])), (u("WI", 0, 1), mark("wt", ap=T.wt[:]))], "ld2", 60)
     dma([(u("AC4", 1 + 512 * q, 513 + 512 * q), mark("ac", ap=T.ac[:])) for q in range(4)], "ld3", 1024)
@@ -512,17 +553,12 @@ def rank_program(g, core, T, topo):
     iota(J144, [[1, 144]], 0)
     iota(J15, [[0, 8], [1, 16]], 0)
     iota(J4, [[1, 8], [0, 16]], 0)
-    iota(u("DUM", 0, 32 * PLAIN), [[0, PLAIN], [16, 32]], 2063, 1)
-    iota(u("J2f"), [[1, 128], [0, 4]], 128)
-    iota(u("J3f"), [[0, 128], [1, 4]], 0)
-    iota(u("t512a"), [[1, 8], [0, 4], [8, 16]], 128)
-    iota(u("t512b"), [[0, 8], [1, 4], [0, 16]], 0)
-    for o, val in ((u("QZ"), 0), (u("DS", 640, 768), 0), (u("MIN5"), LOW), (e16("MIN5"), -LOW), (u("SO", 0, RANKS[PLAIN]), 256), (u("OT", 0, 1), 0)):
+    iota(u("DUM"), [[16, COLS]], 2064, 1)
+    for o, val in ((u("QZ"), 0), (u("DS", 640, 768), 0), (u("MIN5"), LOW), (e16("MIN5"), -LOW), (u("SO", 0, 512), 256), (u("OT", 0, 1), 0), (u("TAB", 0, 32), 0)):
         iota(o, [[0, o[2]]], val)
     FROM = 512 * len(BY_PE)
     if FROM < 2048:
         dma([(u("Z0", a, a + 512), u("QZ")) for a in range(FROM, 2048, 512)], "ld5", 512 - FROM // 4)
-    dma([(u("FREE", a, a + 512), u("J2f")) for a in (0, 512)], "ld6", 512)
     fill(u("UD", 0, 512), 64.0)
     dma([(u("UD", a, a + 512), u("UD", 0, 512)) for a in range(512, 2048, 512)], "ld10", 384)
     for o, val in ((u("MS"), 1.0), (e16("MS"), 0.0), (u("W", 512, 640), 0.0)):
@@ -533,19 +569,22 @@ def rank_program(g, core, T, topo):
     ts(u("E16"), u("J15b", 0, 16), P15, A.is_equal)
     ts(u("EP", 0, 4), u("Jb", 0, 4), P, A.is_equal)
     row0, row4 = u("E16", 0, 1), u("E16", 4, 5)
-    V0, V0P = u("FREE", 1024, 1536), u("V0P")
-    for o, cls, high, sem in ((V0P, "t512b", "t512a", "ld7"), (V0, "J3f", "J2f", "ld8")):
-        ts(o, u(cls), P15, A.is_equal, 64.0, A.mult)
-        dma([(row(o, 4), row(u(high), 4))], sem, 40)
+    V0 = u("FREE", 256, 768)
+    top4 = col(row4, 128.0, A.mult)
+    first = [col(u("E16", c, c + 1), 64.0, A.mult, top4, A.add) for c in range(4)]
+    for c in range(4):
+        ts(u("FREE", 256 + c, 768, 4), J, row4, A.mult, first[c], A.add)
     every = col(P15, 4.0, A.is_lt, 64.0, A.mult)
-    act(u("OT", 2049, 2064), u("MS", 0, 15), F.Identity, scale=0.0, bias=col(row4, 128.0, A.mult, every, A.add))
+    act(u("OT", 2049, 2064), u("MS", 0, 15), F.Identity, scale=0.0, bias=col(every, top4, A.add))
     ts(IDB, J, P, A.is_equal)
     ts(BD, J4, P4, A.is_equal)
     ts(u("blk"), J8, P4, A.is_equal)
     ts(u("R16"), J15, P15, A.is_equal)
-    for name, src, val in (("nblk", "blk", -1.0), ("w64k", "blk", 65536.0), ("w32", "blk", 32.0),
+    for name, src, val in (("nblk", "blk", -1.0), ("w64k", "blk", 65536.0), ("n64k", "blk", -65536.0), ("w32", "blk", 32.0),
                            ("NBD", "BD", -1.0), ("SEL0R", "BD", row0), ("SEL0", "blk", row0)):
         act(u(name), u(src), F.Identity, scale=val)
+    for a, val in ((0, 64.0), (8, -2.0)):
+        act(u("w64", a, a + 8), u("blk"), F.Identity, scale=val)
     for name, val in (("N40", -2.0 ** 40), ("IDF", 1.0), ("NIDB", -1.0), ("N27", -2.0 ** 27), ("N20", -2.0 ** 20), ("P23", 2.0 ** 23),
                       ("P768", 768.0), ("N11", -2.0 ** 11), ("RV0", 90.0 * TAU), ("RV1", 30.0 * TAU), ("RV2", 10.0 * TAU),
                       ("RV3", -54.0 * TAU), ("P20", 2.0 ** 20), (u("ID2", 128, 256), -1.0), ("IDh", 0.5)):
@@ -557,7 +596,7 @@ def rank_program(g, core, T, topo):
     fill(ONE, 1.0)
     for a in (0, 360):
         ts(u("ZALL", a, a + 360), u("MS", 0, 360), 0.0, A.mult)
-    for name, slope, c1, c2 in (("KAs", 4096.0, 2.0 ** 27, -1088.0), ("KAb", -1.0, -2.0 ** 23, 7.0), ("KAn", 512.0, -2.0 ** 24, 0.0), ("KQ5", 16.0, -0.25 if SCAN_I else -7.25, 0.0),
+    for name, slope, c1, c2 in (("KAs", 4096.0, 2.0 ** 27, -1088.0), ("KAb", -1.0, 2.0 ** 17 - 2.0 ** 23, 7.0), ("KAn", 512.0, -2.0 ** 24, 0.0), ("KQ5", 16.0, -0.25 if SCAN_I else -7.25, 0.0),
                                 ("KAr", -1.0, 2048.0, 0.0), ("KAm", 0.0, 2.0 ** 21, -1536.0)):
         b = col(u("EP", 1, 2), c1, A.mult)
         if c2:
@@ -579,14 +618,13 @@ def rank_program(g, core, T, topo):
     select(u("YO"), u("QZ", 0, 256), [[16, 8], [200, 2], [1, 16]], A.not_equal, 1.0, -200, -1)
     ts(u("kq", 0, 4), u("E16", 0, 4), 2.0 ** 19, A.mult, hw, A.add)
     at = col(P4, 16.0, A.mult, 15.0, A.add)
-    for name, w in [("og%d" % c, u("kq", c, c + 1)) for c in range(4)] + [("w8k", 8192.0), ("Y", row0), ("YH", hw), ("YK", col(P15, float(PLAIN), A.is_ge))]:
+    for name, w in [("og%d" % c, u("kq", c, c + 1)) for c in range(4)] + [("w8k", 8192.0), ("YH", hw), ("YK", 1.0)]:
         ts(u(name), J144, at, A.is_equal, w, A.mult)
     select(u("TRIm"), u("N11"), [[-1, 128]], A.is_ge, 1.0, 0, 1)
     select(u("NTRIm"), u("P11"), [[-1, 128]], A.is_ge, -1.0, 0, 1)
     ts(u("b2"), IDB, -4.0, A.mult)
     ts(u("b1"), J, P, A.is_lt)
-    tt(u("BTI"), u("b1"), BD, A.mult)
-    tt(u("BTI"), u("BTI"), u("P11"), A.add)
+    select(u("BTU"), BD, [[-1, 128]], A.is_gt, 0.0, 0, 1)
     ts(u("b1"), u("b1"), -56.0, A.mult, -8.0, A.add)
     tt(u("PEN", 0, 128), u("b1"), u("b2"), A.add)
     cp(u("PEN", 128, 256), u("PEN", 0, 128))
@@ -611,9 +649,8 @@ def rank_program(g, core, T, topo):
     ts(u("KV"), J, 0.0, A.mult, -1023.5, A.add)
     ts(u("CIX"), u("Jb", 0, 32), 16.0, A.mult, P15, A.add)
     ts(u("CB"), u("CT"), 16.0, A.mult, 7.0, A.add)
-    ts(u("C512"), u("CIX"), 500.0, A.add)
     fill(u("MINR"), LOW)
-    ts(e16("MINR"), u("CT"), 4.0, A.mult, 1024.0, A.add)
+    ts(e16("MINR"), u("CT"), 4.0, A.mult, 256.0, A.add)
     fill(u("MAXT"), -LOW)
     ts(u("MAXT", 0, 256, 32), u("CT"), -1.0, A.mult, -512.0, A.add)
     ts(u("sp4", 0, 4), u("Jb", 0, 4), col(P15, -9.0, A.add), A.is_equal, 4.0, A.mult)
@@ -621,11 +658,14 @@ def rank_program(g, core, T, topo):
     fill(u("two"), 2.0)
     scan(u("two"), u("two"), u("E16"), A.mult, A.add)
     half = col(u("two", 15, 16), 2.0 ** -16, A.mult)
-    iota(u("QR"), [[1, 512]], 0)
     for q in range(2):
-        ts(u("RH", 512 * q, 512 * q + 512), u("QR"), half, A.mult, 1536 + 2.0 ** -11 - 0.5 * q, A.add)
-    scan(u("OCC"), u("RH", 0, 512), u("RH", 512, 1024), A.max, A.subtract)
-    ts(u("CODE"), u("OCC"), col(nine, 2.0, A.mult), A.mult, col(nine, -1.0, A.mult), A.add)
+        ts(u("RH", 128 * q, 128 * q + 128), J, half, A.mult, 1536 + 2.0 ** -11 - 0.5 * q, A.add)
+    scan(u("OCC"), u("RH", 0, 128), u("RH", 128, 256), A.max, A.subtract)
+    twice, sign = col(nine, 2.0, A.mult), [col(nine, -1.0, A.mult)]
+    for q in range(4):
+        if q:
+            sign.append(col(u("E16", 7 + q // 2, 8 + q // 2), 2.0, A.mult, sign[q - 1 - (q == 2) - (q == 3)], A.add))
+        ts(u("CODE", 128 * q, 128 * q + 128), u("OCC"), twice, A.mult, sign[q], A.add)
     tt(u("CODE", 0, 4), u("CODE", 0, 4), u("sp4", 0, 4), A.add)
     fill(u("two"), 0.5)
     scan(u("two"), u("two"), u("E16"), A.mult, A.add)
@@ -636,7 +676,9 @@ def rank_program(g, core, T, topo):
     oddg = col(u("PIi", 3, 4), 1.0, A.mult)
     ts(u("kp4", 0, 4), u("sp4", 0, 4), 0.25, A.mult, nine, A.add)
     row15 = u("E16", 15, 16)
-    ts(u("MK"), u("QR"), col(row15, -1.0, A.mult), A.mult, col(row15, -512.0, A.mult), A.add)
+    four15 = col(row15, -4.0, A.mult)
+    for c in range(4):
+        ts(u("MK", 128 * c, 128 * c + 128), J, four15, A.mult, col(row15, -512.0 - c, A.mult), A.add)
     but15, top15 = col(P15, 15.0, A.is_lt), col(row15, 2216.0, A.mult)
     fill(u("H15"), 0.0)
     ts(e16("H15", 15), u("nblk"), hw, A.mult)
@@ -645,10 +687,8 @@ def rank_program(g, core, T, topo):
     fill(e16("MC2"), 0.0)
     ts(u("blk2"), J8, col(P15, odd, A.subtract, 0.5, A.mult), A.is_equal)
     ts(u("nblk2"), u("blk2"), -1.0, A.mult)
-    for a in range(0, 2048, 512):
-        select(u("EXP", a, a + 512), u("QZ"), [[1, 32], [0, 16]], A.not_equal, 1.0, a // 16, -1)
-        if a < FROM:
-            select(u("EXA", a, a + 512), u("QZ"), [[1, 4], [16, 8], [0, 16]], A.not_equal, 1.0, a // 128, -1)
+    for a in range(0, FROM, 512):
+        select(u("EXA", a, a + 512), u("QZ"), [[1, 4], [16, 8], [0, 16]], A.not_equal, 1.0, a // 128, -1)
     ts(u("PC", 12, 14), u("LI"), -65536.0, A.mult)
     wt = col(u("WI", 0, 1), 1.0, A.mult)
     ts(u("WTp"), BD, wt, A.mult)
@@ -662,6 +702,18 @@ def rank_program(g, core, T, topo):
     for s in (1, 2, 3, 4, 8, 12):
         select(u("SH", 128 * s, 128 * s + 128), BD, [[1, 128]], A.is_equal, 0.0, -s, -1)
     fourth = col(u("PIi", 4, 5), 3.0, A.is_equal, -128.0, A.mult)
+    first16, even, four = col(P4, 16.0, A.mult), col(P4, oddg, A.subtract), col(u("PIi", 4, 5), 1.0, A.mult)
+    ts(u("b2"), J, col(even, 16.0, A.mult, 31.0, A.add), A.is_le)
+    select(u("TR32"), u("b2"), [[1, 128]], A.is_ge, 0.0, 0, -1)
+    for q in range(2):
+        ts(u("SG%d" % q), J4, col(even, float(q), A.add) if q else even, A.is_equal, -1.0, A.mult)
+        ts(u("SF%d" % q), J, col(even, 16.0, A.mult, 16.0 * q + 4, A.add), A.is_equal, 4.0, A.mult)
+    here = col(four, first16, A.add)
+    ts(u("LW0"), J, col(fourth, 1.0 / 32, A.mult, col(here, 1.0, A.add), A.add), A.is_equal, 64.0, A.mult)
+    ts(u("LW1"), J, here, A.is_equal, -64.0, A.mult)
+    ts(u("LW2"), J, col(first16, 4.0, A.add), A.is_equal, col(fourth, -1.0 / 128, A.mult), A.mult)
+    fill(u("PX", 32, 48), 4096.0)
+    fill(u("FREE", 0, 256), 0.0)
     ts(u("A4n"), BD, fourth, A.mult)
     ts(u("B4"), BD, col(fourth, 4.0, A.mult, 128.0, A.add), A.mult)
 
@@ -671,58 +723,50 @@ def rank_program(g, core, T, topo):
         ts(u("PR5"), u("MI"), 2048, A.is_lt)
         ts(u("p6"), u("MI"), 1, A.add)
         tt(LISTS, u("p6"), u("PR5"), A.mult)
-        w = 32 * PLAIN
-        ts(u("p7", 0, w), u("MT", 0, w), -2047.5, A.add, 8192.0, A.mult)
-        tt(u("p7", 256, 256 + w), u("DUM", 0, w), u("p7", 0, w), A.min)
-        tt(u("TGS", 0, w), u("MT", 0, w), u("p7", 256, 256 + w), A.max)
-        ts(u("INO", 0, w), u("TGS", 0, w), 1.0, A.add)
-        for k in range(PLAIN):
-            act(ix(u("OT"), u("INO", 32 * k, 32 * k + 32)), V0P, F.Silu)
         up = col(P15, 0.0, A.is_gt, -1.0, A.mult)
         ts(u("UP"), J, col(P, -1.0, A.add), A.is_equal, up, A.mult)
         ts(u("UP11"), u("UP"), -2048.0, A.mult)
         scan(u("PF"), u("PR5"), u("PR5"), A.add, A.max)
+        many = u("LL", 0, 1)
+        ts(many, u("PF", 511, 512), 1.0 / 16, A.mult, 128.46875, A.add)
+        mm(u("p4", 200, 201), (u("BTU"), many), (IDB, many))
+        ends = col(u("p4", 200, 201), col(P15, -128.0, A.mult, 2048.0, A.add), A.subtract)
+        ts(u("ZE"), J144, ends, A.is_ge, col(many, -1.0, A.mult, col(row0, -1024.0, A.mult, 128 - 1.0 / 32, A.add), A.add), A.mult)
+        ts(u("JM"), J144, -256.0, A.add)
+        mm(u("p4", 208, 208 + COLS), (IDB, u("JM")), (BD, u("ZE")), (IDB, u("PENW"), u("p4", 208, 336)), (IDB, u("PENW", 0, 16), u("p4", 336, 352)))
+        mm(u("p4", 352, 352 + COLS), (IDB, u("JM")), (BD, u("ZE")))
+        scan(u("TGS", 0, COLS), u("MS", 0, COLS), u("p4", 208, 208 + COLS), A.mult, A.min)
+        ts(u("IX", 0, COLS // 16), e16("TGS", 15, COLS), 32.0, A.mult, col(oddg, 16.0, A.mult, 8192.0 + 47, A.add), A.add)
+        ts(u("WP", 0, COLS), u("p4", 352, 352 + COLS), 1.5 * 2.0 ** 23 + 256, A.add, 1.5 * 2.0 ** 23, A.subtract)
+        ts(u("PO"), u("WP", 0, COLS), 16.0, A.mult, P15, A.add)
         mm(u("p6", 440, 441), (u("UP"), u("PF", 511, 512)))
         mm(u("p5"), (IDB, u("PF")), (u("UP"), u("PF")), (u("N11"), u("PR5")), (u("UP11"), u("PR5")))
         ts(u("PF"), u("p5"), u("p6", 440, 441), A.subtract, 0.0, A.min)
-        mm(u("p6", 448, 480), *[(u("YK", 15 - r, 143 - r), u("PF", 32 * r, 32 * r + 32)) for r in range(16)])
+        mm(u("p6", 448, 480), *[(u("YK", 15 - r, 143 - r), e16("PF", r)) for r in range(16)])
         ts(u("r1"), u("CIX"), -1535.0, A.add)
         tt(u("r2"), u("p6", 448, 480), u("r1"), A.min)
         ts(u("F16"), u("r2"), 2047.0, A.add)
-        act(ix(u("SO"), u("F16")), V0P, F.Silu)
-        dma([(u("EV", a, a + 128), u("SO", 0, 128)) for a in range(0, 512, 128)], "ld9", 256)
-        n, left = RANKS[PLAIN], 16 - PLAIN
-        wide = -(-(n - 128) // 32) * 2
-        cp(u("DU", 0, n), u("SO", 0, n))
-        mm(u("p6", 480, 480 + n // 16), *[(u("YH", 15 - r, 143 - r), u("DU", r, n, 16)) for r in range(16)])
-        ts(u("HL", 0, n // 16), u("p6", 480, 480 + n // 16), -512.0, A.add)
-        cp(u("PF", 0, n), ix(u("W"), u("HL", 0, n // 16)))
-        ts(u("PR5", 0, n), u("PF", 0, n), 0.0, A.is_gt)
-        iota(u("PC", 76, 80), [[128, 4]], 2064 - 1536, 1)
-        for q in range(0, n, 128):
-            m = min(128, n - q)
-            ps, full = u("p5", q, q + 128, 1, (0, m)), u("PR5", q, q + m)
-            mm(ps, (u("ONEB", 0, m), u("KAm")), (u("PF", q, q + m), IDB), (full, u("N20")), (full, u("N20")))
-            if q:
-                ts(u("LT", q, q + 128, 1, (0, m)), ps, u("PC", 76 + q // 128, 77 + q // 128, 1, (0, m)), A.min)
-            else:
-                tt(u("LT", 0, 128), ps, u("DUL"), A.min)
-            for j in range(m // 16):
-                unfold("p4", 296 + q // 16 - 8 + j if q else 200 + j, wide if q else 8, "LT", q + PLAIN, j, left, m)
-            if not q:
-                ts(u("INO", 256, 256 + 8 * left), u("p4", 200, 200 + 8 * left), 1536.0, A.add)
-                for a in range(0, 8 * left, 32):
-                    b = min(a + 32, 8 * left)
-                    act(ix(u("OT"), u("INO", 256 + a, 256 + b)), u("EV", 0, 16 * (b - a)), F.Silu)
-        if n % 32:
-            unfold("p4", 295 + wide, wide, "LT", PLAIN, 0, left)
-        ts(u("INO", 352, 352 + wide * left), u("p4", 296, 296 + wide * left), 1536.0, A.add)
-        for k, m in enumerate(RANKS[PLAIN:-1]):
-            act(ix(u("OT"), u("INO", 352 + wide * k, 344 + wide * k + m // 16)), u("SO", 128, m), F.Silu)
+        cp(ix(u("SO"), u("F16")), V0)
+        mm(u("p6", 480, 512), *[(u("YH", 15 - r, 143 - r), u("SO", r, 512, 16)) for r in range(16)])
+        for q in range(2):
+            ts(u("HR", q, 64, 2), u("p6", 480, 512), -512.0, A.add)
+        for a in (0, 512):
+            cp(u("EV", a, a + 512), ix(u("W"), u("HR", a // 16, a // 16 + 32)))
+            turn(u("TAB", 32 + a, 544 + a), u("EV", a, a + 512))
+        cp(u("WP", 0, COLS), ix(u("TAB"), u("IX", 0, COLS // 16)))
+        ts(u("p7", 0, COLS), u("WP", 0, COLS), -8192.0, A.mult, 8192.0, A.add)
+        tt(u("p7", 256, 256 + COLS), u("DUM"), u("p7", 0, COLS), A.min)
+        tt(u("TGS", 0, COLS), u("WP", 0, COLS), u("p7", 256, 256 + COLS), A.max)
+        cp(u("INO"), u("TGS", 0, COLS))
+        for a, b in zip((0,) + CUT_I, CUT_I + (COLS,)):
+            cp(u("PAY", 16 * a, 16 * b), ix(u("SO", 0, 512), u("PO", a, b)))
+            act(ix(u("OT"), u("INO", a, b)), u("PAY", 16 * a, 16 * b), F.Silu)
 
-    def gather(out, win, off, cuts, many):
+    def gather(out, win, off, cuts, many, neg=False):
         for k, (a, b) in enumerate(zip((0,) + cuts, cuts + (128,))):
-            if k < many:
+            if neg:
+                act(u(out, 16 * a, 16 * b), ix(win, u(off, a, b)), F.Identity, scale=-1.0)
+            elif k < many:
                 cp(u(out, 16 * a, 16 * b), ix(win, u(off, a, b)))
             else:
                 act(u(out, 16 * a, 16 * b), ix(win, u(off, a, b)), F.Copy)
@@ -731,11 +775,11 @@ def rank_program(g, core, T, topo):
         s1 = "S1%d" % (t % 2)
         lanes = u("W", t % 4, 512, 4)
         cp(u("OWN"), lanes)
-        gather("T", X, "OWN", CUT_T, 2 if t else 3)
+        gather("T", X, "OWN", CUT_T, 0, True)
         ts(u("OWNH"), lanes, 0.0, A.max)
         ts(u("PRE"), u("OWNH"), 0.0, A.is_gt)
         k = u("p3", 0, 128)
-        mm(k, (ONE, u("KAs")), (u("PRE"), u("N27")), (u("OWNH"), IDB), *sums("p3", 0, "T", "w64k"))
+        mm(k, (ONE, u("KAs")), (u("PRE"), u("N27")), (u("OWNH"), IDB), *sums("p3", 0, "T", u("n64k")))
         scan(u(s1), u("MINs"), k, A.max, A.min)
         low(e16("ZS", 0, 128), e16(s1, 15), u("hi8"), 4096)
         tile("ZS", "HS", u("p4", 0, 8), "blk", "nblk", "MC")
@@ -750,9 +794,9 @@ def rank_program(g, core, T, topo):
         for a in range(0, 2048, CUT_S):
             if a >= FROM:
                 scan(u("REP", a, a + CUT_S), u("MS", 0, CUT_S), u("Z0", a, a + CUT_S), A.mult, A.add)
-            scan(u("US", a, a + CUT_S), u("MS", 0, CUT_S), u("T", a, a + CUT_S), A.mult, A.max)
-        cp(e16("UD"), e16("US", 15))
-        mm(u("p4", 8, 16), (ONE, u("L2N")), (e16("US", 15), u("w64k")))
+            scan(u("US", a, a + CUT_S), u("MS", 0, CUT_S), u("T", a, a + CUT_S), A.mult, A.min)
+        ts(e16("UD"), e16("US", 15), -1.0, A.mult)
+        mm(u("p4", 8, 16), (ONE, u("L2N")), (e16("US", 15), u("n64k")))
         tt(u("wp8"), e16(s1, 15), u("p4", 8, 16), A.is_ge)
         mm(u("p6", 0, 128), (u("PRE"), u("SEL0R")))
         act(u("LR"), u("p6", 0, 128), F.Copy)
@@ -762,56 +806,59 @@ def rank_program(g, core, T, topo):
         cp(u("BT16"), u("p4", 144, 152))
 
     def part_vacant(t):
-        act(u("OCC"), LISTS, F.Sign)
-        mm(u("p6", 128, 160), *[(u("Y", 15 - r, 143 - r), e16("OCC", r)) for r in range(16)])
-        act(u("OCb"), u("p6", 128, 160), F.Copy)
+        b, lo, hi = LISTS[1][0]
+        dma([(u("OCf", 16 * q, 16 * q + 16), (T[b][16 * q:128:32, lo:hi],) + LISTS[1:]) for q in range(2)], "oc%d" % t, 40)
+        ts(u("OCg"), u("OCf"), 0.0, A.is_le)
+        turn(u("OCb"), u("OCg"))
         mm(u("p4", 32, 64), (BD, u("OCb")))
-        mm(u("p4", 64, 96), (u("BTI"), u("OCb")), (IDB, u("CIX")))
+        mm(u("p4", 64, 96), (u("BTU"), u("OCb")))
         scan(u("CS"), u("ONEB", 0, 32), u("p4", 32, 64), A.mult, A.add)
-        tt(u("r1"), u("p4", 64, 96), u("CS"), A.subtract)
-        tt(u("r2"), u("r1"), u("C512"), A.min)
-        ts(u("F16"), u("r2"), float(t % 4), A.add)
-        act(ix(u("FREE", 0, 1024), u("F16")), V0, F.Silu)
-        ts(u("NFF"), u("SEL0R"), u("CS", 31, 32), A.mult)
+        tt(u("PX", 0, 32), u("CS"), u("p4", 64, 96), A.subtract)
+        ts(u("NFF"), u("SEL0R"), u("CS", 31, 32), A.mult, -1.0, A.mult)
+        scan(u("OCt"), u("MS", 0, 32), u("OCg"), A.mult, A.add)
+        mm(u("p4", 96, 98), (u("TR32"), e16("OCt", 15)))
+        for q in range(2):
+            ts(u("MB", 128 * q, 128 * q + 128), J, u("p4", 96 + q, 97 + q), A.is_ge)
+        a, b = u(BANK_V[0], BANK_V[1], BANK_V[1] + 128), u(BANK_V[0], BANK_V[1] + 128, BANK_V[1] + 256)
+        mm(a, (IDB, u("PENW")), *[(u("SG%d" % q), u("MB", 128 * q, 128 * q + 128)) for q in range(2)])
+        scan(u("VB"), u("MS", 0, 128), a, A.mult, A.min)
+        ts(u("V16"), e16("VB", 15), -1.0, A.mult)
+        tt(u("MJ"), ix(u("PX"), u("V16")), J, A.is_le)
+        mm(b, *[(u("SF%d" % q), u("MB", 128 * q, 128 * q + 128)) for q in range(2)], *[(u("LW%d" % q), u("MJ")) for q in range(3)])
+        act(u("FREE", t % 4, t % 4 + 128), b, F.Identity, bias=first[0])
 
     def part_split(t):
         s = u("ZP%d" % (t % 2))
         mm(u("p6", 288, 416), (s, NIDB))
         act(u("ST"), u("p6", 288, 416), F.Copy)
-        for c in range(4):
-            a, b, ps = 512 * c, 512 * c + 512, u("p%d" % (c % 3))
-            mm(ps, (IDB, u("T", a, b)), (u("ST"), u("EXP", a, b)))
-            act(u("SQ", a, b), ps, F.Square)
+        for a in range(0, 2048, 512):
+            x = u("T", a, a + 512)
+            times(u("SQ", a, a + 512), x, x)
+        by_slot("AW", s, 4)
         act(u("SQS"), s, F.Square)
-        k = u(BANK_B[0], BANK_B[1], BANK_B[1] + 128)
-        mm(k, (ONE, u("KAb")), (u("PRE"), u("P23")), *sums(BANK_B[0], BANK_B[1], "SQ", "w32"))
+        k, lv = u("p7", 0, 128), u(BANK_L[0], BANK_L[1], BANK_L[1] + 128)
+        mm(k, (u("PRE"), u("P23")), (ONE, u("KAb")), *sums("p7", 0, "SQ", u("w32")), *sums("p7", 0, "AW", u("w64", 0, 8), True))
         scan(u("SB"), u("MS", 0, 128), k, A.mult, A.max)
         low(e16("ZB", 0, 128), e16("SB", 15), u("hb8"), 32)
         tile("ZB", "HB", u("p4", 16, 24), "nblk", "blk", "MC", (IDB, u("CB")))
         cp(u("B16"), u("p4", 16, 24))
-        act(u("XB"), ix(u("T"), u("B16")), F.Copy)
+        act(u("XB"), ix(u("T"), u("B16")), F.Identity, scale=-1.0)
         act(u("SQB"), u("XB"), F.Square)
-        mm(u("p6", 288, 416), (s, IDB), (u("XB"), NIDB))
-        act(u("WV"), u("p6", 288, 416), F.Copy)
-        for c in range(4):
-            a, b, ps = 512 * c, 512 * c + 512, u("p%d" % (c % 2))
-            mm(ps, (u("WV"), u("EXP", a, b)))
-            tt(u("AW", a, b), u("T", a, b), ps, A.mult)
-        lv = u("p7", 0, 128)
-        mm(lv, (u("PRE"), u("N20")), (u("SQS"), NBD), (u("SQB"), BD), *sums("p7", 0, "AW", "w2"))
+        by_slot("AB", u("XB"), 4)
+        mm(lv, (u("PRE"), u("N20")), (u("SQS"), NBD), *sums(*BANK_L, "AW", u("w64", 8, 16), True), (u("SQB"), BD), *sums(*BANK_L, "AB", u("w2"), True))
         ts(u("LN", 0, 128), lv, -2.0 ** 20, A.is_lt)
         ts(u("LN", 128, 256), lv, -2.0 ** 20, A.is_ge)
         scan(u("XC"), u("MS", 0, 256), u("LN"), A.mult, A.add)
         for q in range(3):
             ts(u("XF", 256 * q, 256 * q + 256), u("XC"), 0.5 ** (q + 1), A.mult, 159.5 + 0.5 ** (q + 2), A.add)
-        pp = u("p7", 128, 384)
+        pp = u("p7", 256, 512)
         mm(pp, (ONE, u("KAp")), (u("P20"), u("LN")), (u("RV3"), u("XC")),
            *[(u("RV%d" % q), u("XF", 256 * q, 256 * q + 256)) for q in range(3)], (u("OWNH"), u("ID2")))
         act(u("Pa", 0, 256), pp, F.Abs, bias=-54.0 * TAU)
-        tt(u("Pa", 0, 255), u("p7", 129, 384), u("Pa", 0, 255), A.min)
+        tt(u("Pa", 0, 255), u("p7", 257, 512), u("Pa", 0, 255), A.min)
         for q, a, b in ((1, "Pa", "Pb"), (2, "Pb", "Pa"), (3, "Pa", "Pb")):
-            act(u("p5", 0, 256), u(a, 0, 256), F.Abs, bias=-2.0 * 3 ** (3 - q) * TAU)
-            tt(u(b, 0, 256), u("p5", 0, 256), u(a, 1 << q, 256 + (1 << q)), A.min)
+            act(u(*BANK_S), u(a, 0, 256), F.Abs, bias=-2.0 * 3 ** (3 - q) * TAU)
+            tt(u(b, 0, 256), u(*BANK_S), u(a, 1 << q, 256 + (1 << q)), A.min)
         ts(u("SL"), u("Pb", 0, 256), TAU, A.min, TAU, A.subtract)
 
     def part_near(t):
@@ -855,7 +902,7 @@ def rank_program(g, core, T, topo):
         for a in range(0, 2048, 512):
             scan(u("AX", a, a + 512), u("UD", a, a + 512), u("DT", a, a + 512), A.min, A.max, 64.0)
         k = u("p3", 384, 512)
-        mm(k, (ONE, u("KAd")), (u("PRD"), u("N27")), (u("IDF"), e16("S1%d" % (t % 2), 15), e16("p3", 399)), *sums("p3", 384, "DT", "w64k")[:15])
+        mm(k, (ONE, u("KAd")), (u("PRD"), u("N27")), (u("IDF"), e16("S1%d" % (t % 2), 15), e16("p3", 399)), *sums("p3", 384, "DT", u("w64k"))[:15])
         mm(u("p4", 160, 176), (ONE, u("THN")), (ONE, u("THZ")), (u("N40"), u("wp8"), u("p4", 161, 176, 2)), (u("P23"), u("SZ")),
            *[(u("EQ", 128 * q, 128 * q + 128), u("C25", 0, 2), u("p4", 160 + 2 * q, 162 + 2 * q)) for q in range(8)], (e16("AX", 14), u("w64d")))
         scan(u("S3"), u("MIN"), k, A.max, A.min)
@@ -874,15 +921,17 @@ def rank_program(g, core, T, topo):
         k0, k1, k2 = u("p7", 384, 512), u("p0", 256, 384), u("p7", 0, 128)
         mm(k0, (ONE, u("NFF")), (u("TRIm"), WR))
         mm(k1, (IDB, u("PENK")), (WR, u("TRIm")))
-        ts(SR, k0, -1536.0, A.is_lt)
+        ts(SR, k0, -2048.0, A.is_lt)
         scan(u("KR"), u("MINR"), k1, A.max, A.min)
         ts(u("RK"), e16("KR", 15), float(cl), A.add)
         mm(k2, (ONE, u("KAr")), (u("TRIm"), u("LR")), (u("NTRIm"), MR), (u("NTRIm"), SR))
         for q in range(2):
             ts(u("EE", 128 * q, 128 * q + 128), k2, 16.0 * q, A.is_equal)
             mm(u("p4", 104 + q, 105 + q), (u("EE", 128 * q, 128 * q + 128), u("PB", 0, 1)))
-        cp(u("SE%d" % t), u("p4", 104, 106))
-        send(u("SE%d" % t), "QI", "q", t, 1)
+        cp(u("SE"), u("p4", 104, 106))
+        cp(e16("QZ"), ix(u("ZP%d" % (t % 2)), u("SE")))
+        for a in (0, 256):
+            scan(u("QRp", a, a + 256), u("MS", 0, 256), u("QZ", a, a + 256), A.mult, A.add)
         mm(u("p4", 176, 192), (IDB, u("PENB")), *[(u("EE", 128 * q, 128 * q + 128), x, u("p4", 176 + 8 * q, 184 + 8 * q))
                                                   for q in range(2) for x in (u("C3K"), e16("ZS", 0, 128))])
         scan(u("SV"), u("MS", 0, 32, 2), u("p4", 176, 192), A.mult, A.min)
@@ -902,7 +951,7 @@ def rank_program(g, core, T, topo):
         scan(u("TGS"), u("MAXT"), u("p0", 0, 256), A.min, A.max)
         ts(u("TG16"), u("TGS", 31, 256, 32), -1.0, A.mult)
         mm(u("p1", 0, 128), (u("SL", 128, 256), NIDB), (MR, u("N20")))
-        tt(u("ELS"), u("p1", 0, 128), u("MK", cl, 512, 4), A.max)
+        tt(u("ELS"), u("p1", 0, 128), u("MK", 128 * cl, 128 * cl + 128), A.max)
         cp(ix(u("W"), u("TG16")), u("ELS"))
         if t + 1 == RO:
             return
@@ -919,10 +968,11 @@ def rank_program(g, core, T, topo):
             unfold("p1", 128 + j, 8, "m2", 0, j, MOVERS)
         ts(u("MVO", 0, 8 * MOVERS), u("p1", 128, 128 + 8 * MOVERS), 1536.0, A.add)
         cp(u("EV", 0, 128), ev)
-        dma([(u("EV", 128 * q, 128 * q + 128), u("EV", 0, 128)) for q in range(1, 4)], "ev%d" % t, 192)
-        for a in range(0, 8 * MOVERS, 32):
-            b = min(a + 32, 8 * MOVERS)
-            act(ix(u("OT"), u("MVO", a, b)), u("EV", 0, 16 * (b - a)), F.Silu)
+        cuts = list(zip((0,) + CUT_M, CUT_M + (MOVERS,)))
+        many = max(b - a for a, b in cuts)
+        dma([(u("EW", 128 * q, 128 * q + 128), u("EV", 0, 128)) for q in range(1, many)], "ev%d" % t, 64 * (many - 1))
+        for a, b in cuts:
+            act(ix(u("OT"), u("MVO", 8 * a, 8 * b)), u("EW", 0, 128 * (b - a)), F.Silu)
         mm(u("p6", 432, 440), (ONE, e16("ZM")))
         act(u("z8"), u("p6", 432, 440), F.Identity, bias=-0.9375, acc=u("mc", 0, 1))
         ts(u("mc", 1, 2), u("mc", 0, 1), 1.5 * 2.0 ** 27, A.add, 1.5 * 2.0 ** 27, A.subtract)
@@ -950,27 +1000,20 @@ def rank_program(g, core, T, topo):
         scan(u("WP"), u("M32"), u("p2", 0, 256), A.mult, A.min)
         ts(u("H16"), u("WP", 31, 256, 32), -1.0, A.mult, -512.0, A.add)
         cp(u("HLA"), ix(LISTS, u("H16")))
+        send(u("HLA"), "HQ", "h", t, -1)
 
-    def part_serve(t):
-        qi = u("QI%d" % t)
-        cp(e16("QZ"), ix(u("QA%d" % t), qi))
-        cp(u("HL"), ix(u("HLA"), qi))
+    def part_meet(t):
+        fill(u("XQ%d" % t, 0, 1), -64.0)
+        cp(u("HL"), ix(u("HQ%d" % t), u("SE")))
         for a, b, ps in ((0, 256, u("p5", 0, 256)), (256, 512, u(BANK_Q, 256, 512))):
-            scan(u("QRp", a, b), u("MS", 0, 256), u("QZ", a, b), A.mult, A.add)
-            tt(u("QD", a, b), ix(X, u("HL", a // 16, b // 16)), u("QRp", a, b), A.subtract)
+            tt(u("QD", a, b), ix(u("XQ%d" % t), u("HL", a // 16, b // 16)), u("QRp", a, b), A.subtract)
             act(u("QS", a, b), u("QD", a, b), F.Square)
             mm(ps, (ONE, u("KQ5")), (IDB, u("QRp", a, b)), (u("IDh"), u("QD", a, b)), (u("B256"), u("QS", a, b)))
-            scan(u("QRi" if SCAN_I else "QR", a, b), u("MIN5"), ps, A.max, A.min)
-        if SCAN_I:
-            ts(u("SN%d" % t), e16("QRi", 15), 15, A.bitwise_and)
-        else:
-            ts(u("hs"), e16("QR", 15), 1.5 * 2.0 ** 27, A.add, 1.5 * 2.0 ** 27, A.subtract)
-            ts(u("ht"), e16("QR", 15), 1.5 * 2.0 ** 23, A.add, 1.5 * 2.0 ** 23 - 7, A.subtract)
-            tt(u("SN%d" % t), u("ht"), u("hs"), A.subtract)
-        send(u("SN%d" % t), "RS", "s", t, -1)
+            scan(u("QRi", a, b), u("MIN5"), ps, A.max, A.min)
+        ts(u("SN"), e16("QRi", 15), 15, A.bitwise_and)
 
     def part_apply(t):
-        cp(ix(X, u("S32")), u("RS%d" % t))
+        cp(ix(X, u("S32")), u("SN"))
 
     part_start()
     for t in range(RO):
@@ -979,6 +1022,7 @@ def rank_program(g, core, T, topo):
         part_split(t)
         if t:
             part_apply(t - 1)
+        send(u("X", 0, 2064), "XQ", "x", t, -1)
         part_near(t)
         part_partner(t)
         part_look(t)
@@ -989,7 +1033,7 @@ def rank_program(g, core, T, topo):
             act(u("p1"), LISTS, F.Identity, bias=-1.0)
             tt(u("YM"), u("t512a"), u("p1"), A.max)
             dma([(mark("ym", ap=T.ym[:]), u("YM"))], "st0", 256)
-        part_serve(t)
+        part_meet(t)
     part_apply(RO - 1)
     dma([(mark("yx", ap=T.yx[:]), u("X", 1, 2049))], "st1", 512)
 
@@ -1050,8 +1094,9 @@ def rank_program(g, core, T, topo):
                 x.then_inc(T.sem[o["dma"]], 16)
             note(e, rd, wr, o["dma"], 16 * len(ins))
         else:
-            cnt[e] += 1
-            ins.then_inc(T.sem[e], 1)
+            for x in ins if isinstance(ins, list) else [ins]:
+                cnt[e] += 1
+                x.then_inc(T.sem[e], 1)
             note(e, rd, wr, e, cnt[e])
     for sem, n in total.items():
         if known["k"].get(sem, 0) < n:

import math
from concourse.mybir import AluOpType as A, ActivationFunctionType as F

RO = 5
S, B, H, I, U = "float32", "bfloat16", "float16", "int32", "uint16"
LOW = 1 - 2 ** 24
TAU = 4096.0
COLS = 144
SCAN_I = True
_BUF = []


def _sb(dtype, cols, names):
    _BUF.extend((n, cols, dtype) for n in names.split())


_sb(B, 2304, "X")
_sb(B, 2048, "T US SQ AX AW AB SH OG DT DU EXA REP Z0")
_sb(B, 512, "MS PR5")
_sb(H, 512, "PF")
_sb(H, COLS, "ZE")
_sb(B, COLS, "JM")
_sb(B, 8, "LL")
_sb(S, 16 * COLS, "PAY")
_sb(S, 1056, "TAB")
_sb(U, COLS, "PO INO")
_sb(U, 64, "HR")
_sb(U, 16, "IX")
_sb(B, 256, "YO")
_sb(B, 144, "YH YK")
_sb(B, 128, "UP UP11 N11 H15")
_sb(H, 128, "PA")
_sb(B, 1024, "SO")
_sb(S, 512, "V0P MK")
_sb(S, COLS, "DUM")
_sb(H, 1024, "RH")
_sb(S, 16, "two")
_sb(B, 128, "MC2 WD")
_sb(B, 2048, "UD")
_sb(B, 128, "P768")
_sb(S, 256, "TGS MAXT")
_sb(S, 128, "KR MINR")
_sb(I, 128, "S2i")
_sb(B, 8, "blk2 nblk2")
_sb(B, 1024, "EQ")
_sb(B, 768, "XF")
_sb(B, 512, "CODE QD QZ QRp QS")
_sb(B, 128, "OCC")
_sb(B, 256, "KQ5")
_sb(S, 256, "MIN5")
_sb(I, 512, "QRi")
_sb(B, 256, "PEN CG ID2 KAp QN LN XC ZMW MWR EE PEN2 M32")
_sb(B, 144, "Jb Y w8k og0 og1 og2 og3")
_sb(B, 128, "J4b J15b b1 b2 R16 MC IDB BD NBD BTI ONEB PRE PRD LR SR XB SQS SQB SEL0R TRIm NTRIm HWN N27 P23 N20 P20 P11 "
            "RV0 RV1 RV2 RV3 ST KAs KAb KAd KAn KAr KAm PENK PRL A4n B4 CN1 QB ZP0 ZP1 WTp IDh B256 B512 N512 HO EH PENW WM")
_sb(B, 32, "OCb")
_sb(B, 16, "THN THZ ROW1 SZ w64d PENB w64")
_sb(B, 8, "blk nblk w64k n64k w32 w2 SEL0 L2N wp8 C25 PB C3K")
_sb(H, 256, "SL CNT CTG")
_sb(H, 144, "ZS HS ZB HB HD")
_sb(H, 128, "OWNH DMH DM2 KV m1 m2 NFF")
_sb(H, 32, "CIX")
_sb(H, 8, "CB")
_sb(S, 4496, "OT")
_sb(S, 768, "FREE")
_sb(S, 48, "PX")
_sb(S, 128, "VB")
_sb(B, 256, "MB")
_sb(B, 128, "MJ BTU TR32 SG0 SG1 SF0 SF1 LW0 LW1 LW2")
_sb(B, 32, "OCt")
_sb(U, 8, "V16")
_sb(S, 768, "DS")
_sb(B, 128, "EVB N40")
_sb(S, 640, "W")
_sb(S, 512, "J2f J3f t512a t512b YM QR D1")
_sb(S, 1024, "EV")
_sb(S, 264, "Pa Pb")
_sb(S, 256, "WP")
_sb(S, 128, "MINs MINn MIN S10 S11 S2 S3 SB ELS IDF VH VR HLA DUL")
_sb(S, 128, "PC")
_sb(S, 32, "CS r1 r2 C512 hs ht")
_sb(S, 16, "E16 KQ SV")
_sb(S, 8, "blkf hi8 hb8 z8 mc kq G4 EP sp4 kp4")
_sb(I, 2192, "AC4")
_sb(I, 512, "MI")
_sb(I, 8, "PIi a8 d8")
_sb(I, 2, "LI WI")
_sb(U, 128, "OWN AN DM MVO")
_sb(U, 32, "F16 HL")
_sb(U, 8, "RK S16 A16 B16 D16 NT16 TG16 BT16 VV16 H16 O16")
_sb(U, 2, "S32 SE")
_sb(I, 32, "SN")
_sb(S, 32, "OCf")
_sb(B, 32, "OCg")
_AT, _end = {}, {}
for _n, _c, _d in _BUF:
    _AT[_n] = ("ar_" + _d, _end.get(_d, 0), _c, _d)
    _end[_d] = _end.get(_d, 0) + -(-_c // 16) * 16
SCRATCH = {"ar_" + _d: ("sbuf", [128, _c], _d) for _d, _c in _end.items()}
for _n, _m, _o, _c in (("NIDB", "ID2", 0, 128), ("ZM", "ZMW", 0, 128), ("ZW", "ZMW", 128, 128), ("MR", "MWR", 0, 128), ("WR", "MWR", 128, 128),
                       ("ZALL", "ZS", 0, 720), ("MIN3", "MINs", 0, 384), ("CT", "CIX", 0, 8), ("EW", "EV", 0, 1024)):
    _AT[_n] = (_AT[_m][0], _AT[_m][1] + _o, _c, _AT[_m][3])
for _t in range(RO):
    for _n, _c, _d in (("QA", 128, B), ("XQ", 2064, B), ("HQ", 128, S)):
        SCRATCH["%s%d" % (_n, _t)] = ("sbuf", [128, _c], _d)
        _AT["%s%d" % (_n, _t)] = ("%s%d" % (_n, _t), 0, _c, _d)
for _k in range(8):
    SCRATCH["p%d" % _k] = ("psum", [128, 512], S)
    _AT["p%d" % _k] = ("p%d" % _k, 0, 512, S)
SEMAPHORES = ["v", "p", "s", "k", "st0", "st1"] + ["ld%d" % i for i in range(11)] + ["ev%d" % i for i in range(RO - 1)] + ["oc%d" % i for i in range(RO)]
for _t in range(RO):
    SEMAPHORES += [a + b + str(_t) for a in "rlfm" for b in "axh"]

CYC, PEC, GAT, SCA, WAY, FIRST = 0.00085, 0.0005, 1.6, 3.7, 2.3, 2.5
LONG = 9.0
START, PERKB = 2.2, 0.005
VIEWS = ((0.23, 0.14, 1.0, 0.8, 0.62), (0.26, 0.13, 1.15, 1.2, 1.3))
PLAN, PASSES = (0.24, 0.14, 1.0, 0.92, 0.8), 4
TURNS, AGAIN, EASE = 110000, 1500, 0.12
SAME = 64
MOVERS = 15
CUT_A, BY_PE, BANK_Q, BANK_A = (32, 64, 104), (0, 1), "p0", ("p2", "p1")
BANK_E, BANK_D, BANK_B = (("p0", 0), ("p1", 0), ("p2", 0), ("p6", 0)), "p2", ("p7", 0)
BANK_L, BANK_S, BANK_V = ("p6", 128), ("p5", 0, 256), ("p0", 0)
CUT_M = (2, 4, 8, 12)
CUT_I = (48, 96)
CUT_T, CUT_D, CUT_O, CUT_S = (32, 64, 96), (32, 64, 96), (32, 64, 96), 512
_ORDER = {}


def _relay(topo, a, b, long):
    if topo.may_write(a, b) and not long:
        return None
    return min((h for h in topo.cores_of(a) if h != a and topo.may_write(h, b)), key=lambda h: (topo.die(h) != topo.die(a), -h if long else h))


def _relay_program(g, core, T, topo):
    used = []
    for t in range(RO):
        for back, buf, arr, fwd, loc in ((0, "QA", "ra", "fa", "ma"), (1, "XQ", "rx", "fx", "mx"), (1, "HQ", "rh", "fh", "mh")):
            for r in range(8):
                x, y = T.cores[r], T.cores[(r + 1 + t % 7) % 8]
                x, y = (y, x) if back else (x, y)
                if _relay(topo, x, y, buf == "XQ") == core:
                    rid, pid = topo.addr(y, core)
                    g.wait_ge(T.sem["%s%d" % (fwd, t)], len(topo.engines(x, core)))
                    g.remote_dma(T["%s%d" % (buf, t)][:], T["%s%d" % (buf, t)][:], T.sem["%s%d" % (arr, t)],
                                 T.sem["%s%d" % (loc, t)], pid, rid, topo.mask(core, y))
                    used.append((T.sem["%s%d" % (loc, t)], len(topo.engines(core, y))))
    for s, n in used:
        g.wait_ge(s, n)


def _psum(b):
    return len(b) == 2 and b[0] == "p"


def _cycles(a, b):
    return max(min(64, a[2]), b[2]) * (4 if a[3] == S else 1)


def _order(ops):
    n = len(ops)
    pred, log = [set() for _ in range(n)], {}
    for i, o in enumerate(ops):
        for kind, lst in ((0, o["rd"]), (1, o["wr"])):
            for (b, lo, hi) in lst:
                pred[i].update(j for (l2, h2, j, wr) in log.get(b, ()) if lo < h2 and l2 < hi and (kind or wr))
        for (b, lo, hi) in o["wr"]:
            log[b] = [x for x in log.get(b, []) if not (lo <= x[0] and x[1] <= hi)] + [(lo, hi, i, True)]
        for (b, lo, hi) in o["rd"]:
            log.setdefault(b, []).append((lo, hi, i, False))
        pred[i].discard(i)
    succ, early = [[] for _ in range(n)], {}
    for i in range(n):
        for j in pred[i]:
            succ[j].append(i)
            if ops[i]["items"] and ops[j]["e"] != "p":
                at = 0.0
                for (_o, a, b) in ops[i]["items"]:
                    if any(x[0] == y[0] and x[1] < y[2] and y[1] < x[2] for x in a[1] + b[1] for y in ops[j]["wr"]):
                        early[(j, i)] = at
                        break
                    at += _cycles(a, b) * PEC
    sends = [[i for i in range(n) if ops[i]["land"] and (ops[i]["land"][0][1] == "x") == long] for long in (0, 1)]
    for j, i in [x for y in sends for x in zip(y, y[1:])]:
        if j not in pred[i]:
            pred[i].add(j)
            succ[j].append(i)
            early[(j, i)] = ops[j]["lat"]
    eng, cost, lat = [o["e"] for o in ops], [o["cost"] for o in ops], [o["lat"] for o in ops]
    banks = [sorted(set(b for (b, _l, _h) in o["rd"] + o["wr"] if _psum(b))) for o in ops]
    views = [([0.0] * n, x[1], [None] * n) for x in VIEWS]
    queue, mine, others, ways = [0] * n, [None] * n, [None] * n, [o["ways"] for o in ops]

    def settle(calls, after):
        for i in calls:
            queue[i] = "vpsky".index(eng[i])
            mine[i] = [3 * int(b[1]) + queue[i] for b in banks[i]]
            others[i] = [3 * int(b[1]) + e for b in banks[i] for e in range(3) if e != queue[i]]
        for (c, xw, inc), (wake, _xw, mul, gat, sca) in zip(views, VIEWS):
            for i in calls:
                c[i] = cost[i] * (mul, gat, sca)[ops[i]["how"]]
            for i in after:
                inc[i] = [(j, c[j] + lat[j] + (xw if eng[j] != eng[i] else 0.0 if eng[i] == "p" else wake) - mul * early.get((j, i), 0.0)) for j in pred[i]]

    def move(i, e):
        eng[i], cost[i] = e, ways[i][e][1]
        settle([i], [i] + succ[i])
    settle(range(n), range(n))

    def times(k, order, lo, hi, start, by, kept, last, user, old=None):
        c, xw, inc = views[k]
        for pos in range(lo, hi):
            if pos % 32 == 0:
                if old and pos >= lo + SAME:
                    was = old[0]
                    d = start[order[pos - 1]] - was[order[pos - 1]]
                    if all(-1e-7 < start[x] - was[x] - d < 1e-7 for x in order[pos - SAME:pos]):
                        for x in order[pos:]:
                            start[x] = was[x] + d
                        kept += old[2][pos // 32:]
                        return
                kept.append((last[:], user[:]))
            a = order[pos]
            s, w = 0.0, -1
            for j, d in inc[a]:
                d += start[j]
                if d > s:
                    s, w = d, j
            j = last[queue[a]]
            if j >= 0 and start[j] + c[j] > s:
                s, w = start[j] + c[j], j
            last[queue[a]] = a
            for q in others[a]:
                j = user[q]
                if j >= 0 and start[j] + c[j] + xw > s:
                    s, w = start[j] + c[j] + xw, j
            for q in mine[a]:
                user[q] = a
            start[a], by[a] = s, w

    def clock(order, lo, hi, old, loss):
        work, late = [], 0.0
        for k in range(len(views)):
            if old:
                start, by, kept, on = old[k]
                w = (start[:], by[:], kept[:lo // 32], kept[lo // 32][0][:], kept[lo // 32][1][:])
                at = next((pos for pos in range(hi, n) if order[pos] in on), n - 1) + 1
                times(k, order, lo // 32 * 32, at, *w)
                late += w[0][order[at - 1]] - start[order[at - 1]] if order[at - 1] in on else -1e9
            else:
                w, at = ([0.0] * n, [-1] * n, [], [-1] * 5, [-1] * 24), 0
            work.append((w, at))
        if late > loss * len(views):
            return None, None
        total, new = 0.0, []
        for k, (w, at) in enumerate(work):
            times(k, order, at, n, *w, old and old[k])
            start, by, c = w[0], w[1], views[k][0]
            a = max(order[-16:], key=lambda i: start[i] + c[i] + lat[i])
            total += start[a] + c[a] + lat[a]
            on = {a: 0}
            while by[a] >= 0:
                a = by[a]
                on[a] = 0
            new.append((start, by, w[2], on))
        return total / len(views), new

    def chain(state):
        pairs = []
        for _start, _by, _kept, on in state:
            way = list(on)
            for k, a in enumerate(way[:-1]):
                if way[k + 1] not in pred[a]:
                    pairs.append((way[k + 1], a))
                    pairs += [(b, a) for b in way[k + 4:k + 17:12] if queue[b] == queue[a]]
        return pairs

    def place(rank, back, choose):
        wake, xw, mul, gat, sca = PLAN
        before, after = (succ, pred) if back else (pred, succ)
        left, start, end, busy = [len(x) for x in before], [0.0] * n, [0.0] * n, {}
        ready = sorted((rank[i], i) for i in range(n) if not left[i])
        while ready:
            a = ready.pop()[1]
            found = None
            for e, c in [(eng[a], cost[a])] + [(e2, x[1]) for e2, x in ways[a].items() if choose and e2 != eng[a]]:
                c *= (mul, gat, sca)[ops[a]["how"]]
                s = lat[a] if back else 0.0
                for j in before[a]:
                    w = xw if eng[j] != e else 0.0 if e == "p" else wake
                    s = max(s, end[j] + w + lat[a if back else j] - mul * early.get((a, j) if back else (j, a), 0.0))
                moved = True
                while moved:
                    moved = False
                    for key, gap in [(e, 0.0)] + [(b, xw) for b in banks[a]]:
                        for lo, hi, e2 in busy.get(key, ()):
                            if (key == e or e2 != e) and lo < s + c + gap and s < hi + gap:
                                s, moved = hi + gap, True
                if found is None or s + 2 * c < found[3] - 0.02:
                    found = (s + c, s, e, s + 2 * c)
            if found[2] != eng[a]:
                move(a, found[2])
            end[a], start[a] = found[:2]
            for key in [eng[a]] + banks[a]:
                busy.setdefault(key, []).append((start[a], end[a], eng[a]))
            for j in after[a]:
                left[j] -= 1
                if not left[j]:
                    ready.append((rank[j], j))
            ready.sort()
        return start, [end[i] + (0.0 if back else lat[i]) for i in range(n)]

    def sort(start):
        at = [0.0] * n
        for i in range(n):
            at[i] = max([start[i]] + [at[j] + 1e-6 for j in pred[i]])
        return sorted(range(n), key=lambda i: at[i])
    way, best, seed = [0.0] * n, None, 12345
    for i in range(n - 1, -1, -1):
        way[i] = cost[i] + lat[i] + max([way[j] + PLAN[0] for j in succ[i]] + [0.0])
    for turn in range(PASSES):
        start, end = place(way, False, True)
        order = sort(start)
        span = clock(order, 0, n, None, 0.0)[0]
        if best is None or span < best[0]:
            best = (span, order, eng[:])
        way = place(end, True, False)[1]
    for i in range(n):
        if eng[i] != best[2][i]:
            move(i, best[2][i])
    order = best[1]
    span, state = clock(order, 0, n, None, 0.0)
    pairs = chain(state)
    for turn in range(TURNS):
        if turn % AGAIN == AGAIN - 1:
            way = place([state[0][0][i] + views[0][0][i] + lat[i] for i in range(n)], True, False)[1]
            trial = sort(place(way, False, False)[0])
            s2, new = clock(trial, 0, n, None, 0.0)
            if s2 < span:
                order, span, state, pairs = trial, s2, new, chain(new)
        seed = (seed * 1103515245 + 12345) % 2147483648
        b, a = pairs[(seed >> 8) % len(pairs)]
        up = bool((seed >> 4) & 1)
        moved = (a if up else b) if (seed >> 5) % 3 == 0 and len(ways[a if up else b]) > 1 else None
        if moved is not None:
            was = eng[moved]
            to = [e for e in ways[moved] if e != was]
            move(moved, to[(seed >> 20) % len(to)])
            trial, i, mid = order, order.index(moved), [moved]
        else:
            i = order.index(b)
            mid = order[i:order.index(a) + 1]
            take = {a if up else b}
            for x in reversed(mid) if up else mid:
                if any(y in take for y in (succ[x] if up else pred[x])):
                    take.add(x)
            if (b if up else a) in take:
                continue
            trial = order[:i] + [x for x in mid if (x in take) == up] + [x for x in mid if (x in take) != up] + order[i + len(mid):]
        seed = (seed * 1103515245 + 12345) % 2147483648
        loss = -EASE * 0.125 ** (turn / TURNS) * math.log((seed + 1) / 2147483648)
        s2, new = clock(trial, i, i + len(mid), state, loss)
        if new and s2 <= span + loss:
            order, span, state, pairs = trial, s2, new, chain(new)
            best = min(best, (span, order, eng[:]))
        elif moved is not None:
            move(moved, was)
    return best[1:]


def rank_program(g, core, T, topo):
    rank = T.rank_of(core)
    if rank is None:
        _relay_program(g, core, T, topo)
        return
    E = {"v": g.vector, "p": g.tensor, "s": g.scalar, "k": g, "y": g.sync}
    v, sc = g.vector, g.scalar
    ops = []

    def u(name, lo=0, hi=None, st=1, p=None):
        buf, o, n, d = _AT[name]
        hi = n if hi is None else hi
        rows = slice(None) if p is None else slice(p[0], p[1])
        ap = T[buf][rows, o + lo:o + hi:st] if st != 1 else T[buf][rows, o + lo:o + hi]
        return (ap, [(buf, o + lo, o + hi)], -(-(hi - lo) // st), d, None)

    def e16(name, k=0, hi=None):
        return u(name, k, hi, 16)

    def ix(win, off):
        return (win[0].indirect(off[0]), win[1] + off[1], 16 * off[2], win[3], off)

    def mark(name, lo=0, hi=1, ap=None):
        return (ap, [(name, lo, hi)], 0, None, None)

    def op(e, fn, outs, ins, cost, dma=None, lat=0.0, items=None, land=None, alt=None):
        rd = [r for x in ins for r in x[1]] + [r for x in outs if x[4] for r in x[1][1:]]
        wr = [r for x in outs for r in (x[1][:1] if x[4] else x[1])]
        ways = {e: (fn, cost)}
        if alt:
            ways[alt[0]] = alt[1:]
        ops.append({"e": e, "fn": fn, "rd": rd, "wr": wr, "cost": cost, "dma": dma, "lat": lat, "items": items, "land": land, "ways": ways,
                    "how": 2 if outs[0][4] else 1 if ins and ins[0][4] else 0})

    def _c(x):
        return x[0] if isinstance(x, tuple) else x

    def _r(*xs):
        return [x for x in xs if isinstance(x, tuple)]

    def cost(o, ins, per):
        if o[4] or (ins and ins[0][4]):
            return 0.05 + o[2] * (SCA if o[4] else GAT) * CYC
        if per == 0.5 and any(x[3] not in (B, H, U) for x in [o] + ins):
            per = 1.0
        return 0.005 + max(64, o[2] * per) * CYC

    def scalar(o, i, f, **kw):
        if o[3] in (S, B) and i[3] in (S, B) and not o[4]:
            return ("s", lambda: sc.activation(o[0], i[0], f, **kw), cost(o, [i], 1.0) + 0.02)

    def cp(o, i):
        op("v", lambda: v.tensor_copy(o[0], i[0]), [o], [i], cost(o, [i], 0.5), alt=scalar(o, i, F.Copy))

    def ts(o, i, s1, o1, s2=None, o2=None):
        if o2 is None:
            alt = (scalar(o, i, F.Identity, scale=_c(s1)) if o1 == A.mult else scalar(o, i, F.Identity, bias=_c(s1)) if o1 == A.add
                   else scalar(o, i, F.Relu) if o1 == A.max and s1 == 0.0 else None)
            op("v", lambda: v.tensor_scalar(o[0], i[0], _c(s1), None, o1), [o], [i] + _r(s1), cost(o, [i], 0.5), alt=alt)
        else:
            alt = scalar(o, i, F.Identity, scale=_c(s1), bias=_c(s2)) if (o1, o2) == (A.mult, A.add) else None
            op("v", lambda: v.tensor_scalar(o[0], i[0], _c(s1), _c(s2), o1, o2), [o], [i] + _r(s1, s2), cost(o, [i], 0.5), alt=alt)

    def tt(o, a, b, o1):
        per = 1.0 if _psum(a[1][0][0]) or _psum(b[1][0][0]) else 2.0
        op("v", lambda: v.tensor_tensor(o[0], a[0], b[0], o1), [o], [a, b], cost(o, [a, b], per))

    def scan(o, a, b, o1, o2, init=0.0, alt=None):
        op("v", lambda: v.tensor_tensor_scan(o[0], a[0], b[0], _c(init), o1, o2), [o], [a, b] + _r(init), cost(o, [a, b], 0.5), alt=alt)

    def times(o, a, b):
        scan(o, a, b, A.min if a is b else A.max, A.mult, alt=scalar(o, a, F.Square) if a is b else None)

    def by_slot(o, a, many):
        for k in range(0, 16, many):
            for j in range(k, k + many):
                times(u(o, 128 * j, 128 * j + 128), a, e16("T", j))
            part = [ops.pop() for _ in range(many)][::-1]
            op("v", lambda part=part: [x["fn"]() for x in part], [u(o, 128 * k, 128 * (k + many))], [a, u("T")], sum(x["cost"] for x in part))

    def turn(o, i):
        op("v", lambda: v.transpose(o[0], i[0]), [o], [i], cost(o, [i], 0.5))

    def fill(o, c):
        kw = {} if o[3] == I else {"allow_small_or_imprecise_dtypes": True}
        alt = ("k", lambda: g.iota(o[0], [[0, o[2]]], int(c), 0, **kw), 0.13 + 2 * o[2] * CYC) if c == int(c) and abs(c) < 2 ** 24 else None
        op("v", lambda: v.memset(o[0], c), [o], [], cost(o, [], 0.5), alt=alt)

    def act(o, i, f, scale=None, bias=None, acc=None):
        kw = {k: _c(x) for k, x in (("scale", scale), ("bias", bias), ("accum_out", acc)) if x is not None}
        fn, per = None, 0.5
        if f in (F.Copy, F.Silu):
            fn = lambda: v.tensor_copy(o[0], i[0])
        elif f == F.Identity and acc is None:
            fn = lambda: v.tensor_scalar(o[0], i[0], kw.get("scale", 1.0), kw.get("bias", 0.0), A.mult, A.add)
        elif f in (F.Relu, F.Sign) and not kw:
            fn = lambda: v.tensor_scalar(o[0], i[0], 0.0, None, A.max if f == F.Relu else A.is_gt)
        elif f == F.Square and not _psum(i[1][0][0]):
            fn, per = lambda: v.tensor_tensor(o[0], i[0], i[0], A.mult), 2.0
        op("s", lambda: sc.activation(o[0], i[0], f, **kw), [o] + _r(acc), [i] + _r(scale, bias) + [mark("silu")] * (f == F.Silu), cost(o, [i], 1.0) + 0.02,
           alt=fn and ("v", fn, cost(o, [i], per)))

    def iota(o, pat, base, cm=0, after=None):
        kw = {} if o[3] == I else {"allow_small_or_imprecise_dtypes": True}
        alt = ("v", lambda: v.memset(o[0], base if o[3] == I else float(base)), cost(o, [], 0.5)) if pat == [[0, o[2]]] and not cm else None
        op("k", lambda: g.iota(o[0], pat, base, cm, **kw), [o], _r(after), 0.13 + 2 * o[2] * CYC, alt=alt)

    def select(o, i, pat, test, other, base, cm):
        op("k", lambda: g.affine_select(o[0], i[0], pat, test, other, base, cm), [o], [i], 0.2 + 2 * o[2] * CYC)

    def mm(out, *pairs, ends=(True, True), size=0):
        items = [(x[2] if len(x) > 2 else out, x[0], x[1]) for x in pairs]
        keys = [mark("keys")] if out[1][0][0] == "p3" else []
        size = size or len(items)
        flags = [(j % size == 0 and ends[0], j % size == size - 1 and ends[1]) for j in range(len(items))]
        op("p", flags, [x[0] for x in items] + keys, [y for x in items for y in x[1:]], sum(_cycles(a, b) for _o, a, b in items) * PEC, items=items)

    def dma(pairs, sem, kb):
        op("y", lambda: [g.sync.dma_start(o[0], i[0]) for o, i in pairs], [o for o, i in pairs], [i for o, i in pairs],
           max(0.1 * len(pairs), kb * PERKB), dma=sem, lat=START)

    def row(x, k):
        b, lo, hi = x[1][0]
        return (T[b][k:128:16, lo:hi],) + x[1:]

    def times_id(name, val):
        o = u(name) if isinstance(name, str) else name
        act(o, IDB, F.Identity, scale=val)
        ops[-1]["ways"]["k"] = (lambda: g.affine_select(o[0], IDB[0], [[-1, 128]], A.not_equal, val, 0, 1), 0.2 + 256 * CYC)

    def unfold(ps, first, step, src, at, j, n, rows=128):
        pairs = []
        for h in range(4):
            for m, w, lo, q in ((32, "YO", 32 * j, 1), (16, "IDB", 16 * j, 0)):
                pairs.append((u(w, lo, lo + m, 1, (0, rows)), u(src, at + 32 * h + 16 * q, at + 32 * h + 16 * q + n, 1, (0, rows)),
                              u(ps, first, first + step * (n - 1) + 1, step, (32 * h, 32 * h + m))))
        mm(pairs[0][2], *pairs, size=2)

    def send(src, buf, kind, t, way):
        dst, back = T.cores[(rank + way * (1 + t % 7)) % 8], T.cores[(rank - way * (1 + t % 7)) % 8]
        buf, sem, fwd, loc = buf + str(t), "r%s%d" % (kind, t), "f%s%d" % (kind, t), "l%s%d" % (kind, t)
        to, via = _relay(topo, core, dst, kind == "x"), _relay(topo, back, core, kind == "x")
        d = dst if to is None else to
        rid, pid = topo.addr(d, core)
        op("k", lambda: g.remote_dma(T[buf][:], src[0], T.sem[sem if to is None else fwd], T.sem[loc], pid, rid, topo.mask(core, d)),
           [u(buf)], [src], 0.3, lat=(WAY + (FIRST if t == 0 and kind != "h" else 0)) * (1 if to is None else 2) + LONG * (kind == "x"),
           land=(sem, len(topo.engines(back if via is None else via, core)), loc, len(topo.engines(core, d))))

    def sums(ps, base, src, w, by_slot=False):
        return [(u(src, 128 * k, 128 * k + 128) if by_slot else e16(src, k), w, u(ps, base + k, base + 128, 16)) for k in range(16)]

    def tile(z, h, ps, a, b, mask, *more):
        scan(u(h, 0, 128), u(mask), u(z, 0, 128), A.mult, A.add)
        mm(ps, (u(h, 0, 128), u(a)), (u(h, 1, 129), u(b)), (u(z, 1, 129), u(a)), *more)

    def low(z, key, hi, step):
        c = 1.5 * 2.0 ** 23 * step
        ts(hi, key, c, A.add, c, A.subtract)
        tt(z, key, hi, A.subtract)

    fill(u("X", 0, 16), 0.0)
    fill(u("X", 2048, 2216), 0.0)
    fill(u("X", 2216, 2224), 64.0)
    fill(u("AC4", 0, 8), 0)
    fill(u("AC4", 2048, 2192), 2048)
    dma([(u("MI"), mark("ml", ap=T.ml[:]))], "ld0", 256)
    dma([(u("X", 1, 2049), mark("x0", ap=T.x0[:]))], "ld1", 512)
    dma([(u("LI"), mark("lims", ap=T.lims[:])), (u("WI", 0, 1), mark("wt", ap=T.wt[:]))], "ld2", 60)
    dma([(u("AC4", 1 + 512 * q, 513 + 512 * q), mark("ac", ap=T.ac[:])) for q in range(4)], "ld3", 1024)
    J, J4, J15, J144, J8 = u("Jb", 0, 128), u("J4b"), u("J15b"), u("Jb"), u("Jb", 0, 8)
    P, P4, P15 = u("PC", 0, 1), u("PC", 1, 2), u("PC", 2, 3)
    IDB, NIDB, ONE, BD, NBD = u("IDB"), u("NIDB"), u("ONEB"), u("BD"), u("NBD")
    used = [16]

    def col(src, s1, o1, s2=None, o2=None):
        c = u("PC", used[0], used[0] + 1)
        used[0] += 1
        ts(c, src, s1, o1, s2, o2)
        return c
    iota(u("PIi", 0, 1), [[0, 1]], 0, 1)
    iota(J144, [[1, 144]], 0)
    iota(J15, [[0, 8], [1, 16]], 0)
    iota(J4, [[1, 8], [0, 16]], 0)
    iota(u("DUM"), [[16, COLS]], 2064, 1)
    for o, val in ((u("QZ"), 0), (u("DS", 640, 768), 0), (u("MIN5"), LOW), (e16("MIN5"), -LOW), (u("SO", 0, 512), 256), (u("OT", 0, 1), 0), (u("TAB", 0, 32), 0)):
        iota(o, [[0, o[2]]], val)
    FROM = 512 * len(BY_PE)
    if FROM < 2048:
        dma([(u("Z0", a, a + 512), u("QZ")) for a in range(FROM, 2048, 512)], "ld5", 512 - FROM // 4)
    fill(u("UD", 0, 512), 64.0)
    dma([(u("UD", a, a + 512), u("UD", 0, 512)) for a in range(512, 2048, 512)], "ld10", 384)
    for o, val in ((u("MS"), 1.0), (e16("MS"), 0.0), (u("W", 512, 640), 0.0)):
        fill(o, val)
    ts(u("PIi", 1, 2), u("PIi", 0, 1), 4, A.logical_shift_right)
    ts(u("PIi", 2, 3), u("PIi", 0, 1), 15, A.bitwise_and)
    cp(u("PC", 0, 3), u("PIi", 0, 3))
    ts(u("E16"), u("J15b", 0, 16), P15, A.is_equal)
    ts(u("EP", 0, 4), u("Jb", 0, 4), P, A.is_equal)
    row0, row4 = u("E16", 0, 1), u("E16", 4, 5)
    V0 = u("FREE", 256, 768)
    top4 = col(row4, 128.0, A.mult)
    first = [col(u("E16", c, c + 1), 64.0, A.mult, top4, A.add) for c in range(4)]
    for c in range(4):
        ts(u("FREE", 256 + c, 768, 4), J, row4, A.mult, first[c], A.add)
    every = col(P15, 4.0, A.is_lt, 64.0, A.mult)
    act(u("OT", 2049, 2064), u("MS", 0, 15), F.Identity, scale=0.0, bias=col(every, top4, A.add))
    ts(IDB, J, P, A.is_equal)
    ts(BD, J4, P4, A.is_equal)
    ts(u("blk"), J8, P4, A.is_equal)
    ts(u("R16"), J15, P15, A.is_equal)
    for name, src, val in (("nblk", "blk", -1.0), ("w64k", "blk", 65536.0), ("n64k", "blk", -65536.0), ("w32", "blk", 32.0),
                           ("NBD", "BD", -1.0), ("SEL0R", "BD", row0), ("SEL0", "blk", row0)):
        act(u(name), u(src), F.Identity, scale=val)
    for a, val in ((0, 64.0), (8, -2.0)):
        act(u("w64", a, a + 8), u("blk"), F.Identity, scale=val)
    for name, val in (("N40", -2.0 ** 40), ("IDF", 1.0), ("NIDB", -1.0), ("N27", -2.0 ** 27), ("N20", -2.0 ** 20), ("P23", 2.0 ** 23),
                      ("P768", 768.0), ("N11", -2.0 ** 11), ("RV0", 90.0 * TAU), ("RV1", 30.0 * TAU), ("RV2", 10.0 * TAU),
                      ("RV3", -54.0 * TAU), ("P20", 2.0 ** 20), (u("ID2", 128, 256), -1.0), ("IDh", 0.5)):
        times_id(name, val)
    op("s", lambda: sc.activation(u("P11")[0], IDB[0], F.Silu, scale=2.0 ** 11), [u("P11"), mark("silu")], [IDB], 1.5)
    act(u("CN1"), u("R16"), F.Identity, scale=8192.0, bias=-8192.0)
    ts(u("MC"), J15, P15, A.is_le)
    fill(e16("MC"), 0.0)
    fill(ONE, 1.0)
    for a in (0, 360):
        ts(u("ZALL", a, a + 360), u("MS", 0, 360), 0.0, A.mult)
    for name, slope, c1, c2 in (("KAs", 4096.0, 2.0 ** 27, -1088.0), ("KAb", -1.0, 2.0 ** 17 - 2.0 ** 23, 7.0), ("KAn", 512.0, -2.0 ** 24, 0.0), ("KQ5", 16.0, -0.25 if SCAN_I else -7.25, 0.0),
                                ("KAr", -1.0, 2048.0, 0.0), ("KAm", 0.0, 2.0 ** 21, -1536.0)):
        b = col(u("EP", 1, 2), c1, A.mult)
        if c2:
            ts(b, u("EP", 2, 3), c2, A.mult, b, A.add)
        ts(u(name, 0, 128), J15, col(u("EP", 0, 1), slope, A.mult), A.mult, b, A.add)
    b = col(u("EP", 1, 2), -128.0 * 160 * TAU, A.mult)
    ts(b, u("EP", 2, 3), -2.0 * 160 * TAU, A.mult, b, A.add)
    ts(b, u("EP", 3, 4), 81.0 * TAU, A.mult, b, A.add)
    ts(u("KAp"), u("MS", 0, 256), 0.0, A.mult, b, A.add)
    cp(u("KQ5", 128, 256), u("KQ5", 0, 128))
    for o, val in ((u("KAd"), 2 ** 20), (u("THZ"), 0), (u("MIN3"), LOW), (u("ZMW"), 0), (e16("KAd", 15), 0), (u("Pa", 256, 264), 2 ** 20), (u("Pb", 256, 264), 2 ** 20), (e16("MIN"), -LOW)):
        iota(o, [[0, o[2]]], val)
    fill(u("C25"), 2.0 ** 25)
    iota(e16("MINs"), [[0, 8]], 255 * 65536 + 2049 - 1088, 1)
    hw = col(P15, 4.0, A.is_lt, P15, A.mult)
    ts(hw, hw, 1.0 / 64, A.mult, col(row4, 4.0, A.mult), A.add)
    ts(u("HWN"), NBD, hw, A.mult)
    iota(u("DUL"), [[0, 16], [128, 8]], 2064 - 1536, 1)
    select(u("YO"), u("QZ", 0, 256), [[16, 8], [200, 2], [1, 16]], A.not_equal, 1.0, -200, -1)
    ts(u("kq", 0, 4), u("E16", 0, 4), 2.0 ** 19, A.mult, hw, A.add)
    at = col(P4, 16.0, A.mult, 15.0, A.add)
    for name, w in [("og%d" % c, u("kq", c, c + 1)) for c in range(4)] + [("w8k", 8192.0), ("YH", hw), ("YK", 1.0)]:
        ts(u(name), J144, at, A.is_equal, w, A.mult)
    select(u("TRIm"), u("N11"), [[-1, 128]], A.is_ge, 1.0, 0, 1)
    select(u("NTRIm"), u("P11"), [[-1, 128]], A.is_ge, -1.0, 0, 1)
    ts(u("b2"), IDB, -4.0, A.mult)
    ts(u("b1"), J, P, A.is_lt)
    select(u("BTU"), BD, [[-1, 128]], A.is_gt, 0.0, 0, 1)
    ts(u("b1"), u("b1"), -56.0, A.mult, -8.0, A.add)
    tt(u("PEN", 0, 128), u("b1"), u("b2"), A.add)
    cp(u("PEN", 128, 256), u("PEN", 0, 128))
    for name, src, val in (("w2", u("blk"), 2.0), ("B256", BD, 256.0), ("B512", BD, 512.0), ("N512", BD, -512.0)):
        ts(u(name), src, val, A.mult)
    for q, val in enumerate((640 - 2048, 128 - 2048)):
        ts(u("CNT", 128 * q, 128 * q + 128), u("R16"), 8192.0 + val, A.mult, -8192.0, A.add)
        ts(u("CTG", q, 256, 2), u("R16"), 8192.0 - (255.5 + 768, 256.0)[q], A.mult, -8192.0, A.add)
    ts(u("PENW"), u("R16"), -2.0 ** 17, A.mult, 2.0 ** 17, A.add)
    ts(u("PENK"), u("R16"), 2048 - 2.0 ** 17, A.mult, 2.0 ** 17, A.add)
    ts(u("PEN2", 0, 256, 2), u("R16"), 512 - 2.0 ** 17, A.mult, 2.0 ** 17, A.add)
    cp(u("PEN2", 1, 256, 2), u("PENW"))
    iota(u("M32"), [[0, 256]], 1)
    iota(u("M32", 0, 256, 32), [[0, 8]], 0)
    ts(u("b1"), J15, col(P15, 1.0, A.add), A.is_equal, 4096.0, A.mult)
    ts(u("b2"), u("R16"), -2.0 ** 20, A.mult)
    tt(u("WM"), u("b1"), u("b2"), A.add)
    held = col(P15, 15.0, A.is_lt, 4096.0, A.mult)
    spare = [col(P15, 2177.0 + 16 * q, A.add) for q in range(2)]
    cp(u("PB", 0, 1), P)
    fill(u("C3K"), 1088.0 - 4096.0)
    ts(u("KV"), J, 0.0, A.mult, -1023.5, A.add)
    ts(u("CIX"), u("Jb", 0, 32), 16.0, A.mult, P15, A.add)
    ts(u("CB"), u("CT"), 16.0, A.mult, 7.0, A.add)
    fill(u("MINR"), LOW)
    ts(e16("MINR"), u("CT"), 4.0, A.mult, 256.0, A.add)
    fill(u("MAXT"), -LOW)
    ts(u("MAXT", 0, 256, 32), u("CT"), -1.0, A.mult, -512.0, A.add)
    ts(u("sp4", 0, 4), u("Jb", 0, 4), col(P15, -9.0, A.add), A.is_equal, 4.0, A.mult)
    nine = col(P15, 9.0, A.is_lt)
    fill(u("two"), 2.0)
    scan(u("two"), u("two"), u("E16"), A.mult, A.add)
    half = col(u("two", 15, 16), 2.0 ** -16, A.mult)
    for q in range(2):
        ts(u("RH", 128 * q, 128 * q + 128), J, half, A.mult, 1536 + 2.0 ** -11 - 0.5 * q, A.add)
    scan(u("OCC"), u("RH", 0, 128), u("RH", 128, 256), A.max, A.subtract)
    twice, sign = col(nine, 2.0, A.mult), [col(nine, -1.0, A.mult)]
    for q in range(4):
        if q:
            sign.append(col(u("E16", 7 + q // 2, 8 + q // 2), 2.0, A.mult, sign[q - 1 - (q == 2) - (q == 3)], A.add))
        ts(u("CODE", 128 * q, 128 * q + 128), u("OCC"), twice, A.mult, sign[q], A.add)
    tt(u("CODE", 0, 4), u("CODE", 0, 4), u("sp4", 0, 4), A.add)
    fill(u("two"), 0.5)
    scan(u("two"), u("two"), u("E16"), A.mult, A.add)
    ts(u("WD"), NBD, col(u("two", 15, 16), 2.0 ** 14, A.mult, nine, A.mult), A.mult)
    ts(u("PIi", 3, 4), u("PIi", 1, 2), 1, A.bitwise_and)
    ts(u("PIi", 4, 5), u("PIi", 0, 1), 3, A.bitwise_and)
    ts(u("PIi", 5, 6), u("PIi", 0, 1), 1, A.bitwise_and)
    oddg = col(u("PIi", 3, 4), 1.0, A.mult)
    ts(u("kp4", 0, 4), u("sp4", 0, 4), 0.25, A.mult, nine, A.add)
    row15 = u("E16", 15, 16)
    four15 = col(row15, -4.0, A.mult)
    for c in range(4):
        ts(u("MK", 128 * c, 128 * c + 128), J, four15, A.mult, col(row15, -512.0 - c, A.mult), A.add)
    but15, top15 = col(P15, 15.0, A.is_lt), col(row15, 2216.0, A.mult)
    fill(u("H15"), 0.0)
    ts(e16("H15", 15), u("nblk"), hw, A.mult)
    odd = col(u("PIi", 5, 6), 1.0, A.mult)
    ts(u("MC2"), J15, col(odd, 8.0, A.mult, P4, A.add), A.is_le)
    fill(e16("MC2"), 0.0)
    ts(u("blk2"), J8, col(P15, odd, A.subtract, 0.5, A.mult), A.is_equal)
    ts(u("nblk2"), u("blk2"), -1.0, A.mult)
    for a in range(0, FROM, 512):
        select(u("EXA", a, a + 512), u("QZ"), [[1, 4], [16, 8], [0, 16]], A.not_equal, 1.0, a // 128, -1)
    ts(u("PC", 12, 14), u("LI"), -65536.0, A.mult)
    wt = col(u("WI", 0, 1), 1.0, A.mult)
    ts(u("WTp"), BD, wt, A.mult)
    less = col(u("EP", 1, 2), -2048.0, A.mult)
    ts(u("L2N"), u("SEL0"), u("PC", 13, 14), A.mult, less, A.add)
    ts(u("THN"), u("SEL0R", 0, 128, 8), u("PC", 12, 13), A.mult, less, A.add)
    ts(u("ROW1"), u("Jb", 0, 16), 0.0, A.mult, col(less, 32.0, A.mult), A.add)
    ts(u("w64d"), u("BD", 0, 128, 8), 65536.0, A.mult)
    for q in range(2):
        ts(u("PENB", 8 * q, 8 * q + 8), u("blk"), -2.0 ** 17, A.mult, 2.0 ** 17, A.add)
    for s in (1, 2, 3, 4, 8, 12):
        select(u("SH", 128 * s, 128 * s + 128), BD, [[1, 128]], A.is_equal, 0.0, -s, -1)
    fourth = col(u("PIi", 4, 5), 3.0, A.is_equal, -128.0, A.mult)
    first16, even, four = col(P4, 16.0, A.mult), col(P4, oddg, A.subtract), col(u("PIi", 4, 5), 1.0, A.mult)
    ts(u("b2"), J, col(even, 16.0, A.mult, 31.0, A.add), A.is_le)
    select(u("TR32"), u("b2"), [[1, 128]], A.is_ge, 0.0, 0, -1)
    for q in range(2):
        ts(u("SG%d" % q), J4, col(even, float(q), A.add) if q else even, A.is_equal, -1.0, A.mult)
        ts(u("SF%d" % q), J, col(even, 16.0, A.mult, 16.0 * q + 4, A.add), A.is_equal, 4.0, A.mult)
    here = col(four, first16, A.add)
    ts(u("LW0"), J, col(fourth, 1.0 / 32, A.mult, col(here, 1.0, A.add), A.add), A.is_equal, 64.0, A.mult)
    ts(u("LW1"), J, here, A.is_equal, -64.0, A.mult)
    ts(u("LW2"), J, col(first16, 4.0, A.add), A.is_equal, col(fourth, -1.0 / 128, A.mult), A.mult)
    fill(u("PX", 32, 48), 4096.0)
    fill(u("FREE", 0, 256), 0.0)
    ts(u("A4n"), BD, fourth, A.mult)
    ts(u("B4"), BD, col(fourth, 4.0, A.mult, 128.0, A.add), A.mult)

    X, LISTS, OWNERS = u("X", 0, 2224), u("W", 0, 512), u("OT", 0, 2064)

    def part_start():
        ts(u("PR5"), u("MI"), 2048, A.is_lt)
        ts(u("p6"), u("MI"), 1, A.add)
        tt(LISTS, u("p6"), u("PR5"), A.mult)
        up = col(P15, 0.0, A.is_gt, -1.0, A.mult)
        ts(u("UP"), J, col(P, -1.0, A.add), A.is_equal, up, A.mult)
        ts(u("UP11"), u("UP"), -2048.0, A.mult)
        scan(u("PF"), u("PR5"), u("PR5"), A.add, A.max)
        many = u("LL", 0, 1)
        ts(many, u("PF", 511, 512), 1.0 / 16, A.mult, 128.46875, A.add)
        mm(u("p4", 200, 201), (u("BTU"), many), (IDB, many))
        ends = col(u("p4", 200, 201), col(P15, -128.0, A.mult, 2048.0, A.add), A.subtract)
        ts(u("ZE"), J144, ends, A.is_ge, col(many, -1.0, A.mult, col(row0, -1024.0, A.mult, 128 - 1.0 / 32, A.add), A.add), A.mult)
        ts(u("JM"), J144, -256.0, A.add)
        mm(u("p4", 208, 208 + COLS), (IDB, u("JM")), (BD, u("ZE")), (IDB, u("PENW"), u("p4", 208, 336)), (IDB, u("PENW", 0, 16), u("p4", 336, 352)))
        mm(u("p4", 352, 352 + COLS), (IDB, u("JM")), (BD, u("ZE")))
        scan(u("TGS", 0, COLS), u("MS", 0, COLS), u("p4", 208, 208 + COLS), A.mult, A.min)
        ts(u("IX", 0, COLS // 16), e16("TGS", 15, COLS), 32.0, A.mult, col(oddg, 16.0, A.mult, 8192.0 + 47, A.add), A.add)
        ts(u("WP", 0, COLS), u("p4", 352, 352 + COLS), 1.5 * 2.0 ** 23 + 256, A.add, 1.5 * 2.0 ** 23, A.subtract)
        ts(u("PO"), u("WP", 0, COLS), 16.0, A.mult, P15, A.add)
        mm(u("p6", 440, 441), (u("UP"), u("PF", 511, 512)))
        mm(u("p5"), (IDB, u("PF")), (u("UP"), u("PF")), (u("N11"), u("PR5")), (u("UP11"), u("PR5")))
        ts(u("PF"), u("p5"), u("p6", 440, 441), A.subtract, 0.0, A.min)
        mm(u("p6", 448, 480), *[(u("YK", 15 - r, 143 - r), e16("PF", r)) for r in range(16)])
        ts(u("r1"), u("CIX"), -1535.0, A.add)
        tt(u("r2"), u("p6", 448, 480), u("r1"), A.min)
        ts(u("F16"), u("r2"), 2047.0, A.add)
        cp(ix(u("SO"), u("F16")), V0)
        mm(u("p6", 480, 512), *[(u("YH", 15 - r, 143 - r), u("SO", r, 512, 16)) for r in range(16)])
        for q in range(2):
            ts(u("HR", q, 64, 2), u("p6", 480, 512), -512.0, A.add)
        for a in (0, 512):
            cp(u("EV", a, a + 512), ix(u("W"), u("HR", a // 16, a // 16 + 32)))
            turn(u("TAB", 32 + a, 544 + a), u("EV", a, a + 512))
        cp(u("WP", 0, COLS), ix(u("TAB"), u("IX", 0, COLS // 16)))
        ts(u("p7", 0, COLS), u("WP", 0, COLS), -8192.0, A.mult, 8192.0, A.add)
        tt(u("p7", 256, 256 + COLS), u("DUM"), u("p7", 0, COLS), A.min)
        tt(u("TGS", 0, COLS), u("WP", 0, COLS), u("p7", 256, 256 + COLS), A.max)
        cp(u("INO"), u("TGS", 0, COLS))
        for a, b in zip((0,) + CUT_I, CUT_I + (COLS,)):
            cp(u("PAY", 16 * a, 16 * b), ix(u("SO", 0, 512), u("PO", a, b)))
            act(ix(u("OT"), u("INO", a, b)), u("PAY", 16 * a, 16 * b), F.Silu)

    def gather(out, win, off, cuts, many, neg=False):
        for k, (a, b) in enumerate(zip((0,) + cuts, cuts + (128,))):
            if neg:
                act(u(out, 16 * a, 16 * b), ix(win, u(off, a, b)), F.Identity, scale=-1.0)
            elif k < many:
                cp(u(out, 16 * a, 16 * b), ix(win, u(off, a, b)))
            else:
                act(u(out, 16 * a, 16 * b), ix(win, u(off, a, b)), F.Copy)

    def part_own(t):
        s1 = "S1%d" % (t % 2)
        lanes = u("W", t % 4, 512, 4)
        cp(u("OWN"), lanes)
        gather("T", X, "OWN", CUT_T, 0, True)
        ts(u("OWNH"), lanes, 0.0, A.max)
        ts(u("PRE"), u("OWNH"), 0.0, A.is_gt)
        k = u("p3", 0, 128)
        mm(k, (ONE, u("KAs")), (u("PRE"), u("N27")), (u("OWNH"), IDB), *sums("p3", 0, "T", u("n64k")))
        scan(u(s1), u("MINs"), k, A.max, A.min)
        low(e16("ZS", 0, 128), e16(s1, 15), u("hi8"), 4096)
        tile("ZS", "HS", u("p4", 0, 8), "blk", "nblk", "MC")
        ts(u("S16"), u("p4", 0, 8), 1088.0, A.add)
        cp(u("ZP%d" % (t % 2)), ix(X, u("S16")))
        send(u("ZP%d" % (t % 2)), "QA", "a", t, 1)
        tile("ZS", "HD", u("p4", 24, 32), "blk2", "nblk2", "MC2")
        ts(u("A16"), u("p4", 24, 32), 1088.0, A.add)
        ts(u("AN"), ix(u("AC4"), u("A16")), 1, A.add)
        if FROM < 2048:
            cp(u("Z0", FROM, 2048, 16), ix(X, u("A16", FROM // 256, 8)))
        for a in range(0, 2048, CUT_S):
            if a >= FROM:
                scan(u("REP", a, a + CUT_S), u("MS", 0, CUT_S), u("Z0", a, a + CUT_S), A.mult, A.add)
            scan(u("US", a, a + CUT_S), u("MS", 0, CUT_S), u("T", a, a + CUT_S), A.mult, A.min)
        ts(e16("UD"), e16("US", 15), -1.0, A.mult)
        mm(u("p4", 8, 16), (ONE, u("L2N")), (e16("US", 15), u("n64k")))
        tt(u("wp8"), e16(s1, 15), u("p4", 8, 16), A.is_ge)
        mm(u("p6", 0, 128), (u("PRE"), u("SEL0R")))
        act(u("LR"), u("p6", 0, 128), F.Copy)
        mm(u("p6", 160, 288), (IDB, u("CN1")), (u("PRE"), u("B4")))
        act(u("QB"), u("p6", 160, 288), F.Relu)
        mm(u("p4", 144, 152), (IDB, u("CT")), (u("QB"), u("blk")))
        cp(u("BT16"), u("p4", 144, 152))

    def part_vacant(t):
        b, lo, hi = LISTS[1][0]
        dma([(u("OCf", 16 * q, 16 * q + 16), (T[b][16 * q:128:32, lo:hi],) + LISTS[1:]) for q in range(2)], "oc%d" % t, 40)
        ts(u("OCg"), u("OCf"), 0.0, A.is_le)
        turn(u("OCb"), u("OCg"))
        mm(u("p4", 32, 64), (BD, u("OCb")))
        mm(u("p4", 64, 96), (u("BTU"), u("OCb")))
        scan(u("CS"), u("ONEB", 0, 32), u("p4", 32, 64), A.mult, A.add)
        tt(u("PX", 0, 32), u("CS"), u("p4", 64, 96), A.subtract)
        ts(u("NFF"), u("SEL0R"), u("CS", 31, 32), A.mult, -1.0, A.mult)
        scan(u("OCt"), u("MS", 0, 32), u("OCg"), A.mult, A.add)
        mm(u("p4", 96, 98), (u("TR32"), e16("OCt", 15)))
        for q in range(2):
            ts(u("MB", 128 * q, 128 * q + 128), J, u("p4", 96 + q, 97 + q), A.is_ge)
        a, b = u(BANK_V[0], BANK_V[1], BANK_V[1] + 128), u(BANK_V[0], BANK_V[1] + 128, BANK_V[1] + 256)
        mm(a, (IDB, u("PENW")), *[(u("SG%d" % q), u("MB", 128 * q, 128 * q + 128)) for q in range(2)])
        scan(u("VB"), u("MS", 0, 128), a, A.mult, A.min)
        ts(u("V16"), e16("VB", 15), -1.0, A.mult)
        tt(u("MJ"), ix(u("PX"), u("V16")), J, A.is_le)
        mm(b, *[(u("SF%d" % q), u("MB", 128 * q, 128 * q + 128)) for q in range(2)], *[(u("LW%d" % q), u("MJ")) for q in range(3)])
        act(u("FREE", t % 4, t % 4 + 128), b, F.Identity, bias=first[0])

    def part_split(t):
        s = u("ZP%d" % (t % 2))
        mm(u("p6", 288, 416), (s, NIDB))
        act(u("ST"), u("p6", 288, 416), F.Copy)
        for a in range(0, 2048, 512):
            x = u("T", a, a + 512)
            times(u("SQ", a, a + 512), x, x)
        by_slot("AW", s, 4)
        act(u("SQS"), s, F.Square)
        k, lv = u("p7", 0, 128), u(BANK_L[0], BANK_L[1], BANK_L[1] + 128)
        mm(k, (u("PRE"), u("P23")), (ONE, u("KAb")), *sums("p7", 0, "SQ", u("w32")), *sums("p7", 0, "AW", u("w64", 0, 8), True))
        scan(u("SB"), u("MS", 0, 128), k, A.mult, A.max)
        low(e16("ZB", 0, 128), e16("SB", 15), u("hb8"), 32)
        tile("ZB", "HB", u("p4", 16, 24), "nblk", "blk", "MC", (IDB, u("CB")))
        cp(u("B16"), u("p4", 16, 24))
        act(u("XB"), ix(u("T"), u("B16")), F.Identity, scale=-1.0)
        act(u("SQB"), u("XB"), F.Square)
        by_slot("AB", u("XB"), 4)
        mm(lv, (u("PRE"), u("N20")), (u("SQS"), NBD), *sums(*BANK_L, "AW", u("w64", 8, 16), True), (u("SQB"), BD), *sums(*BANK_L, "AB", u("w2"), True))
        ts(u("LN", 0, 128), lv, -2.0 ** 20, A.is_lt)
        ts(u("LN", 128, 256), lv, -2.0 ** 20, A.is_ge)
        scan(u("XC"), u("MS", 0, 256), u("LN"), A.mult, A.add)
        for q in range(3):
            ts(u("XF", 256 * q, 256 * q + 256), u("XC"), 0.5 ** (q + 1), A.mult, 159.5 + 0.5 ** (q + 2), A.add)
        pp = u("p7", 256, 512)
        mm(pp, (ONE, u("KAp")), (u("P20"), u("LN")), (u("RV3"), u("XC")),
           *[(u("RV%d" % q), u("XF", 256 * q, 256 * q + 256)) for q in range(3)], (u("OWNH"), u("ID2")))
        act(u("Pa", 0, 256), pp, F.Abs, bias=-54.0 * TAU)
        tt(u("Pa", 0, 255), u("p7", 257, 512), u("Pa", 0, 255), A.min)
        for q, a, b in ((1, "Pa", "Pb"), (2, "Pb", "Pa"), (3, "Pa", "Pb")):
            act(u(*BANK_S), u(a, 0, 256), F.Abs, bias=-2.0 * 3 ** (3 - q) * TAU)
            tt(u(b, 0, 256), u(*BANK_S), u(a, 1 << q, 256 + (1 << q)), A.min)
        ts(u("SL"), u("Pb", 0, 256), TAU, A.min, TAU, A.subtract)

    def part_near(t):
        iota(e16("MINn"), [[0, 8]], 13 * 2 ** 20 + t % 4)
        gather("OG", OWNERS, "AN", CUT_O, 0 if t else 2)
        k = u("p3", 256, 384)
        mm(k, (ONE, u("KAn")), *[(u("og%d" % (t % 4), 15 - r, 143 - r), u("OG", 128 * r, 128 * r + 128)) for r in range(16)], ends=(True, False))
        for c, (a, b) in enumerate(zip((0,) + CUT_A, CUT_A + (128,))):
            if c in BY_PE:
                act(u("AX", 16 * a, 16 * b), ix(X, u("AN", a, b)), F.Copy)
                ps = u(BANK_A[c], 0, 16 * (b - a))
                mm(ps, (u("ST"), u("EXA", 16 * a, 16 * b)), (IDB, u("AX", 16 * a, 16 * b)))
                act(u("DU", 16 * a, 16 * b), ps, F.Square)
            else:
                tt(u("AX", 16 * a, 16 * b), ix(X, u("AN", a, b)), u("REP", 16 * a, 16 * b), A.subtract)
                act(u("DU", 16 * a, 16 * b), u("AX", 16 * a, 16 * b), F.Square)
            mm(k, *[(u("w8k", 15 - r, 143 - r), u("DU", 128 * r, 128 * r + 128)) for r in range(a // 8, b // 8)], ends=(False, b == 128))
        if SCAN_I:
            scan(u("S2i"), u("MINn"), k, A.max, A.min)
            ts(u("d8"), e16("S2i", 15), 511, A.bitwise_and)
        else:
            scan(u("S2"), u("MINn"), k, A.max, A.min)
            cp(u("a8"), e16("S2", 15))
            ts(u("d8"), u("a8"), 511, A.bitwise_and)
        cp(u("D16"), u("d8"))

    def part_partner(t):
        lists = ix(LISTS, u("D16"))
        ts(u("DM"), lists, but15, A.mult, top15, A.add)
        gather("DT", X, "DM", CUT_D, 2)
        ts(u("DMH"), lists, 0.0, A.max)
        ts(u("PRD"), u("DMH"), 0.0, A.is_gt)
        act(u("CG", 0, 128), ix(u("CODE"), u("D16")), F.Identity, scale=u("kp4", t % 4, t % 4 + 1))
        ts(u("CG", 128, 256), u("CG", 0, 128), oddg, A.mult)
        for h, (ps, a) in enumerate(BANK_E):
            parts = [u("CG", 128 * q, 128 * q + 128, 1, (32 * h, 32 * h + 16 + 16 * q)) for q in range(2)]
            mm(u(ps, a, a + 256), (IDB, u("PEN")), *[(x, x, u(ps, a + 128 * q, a + 128 * q + 128)) for q, x in enumerate(parts)])
            act(u("EQ", 256 * h, 256 * h + 256), u(ps, a, a + 256), F.Relu)
        mm(u("p6", 416, 432), (u("PRE"), u("BD", 0, 128, 8)), (u("PRD"), u("BD", 0, 128, 8)))
        act(u("SZ"), u("p6", 416, 432), F.Relu, scale=32.0, bias=-512.0)
        for a in range(0, 2048, 512):
            scan(u("AX", a, a + 512), u("UD", a, a + 512), u("DT", a, a + 512), A.min, A.max, 64.0)
        k = u("p3", 384, 512)
        mm(k, (ONE, u("KAd")), (u("PRD"), u("N27")), (u("IDF"), e16("S1%d" % (t % 2), 15), e16("p3", 399)), *sums("p3", 384, "DT", u("w64k"))[:15])
        mm(u("p4", 160, 176), (ONE, u("THN")), (ONE, u("THZ")), (u("N40"), u("wp8"), u("p4", 161, 176, 2)), (u("P23"), u("SZ")),
           *[(u("EQ", 128 * q, 128 * q + 128), u("C25", 0, 2), u("p4", 160 + 2 * q, 162 + 2 * q)) for q in range(8)], (e16("AX", 14), u("w64d")))
        scan(u("S3"), u("MIN"), k, A.max, A.min)
        for src, step, out in (("DMH", 1, "D1"), ("DM2", 4, "DS")):
            mm(u(BANK_D), *[(u("SH", 128 * step * q, 128 * step * q + 128) if q else IDB, u(src), u(BANK_D, 128 * q, 128 * q + 128)) for q in range(4)], size=1)
            act(u(out, 0, 512), u(BANK_D), F.Copy)
            if step == 1:
                cp(u("DM2"), ix(u("D1"), u("BT16")))

    def part_finish(t):
        cl, ev = t % 4, u("EVB")
        MR, WR, SR = u("MR"), u("WR"), u("SR")
        tt(e16("ZM"), e16("S3", 15), u("p4", 160, 176, 2), A.is_ge)
        tt(e16("ZW"), e16("S3", 15), u("p4", 161, 176, 2), A.is_lt)
        scan(u("MWR"), u("MS", 0, 256), u("ZMW"), A.mult, A.add)
        k0, k1, k2 = u("p7", 384, 512), u("p0", 256, 384), u("p7", 0, 128)
        mm(k0, (ONE, u("NFF")), (u("TRIm"), WR))
        mm(k1, (IDB, u("PENK")), (WR, u("TRIm")))
        ts(SR, k0, -2048.0, A.is_lt)
        scan(u("KR"), u("MINR"), k1, A.max, A.min)
        ts(u("RK"), e16("KR", 15), float(cl), A.add)
        mm(k2, (ONE, u("KAr")), (u("TRIm"), u("LR")), (u("NTRIm"), MR), (u("NTRIm"), SR))
        for q in range(2):
            ts(u("EE", 128 * q, 128 * q + 128), k2, 16.0 * q, A.is_equal)
            mm(u("p4", 104 + q, 105 + q), (u("EE", 128 * q, 128 * q + 128), u("PB", 0, 1)))
        cp(u("SE"), u("p4", 104, 106))
        cp(e16("QZ"), ix(u("ZP%d" % (t % 2)), u("SE")))
        for a in (0, 256):
            scan(u("QRp", a, a + 256), u("MS", 0, 256), u("QZ", a, a + 256), A.mult, A.add)
        mm(u("p4", 176, 192), (IDB, u("PENB")), *[(u("EE", 128 * q, 128 * q + 128), x, u("p4", 176 + 8 * q, 184 + 8 * q))
                                                  for q in range(2) for x in (u("C3K"), e16("ZS", 0, 128))])
        scan(u("SV"), u("MS", 0, 32, 2), u("p4", 176, 192), A.mult, A.min)
        for q in range(2):
            ts(u("S32", q, q + 1), u("SV", 8 * q + 7, 8 * q + 8), 4096.0, A.add, spare[q], A.min)
        a, b = u("p6", 0, 128), u("p6", 128, 256)
        mm(u("p6", 0, 256), (IDB, u("CNT")), (u("PRE"), u("A4n"), a), (u("P11"), MR, a), (u("P11"), SR, b))
        act(u("QN"), u("p6", 0, 256), F.Relu)
        mm(u("p4", 120, 128), (IDB, u("CT")), (u("QN", 0, 128), u("nblk")), (u("QN", 128, 256), u("nblk")))
        ts(u("NT16"), u("p4", 120, 128), 640.0, A.add)
        act(ev, ix(u("FREE"), u("RK")), F.Copy)
        mm(u("p6", 288, 416), (u("SL", 0, 128), NIDB), (NIDB, u("OWNH")), (u("H15"), ev))
        cp(u("DS", 512, 640), u("p6", 288, 416))
        tt(u("W", cl, 512, 4), ix(u("DS"), u("NT16")), u("OWNH"), A.add)
        a, b = u("p0", 0, 256, 2), u("p0", 1, 256, 2)
        mm(u("p0", 0, 256), (IDB, u("CTG")), (u("WD"), u("CG", 0, 128), a), (MR, u("P768"), a), (SR, u("P768"), b), (u("HWN"), ev, b))
        scan(u("TGS"), u("MAXT"), u("p0", 0, 256), A.min, A.max)
        ts(u("TG16"), u("TGS", 31, 256, 32), -1.0, A.mult)
        mm(u("p1", 0, 128), (u("SL", 128, 256), NIDB), (MR, u("N20")))
        tt(u("ELS"), u("p1", 0, 128), u("MK", 128 * cl, 128 * cl + 128), A.max)
        cp(ix(u("W"), u("TG16")), u("ELS"))
        if t + 1 == RO:
            return
        a, b = u("p7", 128, 256), u("p7", 256, 384)
        mm(a, (ONE, u("KAm")), (u("DMH"), IDB), (u("PRD"), u("N20")), (u("N20"), MR))
        if MOVERS == 15:
            ts(u("PRL"), u("SL", 128, 256), 0.0, A.is_lt)
            mm(b, (ONE, u("KAm")), (NIDB, u("SL", 128, 256)), (u("N20"), u("PRL")), (u("N20"), SR))
        else:
            mm(b, (ONE, u("KAm")), (u("OWNH"), IDB), (u("N20"), u("LN", 0, 128)), (u("N20"), SR))
        tt(u("m1"), a, u("DUL"), A.min)
        tt(u("m2"), b, u("m1"), A.min)
        for j in range(8):
            unfold("p1", 128 + j, 8, "m2", 0, j, MOVERS)
        ts(u("MVO", 0, 8 * MOVERS), u("p1", 128, 128 + 8 * MOVERS), 1536.0, A.add)
        cp(u("EV", 0, 128), ev)
        cuts = list(zip((0,) + CUT_M, CUT_M + (MOVERS,)))
        many = max(b - a for a, b in cuts)
        dma([(u("EW", 128 * q, 128 * q + 128), u("EV", 0, 128)) for q in range(1, many)], "ev%d" % t, 64 * (many - 1))
        for a, b in cuts:
            act(ix(u("OT"), u("MVO", 8 * a, 8 * b)), u("EW", 0, 128 * (b - a)), F.Silu)
        mm(u("p6", 432, 440), (ONE, e16("ZM")))
        act(u("z8"), u("p6", 432, 440), F.Identity, bias=-0.9375, acc=u("mc", 0, 1))
        ts(u("mc", 1, 2), u("mc", 0, 1), 1.5 * 2.0 ** 27, A.add, 1.5 * 2.0 ** 27, A.subtract)
        ts(u("mc", 2, 3), u("mc", 0, 1), u("mc", 1, 2), A.subtract, 7.5, A.add)
        act(u("THZ"), u("ROW1"), F.Identity, scale=u("mc", 2, 3))

    def part_look(t):
        qa, a, b, c = u("QA%d" % t), u("p5", 256, 384), u("p5", 384, 512), u("p5", 256, 384)
        mm(a, (IDB, u("KV")), (u("WTp"), qa))
        mm(b, (IDB, ONE), (u("WTp"), qa))
        ts(u("VH"), a, 1.5 * 2.0 ** 34, A.add, 1.5 * 2.0 ** 34, A.subtract)
        tt(u("VR"), b, u("VH"), A.subtract)
        scan(u("WP", 0, 128), u("WM"), u("VR"), A.add, A.max)
        ts(u("VV16"), e16("WP", 15, 128), held, A.subtract)
        act(u("HO"), ix(OWNERS, u("VV16")), F.Copy)
        mm(c, (IDB, u("PENW")), (u("HWN"), u("HO")))
        scan(u("WP", 0, 128), u("MS", 0, 128), c, A.mult, A.min)
        ts(u("O16"), e16("WP", 15, 128), -1.0, A.mult, -512.0, A.add)

    def part_host(t):
        ts(u("PA"), ix(LISTS, u("O16")), 0.0, A.min)
        tt(u("EH"), ix(LISTS, u("O16")), u("VR"), A.is_equal)
        a, b = u("p2", 0, 256, 2), u("p2", 1, 256, 2)
        mm(u("p2", 0, 256), (IDB, u("PEN2")), (u("HWN"), u("HO"), a), (BD, u("PA"), b), (u("N512"), u("EH"), a), (u("B512"), u("EH"), b))
        scan(u("WP"), u("M32"), u("p2", 0, 256), A.mult, A.min)
        ts(u("H16"), u("WP", 31, 256, 32), -1.0, A.mult, -512.0, A.add)
        cp(u("HLA"), ix(LISTS, u("H16")))
        send(u("HLA"), "HQ", "h", t, -1)

    def part_meet(t):
        fill(u("XQ%d" % t, 0, 1), -64.0)
        cp(u("HL"), ix(u("HQ%d" % t), u("SE")))
        for a, b, ps in ((0, 256, u("p5", 0, 256)), (256, 512, u(BANK_Q, 256, 512))):
            tt(u("QD", a, b), ix(u("XQ%d" % t), u("HL", a // 16, b // 16)), u("QRp", a, b), A.subtract)
            act(u("QS", a, b), u("QD", a, b), F.Square)
            mm(ps, (ONE, u("KQ5")), (IDB, u("QRp", a, b)), (u("IDh"), u("QD", a, b)), (u("B256"), u("QS", a, b)))
            scan(u("QRi", a, b), u("MIN5"), ps, A.max, A.min)
        ts(u("SN"), e16("QRi", 15), 15, A.bitwise_and)

    def part_apply(t):
        cp(ix(X, u("S32")), u("SN"))

    part_start()
    for t in range(RO):
        part_own(t)
        part_vacant(t)
        part_split(t)
        if t:
            part_apply(t - 1)
        send(u("X", 0, 2064), "XQ", "x", t, -1)
        part_near(t)
        part_partner(t)
        part_look(t)
        part_finish(t)
        part_host(t)
        if t + 1 == RO:
            ts(u("t512a"), LISTS, 0.0, A.is_le, 2048.0, A.mult)
            act(u("p1"), LISTS, F.Identity, bias=-1.0)
            tt(u("YM"), u("t512a"), u("p1"), A.max)
            dma([(mark("ym", ap=T.ym[:]), u("YM"))], "st0", 256)
        part_meet(t)
    part_apply(RO - 1)
    dma([(mark("yx", ap=T.yx[:]), u("X", 1, 2049))], "st1", 512)

    if "o" not in _ORDER:
        _ORDER["o"] = _order(ops)
    cnt = {"v": 0, "p": 0, "s": 0, "k": 0}
    known = {e: {} for e in E}
    snap, log, total = {}, {}, {}

    def wait(e, reads, writes):
        w = {}
        for kind, lst in ((0, reads), (1, writes)):
            for (b, lo, hi) in lst:
                for (l2, h2, e2, sem, val, wr) in log.get(b, ()):
                    clash = lo < h2 and l2 < hi and (kind or wr)
                    if (e2 != e or (e != "p" and clash)) if _psum(b) else clash:
                        w[sem] = max(w.get(sem, 0), val)
        for sem, val in w.items():
            if known[e].get(sem, 0) < val:
                E[e].wait_ge(T.sem[sem], val)
                known[e][sem] = val
                for s2, v2 in snap.get((sem, val), {}).items():
                    known[e][s2] = max(known[e].get(s2, 0), v2)

    def note(e, reads, writes, sem, val):
        snap[(sem, val)] = dict(known[e])
        total[sem] = val
        for (b, lo, hi) in writes:
            log[b] = [x for x in log.get(b, []) if not (lo <= x[0] and x[1] <= hi and (x[2] == e or not _psum(b)))] + [(lo, hi, e, sem, val, True)]
        for (b, lo, hi) in reads:
            log[b] = [x for x in log.get(b, []) if not (x[2] == e and not x[5] and lo <= x[0] and x[1] <= hi and x[3] == sem)] + [(lo, hi, e, sem, val, False)]

    order, queues = _ORDER["o"]
    for i in order:
        o = ops[i]
        e, rd, wr = queues[i], o["rd"], o["wr"]
        o["fn"] = o["ways"][e][0]
        if o["land"]:
            sem, landed, loc, left = o["land"]
            wait(e, rd, [])
            o["fn"]()
            note(e, rd, [], loc, left)
            snap[(loc, left)] = {}
            log[wr[0][0]] = [(wr[0][1], wr[0][2], "far", sem, landed, True)]
            total[sem] = landed
            continue
        if o["items"]:
            wr = [x for x in wr if _psum(x[0])]
            wait(e, [], wr)
            for j, (x, a, b) in enumerate(o["items"]):
                wait(e, a[1] + b[1], [])
                ins = g.tensor.matmul(x[0], a[0], b[0], *o["fn"][j])
        else:
            wait(e, rd, wr)
            ins = o["fn"]()
        if o["dma"]:
            for x in ins:
                x.then_inc(T.sem[o["dma"]], 16)
            note(e, rd, wr, o["dma"], 16 * len(ins))
        else:
            for x in ins if isinstance(ins, list) else [ins]:
                cnt[e] += 1
                x.then_inc(T.sem[e], 1)
            note(e, rd, wr, e, cnt[e])
    for sem, n in total.items():
        if known["k"].get(sem, 0) < n:
            g.wait_ge(T.sem[sem], n)
